import numpy as np, ml_dtypes
CORES = [3,11,19,27,35,43,51,59]
N = 8
BF = ml_dtypes.bfloat16
def gentries(a):
    return np.ascontiguousarray(a.reshape(8, 16, -1).transpose(0, 2, 1)).reshape(8, -1)
def gtable(e):
    e = np.asarray(e); return np.ascontiguousarray(e.reshape(8, -1, 16).transpose(0, 2, 1)).reshape(128, -1).astype(np.int32)
R, L, W, RO = 128, 32, 8192, 3
H, SP = L // 2, W // R
def parts(rng):
    X = (rng.integers(0, 256, (N, 8, 16, W)) * rng.integers(64, 257, (N, 8, 1, W))) >> 8
    A = rng.integers(0, W, (N, 8, R, L))
    z = np.maximum(rng.integers(0, 256, (N, 8, 16, R)), rng.integers(0, 256, (N, 8, 1, R)) * rng.integers(0, 2, (N, 8, 1, R)))
    w = rng.integers(0, 256, (N, 8, 16)); T = np.exp2(4 + 5.5 * rng.random((N, 8))).astype(np.int64)
    return X, A, z, w, T
def pack(X, A, z, w, T):
    return {"xd": np.ascontiguousarray(X.reshape(N, 128, W)).astype(np.float32).astype(BF), "ra": np.stack([gtable(a.reshape(8, -1)) for a in A]),
            "zu": np.ascontiguousarray(z.reshape(N, 128, R)).astype(np.float32).astype(BF), "wg": np.ascontiguousarray(w.reshape(N, 128, 1)).astype(np.int32),
            "th": np.repeat(T.reshape(N, 8, 1), 16, axis=2).reshape(N, 128, 1).astype(np.int32)}
def setup_inputs(rng):
    return pack(*parts(rng))
def setup_inputs_ties(rng):
    X, A, z, w, T = parts(rng); m = rng.integers(2, 254 // L + 1, (N, 8)); k = np.arange(L)
    at = rng.integers(0, 16, (N, 8, 1, W)); e = rng.integers(-1, 2, (N, 8, 1, W))
    X = m[:, :, None, None] * (1 + np.arange(W) % L) + e * (np.arange(16)[:, None] == at)
    lev = (2 * k[None, :] + ((np.arange(N) // 2) % 2)[:, None]) % L
    A = L * rng.integers(0, W // L, (N, 8, R, L)) + lev[:, None, None, :]
    o = rng.permutation(8); T = m * np.array([16, 16, 32, 32, 0, 0, 16, 16])[o] + np.array([0, 0, 0, 0, 1, 2, 1, -1])[o]
    z = np.where(rng.random((N, 8, 1, R)) < 0.75, 255, z)
    return pack(X, A, z, w, T)
def setup_inputs_near(rng):
    X0, A, z, w, T = parts(rng); o = [int(v) for v in rng.permutation(8)]; q = [int(v) for v in rng.permutation(N)]; p = (q[1] - 1) % N
    T = rng.integers(2049, 4081, (N, 8)); T[:, o[1]] = 4080; T[:, o[2]] = 2049; T[:, o[3]] = 4 * rng.integers(513, 1020, N)
    e = np.array([-1, 0, 1, -1])[np.arange(W) % 4]
    m = np.maximum(4080 - T[:, :, None] - e, 0)[:, :, None, :]; b = m >> 4
    v = rng.integers(-b, b + 1, (N, 8, 8, W))
    X = 255 - np.concatenate([b + v, b - v], axis=2) - (((np.arange(16)[:, None] + rng.integers(0, 16, (N, 8, 1, W))) & 15) < (m & 15)).astype(np.int64)
    z = np.where(rng.random((N, 8, 1, R)) < 0.75, 255, z); z[p] = 255; z[:, o[0]] = 255
    for r in range(N):
        n = 3 * R - 1 if r == p else int(rng.integers(R, 6 * R))
        yes = (rng.permutation(7 * R) < n).reshape(7, R); c = 4 * rng.integers(0, W // 4, (7, R)); i = rng.integers(0, 2, (7, R))
        A[r, o[1:], :, 0] = np.where(yes, c + 1 + i, np.where(rng.random((7, R)) < 0.5, c + 3 * i, (W - 1) * i))
    X[:, o[0]] = np.arange(W) * 256 // W; T[:, o[0]] = rng.integers(1, 17, N); S = W // (H + 1)
    low = ((np.arange(N) // 2) % 2 == 0)[:, None, None]
    A[:, o[0], :, :H] = np.where(low, 0, S * (1 + np.arange(H)) + rng.integers(0, S // 2, (N, R, H)))
    X[q[0]] = X0[q[0]]; X[q[0], :, :, 31::32] = 255; T[q[0]] = 4080
    for g in range(8):
        f = int(rng.integers(0, 16)); X[q[0], g, f] = np.minimum(X[q[0], g, f], 254)
    return pack(X, A, z, w, T)
def setup_inputs_corners(rng):
    X, A, z, w, T = parts(rng); o = [int(v) for v in rng.permutation(8)]; q = rng.permutation(N)
    A[:, o[0]] = A[:, o[0], :, :1].copy(); T[:, o[0]] = 1
    A[:, o[1]] = rng.choice(np.array([0, W - 1]), (N, R, L))
    z[:, o[2], :, ::2] = 0; z[:, o[2], :, 1::4] = 255; T[:, o[2]] = np.arange(N) % 2
    X[:, o[3], :, ::3] = 255; z[:, o[3]] = 255; T[:, o[3]] = 4080
    w[:, o[4]] = 0
    w[:, o[5]] = 255; z[:, o[5]] = 255; X[:, o[5]] = np.where(rng.random((N, 1, W)) < 0.5, 255, X[:, o[5]])
    A[:, o[6]] = A[0, o[6], 0].copy()
    A[:, o[7]] = np.sort(A[:, o[7]], axis=-1); X[:, o[7]] = np.arange(W) * 240 // W + rng.integers(0, 16, (N, 16, W)); z[:, o[7]] = 255; T[:, o[7]] = 1
    T[q[0]] = 0; T[q[1]] = 4080
    return pack(X, A, z, w, T)
def setup_inputs_ends(rng):
    c = rng.integers(0, 3, (N, 8, 1, W)); X = 255 * np.where(c == 2, rng.integers(0, 2, (N, 8, 16, W)), c)
    X[:, 7, :, W - 1] = 255; X[:, 7, :, 0] = 0; X[:, 3, :, W - 1] = 0; X[:, 3, :, 0] = 255
    p = rng.random((N, 8, R, L)); A = np.where(p < 0.4, 0, np.where(p < 0.8, W - 1, rng.integers(0, W, (N, 8, R, L))))
    c = rng.integers(0, 4, (N, 8, 1, R)); z = 255 * np.where(c == 3, rng.integers(0, 2, (N, 8, 16, R)), (c > 0).astype(np.int64))
    c = rng.integers(0, 3, (N, 8, 1)); w = 255 * np.where(c == 2, rng.integers(0, 2, (N, 8, 16)), c)
    w[:, 7] = 255; w[:, 0, 0] = 0; w[:, 0, 15] = 255
    T = 4080 * rng.integers(0, 2, (N, 8)); T[:, 7] = 4080; T[:, 0] = 0; T[0, 1:7] = 0
    z[:, 7, :, R - 2:] = 255; z[:, 0, :, 0] = 0
    A[:, 7, R - 2, 0] = W - 1; A[:, 7, R - 1] = 0
    A[(np.arange(N) // 2) % 2 == 1, 7, R - 1, H - 1] = W - 1
    return pack(X, A, z, w, T)
def setup_inputs_spread(rng):
    X, A, z, w, T = parts(rng)
    X = (np.exp2(8 * rng.random((N, 8, 1, W))) * rng.random((N, 8, 16, W)) * (rng.random((N, 8, 1, W)) > 0.0625)).astype(np.int64)
    A = np.minimum((W * rng.random((N, 8, R, L)) ** rng.choice(np.array([1.0, 2.0, 6.0]), (N, 8, R, 1))).astype(np.int64), W - 1)
    z = np.where(rng.random((N, 8, 1, R)) < 0.5, z, (np.exp2(8 * rng.random((N, 8, 1, R))) * rng.random((N, 8, 16, R))).astype(np.int64))
    w = np.minimum(np.exp2(8 * rng.random((N, 8, 16))).astype(np.int64) - rng.integers(0, 2, (N, 8, 16)), 255)
    T = np.minimum(np.exp2(12 * rng.random((N, 8))).astype(np.int64) - 1, 4080)
    return pack(X, A, z, w, T)
def check_inputs(d):
    bad = []
    for k, lo, hi in (("xd", 0, 255), ("ra", 0, W - 1), ("zu", 0, 255), ("wg", 0, 255), ("th", 0, 4080)):
        v = np.asarray(d[k]).astype(np.float64)
        if not (np.min(v) >= lo and np.max(v) <= hi): bad.append("range of " + k)
        elif np.any(v != np.floor(v)): bad.append("whole numbers of " + k)
    v = np.asarray(d["th"]).reshape(-1, 16)
    if np.any(v != v[:, :1]): bad.append("th alike in a group")
    return bad
def reference(xd, ra, zu, wg, th):
    X = xd.astype(np.float32).astype(np.int64).reshape(N, 8, 16, W); z = zu.astype(np.float32).astype(np.int64).reshape(N, 8, 16, R)
    A = np.stack([gentries(a) for a in ra]).astype(np.int64).reshape(N, 8, R, L)
    w = wg.astype(np.int64).reshape(N, 8, 16, 1); T = th.astype(np.int64).reshape(N, 8, 16)[:, :, 0]
    turn = [0] * N
    for rnd in range(RO):
        d = 1 + rnd % (N - 2)
        lost = np.zeros((N, 8, R), bool); beaten = np.zeros((N, 8, R), bool); h = np.zeros((N, 8, R), np.int64)
        D1 = np.zeros((N, 8, R, L), np.int64); D2 = np.zeros((N, 8, R, L), np.int64); nz = np.zeros_like(z); nturn = [0] * N
        for q in range(N):
            r = (q - d) % N; s = (q + 1) % N
            C = np.empty((8, R, L), np.int64)
            C[:, :, 0::2] = A[r][:, :, :H]; C[:, :, 1::2] = np.roll(A[s], -turn[q], axis=1)[:, :, :H]
            x = np.take_along_axis(X[q], C.reshape(8, 1, R * L), 2).reshape(8, 16, R, L)
            top = np.maximum.accumulate(np.minimum(x, z[r][:, :, :, None]), axis=3)
            gain = top.copy(); gain[:, :, :, 1:] -= top[:, :, :, :-1]
            click = np.add.reduce(gain, axis=1) >= T[q][:, None, None]
            D = np.take_along_axis(C, np.argsort(~click, axis=2, kind="stable"), 2)
            n = click.astype(np.int64); a = np.add.reduce(n[:, :, 0::2], axis=2); b = np.add.reduce(n[:, :, 1::2], axis=2)
            E = top[:, :, :, L - 1]
            u = np.add.reduce(w[q] * E, axis=1) & 4095
            lost[r] = b > a; D1[r] = D; h[r] = (((u * u) >> 4) + u) & (W - 1)
            beaten[s] = np.roll(a > b, turn[q], axis=1); D2[s] = np.roll(D, turn[q], axis=1)
            nz[r] = np.abs(255 - z[r] - E)
            place = np.arange(R) * SP + (u & (SP - 1))
            np.put_along_axis(X[q], np.repeat(place[:, None, :], 16, axis=1), E, 2)
            nturn[q] = int(np.add.reduce(n.reshape(-1))) % R
        A3 = A.copy(); A3[:, :, :, H - 1] = h
        A = np.where(lost[:, :, :, None], D1, np.where(beaten[:, :, :, None], D2, A3)); z = nz; turn = nturn
    return {"ya": np.stack([gtable(a.reshape(8, -1)) for a in A]).astype(np.float32), "yz": z.reshape(N, 128, R).astype(np.float32)}

@@ -1,0 +1,433 @@
+from concourse.bass import DstId, RemoteDMATransfer
+from concourse.mybir import AluOpType, ActivationFunctionType
+
+A = AluOpType
+F = ActivationFunctionType
+N, RO, PAD = 8, 3, 2
+f32, bf, i32, u16 = "float32", "bfloat16", "int32", "uint16"
+
+
+def sb(shape, d):
+    return ("sbuf", [128] + list(shape), d)
+
+
+SCRATCH = {
+    "X": sb([8192], bf), "xg": sb([4096], bf), "zrep": sb([4096], bf), "top": sb([4096 + 16], bf),
+    "rai": sb([256], i32), "zown": sb([128], bf), "wi": sb([4], i32), "ti": sb([4], i32), "lo0": sb([128], u16),
+    "jf": sb([144], f32), "jt": sb([256], f32), "ci": sb([8], i32), "cf": sb([16], f32),
+    "ibf": sb([128], bf), "isc": sb([128], f32), "p0": sb([128], f32), "pbp": sb([128], bf), "pbn": sb([128], bf),
+    "gp": sb([8], bf), "gn": sb([8], bf), "wgr": sb([8], bf), "blk": sb([128], bf), "ones": sb([128], bf),
+    "onef": sb([128], f32), "ww": sb([144], bf), "c1i": sb([384], bf), "tm": sb([256], f32), "trep": sb([256], f32),
+    "jl": sb([16], f32), "ja": sb([8], i32), "jb": sb([8], i32), "jc": sb([8], i32), "pip": sb([8], u16), "plb": sb([8], i32),
+    "zl": sb([384], bf), "zfin": sb([128], f32), "nzb": sb([256], bf), "nzf": sb([128], f32),
+    "offF": sb([128], u16), "offS": sb([128], u16), "off0F": sb([128], u16), "off0S": sb([128], u16),
+    "mF": sb([128], i32), "mS": sb([128], i32), "fi": sb([128], i32), "si": sb([128], i32),
+    "basF": sb([128], f32), "basS": sb([128], f32),
+    "u3": sb([256], bf), "u2": sb([256], bf),
+    "b0": sb([8, 2, 2, 2, 2], f32), "b1": sb([8, 2, 2, 2, 2], f32), "b4": sb([16, 2, 4], f32), "b5": sb([8, 2, 8], f32),
+    "dlo": sb([128], f32), "dhi": sb([128], f32),
+    "ha": sb([8], i32), "hb": sb([8], i32), "hc": sb([8], i32), "hpad": sb([128], f32), "a3": sb([128], f32),
+    "d1": sb([128], bf), "s1": sb([128], bf), "s2": sb([128], bf), "dl": sb([128], bf),
+    "junk": sb([256], f32), "tot": sb([4], f32), "tl": sb([24], i32), "tl2": sb([24], i32), "lst": sb([48], u16),
+    "pa_": sb([8], i32), "pb_": sb([8], i32), "pl": sb([8], u16),
+    "o1": sb([768], f32), "o2": sb([768], f32),
+    "lS": sb([256], f32), "lF1": sb([256], f32), "lF2": sb([256], f32),
+    "lH1": sb([256], f32), "lH2": sb([256], f32), "lE1": sb([256], f32), "lE2": sb([256], f32),
+    "ulF": sb([8], u16), "ulH1": sb([8], u16), "ulH2": sb([8], u16),
+    "hx": sb([128], f32), "fin": sb([256], i32), "fin2": sb([256], i32), "yo": sb([256], f32),
+    "pg": ("psum", [128, 512], f32), "pb": ("psum", [128, 512], f32), "pa": ("psum", [128, 4, 8, 2, 2, 2, 2], f32),
+    "pt": ("psum", [128, 512], f32), "pv": ("psum", [128, 512], f32), "ph": ("psum", [128, 512], f32),
+    "pc": ("psum", [128, 512], f32), "pd": ("psum", [128, 512], f32),
+}
+POOL = {"V": 24, "S": 36, "P": 40, "G": 4, "Y": 10}
+ARR = ["z0", "z1", "z2", "zf", "F0", "S0", "S1", "S2", "Fa1", "Fa2", "Fb1", "Fb2", "Ha0", "Ha1", "Hb0", "Hb1",
+       "Ea", "Eb", "uF", "uH1", "uH2"]
+SEMAPHORES = [q + str(k) for q in POOL for k in range(POOL[q])] + ["r" + a for a in ARR] + ["sent"]
+STAGES = [0, 1, 0, 2, 1, 0, 3, 2, 1, 0, 4, 3, 2, 1, 0]
+FIRST = {1: 2, 3: 3, 6: 4, 10: 5}
+
+
+def rank_program(g, core, T, topo):
+    q = T.rank_of(core)
+    if q is None:
+        return
+    V, S, P, Y = g.vector, g.scalar, g.tensor, g.sync
+    Q = {"V": V, "S": S, "P": P, "G": g, "Y": Y}
+    know = {k: {} for k in Q}
+    cnt, waited, lastw, readers, bank = {}, {}, {}, {}, {}
+
+    def wait(qn, deps):
+        need = {}
+        for e in deps:
+            if know[qn].get(e[0], 0) < e[1] and (e[0] not in need or need[e[0]][1] < e[1]):
+                need[e[0]] = e
+        for s in sorted(need, key=lambda x: -len(need[x][2])):
+            e = need[s]
+            if know[qn].get(s, 0) >= e[1]:
+                continue
+            Q[qn].wait_ge(T.sem[s], e[1])
+            waited[s] = max(waited.get(s, 0), e[1])
+            know[qn][s] = e[1]
+            for k, v in e[2].items():
+                if know[qn].get(k, 0) < v:
+                    know[qn][k] = v
+
+    def deps_of(qn, r, w, banks):
+        d = [lastw[k] for k in list(r) + list(w) if k in lastw]
+        for k in w:
+            d += readers.get(k, [])
+        for b in banks:
+            d += [e for o, e in bank.get(b, {}).items() if o != qn]
+        return d
+
+    def op(qn, fns, r=(), w=(), banks=(), inc=1):
+        wait(qn, deps_of(qn, r, w, banks))
+        s = [x for x in (qn + str(k) for k in range(POOL[qn])) if know[qn].get(x, 0) == cnt.get(x, 0)][0]
+        fns = fns if isinstance(fns, list) else [fns]
+        for fn in fns:
+            fn().then_inc(T.sem[s], inc)
+        cnt[s] = cnt.get(s, 0) + inc * len(fns)
+        e = (s, cnt[s], dict(know[qn]))
+        for k in r:
+            readers.setdefault(k, []).append(e)
+        for k in w:
+            lastw[k] = e
+            readers[k] = []
+        for b in banks:
+            bank.setdefault(b, {})[qn] = e
+        return e
+
+    def send(parts, r):
+        wait("G", deps_of("G", r, (), ()))
+        ts = []
+        for k, (dst, src, land, name) in enumerate(parts):
+            dc = T.cores[dst % N]
+            eng = topo.engines(core, dc)
+            m = len(eng) // len(parts)
+            mask = 0
+            for e in eng[k * m:(k + 1) * m]:
+                mask |= 1 << e
+            rid, pid = topo.addr(dc)[:2]
+            ts.append((rid, pid, mask, src, land, name))
+            cnt["sent"] = cnt.get("sent", 0) + m
+        if len(ts) == 1:
+            rid, pid, mask, src, land, name = ts[0]
+            g.remote_dma(land, src, T.sem["r" + name], T.sem.sent, pid, rid, mask)
+        else:
+            g.remote_dma_fused([RemoteDMATransfer(dst_ids=[DstId(rid=a, pnc=b)], dma_engine_mask=m, remote_sem=T.sem["r" + nm],
+                                                  src=s, dst=l) for a, b, m, s, l, nm in ts], local_sem=T.sem.sent)
+
+    def expect(name, src, share):
+        n = len(topo.engines(T.cores[src % N], core)) // share
+        cnt["r" + name] = n
+        lastw["L" + name] = ("r" + name, n, {})
+
+    def tcopy(o, i):
+        return lambda: V.tensor_copy(o, i)
+
+    def tt(o, a, b, x):
+        return lambda: V.tensor_tensor(o, a, b, x)
+
+    def ts1(o, a, s, x):
+        return lambda: V.tensor_scalar(o, a, s, None, x)
+
+    def ts2(o, a, s1, s2, x1, x2):
+        return lambda: V.tensor_scalar(o, a, s1, s2, x1, x2)
+
+    def mm(o, l, r, st=True, sp=True):
+        return lambda: P.matmul(o, l, r, st, sp)
+
+    def act(o, i, fn, **kw):
+        return lambda: S.activation(o, i, fn, **kw)
+
+    expect("z0", q - 1, 1)
+    expect("F0", q - 1, 2)
+    expect("S0", q + 1, 2)
+    for t in (1, 2):
+        expect("z%d" % t, q - 1, 1)
+        expect("S%d" % t, q + t + 1, 1)
+        expect("Fa%d" % t, q - 1, 2)
+        expect("Fb%d" % t, q - t - 2, 2)
+        expect("Ha%d" % (t - 1), q + t, 2)
+        expect("Hb%d" % (t - 1), q - 1, 2)
+    expect("zf", q + 3, 1)
+    expect("Ea", q + 3, 2)
+    expect("Eb", q - 1, 2)
+    expect("uF", q - 4, 2)
+    expect("uH1", q - 1, 2)
+    expect("uH2", q - 1, 1)
+
+    op("Y", lambda: Y.dma_start(T.zown[:], T.zu[:]), w=["zown"], inc=16)
+    op("S", lambda: S.dma_start(T.rai[:], T.ra[:]), w=["rai"], inc=16)
+    op("Y", lambda: Y.dma_start(T.wi[:, 0:1], T.wg[:]), w=["wi"], inc=16)
+    op("Y", lambda: Y.dma_start(T.ti[:, 0:1], T.th[:]), w=["ti"], inc=16)
+    op("S", lambda: S.dma_start(T.X[:], T.xd[:]), w=["X"], inc=16)
+
+    cf, ci, jf, jt = T.cf, T.ci, T.jf, T.jt
+    op("G", lambda: g.iota(ci[:, 0:1], [[0, 1]], 0, 1), w=["ci0"])
+    op("G", lambda: g.iota(jf[:], [[1, 144]], 0, 0, allow_small_or_imprecise_dtypes=True), w=["jf"])
+    op("G", lambda: g.iota(jt[:], [[1, 8], [0, 32]], 0, 0, allow_small_or_imprecise_dtypes=True), w=["jt"])
+    send([(q + 1, T.zown[:], T.zl[:, 0:128], "z0")], ["zown"])
+
+    op("V", [lambda: V.memset(T.top[:, 0:PAD], 0.0), lambda: V.memset(T.hpad[:], 0.0), lambda: V.memset(T.ones[:], 1.0),
+             lambda: V.memset(T.onef[:], 1.0)], w=["pad", "hpad", "ones"])
+    op("V", [ts1(ci[:, 1:2], ci[:, 0:1], 15, A.bitwise_and), ts1(ci[:, 2:3], ci[:, 0:1], 4, A.arith_shift_right),
+             ts1(ci[:, 3:4], ci[:, 0:1], 31, A.bitwise_and), ts1(ci[:, 4:5], ci[:, 0:1], 5, A.arith_shift_right)], r=["ci0"], w=["ci"])
+    op("V", [tcopy(cf[:, 0:5], ci[:, 0:5]), ts1(cf[:, 5:6], ci[:, 1:2], 16384.0, A.mult),
+             ts2(cf[:, 6:7], ci[:, 1:2], 16384.0, 8192.0, A.mult, A.add), ts2(cf[:, 7:8], ci[:, 2:3], 16.0, 15.0, A.mult, A.add)],
+       r=["ci", "ci0"], w=["cf"])
+    op("V", tcopy(T.lo0[:], T.rai[:, 0:256:2]), r=["rai"], w=["lo0"])
+    send([(q + 1, T.lo0[:], T.off0F[:], "F0"), (q - 1, T.lo0[:], T.off0S[:], "S0")], ["lo0"])
+    op("V", [ts2(cf[:, 10:11], ci[:, 3:4], 4.0, cf[:, 4:5], A.mult, A.add),
+             ts2(T.jl[:, 0:8], jf[:, 0:8], 16.0, cf[:, 1:2], A.mult, A.add),
+             ts1(T.ibf[:], jf[:, 0:128], cf[:, 0:1], A.is_equal),
+             ts2(T.isc[:], jf[:, 0:128], cf[:, 0:1], 2.0 ** -18, A.is_equal, A.mult),
+             ts1(T.gp[:], jf[:, 0:8], cf[:, 2:3], A.is_equal),
+             ts2(T.gn[:], jf[:, 0:8], cf[:, 2:3], -1.0, A.is_equal, A.mult),
+             ts1(T.blk[:], jt[:, 0:256:2], cf[:, 2:3], A.is_equal)], r=["cf", "ci", "jf", "jt"], w=["k1"])
+    op("V", [tcopy(cf[:, 8:9], T.wi[:, 0:1]), ts1(cf[:, 9:10], T.ti[:, 0:1], 1.0 / 16, A.mult), tcopy(T.ja[:], T.jl[:, 0:8]),
+             ts1(T.plb[:], T.jl[:, 0:8], 64.0, A.mult),
+             ts2(T.p0[:], jf[:, 0:128], cf[:, 10:11], 2.0 ** 18, A.is_equal, A.mult),
+             ts1(T.pbp[:], jf[:, 0:128], cf[:, 10:11], A.is_equal),
+             ts2(T.pbn[:], jf[:, 0:128], cf[:, 10:11], -1.0, A.is_equal, A.mult)], r=["k1", "wi", "ti"], w=["k2"])
+    op("V", [ts1(T.jb[:], T.ja[:], 31, A.bitwise_and), ts1(T.jc[:], T.ja[:], 5, A.arith_shift_right),
+             ts2(T.tm[:], jt[:], cf[:, 2:3], cf[:, 9:10], A.is_equal, A.mult),
+             ts2(T.wgr[:], jf[:, 0:8], cf[:, 2:3], cf[:, 8:9], A.is_equal, A.mult),
+             ts2(T.ww[:], jf[:], cf[:, 7:8], cf[:, 8:9], A.is_equal, A.mult)]
+       + [ts1(T.c1i[:, 128 * t:128 * t + 128], T.ibf[:], float((3 * t + 3) << 19), A.mult) for t in range(RO)], r=["k2"], w=["k3"])
+    op("P", mm(T.pd[:, 0:256], T.onef[:], T.tm[:]), r=["k3", "ones"], w=["pd"], banks=["pd"])
+    op("S", act(T.trep[:], T.pd[:, 0:256], F.Copy), r=["pd"], w=["trep"], banks=["pd"])
+    op("V", [ts1(T.ja[:], T.jb[:], 4.0, A.mult), tcopy(T.ph[:, 128:256], T.rai[:, 1:256:2])], r=["k3", "rai"], w=["k4", "hacc"], banks=["ph"])
+    op("V", tt(T.jl[:, 8:16], T.ja[:], T.jc[:], A.add), r=["k4"], w=["k5"])
+    op("V", tcopy(T.pip[:], T.jl[:, 8:16]), r=["k5"], w=["pip"])
+
+    def zslot(t):
+        return T.zl[:, 128 * t:128 * t + 128]
+
+    def spread_z(t, nv):
+        ks = list(range(1, 32))
+        if nv:
+            op("V", [tcopy(T.zrep[:, k:4096:32], zslot(t)) for k in ks[:nv]], r=["Lz%d" % t], w=["zrV"])
+        op("S", [act(T.zrep[:, k:4096:32], zslot(t), F.Copy) for k in ks[nv:]], r=["Lz%d" % t], w=["zrS"] + ([] if nv else ["zrV"]))
+
+    def base(role, lst, key):
+        src, dst, col = (T.fi, T.basF, 5) if role == "F" else (T.si, T.basS, 6)
+        op("V", ts1(dst[:], src[:].indirect(lst), cf[:, col:col + 1], A.add), r=["i" + role, key, "cf"], w=["bas" + role])
+        c0 = 0 if role == "F" else 128
+        op("P", mm(T.pb[:, c0:c0 + 128], dst[:], T.isc[:]), r=["bas" + role, "k1"], w=["pb" + role], banks=["pb"])
+
+    spread_z(0, 21)
+    op("V", [tcopy(T.fi[:], T.off0F[:]), tcopy(T.si[:], T.off0S[:])], r=["LF0", "LS0"], w=["iF", "iS"])
+    base("F", T.pip[:], "pip")
+    base("S", T.pip[:], "pip")
+
+    E = T.top[:, PAD + 31:PAD + 4096:32]
+    tops = ["top%d" % c for c in range(7)] + ["top7a", "top7b"]
+
+    for t in range(RO):
+        d = t + 1
+        last = t == RO - 1
+        ch, c2, c1 = (3 * t + 1) << 19, (3 * t + 2) << 19, (3 * t + 3) << 19
+        offs = {"F": T.off0F if t == 0 else T.offF, "S": T.off0S if t == 0 else T.offS}
+        okey = {"F": "LF0" if t == 0 else "offF", "S": "LS0" if t == 0 else "offS"}
+        mkey, mbuf = ("iF", T.fi) if t == 0 else ("mF", T.mF)
+
+        def gather(qn, role, c):
+            o = T.xg[:, 512 * c + (role == "S"):512 * c + 512:2]
+            i = T.X[:].indirect(offs[role][:, 16 * c:16 * c + 16])
+            op(qn, tcopy(o, i) if qn == "V" else act(o, i, F.Copy), r=["X", okey[role]], w=["x%s%d" % (role, c)])
+
+        def fix(c, e):
+            op("V", tt(T.zrep[:, 512 * c:512 * e:32], T.xg[:, 512 * c:512 * e:32], T.zl[:, 128 * t + 16 * c:128 * t + 16 * e], A.min),
+               r=["xF%d" % k for k in range(c, e)] + ["Lz%d" % t], w=["zf%d" % k for k in range(c, e)])
+
+        def scan(c, part=""):
+            a, b = {"": (0, 512), "a": (0, 256), "b": (256, 512)}[part]
+            a, b = a + 512 * c, b + 512 * c
+            key = "top%d%s" % (c, part)
+            op("V", lambda: V.tensor_tensor_scan(T.top[:, PAD + a:PAD + b], T.xg[:, a:b], T.zrep[:, a:b], 0.0, A.max, A.min),
+               r=["xF%d" % c, "xS%d" % c, "zf%d" % c, "zrV", "zrS"], w=[key])
+            if part == "b":
+                op("P", mm(T.pv[:, 8:16], E, T.wgr[:]), r=tops + ["k3"], w=["v2"], banks=["pv"])
+            fns = []
+            for ib in range(a // 128, b // 128):
+                c0 = PAD + 128 * ib
+                fns += [mm(T.pg[:, ib:256:32], T.top[:, c0:c0 + 128], T.gp[:], True, False),
+                        mm(T.pg[:, ib:256:32], T.top[:, c0 - 1:c0 + 127], T.gn[:], False, True)]
+            k = tops.index(key)
+            op("P", fns, r=[key, tops[k - 1] if k else "pad", "k1"], w=["gain" + key], banks=["pg"])
+
+        if t == 0:
+            seqS = "S0 F1 S1 S2 S3 S4 S5 F7 S6 S7"
+            seqV = "g0 f0 s0 g2 f1 g3 s1 f23 s2 g4 s3 g5 f45 s4 g6 s5 f67 s6"
+        else:
+            seqS = "S0 S1 F1 S2 F3 S3 S4 S5 S6 F7 S7"
+            seqV = "g0 b0 f0 s0 f1 g2 s1 f23 s2 g4 s3 g5 f45 s4 g6 s5 f67 s6"
+        for x in seqS.split():
+            gather("S", x[0], int(x[1]))
+        for x in seqV.split():
+            c = int(x[1])
+            if x[0] == "g":
+                gather("V", "F", c)
+            elif x[0] == "b":
+                base("F", T.pip[:], "pip")
+            elif x[0] == "f":
+                fix(c, int(x[-1]) + 1)
+                if x[-1] == "7":
+                    op("P", [mm(T.pv[32 * j:32 * j + 32, 0:8], T.zrep[:, 32 * j:4096:128], T.gp[:]) for j in range(4)],
+                       r=["zf%d" % k for k in range(8)] + ["k1"], w=["s0"], banks=["pv"])
+            else:
+                scan(c)
+        scan(7, "a")
+        scan(7, "b")
+
+        op("P", [mm(T.pc[:, 0:128], T.ibf[:], zslot(t), True, False), mm(T.pc[:, 0:128], T.ibf[:], E, False, True)],
+           r=tops + ["Lz%d" % t, "k1"], w=["ze"], banks=["pc"])
+        nz = T.nzf[:] if last else T.nzb[:, 128 * t:128 * t + 128]
+        op("S", act(nz, T.pc[:, 0:128], F.Abs, bias=255.0, scale=-1.0), r=["ze"], w=["nz%d" % t], banks=["pc"])
+        if last:
+            send([(q - d, nz, T.zfin[:], "zf")], ["nz%d" % t])
+        else:
+            send([(q + 1, nz, zslot(t + 1), "z%d" % (t + 1))], ["nz%d" % t])
+
+        fill = [
+            lambda: op("V", tcopy(T.ha[:], T.pv[:, 8:16]), r=["v2"], w=["ha"], banks=["pv"]),
+            lambda: op("V", ts1(T.hb[:], T.ha[:], 4095, A.bitwise_and), r=["ha"], w=["hb"]),
+            lambda: op("V", tt(T.ha[:], T.hb[:], T.hb[:], A.mult), r=["hb"], w=["ha"]),
+            lambda: op("V", ts1(T.hc[:], T.ha[:], 4, A.arith_shift_right), r=["ha"], w=["hc"]),
+            lambda: op("V", tt(T.ha[:], T.hc[:], T.hb[:], A.add), r=["hc", "hb"], w=["ha"]),
+            lambda: op("V", ts1(T.hc[:], T.ha[:], 8191, A.bitwise_and), r=["ha"], w=["hc"]),
+            lambda: (op("V", ts2(T.hpad[:, 15:128:16], T.hc[:], float(ch), 2.0 ** 18, A.add, A.mult), r=["hc"], w=["hpad"]),
+                     op("P", mm(T.ph[:, 0:128], T.hpad[:], T.isc[:]), r=["hpad", "k1"], w=["ht"], banks=["ph"])),
+        ]
+        fill.pop(0)()
+        fill.pop(0)()
+
+        op("V", tt(T.u3[:], T.pg[:, 0:256], T.trep[:], A.is_lt), r=["gain" + k for k in tops] + ["trep"], w=["u3"], banks=["pg"])
+        fill.pop(0)()
+        op("V", lambda: V.transpose(T.u2[:], T.u3[:]), r=["u3"], w=["u2", "u2f"])
+        fill.pop(0)()
+        op("V", tt(T.u2[:, 0:256:32], T.pv[:, 0:8], T.trep[:, 0:256:32], A.is_lt), r=["s0", "trep", "u2"], w=["u2f"], banks=["pv"])
+        op("V", tt(T.b0[:], T.u2[:, 1:256:2], T.pb[:, 128:256], A.add), r=["u2", "pbS"], w=["B0"], banks=["pb"])
+        op("V", tt(T.pa[:, 0], T.u2[:, 0:256:2], T.pb[:, 0:128], A.add), r=["u2", "u2f", "pbF"], w=["A0"], banks=["pb", "pa"])
+
+        op("P", [mm(T.pc[:, 128:256], T.u2[:, 0:256:2], T.pbp[:], True, False), mm(T.pc[:, 128:256], T.u2[:, 1:256:2], T.pbn[:], False, True)],
+           r=["u2", "u2f", "k2"], w=["df"], banks=["pc"])
+        if not last:
+            op("P", mm(T.pd[:, 0:256], T.ones[:], T.u2[:]), r=["u2", "u2f", "ones"], w=["pd"], banks=["pd"])
+        op("S", act(T.d1[:], T.pc[:, 128:256], F.Copy), r=["df"], w=["d1"], banks=["pc"])
+        op("P", mm(T.pc[:, 256:384], T.blk[:], T.d1[:]), r=["d1", "k1"], w=["ab"], banks=["pc"])
+        if not last:
+            op("S", act(T.junk[:], T.pd[:, 0:256], F.Identity, accum_out=T.tot[:, 0:1]), r=["pd"], w=["tot"], banks=["pd"])
+            op("P", [mm(T.pv[:, 16:24], T.ww[:, 15 - c:143 - c], T.top[:, PAD + 32 * c + 31:PAD + 4096:512], c == 0, c == 15)
+                     for c in range(16)], r=tops + ["k3"], w=["vd"], banks=["pv"])
+        op("S", [act(T.s1[:], T.pc[:, 256:384], F.Sign, bias=-0.5), act(T.s2[:], T.pc[:, 256:384], F.Sign, bias=-0.5, scale=-1.0)],
+           r=["ab"], w=["s1", "s2"], banks=["pc"])
+        op("S", act(T.dl[:], T.s2[:], F.Identity, scale=float(c1 + c2)), r=["s2"], w=["dl"])
+        if not last:
+            spread_z(t + 1, 0)
+
+        def view(buf, pre, pair, bit, val):
+            rem = [b for b in (4, 3, 2, 1, 0) if b != pair]
+            return buf[(slice(None),) + pre + (slice(None),) + tuple(val if b == bit else slice(None) for b in rem)]
+
+        gen = [T.b0, T.b1]
+        cI = T.c1i[:, 128 * t:128 * t + 128]
+        for s, pr in enumerate(STAGES):
+            lev = FIRST.get(s, 0)
+            src_b = gen[s % 2]
+
+            def in_b(bit, v):
+                if lev >= 4:
+                    return (T.b4 if lev == 4 else T.b5)[:, :, 1 - v, ::-1]
+                return view(src_b, (), pr, bit, 1 - v if lev else v)
+
+            if s < 14:
+                nx, nlev = STAGES[s + 1], FIRST.get(s + 1, 0)
+                fns = []
+                for nv in (0, 1):
+                    for dd in (0, 1):
+                        if nv == 0:
+                            o = view(T.pa, ((s + 1) % 2,), nx, pr, dd)
+                        elif nlev >= 4:
+                            o = (T.b4 if nlev == 4 else T.b5)[:, :, :, dd::2]
+                        else:
+                            o = view(gen[(s + 1) % 2], (), nx, pr, 1 - dd if nlev == 3 else dd)
+                        fns.append(tt(o, view(T.pa, (s % 2,), pr, nx, nv), in_b(nx, nv), A.max if dd else A.min))
+                op("V", fns, r=["A%d" % (s % 2), "B%d" % (s % 2)], w=["A%d" % ((s + 1) % 2), "B%d" % ((s + 1) % 2)], banks=["pa"])
+                if fill:
+                    fill.pop(0)()
+                if s == 8:
+                    op("P", mm(T.pt[:, 0:128], cI, T.s1[:], True, False), r=["s1", "k3"], w=["tlo"], banks=["pt"])
+                    op("P", mm(T.pg[:, 256:384], cI, T.s1[:], True, False), r=["s1", "k3"], w=["thi"], banks=["pg"])
+                    op("V", tt(T.a3[:], T.ph[:, 0:128], mbuf[:], A.max), r=["ht", mkey], w=["a3"], banks=["ph"])
+            else:
+                for hv, o, key, ps, bk in ((0, T.dlo, "lo", T.pt[:, 0:128], "pt"), (1, T.dhi, "hi", T.pg[:, 256:384], "pg")):
+                    op("V", [tt(o[:, dd:128:2], view(T.pa, (s % 2,), pr, 4, hv), in_b(4, hv), A.max if dd else A.min) for dd in (0, 1)],
+                       r=["A%d" % (s % 2), "B%d" % (s % 2)], w=["d" + key], banks=["pa"])
+                    op("P", mm(ps, o[:], T.p0[:], False, True), r=["d" + key, "k2"], w=["t" + key], banks=[bk])
+
+        o0 = 256 * t
+        p1lo, p1hi, p2lo, p2hi = T.o1[:, o0:o0 + 128], T.o1[:, o0 + 128:o0 + 256], T.o2[:, o0:o0 + 128], T.o2[:, o0 + 128:o0 + 256]
+        op("V", tt(p1lo, T.pt[:, 0:128], T.a3[:], A.max), r=["tlo", "a3"], w=["p1lo"], banks=["pt"])
+        if not last:
+            sl = slice(128 * t, 128 * t + 128)
+            send([(q - d - 1, p1lo, T.lS[:, sl], "S%d" % d)], ["p1lo"])
+        op("V", tt(p2lo, T.pt[:, 0:128], T.dl[:], A.add), r=["tlo", "dl"], w=["p2lo"], banks=["pt"])
+        if not last:
+            send([(q + 1, p1lo, T.lF1[:, sl], "Fa%d" % d), (q + d + 2, p2lo, T.lF2[:, sl], "Fb%d" % d)], ["p1lo", "p2lo"])
+        op("V", [tt(p2hi, T.pg[:, 256:384], T.dl[:], A.add), tcopy(p1hi, T.pg[:, 256:384])], r=["thi", "dl"], w=["phi"], banks=["pg"])
+        if last:
+            send([(q - d, T.o1[:, o0:o0 + 256], T.lE1[:], "Ea"), (q + 1, T.o2[:, o0:o0 + 256], T.lE2[:], "Eb")], ["p1lo", "p2lo", "phi"])
+        else:
+            send([(q - d, p1hi, T.lH1[:, sl], "Ha%d" % t), (q + 1, p2hi, T.lH2[:, sl], "Hb%d" % t)], ["phi"])
+
+        if not last:
+            l0 = 24 * t
+            op("V", [ts2(T.tl[:, 0:16], T.jl[:], T.tot[:, 0:1], 32768.0, A.subtract, A.add),
+                     ts1(T.tl[:, 16:24], T.jl[:, 0:8], T.tot[:, 0:1], A.add), tcopy(T.pa_[:], T.pv[:, 16:24])],
+               r=["tot", "k5", "vd"], w=["tl", "pa_"], banks=["pv"])
+            op("V", [ts1(T.tl2[:], T.tl[:], 127, A.bitwise_and), ts1(T.pb_[:], T.pa_[:], 63, A.bitwise_and)], r=["tl", "pa_"], w=["tl2", "pb_"])
+            op("V", [tcopy(T.lst[:, l0:l0 + 24], T.tl2[:]), tt(T.pa_[:], T.pb_[:], T.plb[:], A.add)], r=["tl2", "pb_", "k2"], w=["lst%d" % t, "pa_"])
+            un = T.lst[:, l0 + 16:l0 + 24]
+            if t == 0:
+                send([(q + 4, un, T.ulF[:], "uF"), (q + 1, un, T.ulH1[:], "uH1")], ["lst0"])
+            else:
+                send([(q + 1, un, T.ulH2[:], "uH2")], ["lst1"])
+            op("V", tcopy(T.pl[:], T.pa_[:]), r=["pa_"], w=["pl"])
+            op("V", tcopy(T.X[:].indirect(T.pl[:]), E), r=["pl"] + tops, w=["X"])
+        else:
+            op("V", [tt(T.junk[:, 0:128], T.lH2[:, 0:128], T.lH1[:, 0:128], A.max),
+                     tt(T.junk[:, 128:256], T.lH2[:, 128:256].indirect(T.ulH1[:]), T.lH1[:, 128:256], A.max)],
+               r=["LHa0", "LHb0", "LHa1", "LHb1", "LuH1", "tot"], w=["jk"])
+            for k in (0, 1):
+                op("V", tt(T.ph[:, 128:256], T.junk[:, 128 * k:128 * k + 128], T.ph[:, 128:256], A.max), r=["jk"], w=["hacc"], banks=["ph"])
+
+        if not last:
+            own = p2lo if t == 0 else p2lo.indirect(T.lst[:, 16:24])
+            op("V", tt(T.mS[:], own, T.lS[:, sl], A.max), r=["p2lo", "LS%d" % d, "lst0"], w=["mS"])
+            op("V", ts1(T.si[:], T.mS[:], 8191, A.bitwise_and), r=["mS"], w=["iS"])
+            op("V", tcopy(T.offS[:], T.si[:].indirect(T.lst[:, l0:l0 + 8])), r=["iS", "lst%d" % t], w=["offS"])
+            base("S", T.lst[:, l0 + 8:l0 + 16], "lst%d" % t)
+            far = T.lF2[:, sl] if t == 0 else T.lF2[:, sl].indirect(T.ulF[:])
+            op("V", tt(T.mF[:], far, T.lF1[:, sl], A.max), r=["LFa%d" % d, "LFb%d" % d] + (["LuF"] if t else []), w=["mF"])
+            op("V", ts1(T.fi[:], T.mF[:], 8191, A.bitwise_and), r=["mF"], w=["iF"])
+            op("V", tcopy(T.offF[:], T.fi[:]), r=["iF"], w=["offF"])
+
+    wait("Y", [lastw["Lzf"]])
+    op("Y", lambda: Y.dma_start(T.yz[:], T.zfin[:]), w=["yz"], inc=16)
+    op("V", [tt(T.hx[:], T.lE1[:, 128:256], T.ph[:, 128:256], A.max),
+             tt(T.fin[:, 0:128], T.lE2[:, 0:128].indirect(T.ulH2[:]), T.lE1[:, 0:128], A.max)],
+       r=["LEa", "LEb", "LuH2", "hacc"], w=["hx", "finlo"], banks=["ph"])
+    op("V", [tt(T.fin[:, 128:256], T.lE2[:, 128:256].indirect(T.ulH2[:]), T.hx[:], A.max),
+             ts1(T.fin2[:, 0:128], T.fin[:, 0:128], 8191, A.bitwise_and)], r=["hx", "finlo"], w=["finhi", "f2lo"])
+    op("V", [ts1(T.fin2[:, 128:256], T.fin[:, 128:256], 8191, A.bitwise_and), tcopy(T.yo[:, 0:256:2], T.fin2[:, 0:128])],
+       r=["finhi", "f2lo"], w=["f2hi", "yolo"])
+    op("V", tcopy(T.yo[:, 1:256:2], T.fin2[:, 128:256]), r=["f2hi"], w=["yohi"])
+    op("Y", lambda: Y.dma_start(T.ya[:], T.yo[:]), r=["yolo", "yohi"], w=["ya"], inc=16)
+    for s in cnt:
+        if s[0] != "Y" and waited.get(s, 0) < cnt[s]:
+            g.wait_ge(T.sem[s], cnt[s])
+    for s in cnt:
+        if s[0] == "Y" and waited.get(s, 0) < cnt[s]:
+            Y.wait_ge(T.sem[s], cnt[s])

@@ -24,7 +24,8 @@ SCRATCH = {
     "mF": sb([128], i32), "mS": sb([128], i32), "fi": sb([128], i32), "si": sb([128], i32),
     "basF": sb([128], f32), "basS": sb([128], f32),
     "u3": sb([256], bf), "u2": sb([256], bf),
-    "b0": sb([8, 2, 2, 2, 2], f32), "b1": sb([8, 2, 2, 2, 2], f32), "b4": sb([16, 2, 4], f32), "b5": sb([8, 2, 8], f32),
+    "b0": sb([8, 2, 2, 2, 2], f32), "cc": sb([8, 2, 2, 2, 2, 2], f32), "b4": sb([16, 8], f32), "b5": sb([8, 16], f32),
+    "u0": sb([8], bf), "trep3": sb([256], f32),
     "dlo": sb([128], f32), "dhi": sb([128], f32),
     "ha": sb([8], i32), "hb": sb([8], i32), "hc": sb([8], i32), "hpad": sb([128], f32), "a3": sb([128], f32),
     "d1": sb([128], bf), "s1": sb([128], bf), "s2": sb([128], bf), "dl": sb([128], bf),
@@ -183,6 +184,7 @@ def rank_program(g, core, T, topo):
              ts1(T.ibf[:], jf[:, 0:128], cf[:, 0:1], A.is_equal),
              ts2(T.isc[:], jf[:, 0:128], cf[:, 0:1], 2.0 ** -18, A.is_equal, A.mult),
              ts1(T.gp[:], jf[:, 0:8], cf[:, 2:3], A.is_equal),
+             ts1(cf[:, 11:12], cf[:, 3:4], 0.0, A.not_equal), ts2(cf[:, 12:13], cf[:, 3:4], 0.0, -8192.0, A.is_equal, A.mult),
              ts2(T.gn[:], jf[:, 0:8], cf[:, 2:3], -1.0, A.is_equal, A.mult),
              ts1(T.blk[:], jt[:, 0:256:2], cf[:, 2:3], A.is_equal)], r=["cf", "ci", "jf", "jt"], w=["k1"])
     op("V", [tcopy(cf[:, 8:9], T.wi[:, 0:1]), ts1(cf[:, 9:10], T.ti[:, 0:1], 1.0 / 16, A.mult), tcopy(T.ja[:], T.jl[:, 0:8]),
@@ -196,7 +198,8 @@ def rank_program(g, core, T, topo):
              ts2(T.ww[:], jf[:], cf[:, 7:8], cf[:, 8:9], A.is_equal, A.mult)]
        + [ts1(T.c1i[:, 128 * t:128 * t + 128], T.ibf[:], float((3 * t + 3) << 19), A.mult) for t in range(RO)], r=["k2"], w=["k3"])
     op("P", mm(T.pd[:, 0:256], T.onef[:], T.tm[:]), r=["k3", "ones"], w=["pd"], banks=["pd"])
-    op("S", act(T.trep[:], T.pd[:, 0:256], F.Copy), r=["pd"], w=["trep"], banks=["pd"])
+    op("S", [act(T.trep[:], T.pd[:, 0:256], F.Copy), act(T.trep3[:], T.pd[:, 0:256], F.Identity, scale=cf[:, 11:12], bias=cf[:, 12:13])],
+       r=["pd", "k1"], w=["trep", "trep3"], banks=["pd"])
     op("V", [ts1(T.ja[:], T.jb[:], 4.0, A.mult), tcopy(T.ph[:, 128:256], T.rai[:, 1:256:2])], r=["k3", "rai"], w=["k4", "hacc"], banks=["ph"])
     op("V", tt(T.jl[:, 8:16], T.ja[:], T.jc[:], A.add), r=["k4"], w=["k5"])
     op("V", tcopy(T.pip[:], T.jl[:, 8:16]), r=["k5"], w=["pip"])
@@ -212,12 +215,12 @@ def rank_program(g, core, T, topo):
 
     def base(role, lst, key):
         src, dst, col = (T.fi, T.basF, 5) if role == "F" else (T.si, T.basS, 6)
-        op("V", ts1(dst[:], src[:].indirect(lst), cf[:, col:col + 1], A.add), r=["i" + role, key, "cf"], w=["bas" + role])
+        op("V", ts1(dst[:], src[:].indirect(lst), cf[:, col:col + 1], A.add), r=["i" + role + "a", "i" + role + "b", key, "cf"], w=["bas" + role])
         c0 = 0 if role == "F" else 128
         op("P", mm(T.pb[:, c0:c0 + 128], dst[:], T.isc[:]), r=["bas" + role, "k1"], w=["pb" + role], banks=["pb"])
 
     spread_z(0, 21)
-    op("V", [tcopy(T.fi[:], T.off0F[:]), tcopy(T.si[:], T.off0S[:])], r=["LF0", "LS0"], w=["iF", "iS"])
+    op("V", [tcopy(T.fi[:], T.off0F[:]), tcopy(T.si[:], T.off0S[:])], r=["LF0", "LS0"], w=["iFa", "iFb", "iSa", "iSb"])
     base("F", T.pip[:], "pip")
     base("S", T.pip[:], "pip")
 
@@ -229,13 +232,23 @@ def rank_program(g, core, T, topo):
         last = t == RO - 1
         ch, c2, c1 = (3 * t + 1) << 19, (3 * t + 2) << 19, (3 * t + 3) << 19
         offs = {"F": T.off0F if t == 0 else T.offF, "S": T.off0S if t == 0 else T.offS}
-        okey = {"F": "LF0" if t == 0 else "offF", "S": "LS0" if t == 0 else "offS"}
         mkey, mbuf = ("iF", T.fi) if t == 0 else ("mF", T.mF)
+
+        def merge(step, part):
+            a, b = (0, 32) if part == "a" else (32, 128)
+            o = 128 * (t - 1)
+            if step == "m":
+                far = T.lF2[:, o + a:o + b] if t == 1 else T.lF2[:, o:o + 128].indirect(T.ulF[:, a // 16:b // 16])
+                op("V", tt(T.mF[:, a:b], far, T.lF1[:, o + a:o + b], A.max), r=["LFa%d" % t, "LFb%d" % t] + (["LuF"] if t == 2 else []), w=["mF" + part])
+            elif step == "a":
+                op("V", ts1(T.fi[:, a:b], T.mF[:, a:b], 8191, A.bitwise_and), r=["mF" + part], w=["iF" + part])
+            else:
+                op("V", tcopy(T.offF[:, a:b], T.fi[:, a:b]), r=["iF" + part], w=["offF" + part])
 
         def gather(qn, role, c):
             o = T.xg[:, 512 * c + (role == "S"):512 * c + 512:2]
             i = T.X[:].indirect(offs[role][:, 16 * c:16 * c + 16])
-            op(qn, tcopy(o, i) if qn == "V" else act(o, i, F.Copy), r=["X", okey[role]], w=["x%s%d" % (role, c)])
+            op(qn, tcopy(o, i) if qn == "V" else act(o, i, F.Copy), r=["X", "L%s0" % role if t == 0 else "off" + role + "ab"[c > 1]], w=["x%s%d" % (role, c)])
 
         def fix(c, e):
             op("V", tt(T.zrep[:, 512 * c:512 * e:32], T.xg[:, 512 * c:512 * e:32], T.zl[:, 128 * t + 16 * c:128 * t + 16 * e], A.min),
@@ -259,15 +272,19 @@ def rank_program(g, core, T, topo):
 
         if t == 0:
             seqS = "S0 F1 S1 S2 S3 S4 S5 F7 S6 S7"
-            seqV = "g0 f0 s0 g2 f1 g3 s1 f23 s2 g4 s3 g5 f45 s4 g6 s5 f67 s6"
+            seqV = "A0 g0 g2 f01 g3 s0 s1 f23 g4 s2 g5 s3 f45 g6 s4 f67 s5 s6"
         else:
-            seqS = "S0 S1 F1 S2 F3 S3 S4 S5 S6 F7 S7"
-            seqV = "g0 b0 f0 s0 f1 g2 s1 f23 s2 g4 s3 g5 f45 s4 g6 s5 f67 s6"
-        for x in seqS.split():
-            gather("S", x[0], int(x[1]))
+            seqS = "S0 S1 F1 S2 F3 S3 S4 S5 F7 S6 S7"
+            seqV = "ma mb aa ab oa g0 ob A0 f0 b0 s0 f1 g2 s1 f23 g4 s2 g5 s3 f45 g6 s4 f67 s5 s6"
         for x in seqV.split():
+            if x[0] in "mao":
+                merge(x[0], x[1])
+                continue
             c = int(x[1])
-            if x[0] == "g":
+            if x[0] == "A":
+                for y in seqS.split():
+                    gather("S", y[0], int(y[1]))
+            elif x[0] == "g":
                 gather("V", "F", c)
             elif x[0] == "b":
                 base("F", T.pip[:], "pip")
@@ -300,72 +317,100 @@ def rank_program(g, core, T, topo):
             lambda: (op("V", ts2(T.hpad[:, 15:128:16], T.hc[:], float(ch), 2.0 ** 18, A.add, A.mult), r=["hc"], w=["hpad"]),
                      op("P", mm(T.ph[:, 0:128], T.hpad[:], T.isc[:]), r=["hpad", "k1"], w=["ht"], banks=["ph"])),
         ]
+        op("V", tt(T.u0[:], T.pv[:, 0:8], T.trep[:, 0:256:32], A.is_lt), r=["s0", "trep"], w=["u0"], banks=["pv"])
         fill.pop(0)()
+        op("V", tt(T.pb[:, 0:128:16], T.pb[:, 0:128:16], T.u0[:], A.add), r=["u0"], w=["pbF"], banks=["pb"])
         fill.pop(0)()
 
-        op("V", tt(T.u3[:], T.pg[:, 0:256], T.trep[:], A.is_lt), r=["gain" + k for k in tops] + ["trep"], w=["u3"], banks=["pg"])
+        for h in (0, 1):
+            op("V", tt(T.u3[:, 128 * h:128 * h + 128], T.pg[:, 128 * h:128 * h + 128], T.trep3[:, 128 * h:128 * h + 128], A.is_lt),
+               r=["gain" + k for k in tops] + ["trep3"], w=["u3%d" % h], banks=["pg"])
         fill.pop(0)()
-        op("V", lambda: V.transpose(T.u2[:], T.u3[:]), r=["u3"], w=["u2", "u2f"])
+        for h in (0, 1):
+            op("V", lambda: V.transpose(T.u2[:, 128 * h:128 * h + 128], T.u3[:, 128 * h:128 * h + 128]), r=["u3%d" % h], w=["u2%d" % h])
         fill.pop(0)()
-        op("V", tt(T.u2[:, 0:256:32], T.pv[:, 0:8], T.trep[:, 0:256:32], A.is_lt), r=["s0", "trep", "u2"], w=["u2f"], banks=["pv"])
-        op("V", tt(T.b0[:], T.u2[:, 1:256:2], T.pb[:, 128:256], A.add), r=["u2", "pbS"], w=["B0"], banks=["pb"])
-        op("V", tt(T.pa[:, 0], T.u2[:, 0:256:2], T.pb[:, 0:128], A.add), r=["u2", "u2f", "pbF"], w=["A0"], banks=["pb", "pa"])
-
-        op("P", [mm(T.pc[:, 128:256], T.u2[:, 0:256:2], T.pbp[:], True, False), mm(T.pc[:, 128:256], T.u2[:, 1:256:2], T.pbn[:], False, True)],
-           r=["u2", "u2f", "k2"], w=["df"], banks=["pc"])
+        for h in (0, 1):
+            op("V", [tt(T.b0[:, 4 * h:4 * h + 4], T.u2[:, 128 * h + 1:128 * h + 128:2], T.pb[:, 128 + 64 * h:192 + 64 * h], A.add),
+                     tt(T.pa[:, 0, 4 * h:4 * h + 4], T.u2[:, 128 * h:128 * h + 128:2], T.pb[:, 64 * h:64 * h + 64], A.add)],
+               r=["u2%d" % h, "pbS", "pbF"], w=["AB%d" % h], banks=["pb", "pa"])
         if not last:
-            op("P", mm(T.pd[:, 0:256], T.ones[:], T.u2[:]), r=["u2", "u2f", "ones"], w=["pd"], banks=["pd"])
-        op("S", act(T.d1[:], T.pc[:, 128:256], F.Copy), r=["df"], w=["d1"], banks=["pc"])
-        op("P", mm(T.pc[:, 256:384], T.blk[:], T.d1[:]), r=["d1", "k1"], w=["ab"], banks=["pc"])
-        if not last:
-            op("S", act(T.junk[:], T.pd[:, 0:256], F.Identity, accum_out=T.tot[:, 0:1]), r=["pd"], w=["tot"], banks=["pd"])
             op("P", [mm(T.pv[:, 16:24], T.ww[:, 15 - c:143 - c], T.top[:, PAD + 32 * c + 31:PAD + 4096:512], c == 0, c == 15)
                      for c in range(16)], r=tops + ["k3"], w=["vd"], banks=["pv"])
-        op("S", [act(T.s1[:], T.pc[:, 256:384], F.Sign, bias=-0.5), act(T.s2[:], T.pc[:, 256:384], F.Sign, bias=-0.5, scale=-1.0)],
-           r=["ab"], w=["s1", "s2"], banks=["pc"])
-        op("S", act(T.dl[:], T.s2[:], F.Identity, scale=float(c1 + c2)), r=["s2"], w=["dl"])
-        if not last:
-            spread_z(t + 1, 0)
 
-        def view(buf, pre, pair, bit, val):
-            rem = [b for b in (4, 3, 2, 1, 0) if b != pair]
-            return buf[(slice(None),) + pre + (slice(None),) + tuple(val if b == bit else slice(None) for b in rem)]
+        def who_won():
+            op("V", tcopy(T.u2[:, 0:256:32], T.u0[:]), r=["u0"], w=["u20", "u21"])
+            uk = ["u20", "u21"]
+            op("P", [mm(T.pc[:, 128:256], T.u2[:, 0:256:2], T.pbp[:], True, False), mm(T.pc[:, 128:256], T.u2[:, 1:256:2], T.pbn[:], False, True)],
+               r=uk + ["k2"], w=["df"], banks=["pc"])
+            if not last:
+                op("P", mm(T.pd[:, 0:256], T.ones[:], T.u2[:]), r=uk + ["ones"], w=["pd"], banks=["pd"])
+            op("S", act(T.d1[:], T.pc[:, 128:256], F.Copy), r=["df"], w=["d1"], banks=["pc"])
+            op("P", mm(T.pc[:, 256:384], T.blk[:], T.d1[:]), r=["d1", "k1"], w=["ab"], banks=["pc"])
+            if not last:
+                op("S", act(T.junk[:], T.pd[:, 0:256], F.Identity, accum_out=T.tot[:, 0:1]), r=["pd"], w=["tot"], banks=["pd"])
+            op("S", [act(T.s1[:], T.pc[:, 256:384], F.Sign, bias=-0.5), act(T.s2[:], T.pc[:, 256:384], F.Sign, bias=-0.5, scale=-1.0)],
+               r=["ab"], w=["s1", "s2"], banks=["pc"])
+            op("S", act(T.dl[:], T.s2[:], F.Identity, scale=float(c1 + c2)), r=["s2"], w=["dl"])
+            if not last:
+                spread_z(t + 1, 0)
 
-        gen = [T.b0, T.b1]
+        def view(buf, pre, gs, pair, fixed, flip=()):
+            return buf[(slice(None),) + pre + (gs,) + tuple(
+                fixed[b] if b in fixed else slice(None, None, -1 if b in flip else None) for b in (4, 3, 2, 1, 0) if b != pair)]
+
         cI = T.c1i[:, 128 * t:128 * t + 128]
-        for s, pr in enumerate(STAGES):
-            lev = FIRST.get(s, 0)
-            src_b = gen[s % 2]
-
-            def in_b(bit, v):
-                if lev >= 4:
-                    return (T.b4 if lev == 4 else T.b5)[:, :, 1 - v, ::-1]
-                return view(src_b, (), pr, bit, 1 - v if lev else v)
-
-            if s < 14:
-                nx, nlev = STAGES[s + 1], FIRST.get(s + 1, 0)
-                fns = []
-                for nv in (0, 1):
-                    for dd in (0, 1):
-                        if nv == 0:
-                            o = view(T.pa, ((s + 1) % 2,), nx, pr, dd)
-                        elif nlev >= 4:
-                            o = (T.b4 if nlev == 4 else T.b5)[:, :, :, dd::2]
-                        else:
-                            o = view(gen[(s + 1) % 2], (), nx, pr, 1 - dd if nlev == 3 else dd)
-                        fns.append(tt(o, view(T.pa, (s % 2,), pr, nx, nv), in_b(nx, nv), A.max if dd else A.min))
-                op("V", fns, r=["A%d" % (s % 2), "B%d" % (s % 2)], w=["A%d" % ((s + 1) % 2), "B%d" % ((s + 1) % 2)], banks=["pa"])
-                if fill:
-                    fill.pop(0)()
-                if s == 8:
-                    op("P", mm(T.pt[:, 0:128], cI, T.s1[:], True, False), r=["s1", "k3"], w=["tlo"], banks=["pt"])
-                    op("P", mm(T.pg[:, 256:384], cI, T.s1[:], True, False), r=["s1", "k3"], w=["thi"], banks=["pg"])
-                    op("V", tt(T.a3[:], T.ph[:, 0:128], mbuf[:], A.max), r=["ht", mkey], w=["a3"], banks=["ph"])
-            else:
-                for hv, o, key, ps, bk in ((0, T.dlo, "lo", T.pt[:, 0:128], "pt"), (1, T.dhi, "hi", T.pg[:, 256:384], "pg")):
-                    op("V", [tt(o[:, dd:128:2], view(T.pa, (s % 2,), pr, 4, hv), in_b(4, hv), A.max if dd else A.min) for dd in (0, 1)],
-                       r=["A%d" % (s % 2), "B%d" % (s % 2)], w=["d" + key], banks=["pa"])
-                    op("P", mm(ps, o[:], T.p0[:], False, True), r=["d" + key, "k2"], w=["t" + key], banks=[bk])
+        l0 = 24 * t
+        mx = (A.min, A.max)
+        for s, pr in enumerate(STAGES[:14]):
+            lev, nx, nlev = FIRST.get(s, 0), STAGES[s + 1], FIRST.get(s + 1, 0)
+            for h in (0, 1):
+                gs = slice(4 * h, 4 * h + 4)
+                if s % 2 == 0:
+                    ib_ = T.b4[:, 8 * h:8 * h + 8, ::-1] if lev == 4 else T.b5[:, gs, ::-1] if lev == 5 else T.b0[:, gs]
+                    op("V", [tt(view(T.cc, (), gs, -1, {pr: dd}), T.pa[:, 0, gs], ib_, mx[dd]) for dd in (0, 1)],
+                       r=["AB%d" % h], w=["C%d" % h], banks=["pa"])
+                else:
+                    fns = []
+                    for nv in (0, 1):
+                        for dd in (0, 1):
+                            if nv == 0:
+                                o = view(T.pa, (0,), gs, nx, {pr: dd})
+                            elif nlev == 4:
+                                o = T.b4[:, 8 * h:8 * h + 8, dd::2]
+                            elif nlev == 5:
+                                o = T.b5[:, gs, dd::2]
+                            else:
+                                o = view(T.b0, (), gs, nx, {pr: dd})
+                            fns.append(tt(o, view(T.cc, (), gs, -1, {pr: 0, nx: nv}),
+                                          view(T.cc, (), gs, -1, {pr: 1, nx: 1 - nv if lev else nv}, (0,) if lev == 3 else ()), mx[dd]))
+                    op("V", fns, r=["C%d" % h], w=["AB%d" % h], banks=["pa"])
+            if s == 0:
+                fill.pop(0)()
+            if s == 1:
+                who_won()
+            if s in (2, 4):
+                fill.pop(0)()
+            if s == 8:
+                op("P", mm(T.pt[:, 0:128], cI, T.s1[:], True, False), r=["s1", "k3"], w=["tlo"], banks=["pt"])
+                op("P", mm(T.pg[:, 256:384], cI, T.s1[:], True, False), r=["s1", "k3"], w=["thi"], banks=["pg"])
+            if s == 8 and not last:
+                op("V", [ts2(T.tl[:, 0:16], T.jl[:], T.tot[:, 0:1], 32768.0, A.subtract, A.add),
+                         ts1(T.tl[:, 16:24], T.jl[:, 0:8], T.tot[:, 0:1], A.add)], r=["tot", "k5"], w=["tl"])
+            if s == 6 and not last:
+                op("V", tcopy(T.pa_[:], T.pv[:, 16:24]), r=["vd"], w=["pa_"], banks=["pv"])
+            if s == 10 and not last:
+                op("V", [ts1(T.tl2[:], T.tl[:], 127, A.bitwise_and), ts1(T.pb_[:], T.pa_[:], 63, A.bitwise_and)], r=["tl", "pa_"], w=["tl2", "pb_"])
+            if s == 12:
+                op("V", tt(T.a3[:], T.ph[:, 0:128], mbuf[:], A.max), r=["ht", mkey + "a", mkey + "b"], w=["a3"], banks=["ph"])
+        for hv, o, key, ps, bk in ((0, T.dlo, "lo", T.pt[:, 0:128], "pt"), (1, T.dhi, "hi", T.pg[:, 256:384], "pg")):
+            for h in (0, 1):
+                gs = slice(4 * h, 4 * h + 4)
+                op("V", [tt(o[:, 64 * h + dd:64 * h + 64:2], view(T.pa, (0,), gs, 0, {4: hv}), view(T.b0, (), gs, 0, {4: hv}), mx[dd])
+                         for dd in (0, 1)], r=["AB%d" % h], w=["d%s%d" % (key, h)], banks=["pa"])
+            op("P", mm(ps, o[:], T.p0[:], False, True), r=["d%s0" % key, "d%s1" % key, "k2"], w=["t" + key], banks=[bk])
+        if not last:
+            op("V", [tcopy(T.lst[:, l0:l0 + 24], T.tl2[:]), tt(T.pa_[:], T.pb_[:], T.plb[:], A.add)], r=["tl2", "pb_", "k2"], w=["lst%d" % t, "pa_"])
+            op("V", tcopy(T.pl[:], T.pa_[:]), r=["pa_"], w=["pl"])
 
         o0 = 256 * t
         p1lo, p1hi, p2lo, p2hi = T.o1[:, o0:o0 + 128], T.o1[:, o0 + 128:o0 + 256], T.o2[:, o0:o0 + 128], T.o2[:, o0 + 128:o0 + 256]
@@ -383,18 +428,11 @@ def rank_program(g, core, T, topo):
             send([(q - d, p1hi, T.lH1[:, sl], "Ha%d" % t), (q + 1, p2hi, T.lH2[:, sl], "Hb%d" % t)], ["phi"])
 
         if not last:
-            l0 = 24 * t
-            op("V", [ts2(T.tl[:, 0:16], T.jl[:], T.tot[:, 0:1], 32768.0, A.subtract, A.add),
-                     ts1(T.tl[:, 16:24], T.jl[:, 0:8], T.tot[:, 0:1], A.add), tcopy(T.pa_[:], T.pv[:, 16:24])],
-               r=["tot", "k5", "vd"], w=["tl", "pa_"], banks=["pv"])
-            op("V", [ts1(T.tl2[:], T.tl[:], 127, A.bitwise_and), ts1(T.pb_[:], T.pa_[:], 63, A.bitwise_and)], r=["tl", "pa_"], w=["tl2", "pb_"])
-            op("V", [tcopy(T.lst[:, l0:l0 + 24], T.tl2[:]), tt(T.pa_[:], T.pb_[:], T.plb[:], A.add)], r=["tl2", "pb_", "k2"], w=["lst%d" % t, "pa_"])
             un = T.lst[:, l0 + 16:l0 + 24]
             if t == 0:
                 send([(q + 4, un, T.ulF[:], "uF"), (q + 1, un, T.ulH1[:], "uH1")], ["lst0"])
             else:
                 send([(q + 1, un, T.ulH2[:], "uH2")], ["lst1"])
-            op("V", tcopy(T.pl[:], T.pa_[:]), r=["pa_"], w=["pl"])
             op("V", tcopy(T.X[:].indirect(T.pl[:]), E), r=["pl"] + tops, w=["X"])
         else:
             op("V", [tt(T.junk[:, 0:128], T.lH2[:, 0:128], T.lH1[:, 0:128], A.max),
@@ -406,13 +444,10 @@ def rank_program(g, core, T, topo):
         if not last:
             own = p2lo if t == 0 else p2lo.indirect(T.lst[:, 16:24])
             op("V", tt(T.mS[:], own, T.lS[:, sl], A.max), r=["p2lo", "LS%d" % d, "lst0"], w=["mS"])
-            op("V", ts1(T.si[:], T.mS[:], 8191, A.bitwise_and), r=["mS"], w=["iS"])
-            op("V", tcopy(T.offS[:], T.si[:].indirect(T.lst[:, l0:l0 + 8])), r=["iS", "lst%d" % t], w=["offS"])
+            op("V", ts1(T.si[:], T.mS[:], 8191, A.bitwise_and), r=["mS"], w=["iSa", "iSb"])
+            op("V", tcopy(T.offS[:, 0:32], T.si[:].indirect(T.lst[:, l0:l0 + 2])), r=["iSa", "lst%d" % t], w=["offSa"])
+            op("V", tcopy(T.offS[:, 32:128], T.si[:].indirect(T.lst[:, l0 + 2:l0 + 8])), r=["iSa", "lst%d" % t], w=["offSb"])
             base("S", T.lst[:, l0 + 8:l0 + 16], "lst%d" % t)
-            far = T.lF2[:, sl] if t == 0 else T.lF2[:, sl].indirect(T.ulF[:])
-            op("V", tt(T.mF[:], far, T.lF1[:, sl], A.max), r=["LFa%d" % d, "LFb%d" % d] + (["LuF"] if t else []), w=["mF"])
-            op("V", ts1(T.fi[:], T.mF[:], 8191, A.bitwise_and), r=["mF"], w=["iF"])
-            op("V", tcopy(T.offF[:], T.fi[:]), r=["iF"], w=["offF"])
 
     wait("Y", [lastw["Lzf"]])
     op("Y", lambda: Y.dma_start(T.yz[:], T.zfin[:]), w=["yz"], inc=16)

@@ -46,6 +46,8 @@ ARR = ["z0", "z1", "z2", "zf", "F0", "S0", "S1", "S2", "Fa1", "Fa2", "Fb1", "Fb2
 SEMAPHORES = [q + str(k) for q in POOL for k in range(POOL[q])] + ["r" + a for a in ARR] + ["sent"]
 STAGES = [0, 1, 0, 2, 1, 0, 3, 2, 1, 0, 4, 3, 2, 1, 0]
 FIRST = {1: 2, 3: 3, 6: 4, 10: 5}
+SEQ0 = ["S0 F1 S1 S2 S3 S4 S5 F7 S6 S7", "A0 g0 g2 f01 g3 s0 s1 f23 g4 s2 g5 s3 f45 g6 s4 f67 s5 s6"]
+SEQ = ["S0 S1 S2 F1 F2 S3 S4 F4 S5 F6 S6 S7", "ma mb aa ab oa b1 g0 ob A0 f0 b0 s0 f1 g3 s1 f23 g5 s2 s3 f45 g7 s4 f67 s5 s6"]
 
 
 def rank_program(g, core, T, topo):
@@ -162,10 +164,11 @@ def rank_program(g, core, T, topo):
     op("S", lambda: S.dma_start(T.rai[:], T.ra[:]), w=["rai"], inc=16)
     op("Y", lambda: Y.dma_start(T.wi[:, 0:1], T.wg[:]), w=["wi"], inc=16)
     op("Y", lambda: Y.dma_start(T.ti[:, 0:1], T.th[:]), w=["ti"], inc=16)
-    op("S", lambda: S.dma_start(T.X[:], T.xd[:]), w=["X"], inc=16)
+    op("S", lambda: S.dma_start(T.X[:, 0:4096], T.xd[:, 0:4096]), w=["X0"], inc=16)
 
     cf, ci, jf, jt = T.cf, T.ci, T.jf, T.jt
     op("G", lambda: g.iota(ci[:, 0:1], [[0, 1]], 0, 1), w=["ci0"])
+    op("G", lambda: g.iota(T.ja[:], [[1, 4], [64, 2]], 0, 0), w=["ja"])
     op("G", lambda: g.iota(jf[:], [[1, 144]], 0, 0, allow_small_or_imprecise_dtypes=True), w=["jf"])
     op("G", lambda: g.iota(jt[:], [[1, 8], [0, 32]], 0, 0, allow_small_or_imprecise_dtypes=True), w=["jt"])
     send([(q + 1, T.zown[:], T.zl[:, 0:128], "z0")], ["zown"])
@@ -175,34 +178,31 @@ def rank_program(g, core, T, topo):
     op("V", [ts1(ci[:, 1:2], ci[:, 0:1], 15, A.bitwise_and), ts1(ci[:, 2:3], ci[:, 0:1], 4, A.arith_shift_right),
              ts1(ci[:, 3:4], ci[:, 0:1], 31, A.bitwise_and), ts1(ci[:, 4:5], ci[:, 0:1], 5, A.arith_shift_right)], r=["ci0"], w=["ci"])
     op("V", [tcopy(cf[:, 0:5], ci[:, 0:5]), ts1(cf[:, 5:6], ci[:, 1:2], 16384.0, A.mult),
-             ts2(cf[:, 6:7], ci[:, 1:2], 16384.0, 8192.0, A.mult, A.add), ts2(cf[:, 7:8], ci[:, 2:3], 16.0, 15.0, A.mult, A.add)],
-       r=["ci", "ci0"], w=["cf"])
-    op("V", tcopy(T.lo0[:], T.rai[:, 0:256:2]), r=["rai"], w=["lo0"])
-    send([(q + 1, T.lo0[:], T.off0F[:], "F0"), (q - 1, T.lo0[:], T.off0S[:], "S0")], ["lo0"])
+             ts2(cf[:, 6:7], ci[:, 1:2], 16384.0, 8192.0, A.mult, A.add), ts2(cf[:, 7:8], ci[:, 2:3], 16.0, 15.0, A.mult, A.add),
+             ts1(cf[:, 13:14], ci[:, 1:2], 4.0, A.mult)], r=["ci", "ci0"], w=["cf"])
     op("V", [ts2(cf[:, 10:11], ci[:, 3:4], 4.0, cf[:, 4:5], A.mult, A.add),
+             ts1(T.jl[:, 8:16], T.ja[:], cf[:, 13:14], A.add), ts1(T.pip[:], T.ja[:], cf[:, 13:14], A.add),
              ts2(T.jl[:, 0:8], jf[:, 0:8], 16.0, cf[:, 1:2], A.mult, A.add),
              ts1(T.ibf[:], jf[:, 0:128], cf[:, 0:1], A.is_equal),
              ts2(T.isc[:], jf[:, 0:128], cf[:, 0:1], 2.0 ** -18, A.is_equal, A.mult),
              ts1(T.gp[:], jf[:, 0:8], cf[:, 2:3], A.is_equal),
              ts1(cf[:, 11:12], cf[:, 3:4], 0.0, A.not_equal), ts2(cf[:, 12:13], cf[:, 3:4], 0.0, -8192.0, A.is_equal, A.mult),
              ts2(T.gn[:], jf[:, 0:8], cf[:, 2:3], -1.0, A.is_equal, A.mult),
-             ts1(T.blk[:], jt[:, 0:256:2], cf[:, 2:3], A.is_equal)], r=["cf", "ci", "jf", "jt"], w=["k1"])
-    op("V", [tcopy(cf[:, 8:9], T.wi[:, 0:1]), ts1(cf[:, 9:10], T.ti[:, 0:1], 1.0 / 16, A.mult), tcopy(T.ja[:], T.jl[:, 0:8]),
-             ts1(T.plb[:], T.jl[:, 0:8], 64.0, A.mult),
+             ts1(T.blk[:], jt[:, 0:256:2], cf[:, 2:3], A.is_equal)], r=["cf", "ci", "jf", "jt", "ja"], w=["k1", "k5", "pip"])
+    op("V", tcopy(T.lo0[:], T.rai[:, 0:256:2]), r=["rai"], w=["lo0"])
+    send([(q + 1, T.lo0[:], T.off0F[:], "F0"), (q - 1, T.lo0[:], T.off0S[:], "S0")], ["lo0"])
+    op("Y", lambda: Y.dma_start(T.X[:, 4096:8192], T.xd[:, 4096:8192]), r=["lo0"], w=["X"], inc=16)
+    op("V", [tcopy(cf[:, 8:9], T.wi[:, 0:1]), ts1(cf[:, 9:10], T.ti[:, 0:1], 1.0 / 16, A.mult)], r=["wi", "ti"], w=["k0"])
+    op("V", [ts1(T.plb[:], T.jl[:, 0:8], 64.0, A.mult),
              ts2(T.p0[:], jf[:, 0:128], cf[:, 10:11], 2.0 ** 18, A.is_equal, A.mult),
              ts1(T.pbp[:], jf[:, 0:128], cf[:, 10:11], A.is_equal),
-             ts2(T.pbn[:], jf[:, 0:128], cf[:, 10:11], -1.0, A.is_equal, A.mult)], r=["k1", "wi", "ti"], w=["k2"])
-    op("V", [ts1(T.jb[:], T.ja[:], 31, A.bitwise_and), ts1(T.jc[:], T.ja[:], 5, A.arith_shift_right),
-             ts2(T.tm[:], jt[:], cf[:, 2:3], cf[:, 9:10], A.is_equal, A.mult),
+             ts2(T.pbn[:], jf[:, 0:128], cf[:, 10:11], -1.0, A.is_equal, A.mult)], r=["k1"], w=["k2"])
+    op("V", [ts2(T.tm[:], jt[:], cf[:, 2:3], cf[:, 9:10], A.is_equal, A.mult),
              ts2(T.wgr[:], jf[:, 0:8], cf[:, 2:3], cf[:, 8:9], A.is_equal, A.mult),
              ts2(T.ww[:], jf[:], cf[:, 7:8], cf[:, 8:9], A.is_equal, A.mult)]
-       + [ts1(T.c1i[:, 128 * t:128 * t + 128], T.ibf[:], float((3 * t + 3) << 19), A.mult) for t in range(RO)], r=["k2"], w=["k3"])
+       + [ts1(T.c1i[:, 128 * t:128 * t + 128], T.ibf[:], float((3 * t + 3) << 19), A.mult) for t in range(RO)], r=["k0", "k1"], w=["k3"])
     op("P", mm(T.pd[:, 0:256], T.onef[:], T.tm[:]), r=["k3", "ones"], w=["pd"], banks=["pd"])
-    op("S", [act(T.trep[:], T.pd[:, 0:256], F.Copy), act(T.trep3[:], T.pd[:, 0:256], F.Identity, scale=cf[:, 11:12], bias=cf[:, 12:13])],
-       r=["pd", "k1"], w=["trep", "trep3"], banks=["pd"])
-    op("V", [ts1(T.ja[:], T.jb[:], 4.0, A.mult), tcopy(T.ph[:, 128:256], T.rai[:, 1:256:2])], r=["k3", "rai"], w=["k4", "hacc"], banks=["ph"])
-    op("V", tt(T.jl[:, 8:16], T.ja[:], T.jc[:], A.add), r=["k4"], w=["k5"])
-    op("V", tcopy(T.pip[:], T.jl[:, 8:16]), r=["k5"], w=["pip"])
+    op("V", tcopy(T.ph[:, 128:256], T.rai[:, 1:256:2]), r=["rai"], w=["hacc"], banks=["ph"])
 
     def zslot(t):
         return T.zl[:, 128 * t:128 * t + 128]
@@ -216,13 +216,18 @@ def rank_program(g, core, T, topo):
     def base(role, lst, key):
         src, dst, col = (T.fi, T.basF, 5) if role == "F" else (T.si, T.basS, 6)
         op("V", ts1(dst[:], src[:].indirect(lst), cf[:, col:col + 1], A.add), r=["i" + role + "a", "i" + role + "b", key, "cf"], w=["bas" + role])
-        c0 = 0 if role == "F" else 128
-        op("P", mm(T.pb[:, c0:c0 + 128], dst[:], T.isc[:]), r=["bas" + role, "k1"], w=["pb" + role], banks=["pb"])
 
-    spread_z(0, 21)
+    def turn_base(role):
+        c0, src = (0, T.basF) if role == "F" else (128, T.basS)
+        op("P", mm(T.pb[:, c0:c0 + 128], src[:], T.isc[:]), r=["bas" + role, "k1"], w=["pb" + role], banks=["pb"])
+
+    spread_z(0, 19)
+    op("S", [act(T.trep[:], T.pd[:, 0:256], F.Copy), act(T.trep3[:], T.pd[:, 0:256], F.Identity, scale=cf[:, 11:12], bias=cf[:, 12:13])],
+       r=["pd", "k1"], w=["trep", "trep3"], banks=["pd"])
     op("V", [tcopy(T.fi[:], T.off0F[:]), tcopy(T.si[:], T.off0S[:])], r=["LF0", "LS0"], w=["iFa", "iFb", "iSa", "iSb"])
-    base("F", T.pip[:], "pip")
     base("S", T.pip[:], "pip")
+    turn_base("S")
+    base("F", T.pip[:], "pip")
 
     E = T.top[:, PAD + 31:PAD + 4096:32]
     tops = ["top%d" % c for c in range(7)] + ["top7a", "top7b"]
@@ -248,7 +253,7 @@ def rank_program(g, core, T, topo):
         def gather(qn, role, c):
             o = T.xg[:, 512 * c + (role == "S"):512 * c + 512:2]
             i = T.X[:].indirect(offs[role][:, 16 * c:16 * c + 16])
-            op(qn, tcopy(o, i) if qn == "V" else act(o, i, F.Copy), r=["X", "L%s0" % role if t == 0 else "off" + role + "ab"[c > 1]], w=["x%s%d" % (role, c)])
+            op(qn, tcopy(o, i) if qn == "V" else act(o, i, F.Copy), r=["X", "X0", "L%s0" % role if t == 0 else "off" + role + "ab"[c > 1]], w=["x%s%d" % (role, c)])
 
         def fix(c, e):
             op("V", tt(T.zrep[:, 512 * c:512 * e:32], T.xg[:, 512 * c:512 * e:32], T.zl[:, 128 * t + 16 * c:128 * t + 16 * e], A.min),
@@ -260,8 +265,6 @@ def rank_program(g, core, T, topo):
             key = "top%d%s" % (c, part)
             op("V", lambda: V.tensor_tensor_scan(T.top[:, PAD + a:PAD + b], T.xg[:, a:b], T.zrep[:, a:b], 0.0, A.max, A.min),
                r=["xF%d" % c, "xS%d" % c, "zf%d" % c, "zrV", "zrS"], w=[key])
-            if part == "b":
-                op("P", mm(T.pv[:, 8:16], E, T.wgr[:]), r=tops + ["k3"], w=["v2"], banks=["pv"])
             fns = []
             for ib in range(a // 128, b // 128):
                 c0 = PAD + 128 * ib
@@ -271,11 +274,9 @@ def rank_program(g, core, T, topo):
             op("P", fns, r=[key, tops[k - 1] if k else "pad", "k1"], w=["gain" + key], banks=["pg"])
 
         if t == 0:
-            seqS = "S0 F1 S1 S2 S3 S4 S5 F7 S6 S7"
-            seqV = "A0 g0 g2 f01 g3 s0 s1 f23 g4 s2 g5 s3 f45 g6 s4 f67 s5 s6"
+            seqS, seqV = SEQ0
         else:
-            seqS = "S0 S1 F1 S2 F3 S3 S4 S5 F7 S6 S7"
-            seqV = "ma mb aa ab oa g0 ob A0 f0 b0 s0 f1 g2 s1 f23 g4 s2 g5 s3 f45 g6 s4 f67 s5 s6"
+            seqS, seqV = SEQ
         for x in seqV.split():
             if x[0] in "mao":
                 merge(x[0], x[1])
@@ -287,7 +288,11 @@ def rank_program(g, core, T, topo):
             elif x[0] == "g":
                 gather("V", "F", c)
             elif x[0] == "b":
-                base("F", T.pip[:], "pip")
+                if c == 0:
+                    base("F", T.pip[:], "pip")
+                else:
+                    base("S", T.lst[:, 24 * t - 16:24 * t - 8], "lst%d" % (t - 1))
+                    turn_base("S")
             elif x[0] == "f":
                 fix(c, int(x[-1]) + 1)
                 if x[-1] == "7":
@@ -297,6 +302,8 @@ def rank_program(g, core, T, topo):
                 scan(c)
         scan(7, "a")
         scan(7, "b")
+        turn_base("F")
+        op("P", mm(T.ph[:, 256:264], E, T.wgr[:]), r=tops + ["k3"], w=["v2"], banks=["ph"])
 
         op("P", [mm(T.pc[:, 0:128], T.ibf[:], zslot(t), True, False), mm(T.pc[:, 0:128], T.ibf[:], E, False, True)],
            r=tops + ["Lz%d" % t, "k1"], w=["ze"], banks=["pc"])
@@ -308,7 +315,7 @@ def rank_program(g, core, T, topo):
             send([(q + 1, nz, zslot(t + 1), "z%d" % (t + 1))], ["nz%d" % t])
 
         fill = [
-            lambda: op("V", tcopy(T.ha[:], T.pv[:, 8:16]), r=["v2"], w=["ha"], banks=["pv"]),
+            lambda: op("V", tcopy(T.ha[:], T.ph[:, 256:264]), r=["v2"], w=["ha"], banks=["ph"]),
             lambda: op("V", ts1(T.hb[:], T.ha[:], 4095, A.bitwise_and), r=["ha"], w=["hb"]),
             lambda: op("V", tt(T.ha[:], T.hb[:], T.hb[:], A.mult), r=["hb"], w=["ha"]),
             lambda: op("V", ts1(T.hc[:], T.ha[:], 4, A.arith_shift_right), r=["ha"], w=["hc"]),
@@ -318,21 +325,20 @@ def rank_program(g, core, T, topo):
                      op("P", mm(T.ph[:, 0:128], T.hpad[:], T.isc[:]), r=["hpad", "k1"], w=["ht"], banks=["ph"])),
         ]
         op("V", tt(T.u0[:], T.pv[:, 0:8], T.trep[:, 0:256:32], A.is_lt), r=["s0", "trep"], w=["u0"], banks=["pv"])
-        fill.pop(0)()
-        op("V", tt(T.pb[:, 0:128:16], T.pb[:, 0:128:16], T.u0[:], A.add), r=["u0"], w=["pbF"], banks=["pb"])
-        fill.pop(0)()
 
         for h in (0, 1):
             op("V", tt(T.u3[:, 128 * h:128 * h + 128], T.pg[:, 128 * h:128 * h + 128], T.trep3[:, 128 * h:128 * h + 128], A.is_lt),
                r=["gain" + k for k in tops] + ["trep3"], w=["u3%d" % h], banks=["pg"])
-        fill.pop(0)()
         for h in (0, 1):
             op("V", lambda: V.transpose(T.u2[:, 128 * h:128 * h + 128], T.u3[:, 128 * h:128 * h + 128]), r=["u3%d" % h], w=["u2%d" % h])
-        fill.pop(0)()
+        op("V", tt(T.pb[:, 0:128:16], T.pb[:, 0:128:16], T.u0[:], A.add), r=["u0"], w=["pbF"], banks=["pb"])
         for h in (0, 1):
-            op("V", [tt(T.b0[:, 4 * h:4 * h + 4], T.u2[:, 128 * h + 1:128 * h + 128:2], T.pb[:, 128 + 64 * h:192 + 64 * h], A.add),
-                     tt(T.pa[:, 0, 4 * h:4 * h + 4], T.u2[:, 128 * h:128 * h + 128:2], T.pb[:, 64 * h:64 * h + 64], A.add)],
-               r=["u2%d" % h, "pbS", "pbF"], w=["AB%d" % h], banks=["pb", "pa"])
+            op("V", tt(T.b0[:, 4 * h:4 * h + 4], T.u2[:, 128 * h + 1:128 * h + 128:2], T.pb[:, 128 + 64 * h:192 + 64 * h], A.add),
+               r=["u2%d" % h, "pbS"], w=["AB%d" % h], banks=["pb"])
+        for h in (0, 1):
+            op("V", tt(T.pa[:, 0, 4 * h:4 * h + 4], T.u2[:, 128 * h:128 * h + 128:2], T.pb[:, 64 * h:64 * h + 64], A.add),
+               r=["u2%d" % h, "pbF"], w=["Ak%d" % h], banks=["pb", "pa"])
+        fill.pop(0)()
         if not last:
             op("P", [mm(T.pv[:, 16:24], T.ww[:, 15 - c:143 - c], T.top[:, PAD + 32 * c + 31:PAD + 4096:512], c == 0, c == 15)
                      for c in range(16)], r=tops + ["k3"], w=["vd"], banks=["pv"])
@@ -368,7 +374,7 @@ def rank_program(g, core, T, topo):
                 if s % 2 == 0:
                     ib_ = T.b4[:, 8 * h:8 * h + 8, ::-1] if lev == 4 else T.b5[:, gs, ::-1] if lev == 5 else T.b0[:, gs]
                     op("V", [tt(view(T.cc, (), gs, -1, {pr: dd}), T.pa[:, 0, gs], ib_, mx[dd]) for dd in (0, 1)],
-                       r=["AB%d" % h], w=["C%d" % h], banks=["pa"])
+                       r=["AB%d" % h, "Ak%d" % h], w=["C%d" % h], banks=["pa"])
                 else:
                     fns = []
                     for nv in (0, 1):
@@ -388,15 +394,15 @@ def rank_program(g, core, T, topo):
                 fill.pop(0)()
             if s == 1:
                 who_won()
-            if s in (2, 4):
+            if s in (2, 4, 5, 6, 8):
                 fill.pop(0)()
             if s == 8:
                 op("P", mm(T.pt[:, 0:128], cI, T.s1[:], True, False), r=["s1", "k3"], w=["tlo"], banks=["pt"])
                 op("P", mm(T.pg[:, 256:384], cI, T.s1[:], True, False), r=["s1", "k3"], w=["thi"], banks=["pg"])
-            if s == 8 and not last:
+            if s == 7 and not last:
                 op("V", [ts2(T.tl[:, 0:16], T.jl[:], T.tot[:, 0:1], 32768.0, A.subtract, A.add),
                          ts1(T.tl[:, 16:24], T.jl[:, 0:8], T.tot[:, 0:1], A.add)], r=["tot", "k5"], w=["tl"])
-            if s == 6 and not last:
+            if s == 3 and not last:
                 op("V", tcopy(T.pa_[:], T.pv[:, 16:24]), r=["vd"], w=["pa_"], banks=["pv"])
             if s == 10 and not last:
                 op("V", [ts1(T.tl2[:], T.tl[:], 127, A.bitwise_and), ts1(T.pb_[:], T.pa_[:], 63, A.bitwise_and)], r=["tl", "pa_"], w=["tl2", "pb_"])
@@ -433,7 +439,10 @@ def rank_program(g, core, T, topo):
                 send([(q + 4, un, T.ulF[:], "uF"), (q + 1, un, T.ulH1[:], "uH1")], ["lst0"])
             else:
                 send([(q + 1, un, T.ulH2[:], "uH2")], ["lst1"])
+            if t:
+                op("V", tcopy(T.hx[:], p2lo.indirect(T.lst[:, 16:24])), r=["p2lo", "lst0"], w=["hx"])
             op("V", tcopy(T.X[:].indirect(T.pl[:]), E), r=["pl"] + tops, w=["X"])
+            op("V", tcopy(T.pa[:, 1], T.hx[:] if t else p2lo), r=["hx", "p2lo"], w=["own"], banks=["pa"])
         else:
             op("V", [tt(T.junk[:, 0:128], T.lH2[:, 0:128], T.lH1[:, 0:128], A.max),
                      tt(T.junk[:, 128:256], T.lH2[:, 128:256].indirect(T.ulH1[:]), T.lH1[:, 128:256], A.max)],
@@ -442,12 +451,10 @@ def rank_program(g, core, T, topo):
                 op("V", tt(T.ph[:, 128:256], T.junk[:, 128 * k:128 * k + 128], T.ph[:, 128:256], A.max), r=["jk"], w=["hacc"], banks=["ph"])
 
         if not last:
-            own = p2lo if t == 0 else p2lo.indirect(T.lst[:, 16:24])
-            op("V", tt(T.mS[:], own, T.lS[:, sl], A.max), r=["p2lo", "LS%d" % d, "lst0"], w=["mS"])
+            op("V", tt(T.mS[:], T.pa[:, 1], T.lS[:, sl], A.max), r=["own", "LS%d" % d], w=["mS"], banks=["pa"])
             op("V", ts1(T.si[:], T.mS[:], 8191, A.bitwise_and), r=["mS"], w=["iSa", "iSb"])
             op("V", tcopy(T.offS[:, 0:32], T.si[:].indirect(T.lst[:, l0:l0 + 2])), r=["iSa", "lst%d" % t], w=["offSa"])
             op("V", tcopy(T.offS[:, 32:128], T.si[:].indirect(T.lst[:, l0 + 2:l0 + 8])), r=["iSa", "lst%d" % t], w=["offSb"])
-            base("S", T.lst[:, l0 + 8:l0 + 16], "lst%d" % t)
 
     wait("Y", [lastw["Lzf"]])
     op("Y", lambda: Y.dma_start(T.yz[:], T.zfin[:]), w=["yz"], inc=16)

@@ -13,46 +13,79 @@ def sb(shape, d):
 
 SCRATCH = {
     "X": sb([8192], bf), "xg": sb([4096], bf), "zrep": sb([4096], bf), "top": sb([4096 + 16], bf),
-    "rai": sb([256], i32), "zown": sb([128], bf), "wi": sb([4], i32), "ti": sb([4], i32), "lo0": sb([128], u16),
+    "rai": sb([256], i32), "zown": sb([128], bf), "wi": sb([256], i32), "wf": sb([256], f32), "lo0": sb([128], u16),
     "jf": sb([144], f32), "jt": sb([256], f32), "ci": sb([8], i32), "cf": sb([16], f32),
     "ibf": sb([128], bf), "isc": sb([128], f32), "p0": sb([128], f32), "pbp": sb([128], bf), "pbn": sb([128], bf),
     "gp": sb([8], bf), "gn": sb([8], bf), "wgr": sb([8], bf), "blk": sb([128], bf), "ones": sb([128], bf),
-    "onef": sb([128], f32), "ww": sb([144], bf), "c1i": sb([384], bf), "tm": sb([256], f32), "trep": sb([256], f32),
-    "jl": sb([16], f32), "ja": sb([8], i32), "jb": sb([8], i32), "jc": sb([8], i32), "pip": sb([8], u16), "plb": sb([8], i32),
+    "onen": sb([128], f32), "ww": sb([144], bf), "c1i": sb([384], bf), "tm": sb([256], f32), "trep": sb([8], f32),
+    "jl": sb([16], f32), "ja": sb([8], i32), "pip": sb([8], u16), "plb": sb([8], i32),
     "zl": sb([384], bf), "zfin": sb([128], f32), "nzb": sb([256], bf), "nzf": sb([128], f32),
     "offF": sb([128], u16), "offS": sb([128], u16), "off0F": sb([128], u16), "off0S": sb([128], u16),
     "mF": sb([128], i32), "mS": sb([128], i32), "fi": sb([128], i32), "si": sb([128], i32),
     "basF": sb([128], f32), "basS": sb([128], f32),
-    "u3": sb([256], bf), "u2": sb([256], bf),
-    "b0": sb([8, 2, 2, 2, 2], f32), "cc": sb([8, 2, 2, 2, 2, 2], f32), "b4": sb([16, 8], f32), "b5": sb([8, 16], f32),
-    "u0": sb([8], bf), "trep3": sb([256], f32),
+    "u3": sb([256], bf), "u2": sb([256], bf), "u0": sb([128], bf), "imk": sb([128], f32),
+    "kF": sb([128], f32), "e0": sb([4, 8, 32], f32), "e1": sb([4, 8, 32], f32),
+    "j16": sb([8, 1, 2, 2, 8], f32), "j8": sb([8, 2, 2, 2, 4], f32), "j4": sb([8, 4, 2, 2, 2], f32), "j2": sb([8, 8, 2, 2], f32),
     "dlo": sb([128], f32), "dhi": sb([128], f32),
-    "ha": sb([8], i32), "hb": sb([8], i32), "hc": sb([8], i32), "hpad": sb([128], f32), "a3": sb([128], f32),
-    "d1": sb([128], bf), "s1": sb([128], bf), "s2": sb([128], bf), "dl": sb([128], bf),
+    "ha": sb([8], i32), "hb": sb([8], i32), "hc": sb([8], i32), "hs": sb([8], f32), "hpad": sb([128], f32), "a3": sb([128], f32),
+    "sgn": sb([256], bf), "alt": sb([256], bf), "hold": sb([128], bf), "ab0": sb([128], bf), "ab": sb([128], bf),
+    "s1": sb([128], bf), "s2": sb([128], bf), "pri": sb([768], bf), "idf": sb([128], f32),
     "junk": sb([256], f32), "tot": sb([4], f32), "tl": sb([24], i32), "tl2": sb([24], i32), "lst": sb([48], u16),
-    "pa_": sb([8], i32), "pb_": sb([8], i32), "pl": sb([8], u16),
+    "pa_": sb([8], i32), "pb_": sb([8], i32), "pc_": sb([8], i32), "pl": sb([8], u16),
     "o1": sb([768], f32), "o2": sb([768], f32),
     "lS": sb([256], f32), "lF1": sb([256], f32), "lF2": sb([256], f32),
     "lH1": sb([256], f32), "lH2": sb([256], f32), "lE1": sb([256], f32), "lE2": sb([256], f32),
-    "ulF": sb([8], u16), "ulH1": sb([8], u16), "ulH2": sb([8], u16),
+    "ulF": sb([8], u16), "ulH2": sb([8], u16), "hi0": sb([128], f32), "lH0": sb([128], f32), "hacc": sb([128], f32),
+    "dl": sb([128], bf),
     "hx": sb([128], f32), "fin": sb([256], i32), "fin2": sb([256], i32), "yo": sb([256], f32),
-    "pg": ("psum", [128, 512], f32), "pb": ("psum", [128, 512], f32), "pa": ("psum", [128, 4, 8, 2, 2, 2, 2], f32),
-    "pt": ("psum", [128, 512], f32), "pv": ("psum", [128, 512], f32), "ph": ("psum", [128, 512], f32),
+    "pg": ("psum", [128, 512], f32), "pb": ("psum", [128, 512], f32),
+    "pt": ("psum", [128, 512], f32), "ph": ("psum", [128, 512], f32),
     "pc": ("psum", [128, 512], f32), "pd": ("psum", [128, 512], f32),
+    "pu": ("psum", [128, 512], f32), "pw": ("psum", [128, 512], f32),
 }
-POOL = {"V": 24, "S": 36, "P": 40, "G": 4, "Y": 10}
+POOL = {"V": 40, "S": 30, "P": 40, "G": 4, "Y": 10}
 ARR = ["z0", "z1", "z2", "zf", "F0", "S0", "S1", "S2", "Fa1", "Fa2", "Fb1", "Fb2", "Ha0", "Ha1", "Hb0", "Hb1",
-       "Ea", "Eb", "uF", "uH1", "uH2"]
+       "Ea", "Eb", "uF", "H0", "uH2"]
 SEMAPHORES = [q + str(k) for q in POOL for k in range(POOL[q])] + ["r" + a for a in ARR] + ["sent"]
-STAGES = [0, 1, 0, 2, 1, 0, 3, 2, 1, 0, 4, 3, 2, 1, 0]
-FIRST = {1: 2, 3: 3, 6: 4, 10: 5}
-SEQ0 = ["S0 F1 S1 S2 S3 S4 S5 F7 S6 S7", "A0 g0 g2 f01 g3 s0 s1 f23 g4 s2 g5 s3 f45 g6 s4 f67 s5 s6"]
-SEQ = ["S0 S1 S2 F1 F2 S3 S4 F4 S5 F6 S6 S7", "ma mb aa ab oa b1 g0 ob A0 f0 b0 s0 f1 g3 s1 f23 g5 s2 s3 f45 g7 s4 f67 s5 s6"]
+STAGES = [(p, sh) for p in (16, 8, 4, 2, 1) for sh in [0] + [x for x in (8, 4, 2, 1) if x >= p]]
+SLOT = {2: 0, 4: 1, 5: 0, 7: 1, 8: 0, 9: 2, 11: 3, 12: 1, 13: 0, 14: 2}
+SEQ0 = ["F1 S0 S1 S23 F6 S45 S6 S7", "A F0 F2 f01 F3 s0 s1 f23 F45 s2 s3 f46 F7 s4 s5 f7 s6"]
+SEQ = ["S0 S13 F1 F2 F46 S4 S6 S7", "b S5 ma mb aa ab oa ob A F0 B f01 F3 s0 s1 f23 F7 s2 f47 s3 s4 s5 s6"]
+
+
+RELAYED = []
+
+
+def helper(core, T, topo):
+    return [c for c in topo.cores_of(core) if topo.die(c) != topo.die(core) and all(topo.may_write(c, x) for x in T.cores if x != core)][0]
+
+
+def spare(core, T, topo):
+    far = topo.engines(core, [x for x in T.cores if x != core][0])
+    return [e for e in topo.engines(core, helper(core, T, topo)) if e not in far]
+
+
+def helper_program(g, core, q, T, topo):
+    land = {"z1": (q + 1, T.zl[:, 128:256]), "Fb1": (q + 3, T.lF2[:, 0:128]), "z2": (q + 1, T.zl[:, 256:384]),
+            "Fb2": (q + 4, T.lF2[:, 128:256]), "zf": (q - 3, T.zfin[:]), "Eb": (q + 1, T.lE2[:])}
+    n = 0
+    for name in RELAYED:
+        dst, ap = land[name]
+        dc = T.cores[dst % N]
+        rid, pid = topo.addr(dc)[:2]
+        g.wait_ge(T.sem["r" + name], len(spare(T.cores[q], T, topo)))
+        g.remote_dma(ap, ap, T.sem["r" + name], T.sem.sent, pid, rid, topo.mask(core, dc))
+        n += len(topo.engines(core, dc))
+    if n:
+        g.wait_ge(T.sem.sent, n)
 
 
 def rank_program(g, core, T, topo):
     q = T.rank_of(core)
     if q is None:
+        for r in range(N):
+            if helper(T.cores[r], T, topo) == core:
+                helper_program(g, core, r, T, topo)
         return
     V, S, P, Y = g.vector, g.scalar, g.tensor, g.sync
     Q = {"V": V, "S": S, "P": P, "G": g, "Y": Y}
@@ -103,12 +136,20 @@ def rank_program(g, core, T, topo):
     def send(parts, r):
         wait("G", deps_of("G", r, (), ()))
         ts = []
-        for k, (dst, src, land, name) in enumerate(parts):
+        direct = [x for x in parts if x[3] not in RELAYED]
+        for dst, src, land, name in parts:
             dc = T.cores[dst % N]
             eng = topo.engines(core, dc)
-            m = len(eng) // len(parts)
+            if name in RELAYED:
+                dc = helper(core, T, topo)
+                eng = spare(core, T, topo)
+                m = len(eng)
+            else:
+                m = len(eng) // len(direct)
+                k = [x[3] for x in direct].index(name)
+                eng = eng[k * m:(k + 1) * m]
             mask = 0
-            for e in eng[k * m:(k + 1) * m]:
+            for e in eng:
                 mask |= 1 << e
             rid, pid = topo.addr(dc)[:2]
             ts.append((rid, pid, mask, src, land, name))
@@ -137,6 +178,9 @@ def rank_program(g, core, T, topo):
     def ts2(o, a, s1, s2, x1, x2):
         return lambda: V.tensor_scalar(o, a, s1, s2, x1, x2)
 
+    def fillc(o, c):
+        return lambda: V.memset(o, c)
+
     def mm(o, l, r, st=True, sp=True):
         return lambda: P.matmul(o, l, r, st, sp)
 
@@ -151,93 +195,143 @@ def rank_program(g, core, T, topo):
         expect("S%d" % t, q + t + 1, 1)
         expect("Fa%d" % t, q - 1, 2)
         expect("Fb%d" % t, q - t - 2, 2)
-        expect("Ha%d" % (t - 1), q + t, 2)
-        expect("Hb%d" % (t - 1), q - 1, 2)
+        expect("Ha%d" % (t - 1), q + t - RO, 2)
+        expect("Hb%d" % (t - 1), q - 1 - RO, 2)
     expect("zf", q + 3, 1)
-    expect("Ea", q + 3, 2)
-    expect("Eb", q - 1, 2)
-    expect("uF", q - 4, 2)
-    expect("uH1", q - 1, 2)
+    expect("Ea", q + 3, 1)
+    expect("Eb", q - 1, 1)
+    expect("uF", q - 4, 1)
+    expect("H0", q - RO, 1)
     expect("uH2", q - 1, 1)
 
     op("Y", lambda: Y.dma_start(T.zown[:], T.zu[:]), w=["zown"], inc=16)
     op("S", lambda: S.dma_start(T.rai[:], T.ra[:]), w=["rai"], inc=16)
-    op("Y", lambda: Y.dma_start(T.wi[:, 0:1], T.wg[:]), w=["wi"], inc=16)
-    op("Y", lambda: Y.dma_start(T.ti[:, 0:1], T.th[:]), w=["ti"], inc=16)
-    op("S", lambda: S.dma_start(T.X[:, 0:4096], T.xd[:, 0:4096]), w=["X0"], inc=16)
+    op("Y", lambda: Y.dma_start(T.wi[0:1, 0:128], T.wg[:]), w=["wi"], inc=16)
+    op("S", lambda: S.dma_start(T.wi[0:1, 128:256], T.th[:]), w=["ti"], inc=16)
+    op("Y", lambda: Y.dma_start(T.X[:, 0:4096], T.xd[:, 0:4096]), w=["X0"], inc=16)
 
     cf, ci, jf, jt = T.cf, T.ci, T.jf, T.jt
     op("G", lambda: g.iota(ci[:, 0:1], [[0, 1]], 0, 1), w=["ci0"])
     op("G", lambda: g.iota(T.ja[:], [[1, 4], [64, 2]], 0, 0), w=["ja"])
     op("G", lambda: g.iota(jf[:], [[1, 144]], 0, 0, allow_small_or_imprecise_dtypes=True), w=["jf"])
-    op("G", lambda: g.iota(jt[:], [[1, 8], [0, 32]], 0, 0, allow_small_or_imprecise_dtypes=True), w=["jt"])
     send([(q + 1, T.zown[:], T.zl[:, 0:128], "z0")], ["zown"])
 
-    op("V", [lambda: V.memset(T.top[:, 0:PAD], 0.0), lambda: V.memset(T.hpad[:], 0.0), lambda: V.memset(T.ones[:], 1.0),
-             lambda: V.memset(T.onef[:], 1.0)], w=["pad", "hpad", "ones"])
+    op("V", [fillc(T.top[:, 0:PAD], 0.0), fillc(T.ones[:], 1.0), fillc(T.onen[:], -1.0), fillc(T.sgn[:], -1.0), fillc(T.hold[:], 1.0)],
+       w=["pad", "ones"])
     op("V", [ts1(ci[:, 1:2], ci[:, 0:1], 15, A.bitwise_and), ts1(ci[:, 2:3], ci[:, 0:1], 4, A.arith_shift_right),
              ts1(ci[:, 3:4], ci[:, 0:1], 31, A.bitwise_and), ts1(ci[:, 4:5], ci[:, 0:1], 5, A.arith_shift_right)], r=["ci0"], w=["ci"])
+    op("V", [fillc(T.hpad[:], 0.0), fillc(T.u0[:], 0.0), fillc(T.ab0[:], 0.0)], w=["hpad", "u0", "ab0"])
     op("V", [tcopy(cf[:, 0:5], ci[:, 0:5]), ts1(cf[:, 5:6], ci[:, 1:2], 16384.0, A.mult),
              ts2(cf[:, 6:7], ci[:, 1:2], 16384.0, 8192.0, A.mult, A.add), ts2(cf[:, 7:8], ci[:, 2:3], 16.0, 15.0, A.mult, A.add),
-             ts1(cf[:, 13:14], ci[:, 1:2], 4.0, A.mult)], r=["ci", "ci0"], w=["cf"])
+             ts1(cf[:, 13:14], ci[:, 1:2], 4.0, A.mult), ts1(cf[:, 14:15], ci[:, 1:2], 15.0, A.not_equal)], r=["ci", "ci0"], w=["cf"])
+    op("V", tcopy(T.lo0[:], T.rai[:, 0:256:2]), r=["rai"], w=["lo0"])
+    send([(q + 1, T.lo0[:], T.off0F[:], "F0"), (q - 1, T.lo0[:], T.off0S[:], "S0")], ["lo0"])
+    op("Y", lambda: Y.dma_start(T.X[:, 4096:8192], T.xd[:, 4096:8192]), r=["lo0"], w=["X"], inc=16)
+    op("G", lambda: g.iota(jt[:], [[1, 8], [0, 32]], 0, 0, allow_small_or_imprecise_dtypes=True), w=["jt"])
+    op("V", tcopy(T.wf[0:1, :], T.wi[0:1, :]), r=["wi", "ti"], w=["wf"])
+    op("P", [mm(T.pd[:, 8 + k:9 + k], T.wf[0:1, 128 * k:128 * k + 128], T.onen[0:1, 0:1]) for k in (0, 1)], r=["wf", "ones"], w=["wt"], banks=["pd"])
     op("V", [ts2(cf[:, 10:11], ci[:, 3:4], 4.0, cf[:, 4:5], A.mult, A.add),
              ts1(T.jl[:, 8:16], T.ja[:], cf[:, 13:14], A.add), ts1(T.pip[:], T.ja[:], cf[:, 13:14], A.add),
              ts2(T.jl[:, 0:8], jf[:, 0:8], 16.0, cf[:, 1:2], A.mult, A.add),
              ts1(T.ibf[:], jf[:, 0:128], cf[:, 0:1], A.is_equal),
-             ts2(T.isc[:], jf[:, 0:128], cf[:, 0:1], 2.0 ** -18, A.is_equal, A.mult),
              ts1(T.gp[:], jf[:, 0:8], cf[:, 2:3], A.is_equal),
-             ts1(cf[:, 11:12], cf[:, 3:4], 0.0, A.not_equal), ts2(cf[:, 12:13], cf[:, 3:4], 0.0, -8192.0, A.is_equal, A.mult),
-             ts2(T.gn[:], jf[:, 0:8], cf[:, 2:3], -1.0, A.is_equal, A.mult),
-             ts1(T.blk[:], jt[:, 0:256:2], cf[:, 2:3], A.is_equal)], r=["cf", "ci", "jf", "jt", "ja"], w=["k1", "k5", "pip"])
-    op("V", tcopy(T.lo0[:], T.rai[:, 0:256:2]), r=["rai"], w=["lo0"])
-    send([(q + 1, T.lo0[:], T.off0F[:], "F0"), (q - 1, T.lo0[:], T.off0S[:], "S0")], ["lo0"])
-    op("Y", lambda: Y.dma_start(T.X[:, 4096:8192], T.xd[:, 4096:8192]), r=["lo0"], w=["X"], inc=16)
-    op("V", [tcopy(cf[:, 8:9], T.wi[:, 0:1]), ts1(cf[:, 9:10], T.ti[:, 0:1], 1.0 / 16, A.mult)], r=["wi", "ti"], w=["k0"])
-    op("V", [ts1(T.plb[:], T.jl[:, 0:8], 64.0, A.mult),
-             ts2(T.p0[:], jf[:, 0:128], cf[:, 10:11], 2.0 ** 18, A.is_equal, A.mult),
-             ts1(T.pbp[:], jf[:, 0:128], cf[:, 10:11], A.is_equal),
-             ts2(T.pbn[:], jf[:, 0:128], cf[:, 10:11], -1.0, A.is_equal, A.mult)], r=["k1"], w=["k2"])
+             ts1(cf[:, 11:12], cf[:, 3:4], 0.0, A.not_equal), ts2(cf[:, 12:13], cf[:, 5:6], cf[:, 14:15], -1.0, A.mult, A.mult),
+             ts2(T.gn[:], jf[:, 0:8], cf[:, 2:3], -1.0, A.is_equal, A.mult)], r=["cf", "ci", "jf", "ja"], w=["kb", "k5", "pip"])
+    op("V", [fillc(T.e0[:, :, :, 24:26], 4.0), fillc(T.e1[:, :, :, 6:8], -1.0)], w=["pads"])
+    op("V", [ts1(cf[:, 8:9], T.pd[:, 8:9], -1.0, A.mult), ts1(cf[:, 9:10], T.pd[:, 9:10], -1.0 / 16, A.mult)], r=["wt"], w=["k0"], banks=["pd"])
+    op("V", [ts1(T.plb[:], T.jl[:, 0:8], 64.0, A.mult), ts1(T.pbp[:], jf[:, 0:128], cf[:, 10:11], A.is_equal),
+             fillc(T.sgn[:, 0:256:32], 0.0), fillc(T.hold[:, 0:128:16], 0.0)], r=["kb", "ones"], w=["kc", "k4"])
+    op("S", [act(T.isc[:], T.ibf[:], F.Identity, scale=2.0 ** -18), act(T.idf[:], T.ibf[:], F.Copy),
+             act(T.imk[:], T.ibf[:], F.Identity, scale=cf[:, 14:15])], r=["kb"], w=["k1"])
     op("V", [ts2(T.tm[:], jt[:], cf[:, 2:3], cf[:, 9:10], A.is_equal, A.mult),
              ts2(T.wgr[:], jf[:, 0:8], cf[:, 2:3], cf[:, 8:9], A.is_equal, A.mult),
-             ts2(T.ww[:], jf[:], cf[:, 7:8], cf[:, 8:9], A.is_equal, A.mult)]
-       + [ts1(T.c1i[:, 128 * t:128 * t + 128], T.ibf[:], float((3 * t + 3) << 19), A.mult) for t in range(RO)], r=["k0", "k1"], w=["k3"])
-    op("P", mm(T.pd[:, 0:256], T.onef[:], T.tm[:]), r=["k3", "ones"], w=["pd"], banks=["pd"])
-    op("V", tcopy(T.ph[:, 128:256], T.rai[:, 1:256:2]), r=["rai"], w=["hacc"], banks=["ph"])
+             ts2(T.ww[:], jf[:], cf[:, 7:8], cf[:, 8:9], A.is_equal, A.mult)], r=["k0", "kb", "jt"], w=["k3"])
+    op("S", [act(T.p0[:], T.pbp[:], F.Identity, scale=2.0 ** 18)]
+       + [act(T.pri[:, 256 * t + 128 * k:256 * t + 128 * k + 128], T.pbp[:], F.Identity, scale=float((3 * t + 3 + k * (3 * t + 2)) << 20))
+          for t in range(RO) for k in (0, 1)], r=["kc"], w=["k2"])
+    op("P", mm(T.pd[:, 0:8], T.onen[:], T.tm[:, 0:256:32]), r=["k3", "ones"], w=["pd"], banks=["pd"])
+    op("V", tcopy(T.hi0[:], T.rai[:, 1:256:2]), r=["rai"], w=["hi0"])
 
     def zslot(t):
         return T.zl[:, 128 * t:128 * t + 128]
 
-    def spread_z(t, nv):
-        ks = list(range(1, 32))
-        if nv:
-            op("V", [tcopy(T.zrep[:, k:4096:32], zslot(t)) for k in ks[:nv]], r=["Lz%d" % t], w=["zrV"])
-        op("S", [act(T.zrep[:, k:4096:32], zslot(t), F.Copy) for k in ks[nv:]], r=["Lz%d" % t], w=["zrS"] + ([] if nv else ["zrV"]))
+    def spread_z(t, qn, a, b, keys):
+        op(qn, [tcopy(T.zrep[:, k:4096:32], zslot(t)) if qn == "V" else act(T.zrep[:, k:4096:32], zslot(t), F.Copy) for k in range(a, b)],
+           r=["Lz%d" % t], w=keys)
 
     def base(role, lst, key):
         src, dst, col = (T.fi, T.basF, 5) if role == "F" else (T.si, T.basS, 6)
         op("V", ts1(dst[:], src[:].indirect(lst), cf[:, col:col + 1], A.add), r=["i" + role + "a", "i" + role + "b", key, "cf"], w=["bas" + role])
 
     def turn_base(role):
-        c0, src = (0, T.basF) if role == "F" else (128, T.basS)
-        op("P", mm(T.pb[:, c0:c0 + 128], src[:], T.isc[:]), r=["bas" + role, "k1"], w=["pb" + role], banks=["pb"])
+        o, src, bk = (T.pb[:, 0:128], T.basF, "pb") if role == "F" else (T.pt[:, 128:256], T.basS, "pt")
+        op("P", mm(o, src[:], T.isc[:], True, role == "S"), r=["bas" + role, "k1"], w=["k" + role], banks=[bk])
 
-    spread_z(0, 19)
-    op("S", [act(T.trep[:], T.pd[:, 0:256], F.Copy), act(T.trep3[:], T.pd[:, 0:256], F.Identity, scale=cf[:, 11:12], bias=cf[:, 12:13])],
-       r=["pd", "k1"], w=["trep", "trep3"], banks=["pd"])
+    spread_z(0, "V", 1, 22, ["zr1", "zr2"])
+    spread_z(0, "S", 22, 32, ["zr0", "zr3"])
+    op("S", act(T.trep[:], T.pd[:, 0:8], F.Identity, scale=-1.0), r=["pd"], w=["trep"], banks=["pd"])
     op("V", [tcopy(T.fi[:], T.off0F[:]), tcopy(T.si[:], T.off0S[:])], r=["LF0", "LS0"], w=["iFa", "iFb", "iSa", "iSb"])
     base("S", T.pip[:], "pip")
     turn_base("S")
     base("F", T.pip[:], "pip")
+    turn_base("F")
 
     E = T.top[:, PAD + 31:PAD + 4096:32]
     tops = ["top%d" % c for c in range(7)] + ["top7a", "top7b"]
+    ALL = slice(0, 8)
+
+    def wires(kind, s, gs, a, b):
+        p, sh = STAGES[s]
+        if s == 0:
+            return (T.kF, T.pu)[kind][:, 128 * kind + 16 * gs.start:128 * kind + 16 * gs.stop]
+        if sh:
+            return (T.e0, T.e1)[kind][:, SLOT[s], gs, a + 8:b + 8]
+        if p == 8:
+            return T.j16[:, gs, 0, a // 8:b // 8, kind]
+        if b - a < 2 * p:
+            return T["j%d" % (2 * p)][:, gs, a // (2 * p), a // p % 2, kind]
+        return T["j%d" % (2 * p)][:, gs, a // (2 * p):b // (2 * p), :, kind]
+
+    def exchange(s, gs, x, a, b, to):
+        p, sh = STAGES[s]
+        if to == 15:
+            out = (T.dlo, T.dhi)[a // 8][:, x:128:2]
+        else:
+            out = wires(x, to, gs, a, b) if STAGES[to][0] == p else T["j%d" % p][:, gs, a // p:b // p, x]
+        if x == 0:
+            return tt(out, wires(1, s, gs, a - sh, b - sh), wires(0, s, gs, a, b), A.max if sh else A.min)
+        return tt(out, wires(1, s, gs, a, b), wires(0, s, gs, a + sh, b + sh), A.min if sh else A.max)
+
+    def stage(s, h):
+        sh = 8 if STAGES[s + 1][1] == 8 else STAGES[s][1] if STAGES[s][1] > 2 else 0
+        op("V", [exchange(s, slice(4 * h, 4 * h + 4), 0, sh, 16, s + 1), exchange(s, slice(4 * h, 4 * h + 4), 1, 0, 16 - sh, s + 1)],
+           r=["w%d_%d" % (s, h), "v%d" % s, "v%dx" % s, "pads"], w=["w%d_%d" % (s + 1, h)], banks=["pu"] * (s == 0))
+
+    def skip(s, n):
+        if STAGES[s][0] == 8:
+            parts = [((0, 0, 8), (1, 8, 16))[n - 1] + (s + 2,)]
+        else:
+            parts = [(0, 4, 8, s + 2), (1, 8, 12, s + 2)] if n == 1 else [(0, 0, 4, s + 3), (1, 12, 16, s + 3)]
+        key = "v%d" % parts[0][3] + "x" * (STAGES[s][0] == 8 and n == 1)
+        op("V", [exchange(s, ALL, *x) for x in parts], r=["w%d_0" % s, "w%d_1" % s], w=[key])
+
+    def last_phase(s, half):
+        lo0, cut, hi1 = {10: (8, 16, 8), 11: (8, 16, 8), 12: (4, 10, 12), 13: (0, 9, 16), 14: (0, 8, 16)}[s]
+        parts = [(1, 0, 8), (0, lo0, cut)] if half == "lo" else [(1, 8, hi1), (0, cut, 16)]
+        r = ["w10_0", "w10_1"] if s == 10 else ["lo%d" % s, "v%d" % s] + ["hi%d" % s] * (half == "hi")
+        op("V", [exchange(s, ALL, x, a, b, s + 1) for x, a, b in parts], r=r + ["pads"], w=[half + str(s + 1)])
+
+    TURN = [("1lo", T.pt[:, 0:128], "pt"), ("1hi", T.pd[:, 256:384], "pd")]
+
+    def turn_back(half):
+        for key, ps, bk in TURN:
+            if key[1:] == half:
+                op("P", mm(ps, T["d" + half][:], T.p0[:], False, True), r=[half + "15", "k2"], w=[key], banks=[bk])
 
     for t in range(RO):
         d = t + 1
         last = t == RO - 1
-        ch, c2, c1 = (3 * t + 1) << 19, (3 * t + 2) << 19, (3 * t + 3) << 19
         offs = {"F": T.off0F if t == 0 else T.offF, "S": T.off0S if t == 0 else T.offS}
-        mkey, mbuf = ("iF", T.fi) if t == 0 else ("mF", T.mF)
 
         def merge(step, part):
             a, b = (0, 32) if part == "a" else (32, 128)
@@ -250,59 +344,64 @@ def rank_program(g, core, T, topo):
             else:
                 op("V", tcopy(T.offF[:, a:b], T.fi[:, a:b]), r=["iF" + part], w=["offF" + part])
 
-        def gather(qn, role, c):
-            o = T.xg[:, 512 * c + (role == "S"):512 * c + 512:2]
-            i = T.X[:].indirect(offs[role][:, 16 * c:16 * c + 16])
-            op(qn, tcopy(o, i) if qn == "V" else act(o, i, F.Copy), r=["X", "X0", "L%s0" % role if t == 0 else "off" + role + "ab"[c > 1]], w=["x%s%d" % (role, c)])
+        def gather(qn, x):
+            role, c, e = x[0], int(x[1]), int(x[-1]) + 1
+            o = T.xg[:, 512 * c + (role == "S"):512 * e:2]
+            i = T.X[:].indirect(offs[role][:, 16 * c:16 * e])
+            op(qn, tcopy(o, i) if qn == "V" else act(o, i, F.Copy),
+               r=["X", "X0"] + (["L%s0" % role] if t == 0 else ["off" + role + "ab"[k > 1] for k in range(c, e)]),
+               w=["x%s%d" % (role, k) for k in range(c, e)])
 
         def fix(c, e):
             op("V", tt(T.zrep[:, 512 * c:512 * e:32], T.xg[:, 512 * c:512 * e:32], T.zl[:, 128 * t + 16 * c:128 * t + 16 * e], A.min),
                r=["xF%d" % k for k in range(c, e)] + ["Lz%d" % t], w=["zf%d" % k for k in range(c, e)])
+            if e == 8:
+                op("P", [mm(T.ph[32 * j:32 * j + 32, 272:280], T.zrep[:, 32 * j:4096:128], T.gp[:]) for j in range(4)],
+                   r=["zf%d" % k for k in range(8)] + ["k1"], w=["s0"], banks=["ph"])
 
         def scan(c, part=""):
             a, b = {"": (0, 512), "a": (0, 256), "b": (256, 512)}[part]
             a, b = a + 512 * c, b + 512 * c
             key = "top%d%s" % (c, part)
             op("V", lambda: V.tensor_tensor_scan(T.top[:, PAD + a:PAD + b], T.xg[:, a:b], T.zrep[:, a:b], 0.0, A.max, A.min),
-               r=["xF%d" % c, "xS%d" % c, "zf%d" % c, "zrV", "zrS"], w=[key])
+               r=["xF%d" % c, "xS%d" % c, "zf%d" % c, "zr0", "zr1", "zr2", "zr3"], w=[key])
             fns = []
             for ib in range(a // 128, b // 128):
                 c0 = PAD + 128 * ib
-                fns += [mm(T.pg[:, ib:256:32], T.top[:, c0:c0 + 128], T.gp[:], True, False),
-                        mm(T.pg[:, ib:256:32], T.top[:, c0 - 1:c0 + 127], T.gn[:], False, True)]
+                fns += [mm(T.pg[:, ib:256:32], T.top[:, c0:c0 + 128], T.gp[:], False, False),
+                        mm(T.pg[:, ib:256:32], T.top[:, c0 - 1:c0 + 127], T.gn[:], False, ib == 31)]
             k = tops.index(key)
             op("P", fns, r=[key, tops[k - 1] if k else "pad", "k1"], w=["gain" + key], banks=["pg"])
 
-        if t == 0:
-            seqS, seqV = SEQ0
-        else:
-            seqS, seqV = SEQ
+        op("P", mm(T.pg[:, 0:256], T.onen[:], T.tm[:], True, False), r=["k3", "ones"], w=["gain" + k for k in tops], banks=["pg"])
+        seqS, seqV = SEQ0 if t == 0 else SEQ
         for x in seqV.split():
             if x[0] in "mao":
                 merge(x[0], x[1])
-                continue
-            c = int(x[1])
-            if x[0] == "A":
+            elif x == "A":
                 for y in seqS.split():
-                    gather("S", y[0], int(y[1]))
-            elif x[0] == "g":
-                gather("V", "F", c)
-            elif x[0] == "b":
-                if c == 0:
-                    base("F", T.pip[:], "pip")
-                else:
-                    base("S", T.lst[:, 24 * t - 16:24 * t - 8], "lst%d" % (t - 1))
-                    turn_base("S")
+                    gather("S", y)
+            elif x == "b":
+                base("S", T.lst[:, 24 * t - 16:24 * t - 8], "lst%d" % (t - 1))
+                turn_base("S")
+            elif x == "B":
+                base("F", T.pip[:], "pip")
+                turn_base("F")
             elif x[0] == "f":
-                fix(c, int(x[-1]) + 1)
-                if x[-1] == "7":
-                    op("P", [mm(T.pv[32 * j:32 * j + 32, 0:8], T.zrep[:, 32 * j:4096:128], T.gp[:]) for j in range(4)],
-                       r=["zf%d" % k for k in range(8)] + ["k1"], w=["s0"], banks=["pv"])
+                fix(int(x[1]), int(x[-1]) + 1)
+            elif x[0] == "s":
+                scan(int(x[1]))
             else:
-                scan(c)
+                gather("V", x)
+        if t == 0:
+            send([(q + RO, T.hi0[:], T.lH0[:], "H0")], ["hi0", "top0"])
         scan(7, "a")
         scan(7, "b")
-        turn_base("F")
+        if t and "B" not in seqV:
+            base("F", T.pip[:], "pip")
+            turn_base("F")
+        op("V", tt(T.u0[:, 0:128:16], T.ph[:, 272:280], T.trep[:], A.is_lt), r=["s0", "trep"], w=["u0"], banks=["ph"])
+        op("P", mm(T.pb[:, 0:128], T.ibf[:], T.u0[:], False, True), r=["u0"], w=["kF"], banks=["pb"])
         op("P", mm(T.ph[:, 256:264], E, T.wgr[:]), r=tops + ["k3"], w=["v2"], banks=["ph"])
 
         op("P", [mm(T.pc[:, 0:128], T.ibf[:], zslot(t), True, False), mm(T.pc[:, 0:128], T.ibf[:], E, False, True)],
@@ -318,155 +417,151 @@ def rank_program(g, core, T, topo):
             lambda: op("V", tcopy(T.ha[:], T.ph[:, 256:264]), r=["v2"], w=["ha"], banks=["ph"]),
             lambda: op("V", ts1(T.hb[:], T.ha[:], 4095, A.bitwise_and), r=["ha"], w=["hb"]),
             lambda: op("V", tt(T.ha[:], T.hb[:], T.hb[:], A.mult), r=["hb"], w=["ha"]),
-            lambda: op("V", ts1(T.hc[:], T.ha[:], 4, A.arith_shift_right), r=["ha"], w=["hc"]),
-            lambda: op("V", tt(T.ha[:], T.hc[:], T.hb[:], A.add), r=["hc", "hb"], w=["ha"]),
-            lambda: op("V", ts1(T.hc[:], T.ha[:], 8191, A.bitwise_and), r=["ha"], w=["hc"]),
-            lambda: (op("V", ts2(T.hpad[:, 15:128:16], T.hc[:], float(ch), 2.0 ** 18, A.add, A.mult), r=["hc"], w=["hpad"]),
-                     op("P", mm(T.ph[:, 0:128], T.hpad[:], T.isc[:]), r=["hpad", "k1"], w=["ht"], banks=["ph"])),
+            lambda: op("V", ts2(T.hc[:], T.ha[:], 4, 8191, A.arith_shift_right, A.bitwise_and), r=["ha"], w=["hc"]),
+            lambda: op("V", tt(T.hpad[:, 15:128:16], T.hc[:], T.hb[:], A.add), r=["hc", "hb"], w=["hpad"]),
         ]
-        op("V", tt(T.u0[:], T.pv[:, 0:8], T.trep[:, 0:256:32], A.is_lt), r=["s0", "trep"], w=["u0"], banks=["pv"])
 
         for h in (0, 1):
-            op("V", tt(T.u3[:, 128 * h:128 * h + 128], T.pg[:, 128 * h:128 * h + 128], T.trep3[:, 128 * h:128 * h + 128], A.is_lt),
-               r=["gain" + k for k in tops] + ["trep3"], w=["u3%d" % h], banks=["pg"])
+            op("V", ts2(T.u3[:, 128 * h:128 * h + 128], T.pg[:, 128 * h:128 * h + 128], 0.0, cf[:, 11:12], A.is_lt, A.mult),
+               r=["gain" + k for k in tops] + ["k1"], w=["u3%d" % h], banks=["pg"])
+        fill.pop(0)()
         for h in (0, 1):
             op("V", lambda: V.transpose(T.u2[:, 128 * h:128 * h + 128], T.u3[:, 128 * h:128 * h + 128]), r=["u3%d" % h], w=["u2%d" % h])
-        op("V", tt(T.pb[:, 0:128:16], T.pb[:, 0:128:16], T.u0[:], A.add), r=["u0"], w=["pbF"], banks=["pb"])
-        for h in (0, 1):
-            op("V", tt(T.b0[:, 4 * h:4 * h + 4], T.u2[:, 128 * h + 1:128 * h + 128:2], T.pb[:, 128 + 64 * h:192 + 64 * h], A.add),
-               r=["u2%d" % h, "pbS"], w=["AB%d" % h], banks=["pb"])
-        for h in (0, 1):
-            op("V", tt(T.pa[:, 0, 4 * h:4 * h + 4], T.u2[:, 128 * h:128 * h + 128:2], T.pb[:, 64 * h:64 * h + 64], A.add),
-               r=["u2%d" % h, "pbF"], w=["Ak%d" % h], banks=["pb", "pa"])
         fill.pop(0)()
+        for h in (0, 1):
+            op("V", [tt(T.kF[:, 64 * h:64 * h + 64], T.u2[:, 128 * h:128 * h + 128:2], T.pb[:, 64 * h:64 * h + 64], A.add),
+                     tt(T.pu[:, 128 + 64 * h:192 + 64 * h], T.u2[:, 128 * h + 1:128 * h + 128:2], T.pt[:, 128 + 64 * h:192 + 64 * h], A.add)],
+               r=["u2%d" % h, "kF", "kS"], w=["w0_%d" % h], banks=["pb", "pt", "pu"])
+        fill.pop(0)()
+
+        uk = ["u20", "u21", "u0"]
+        won = [
+            lambda: op("V", lambda: V.tensor_tensor_scan(T.alt[:], T.sgn[:], T.u2[:], 0.0, A.mult, A.add), r=uk + ["k4"], w=["alt"]),
+            lambda: op("V", tt(T.ab0[:, 0:128:16], T.alt[:, 31:256:32], T.u0[:, 0:128:16], A.subtract), r=["alt", "u0"], w=["ab0"]),
+            lambda: op("V", lambda: V.tensor_tensor_scan(T.ab[:], T.hold[:], T.ab0[:], 0.0, A.mult, A.add), r=["ab0", "k4"], w=["ab"]),
+            lambda: op("V", [ts2(T.s1[:], T.ab[:], 0.0, 0.5, A.is_lt, A.subtract), ts2(T.s2[:], T.ab[:], 0.0, 0.5, A.is_gt, A.subtract)],
+                       r=["ab"], w=["s1", "s2"]),
+        ]
+        won.pop(0)()
         if not last:
-            op("P", [mm(T.pv[:, 16:24], T.ww[:, 15 - c:143 - c], T.top[:, PAD + 32 * c + 31:PAD + 4096:512], c == 0, c == 15)
-                     for c in range(16)], r=tops + ["k3"], w=["vd"], banks=["pv"])
+            op("P", [mm(T.pd[:, 0:256], T.ones[:], T.u2[:], True, False), mm(T.pd[:, 0:128], T.ones[:], T.u0[:], False, True)],
+               r=uk + ["ones"], w=["pd"], banks=["pd"])
+            op("S", act(T.junk[:], T.pd[:, 0:256], F.Identity, accum_out=T.tot[:, 0:1]), r=["pd"], w=["tot"], banks=["pd"])
+            op("P", [mm(T.pc[:, 264:272], T.ww[:, 15 - c:143 - c], T.top[:, PAD + 32 * c + 31:PAD + 4096:512], c == 0, c == 15)
+                     for c in range(16)], r=tops + ["k3"], w=["vd"], banks=["pc"])
 
-        def who_won():
-            op("V", tcopy(T.u2[:, 0:256:32], T.u0[:]), r=["u0"], w=["u20", "u21"])
-            uk = ["u20", "u21"]
-            op("P", [mm(T.pc[:, 128:256], T.u2[:, 0:256:2], T.pbp[:], True, False), mm(T.pc[:, 128:256], T.u2[:, 1:256:2], T.pbn[:], False, True)],
-               r=uk + ["k2"], w=["df"], banks=["pc"])
-            if not last:
-                op("P", mm(T.pd[:, 0:256], T.ones[:], T.u2[:]), r=uk + ["ones"], w=["pd"], banks=["pd"])
-            op("S", act(T.d1[:], T.pc[:, 128:256], F.Copy), r=["df"], w=["d1"], banks=["pc"])
-            op("P", mm(T.pc[:, 256:384], T.blk[:], T.d1[:]), r=["d1", "k1"], w=["ab"], banks=["pc"])
-            if not last:
-                op("S", act(T.junk[:], T.pd[:, 0:256], F.Identity, accum_out=T.tot[:, 0:1]), r=["pd"], w=["tot"], banks=["pd"])
-            op("S", [act(T.s1[:], T.pc[:, 256:384], F.Sign, bias=-0.5), act(T.s2[:], T.pc[:, 256:384], F.Sign, bias=-0.5, scale=-1.0)],
-               r=["ab"], w=["s1", "s2"], banks=["pc"])
-            op("S", act(T.dl[:], T.s2[:], F.Identity, scale=float(c1 + c2)), r=["s2"], w=["dl"])
-            if not last:
-                spread_z(t + 1, 0)
-
-        def view(buf, pre, gs, pair, fixed, flip=()):
-            return buf[(slice(None),) + pre + (gs,) + tuple(
-                fixed[b] if b in fixed else slice(None, None, -1 if b in flip else None) for b in (4, 3, 2, 1, 0) if b != pair)]
-
-        cI = T.c1i[:, 128 * t:128 * t + 128]
-        l0 = 24 * t
-        mx = (A.min, A.max)
-        for s, pr in enumerate(STAGES[:14]):
-            lev, nx, nlev = FIRST.get(s, 0), STAGES[s + 1], FIRST.get(s + 1, 0)
-            for h in (0, 1):
-                gs = slice(4 * h, 4 * h + 4)
-                if s % 2 == 0:
-                    ib_ = T.b4[:, 8 * h:8 * h + 8, ::-1] if lev == 4 else T.b5[:, gs, ::-1] if lev == 5 else T.b0[:, gs]
-                    op("V", [tt(view(T.cc, (), gs, -1, {pr: dd}), T.pa[:, 0, gs], ib_, mx[dd]) for dd in (0, 1)],
-                       r=["AB%d" % h, "Ak%d" % h], w=["C%d" % h], banks=["pa"])
-                else:
-                    fns = []
-                    for nv in (0, 1):
-                        for dd in (0, 1):
-                            if nv == 0:
-                                o = view(T.pa, (0,), gs, nx, {pr: dd})
-                            elif nlev == 4:
-                                o = T.b4[:, 8 * h:8 * h + 8, dd::2]
-                            elif nlev == 5:
-                                o = T.b5[:, gs, dd::2]
-                            else:
-                                o = view(T.b0, (), gs, nx, {pr: dd})
-                            fns.append(tt(o, view(T.cc, (), gs, -1, {pr: 0, nx: nv}),
-                                          view(T.cc, (), gs, -1, {pr: 1, nx: 1 - nv if lev else nv}, (0,) if lev == 3 else ()), mx[dd]))
-                    op("V", fns, r=["C%d" % h], w=["AB%d" % h], banks=["pa"])
-            if s == 0:
+        l0, o0 = 24 * t, 256 * t
+        for s in range(10):
+            stage(s, 0)
+            stage(s, 1)
+            if STAGES[s + 1][1] == 8:
+                skip(s, 1)
+                if s == 1:
+                    skip(s, 2)
+            elif STAGES[s][1] == 8 and s > 2:
+                skip(s - 1, 2)
+            if s < 2:
                 fill.pop(0)()
+            if s in (0, 2, 3):
+                won.pop(0)()
             if s == 1:
-                who_won()
-            if s in (2, 4, 5, 6, 8):
-                fill.pop(0)()
-            if s == 8:
-                op("P", mm(T.pt[:, 0:128], cI, T.s1[:], True, False), r=["s1", "k3"], w=["tlo"], banks=["pt"])
-                op("P", mm(T.pg[:, 256:384], cI, T.s1[:], True, False), r=["s1", "k3"], w=["thi"], banks=["pg"])
-            if s == 7 and not last:
-                op("V", [ts2(T.tl[:, 0:16], T.jl[:], T.tot[:, 0:1], 32768.0, A.subtract, A.add),
-                         ts1(T.tl[:, 16:24], T.jl[:, 0:8], T.tot[:, 0:1], A.add)], r=["tot", "k5"], w=["tl"])
-            if s == 3 and not last:
-                op("V", tcopy(T.pa_[:], T.pv[:, 16:24]), r=["vd"], w=["pa_"], banks=["pv"])
-            if s == 10 and not last:
-                op("V", [ts1(T.tl2[:], T.tl[:], 127, A.bitwise_and), ts1(T.pb_[:], T.pa_[:], 63, A.bitwise_and)], r=["tl", "pa_"], w=["tl2", "pb_"])
-            if s == 12:
-                op("V", tt(T.a3[:], T.ph[:, 0:128], mbuf[:], A.max), r=["ht", mkey + "a", mkey + "b"], w=["a3"], banks=["ph"])
-        for hv, o, key, ps, bk in ((0, T.dlo, "lo", T.pt[:, 0:128], "pt"), (1, T.dhi, "hi", T.pg[:, 256:384], "pg")):
-            for h in (0, 1):
-                gs = slice(4 * h, 4 * h + 4)
-                op("V", [tt(o[:, 64 * h + dd:64 * h + 64:2], view(T.pa, (0,), gs, 0, {4: hv}), view(T.b0, (), gs, 0, {4: hv}), mx[dd])
-                         for dd in (0, 1)], r=["AB%d" % h], w=["d%s%d" % (key, h)], banks=["pa"])
-            op("P", mm(ps, o[:], T.p0[:], False, True), r=["d%s0" % key, "d%s1" % key, "k2"], w=["t" + key], banks=[bk])
-        if not last:
-            op("V", [tcopy(T.lst[:, l0:l0 + 24], T.tl2[:]), tt(T.pa_[:], T.pb_[:], T.plb[:], A.add)], r=["tl2", "pb_", "k2"], w=["lst%d" % t, "pa_"])
-            op("V", tcopy(T.pl[:], T.pa_[:]), r=["pa_"], w=["pl"])
+                op("P", [mm(T.ph[:, 0:128], T.hpad[:], T.idf[:], True, False)]
+                   + [mm(T.ph[:, j:128:4], T.imk[:], T.basF[:, 32 * j:32 * j + 32], False, j == 3) for j in range(4)],
+                   r=["hpad", "basF", "k1"], w=["ht"], banks=["ph"])
+                op("S", act(T.a3[:], T.ph[:, 0:128], F.Identity, bias=cf[:, 12:13]), r=["ht", "k1"], w=["a3"], banks=["ph"])
+            if s == 3:
+                op("P", mm(T.pw[:, 0:128], T.s2[:], T.pri[:, 256 * t + 128:256 * t + 256]), r=["s2", "k2"], w=["pw"], banks=["pw"])
+                op("S", act(T.dl[:], T.pw[:, 0:128], F.Copy), r=["pw"], w=["dl"], banks=["pw"])
+                for key, ps, bk in TURN:
+                    op("P", mm(ps, T.s1[:], T.pri[:, 256 * t:256 * t + 128], True, False), r=["s1", "k2"], w=[key], banks=[bk])
+                if not last:
+                    spread_z(d, "S", 1, 21, ["zr0"])
+            if last and s in (5, 7, 8, 9):
+                a, b, o, r, w = {5: (T.lH2[:, 0:128], T.lH1[:, 0:128], T.junk[:, 0:128], ["LHa0", "LHb0", "tot"], "jk0"),
+                                 7: (T.junk[:, 0:128], T.lH0[:], T.hx[:], ["jk0", "LH0"], "hx"),
+                                 8: (T.lH2[:, 128:256].indirect(T.ulF[:]), T.lH1[:, 128:256], T.junk[:, 128:256], ["LHa1", "LHb1", "LuF"], "jk1"),
+                                 9: (T.junk[:, 128:256], T.hx[:], T.hacc[:], ["jk1", "hx"], "jk6")}[s]
+                op("V", tt(o, a, b, A.max), r=r, w=[w])
 
-        o0 = 256 * t
         p1lo, p1hi, p2lo, p2hi = T.o1[:, o0:o0 + 128], T.o1[:, o0 + 128:o0 + 256], T.o2[:, o0:o0 + 128], T.o2[:, o0 + 128:o0 + 256]
-        op("V", tt(p1lo, T.pt[:, 0:128], T.a3[:], A.max), r=["tlo", "a3"], w=["p1lo"], banks=["pt"])
+        sl = slice(128 * t, 128 * t + 128)
         if not last:
-            sl = slice(128 * t, 128 * t + 128)
-            send([(q - d - 1, p1lo, T.lS[:, sl], "S%d" % d)], ["p1lo"])
-        op("V", tt(p2lo, T.pt[:, 0:128], T.dl[:], A.add), r=["tlo", "dl"], w=["p2lo"], banks=["pt"])
-        if not last:
-            send([(q + 1, p1lo, T.lF1[:, sl], "Fa%d" % d), (q + d + 2, p2lo, T.lF2[:, sl], "Fb%d" % d)], ["p1lo", "p2lo"])
-        op("V", [tt(p2hi, T.pg[:, 256:384], T.dl[:], A.add), tcopy(p1hi, T.pg[:, 256:384])], r=["thi", "dl"], w=["phi"], banks=["pg"])
+            op("V", [ts2(T.tl[:, 0:16], T.jl[:], T.tot[:, 0:1], 32768.0, A.subtract, A.add),
+                     ts1(T.tl[:, 16:24], T.jl[:, 0:8], T.tot[:, 0:1], A.add)], r=["tot", "k5"], w=["tl"])
+        last_phase(10, "lo")
+        skip(10, 1)
+        last_phase(11, "lo")
+        skip(10, 2)
+        last_phase(12, "lo")
         if last:
-            send([(q - d, T.o1[:, o0:o0 + 256], T.lE1[:], "Ea"), (q + 1, T.o2[:, o0:o0 + 256], T.lE2[:], "Eb")], ["p1lo", "p2lo", "phi"])
+            last_phase(12, "hi")
+            last_phase(13, "lo")
+            last_phase(13, "hi")
+            last_phase(14, "lo")
+            turn_back("lo")
+            last_phase(14, "hi")
+            turn_back("hi")
         else:
-            send([(q - d, p1hi, T.lH1[:, sl], "Ha%d" % t), (q + 1, p2hi, T.lH2[:, sl], "Hb%d" % t)], ["phi"])
+            op("V", tcopy(T.pa_[:], T.pc[:, 264:272]), r=["vd"], w=["pa_"], banks=["pc"])
+            op("V", ts1(T.tl2[:], T.tl[:], 127, A.bitwise_and), r=["tl"], w=["tl2"])
+            last_phase(13, "lo")
+            op("V", ts1(T.pb_[:], T.pa_[:], 63, A.bitwise_and), r=["pa_"], w=["pb_"])
+            op("V", tcopy(T.lst[:, l0:l0 + 24], T.tl2[:]), r=["tl2"], w=["lst%d" % t])
+            last_phase(14, "lo")
+            turn_back("lo")
+            op("V", tt(T.pc_[:], T.pb_[:], T.plb[:], A.add), r=["pb_", "k2"], w=["pc_"])
+            last_phase(12, "hi")
+            op("V", tcopy(T.pl[:], T.pc_[:]), r=["pc_"], w=["pl"])
+            spread_z(d, "V", 21, 24, ["zr1"])
 
+        def upper():
+            op("V", [tcopy(p1hi, T.pd[:, 256:384]), tt(p2hi, T.pd[:, 256:384], T.dl[:], A.add)], r=["1hi", "dl"], w=["phi"], banks=["pd"])
+
+        op("V", tt(p1lo, T.pt[:, 0:128], T.a3[:], A.max), r=["1lo", "a3"], w=["p1lo"], banks=["pt"])
         if not last:
-            un = T.lst[:, l0 + 16:l0 + 24]
-            if t == 0:
-                send([(q + 4, un, T.ulF[:], "uF"), (q + 1, un, T.ulH1[:], "uH1")], ["lst0"])
-            else:
-                send([(q + 1, un, T.ulH2[:], "uH2")], ["lst1"])
-            if t:
-                op("V", tcopy(T.hx[:], p2lo.indirect(T.lst[:, 16:24])), r=["p2lo", "lst0"], w=["hx"])
-            op("V", tcopy(T.X[:].indirect(T.pl[:]), E), r=["pl"] + tops, w=["X"])
-            op("V", tcopy(T.pa[:, 1], T.hx[:] if t else p2lo), r=["hx", "p2lo"], w=["own"], banks=["pa"])
+            send([(q - d - 1, p1lo, T.lS[:, sl], "S%d" % d)], ["p1lo"])
+        op("V", tt(p2lo, T.pt[:, 0:128], T.dl[:], A.add), r=["1lo", "dl"], w=["p2lo"], banks=["pt"])
+        if last:
+            op("V", tt(p2hi, T.pd[:, 256:384], T.dl[:], A.add), r=["1hi", "dl"], w=["p2hi"], banks=["pd"])
+            send([(q + 1, T.o2[:, o0:o0 + 256], T.lE2[:], "Eb")], ["p2lo", "p2hi"])
+            op("V", tt(p1hi, T.pd[:, 256:384], T.hacc[:], A.max), r=["1hi", "jk6"], w=["p1hi"], banks=["pd"])
+            send([(q - d, T.o1[:, o0:o0 + 256], T.lE1[:], "Ea")], ["p1lo", "p1hi"])
+            break
+        send([(q + 1, p1lo, T.lF1[:, sl], "Fa%d" % d), (q + d + 2, p2lo, T.lF2[:, sl], "Fb%d" % d)], ["p1lo", "p2lo"])
+
+        if t:
+            op("S", act(T.hx[:], p2lo.indirect(T.lst[:, 16:24]), F.Copy), r=["p2lo", "lst0"], w=["hx"])
+        last_phase(13, "hi")
+        op("V", tcopy(T.X[:].indirect(T.pl[:]), E), r=["pl"] + tops, w=["X"])
+        last_phase(14, "hi")
+        turn_back("hi")
+        spread_z(d, "V", 24, 28, ["zr2"])
+        spread_z(d, "S", 28, 32, ["zr3"])
+        un = T.lst[:, l0 + 16:l0 + 24]
+        if t == 0:
+            send([(q + 4, un, T.ulF[:], "uF")], ["lst0"])
         else:
-            op("V", [tt(T.junk[:, 0:128], T.lH2[:, 0:128], T.lH1[:, 0:128], A.max),
-                     tt(T.junk[:, 128:256], T.lH2[:, 128:256].indirect(T.ulH1[:]), T.lH1[:, 128:256], A.max)],
-               r=["LHa0", "LHb0", "LHa1", "LHb1", "LuH1", "tot"], w=["jk"])
-            for k in (0, 1):
-                op("V", tt(T.ph[:, 128:256], T.junk[:, 128 * k:128 * k + 128], T.ph[:, 128:256], A.max), r=["jk"], w=["hacc"], banks=["ph"])
+            send([(q + 1, un, T.ulH2[:], "uH2")], ["lst1"])
 
-        if not last:
-            op("V", tt(T.mS[:], T.pa[:, 1], T.lS[:, sl], A.max), r=["own", "LS%d" % d], w=["mS"], banks=["pa"])
-            op("V", ts1(T.si[:], T.mS[:], 8191, A.bitwise_and), r=["mS"], w=["iSa", "iSb"])
-            op("V", tcopy(T.offS[:, 0:32], T.si[:].indirect(T.lst[:, l0:l0 + 2])), r=["iSa", "lst%d" % t], w=["offSa"])
-            op("V", tcopy(T.offS[:, 32:128], T.si[:].indirect(T.lst[:, l0 + 2:l0 + 8])), r=["iSa", "lst%d" % t], w=["offSb"])
+        op("V", tt(T.mS[:], T.hx[:] if t else p2lo, T.lS[:, sl], A.max), r=["hx", "p2lo", "LS%d" % d], w=["mS"])
+        upper()
+        send([(q - d + RO, p1hi, T.lH1[:, sl], "Ha%d" % t), (q + 1 + RO, p2hi, T.lH2[:, sl], "Hb%d" % t)], ["phi"])
+        op("V", ts1(T.si[:], T.mS[:], 8191, A.bitwise_and), r=["mS"], w=["iSa", "iSb"])
+        op("V", tcopy(T.offS[:, 0:32], T.si[:].indirect(T.lst[:, l0:l0 + 2])), r=["iSa", "lst%d" % t], w=["offSa"])
+        op("V", tcopy(T.offS[:, 32:128], T.si[:].indirect(T.lst[:, l0 + 2:l0 + 8])), r=["iSa", "lst%d" % t], w=["offSb"])
 
     wait("Y", [lastw["Lzf"]])
     op("Y", lambda: Y.dma_start(T.yz[:], T.zfin[:]), w=["yz"], inc=16)
-    op("V", [tt(T.hx[:], T.lE1[:, 128:256], T.ph[:, 128:256], A.max),
-             tt(T.fin[:, 0:128], T.lE2[:, 0:128].indirect(T.ulH2[:]), T.lE1[:, 0:128], A.max)],
-       r=["LEa", "LEb", "LuH2", "hacc"], w=["hx", "finlo"], banks=["ph"])
-    op("V", [tt(T.fin[:, 128:256], T.lE2[:, 128:256].indirect(T.ulH2[:]), T.hx[:], A.max),
-             ts1(T.fin2[:, 0:128], T.fin[:, 0:128], 8191, A.bitwise_and)], r=["hx", "finlo"], w=["finhi", "f2lo"])
-    op("V", [ts1(T.fin2[:, 128:256], T.fin[:, 128:256], 8191, A.bitwise_and), tcopy(T.yo[:, 0:256:2], T.fin2[:, 0:128])],
-       r=["finhi", "f2lo"], w=["f2hi", "yolo"])
-    op("V", tcopy(T.yo[:, 1:256:2], T.fin2[:, 128:256]), r=["f2hi"], w=["yohi"])
-    op("Y", lambda: Y.dma_start(T.ya[:], T.yo[:]), r=["yolo", "yohi"], w=["ya"], inc=16)
+    halves = [(k, slice(128 * k, 128 * k + 128)) for k in (0, 1)]
+    for k, c in halves:
+        op("V", tcopy(T.junk[:, c], T.lE2[:, c].indirect(T.ulH2[:])), r=["LEb", "LuH2"], w=["jk%d" % k])
+    for k, c in halves:
+        op("V", tt(T.fin[:, c], T.junk[:, c], T.lE1[:, c], A.max), r=["LEa", "jk%d" % k], w=["fin%d" % k])
+    for k, c in halves:
+        op("V", ts1(T.fin2[:, c], T.fin[:, c], 8191, A.bitwise_and), r=["fin%d" % k], w=["msk%d" % k])
+    for k, c in halves:
+        op("V", tcopy(T.yo[:, k:256:2], T.fin2[:, c]), r=["msk%d" % k], w=["yo%d" % k])
+    op("Y", lambda: Y.dma_start(T.ya[:], T.yo[:]), r=["yo0", "yo1"], w=["ya"], inc=16)
     for s in cnt:
         if s[0] != "Y" and waited.get(s, 0) < cnt[s]:
             g.wait_ge(T.sem[s], cnt[s])

@@ -3,7 +3,7 @@ from concourse.mybir import AluOpType, ActivationFunctionType
 
 A = AluOpType
 F = ActivationFunctionType
-N, RO, PAD = 8, 3, 2
+N, RO, PAD, XA = 8, 3, 2, 4096
 f32, bf, i32, u16 = "float32", "bfloat16", "int32", "uint16"
 
 
@@ -15,9 +15,9 @@ SCRATCH = {
     "X": sb([8192], bf), "xg": sb([4096], bf), "zrep": sb([4096], bf), "top": sb([4096 + 16], bf),
     "rai": sb([256], i32), "zown": sb([128], bf), "wi": sb([256], i32), "wf": sb([256], f32), "lo0": sb([128], u16),
     "jf": sb([144], f32), "jt": sb([256], f32), "ci": sb([8], i32), "cf": sb([16], f32),
-    "ibf": sb([128], bf), "isc": sb([128], f32), "p0": sb([128], f32), "pbp": sb([128], bf), "pbn": sb([128], bf),
-    "gp": sb([8], bf), "gn": sb([8], bf), "wgr": sb([8], bf), "blk": sb([128], bf), "ones": sb([128], bf),
-    "onen": sb([128], f32), "ww": sb([144], bf), "c1i": sb([384], bf), "tm": sb([256], f32), "trep": sb([8], f32),
+    "ibf": sb([128], bf), "isc": sb([128], f32), "p0": sb([128], f32), "pbp": sb([128], bf),
+    "gp": sb([8], bf), "gn": sb([8], bf), "wgr": sb([8], bf), "ones": sb([128], bf),
+    "onen": sb([128], f32), "ww": sb([144], bf), "tm": sb([256], f32), "trep": sb([8], f32),
     "jl": sb([16], f32), "ja": sb([8], i32), "pip": sb([8], u16), "plb": sb([8], i32),
     "zl": sb([384], bf), "zfin": sb([128], f32), "nzb": sb([256], bf), "nzf": sb([128], f32),
     "offF": sb([128], u16), "offS": sb([128], u16), "off0F": sb([128], u16), "off0S": sb([128], u16),
@@ -26,13 +26,17 @@ SCRATCH = {
     "u3": sb([256], bf), "u2": sb([256], bf), "u0": sb([128], bf), "imk": sb([128], f32),
     "kF": sb([128], f32), "e0": sb([4, 8, 32], f32), "e1": sb([4, 8, 32], f32),
     "j16": sb([8, 1, 2, 2, 8], f32), "j8": sb([8, 2, 2, 2, 4], f32), "j4": sb([8, 4, 2, 2, 2], f32), "j2": sb([8, 8, 2, 2], f32),
-    "dlo": sb([128], f32), "dhi": sb([128], f32),
-    "ha": sb([8], i32), "hb": sb([8], i32), "hc": sb([8], i32), "hs": sb([8], f32), "hpad": sb([128], f32), "a3": sb([128], f32),
+    "dd": sb([768], f32),
+    "ha": sb([8], i32), "hb": sb([8], i32), "hc": sb([8], i32), "hpad": sb([128], f32),
     "sgn": sb([256], bf), "alt": sb([256], bf), "hold": sb([128], bf), "ab0": sb([128], bf), "ab": sb([128], bf),
-    "s1": sb([128], bf), "s2": sb([128], bf), "pri": sb([768], bf), "idf": sb([128], f32),
-    "junk": sb([256], f32), "tot": sb([4], f32), "tl": sb([24], i32), "tl2": sb([24], i32), "lst": sb([48], u16),
+    "s1": sb([128], bf), "s2": sb([384], bf), "pri": sb([512], bf), "idf": sb([128], f32),
+    "prin": sb([128], bf), "pb22": sb([128], bf), "ic3": sb([128], bf), "sgS": sb([128], bf), "sgF": sb([128], bf),
+    "r1": sb([128], f32), "r2": sb([128], f32), "r3": sb([128], f32), "r2b": sb([128], bf), "r3b": sb([128], bf),
+    "zer": sb([128], bf), "fb": sb([2, 128], f32), "cS": sb([128], f32), "cF": sb([128], f32), "col": sb([12], f32), "lc": sb([8], f32),
+    "lA1": sb([256], f32), "lA2": sb([256], f32), "lAE": sb([256], f32), "lT": sb([384], bf),
+    "junk": sb([256], f32), "tot": sb([4], f32), "tl": sb([20], i32), "tl2": sb([20], i32), "lst": sb([32], u16),
     "pa_": sb([8], i32), "pb_": sb([8], i32), "pc_": sb([8], i32), "pl": sb([8], u16),
-    "o1": sb([768], f32), "o2": sb([768], f32),
+    "o1": sb([768], f32), "o2": sb([256], f32),
     "lS": sb([256], f32), "lF1": sb([256], f32), "lF2": sb([256], f32),
     "lH1": sb([256], f32), "lH2": sb([256], f32), "lE1": sb([256], f32), "lE2": sb([256], f32),
     "ulF": sb([8], u16), "ulH2": sb([8], u16), "hi0": sb([128], f32), "lH0": sb([128], f32), "hacc": sb([128], f32),
@@ -43,17 +47,17 @@ SCRATCH = {
     "pc": ("psum", [128, 512], f32), "pd": ("psum", [128, 512], f32),
     "pu": ("psum", [128, 512], f32), "pw": ("psum", [128, 512], f32),
 }
-POOL = {"V": 40, "S": 30, "P": 40, "G": 4, "Y": 10}
+POOL = {"V": 38, "S": 28, "P": 38, "G": 4, "Y": 10}
 ARR = ["z0", "z1", "z2", "zf", "F0", "S0", "S1", "S2", "Fa1", "Fa2", "Fb1", "Fb2", "Ha0", "Ha1", "Hb0", "Hb1",
-       "Ea", "Eb", "uF", "H0", "uH2"]
+       "Ea", "Eb", "uF", "H0", "cF", "cE", "Aa1", "Aa2", "Ab1", "Ab2", "AE", "T1", "T2", "T3"]
 SEMAPHORES = [q + str(k) for q in POOL for k in range(POOL[q])] + ["r" + a for a in ARR] + ["sent"]
 STAGES = [(p, sh) for p in (16, 8, 4, 2, 1) for sh in [0] + [x for x in (8, 4, 2, 1) if x >= p]]
 SLOT = {2: 0, 4: 1, 5: 0, 7: 1, 8: 0, 9: 2, 11: 3, 12: 1, 13: 0, 14: 2}
 SEQ0 = ["F1 S0 S1 S23 F6 S45 S6 S7", "A F0 F2 f01 F3 s0 s1 f23 F45 s2 s3 f46 F7 s4 s5 f7 s6"]
-SEQ = ["S0 S13 F1 F2 F46 S4 S6 S7", "b S5 ma mb aa ab oa ob A F0 B f01 F3 s0 s1 f23 F7 s2 f47 s3 s4 s5 s6"]
+SEQ = ["S0 S13 F1 F2 F46 S4 S6 S7a S7b", "M b S5a ma mb aa ab oa S5b ob A F0 B f01 F3 s0 s1 f23 F7 s2 f4 f57 s3 s4 s5 s6"]
 
 
-RELAYED = []
+RELAYED = ["H0", "T1", "Aa1", "T2", "Aa2", "T3"]
 
 
 def helper(core, T, topo):
@@ -66,8 +70,8 @@ def spare(core, T, topo):
 
 
 def helper_program(g, core, q, T, topo):
-    land = {"z1": (q + 1, T.zl[:, 128:256]), "Fb1": (q + 3, T.lF2[:, 0:128]), "z2": (q + 1, T.zl[:, 256:384]),
-            "Fb2": (q + 4, T.lF2[:, 128:256]), "zf": (q - 3, T.zfin[:]), "Eb": (q + 1, T.lE2[:])}
+    land = {"H0": (q + RO, T.lH0[:]), "T1": (q + 3, T.lT[:, 0:128]), "Aa1": (q + 1, T.lA1[:, 0:128]), "T2": (q + 4, T.lT[:, 128:256]),
+            "Aa2": (q + 1, T.lA1[:, 128:256]), "T3": (q + 1, T.lT[:, 256:384])}
     n = 0
     for name in RELAYED:
         dst, ap = land[name]
@@ -76,8 +80,7 @@ def helper_program(g, core, q, T, topo):
         g.wait_ge(T.sem["r" + name], len(spare(T.cores[q], T, topo)))
         g.remote_dma(ap, ap, T.sem["r" + name], T.sem.sent, pid, rid, topo.mask(core, dc))
         n += len(topo.engines(core, dc))
-    if n:
-        g.wait_ge(T.sem.sent, n)
+    g.wait_ge(T.sem.sent, n)
 
 
 def rank_program(g, core, T, topo):
@@ -193,22 +196,28 @@ def rank_program(g, core, T, topo):
     for t in (1, 2):
         expect("z%d" % t, q - 1, 1)
         expect("S%d" % t, q + t + 1, 1)
-        expect("Fa%d" % t, q - 1, 2)
-        expect("Fb%d" % t, q - t - 2, 2)
+        expect("Fa%d" % t, q - 1, 1)
+        expect("Fb%d" % t, q - t - 2, 1)
+        expect("Aa%d" % t, q - 1, 1)
+        expect("Ab%d" % t, q + t + 1, 1)
+        expect("T%d" % t, q - t - 2, 1)
         expect("Ha%d" % (t - 1), q + t - RO, 2)
         expect("Hb%d" % (t - 1), q - 1 - RO, 2)
     expect("zf", q + 3, 1)
     expect("Ea", q + 3, 1)
     expect("Eb", q - 1, 1)
-    expect("uF", q - 4, 1)
+    expect("uF", q - 4, 2)
+    expect("cF", q - 4, 2)
     expect("H0", q - RO, 1)
-    expect("uH2", q - 1, 1)
+    expect("cE", q - 1, 1)
+    expect("T3", q - 1, 1)
+    expect("AE", q + 3, 1)
 
     op("Y", lambda: Y.dma_start(T.zown[:], T.zu[:]), w=["zown"], inc=16)
     op("S", lambda: S.dma_start(T.rai[:], T.ra[:]), w=["rai"], inc=16)
     op("Y", lambda: Y.dma_start(T.wi[0:1, 0:128], T.wg[:]), w=["wi"], inc=16)
     op("S", lambda: S.dma_start(T.wi[0:1, 128:256], T.th[:]), w=["ti"], inc=16)
-    op("Y", lambda: Y.dma_start(T.X[:, 0:4096], T.xd[:, 0:4096]), w=["X0"], inc=16)
+    op("Y", lambda: Y.dma_start(T.X[:, 0:XA], T.xd[:, 0:XA]), w=["X0"], inc=16)
 
     cf, ci, jf, jt = T.cf, T.ci, T.jf, T.jt
     op("G", lambda: g.iota(ci[:, 0:1], [[0, 1]], 0, 1), w=["ci0"])
@@ -220,18 +229,17 @@ def rank_program(g, core, T, topo):
        w=["pad", "ones"])
     op("V", [ts1(ci[:, 1:2], ci[:, 0:1], 15, A.bitwise_and), ts1(ci[:, 2:3], ci[:, 0:1], 4, A.arith_shift_right),
              ts1(ci[:, 3:4], ci[:, 0:1], 31, A.bitwise_and), ts1(ci[:, 4:5], ci[:, 0:1], 5, A.arith_shift_right)], r=["ci0"], w=["ci"])
-    op("V", [fillc(T.hpad[:], 0.0), fillc(T.u0[:], 0.0), fillc(T.ab0[:], 0.0)], w=["hpad", "u0", "ab0"])
+    op("V", [fillc(T.hpad[:], 0.0), fillc(T.u0[:], 0.0), fillc(T.ab0[:], 0.0), fillc(T.zer[:], 0.0)], w=["hpad", "u0", "ab0", "ab0z"])
     op("V", [tcopy(cf[:, 0:5], ci[:, 0:5]), ts1(cf[:, 5:6], ci[:, 1:2], 16384.0, A.mult),
              ts2(cf[:, 6:7], ci[:, 1:2], 16384.0, 8192.0, A.mult, A.add), ts2(cf[:, 7:8], ci[:, 2:3], 16.0, 15.0, A.mult, A.add),
              ts1(cf[:, 13:14], ci[:, 1:2], 4.0, A.mult), ts1(cf[:, 14:15], ci[:, 1:2], 15.0, A.not_equal)], r=["ci", "ci0"], w=["cf"])
     op("V", tcopy(T.lo0[:], T.rai[:, 0:256:2]), r=["rai"], w=["lo0"])
     send([(q + 1, T.lo0[:], T.off0F[:], "F0"), (q - 1, T.lo0[:], T.off0S[:], "S0")], ["lo0"])
-    op("Y", lambda: Y.dma_start(T.X[:, 4096:8192], T.xd[:, 4096:8192]), r=["lo0"], w=["X"], inc=16)
     op("G", lambda: g.iota(jt[:], [[1, 8], [0, 32]], 0, 0, allow_small_or_imprecise_dtypes=True), w=["jt"])
     op("V", tcopy(T.wf[0:1, :], T.wi[0:1, :]), r=["wi", "ti"], w=["wf"])
     op("P", [mm(T.pd[:, 8 + k:9 + k], T.wf[0:1, 128 * k:128 * k + 128], T.onen[0:1, 0:1]) for k in (0, 1)], r=["wf", "ones"], w=["wt"], banks=["pd"])
     op("V", [ts2(cf[:, 10:11], ci[:, 3:4], 4.0, cf[:, 4:5], A.mult, A.add),
-             ts1(T.jl[:, 8:16], T.ja[:], cf[:, 13:14], A.add), ts1(T.pip[:], T.ja[:], cf[:, 13:14], A.add),
+             ts1(T.pip[:], T.ja[:], cf[:, 13:14], A.add),
              ts2(T.jl[:, 0:8], jf[:, 0:8], 16.0, cf[:, 1:2], A.mult, A.add),
              ts1(T.ibf[:], jf[:, 0:128], cf[:, 0:1], A.is_equal),
              ts1(T.gp[:], jf[:, 0:8], cf[:, 2:3], A.is_equal),
@@ -240,15 +248,18 @@ def rank_program(g, core, T, topo):
     op("V", [fillc(T.e0[:, :, :, 24:26], 4.0), fillc(T.e1[:, :, :, 6:8], -1.0)], w=["pads"])
     op("V", [ts1(cf[:, 8:9], T.pd[:, 8:9], -1.0, A.mult), ts1(cf[:, 9:10], T.pd[:, 9:10], -1.0 / 16, A.mult)], r=["wt"], w=["k0"], banks=["pd"])
     op("V", [ts1(T.plb[:], T.jl[:, 0:8], 64.0, A.mult), ts1(T.pbp[:], jf[:, 0:128], cf[:, 10:11], A.is_equal),
+             ts2(T.jl[:, 8:10], T.onen[:, 0:2], -32768.0, cf[:, 10:11], A.mult, A.add),
              fillc(T.sgn[:, 0:256:32], 0.0), fillc(T.hold[:, 0:128:16], 0.0)], r=["kb", "ones"], w=["kc", "k4"])
+    op("Y", lambda: Y.dma_start(T.X[:, XA:8192], T.xd[:, XA:8192]), r=["jt"], w=["X"], inc=16)
     op("S", [act(T.isc[:], T.ibf[:], F.Identity, scale=2.0 ** -18), act(T.idf[:], T.ibf[:], F.Copy),
              act(T.imk[:], T.ibf[:], F.Identity, scale=cf[:, 14:15])], r=["kb"], w=["k1"])
     op("V", [ts2(T.tm[:], jt[:], cf[:, 2:3], cf[:, 9:10], A.is_equal, A.mult),
              ts2(T.wgr[:], jf[:, 0:8], cf[:, 2:3], cf[:, 8:9], A.is_equal, A.mult),
              ts2(T.ww[:], jf[:], cf[:, 7:8], cf[:, 8:9], A.is_equal, A.mult)], r=["k0", "kb", "jt"], w=["k3"])
-    op("S", [act(T.p0[:], T.pbp[:], F.Identity, scale=2.0 ** 18)]
+    op("S", [act(T.p0[:], T.pbp[:], F.Identity, scale=2.0 ** 18), act(T.prin[:], T.pbp[:], F.Identity, scale=-2.0 ** 22),
+             act(T.pb22[:], T.pbp[:], F.Identity, scale=2.0 ** 22), act(T.ic3[:], T.ibf[:], F.Identity, scale=3 * 2.0 ** 20)]
        + [act(T.pri[:, 256 * t + 128 * k:256 * t + 128 * k + 128], T.pbp[:], F.Identity, scale=float((3 * t + 3 + k * (3 * t + 2)) << 20))
-          for t in range(RO) for k in (0, 1)], r=["kc"], w=["k2"])
+          for t in range(RO - 1) for k in (0, 1)], r=["kc"], w=["k2"])
     op("P", mm(T.pd[:, 0:8], T.onen[:], T.tm[:, 0:256:32]), r=["k3", "ones"], w=["pd"], banks=["pd"])
     op("V", tcopy(T.hi0[:], T.rai[:, 1:256:2]), r=["rai"], w=["hi0"])
 
@@ -295,7 +306,7 @@ def rank_program(g, core, T, topo):
     def exchange(s, gs, x, a, b, to):
         p, sh = STAGES[s]
         if to == 15:
-            out = (T.dlo, T.dhi)[a // 8][:, x:128:2]
+            out = T.dd[:, 256 * t + 16 * a + x:256 * t + 16 * a + 128:2]
         else:
             out = wires(x, to, gs, a, b) if STAGES[to][0] == p else T["j%d" % p][:, gs, a // p:b // p, x]
         if x == 0:
@@ -321,12 +332,24 @@ def rank_program(g, core, T, topo):
         r = ["w10_0", "w10_1"] if s == 10 else ["lo%d" % s, "v%d" % s] + ["hi%d" % s] * (half == "hi")
         op("V", [exchange(s, ALL, x, a, b, s + 1) for x, a, b in parts], r=r + ["pads"], w=[half + str(s + 1)])
 
-    TURN = [("1lo", T.pt[:, 0:128], "pt"), ("1hi", T.pd[:, 256:384], "pd")]
+    PARTS = (("a", 0, 32), ("b", 32, 128))
 
-    def turn_back(half):
-        for key, ps, bk in TURN:
-            if key[1:] == half:
-                op("P", mm(ps, T["d" + half][:], T.p0[:], False, True), r=[half + "15", "k2"], w=[key], banks=[bk])
+    def minus_threshold():
+        op("P", mm(T.pg[:, 0:256], T.onen[:], T.tm[:], True, False), r=["k3", "ones"], w=["gain" + k for k in tops], banks=["pg"])
+
+    minus_threshold()
+
+    def order(r, rb, c, key, name):
+        op("V", ts2(r[:], jf[:, 0:128], c, 2.0 ** 18, A.is_equal, A.mult), r=[key, "jf"], w=[name + "f"])
+        if rb is None:
+            lastw[name] = lastw[name + "f"]
+        else:
+            op("S", act(rb[:], r[:], F.Identity, scale=16.0), r=[name + "f"], w=[name])
+
+    def fallback(ps, bk, s2, ks, r, rb, kr, old, ko, sg, src, kd, name):
+        op("S", act(sg, old, F.Sign), r=[ko], w=["sg" + name])
+        op("P", [mm(ps, s2, rb[:], True, False), mm(ps, T.ic3[:], sg, False, False)], r=[ks, kr, "sg" + name, "k2"], w=[name + "p"], banks=[bk])
+        op("P", mm(ps, src, r[:], False, True), r=[kd, kr], w=[name], banks=[bk])
 
     for t in range(RO):
         d = t + 1
@@ -335,26 +358,26 @@ def rank_program(g, core, T, topo):
 
         def merge(step, part):
             a, b = (0, 32) if part == "a" else (32, 128)
-            o = 128 * (t - 1)
             if step == "m":
-                far = T.lF2[:, o + a:o + b] if t == 1 else T.lF2[:, o:o + 128].indirect(T.ulF[:, a // 16:b // 16])
-                op("V", tt(T.mF[:, a:b], far, T.lF1[:, o + a:o + b], A.max), r=["LFa%d" % t, "LFb%d" % t] + (["LuF"] if t == 2 else []), w=["mF" + part])
+                ps, bk = (T.ph[:, 128:160], "ph") if part == "a" else (T.pb[:, 128:224], "pb")
+                op("V", tt(T.mF[:, a:b], ps, T.cF[:, a:b], A.max), r=["AF" + part, "cF"], w=["mF" + part], banks=[bk])
             elif step == "a":
                 op("V", ts1(T.fi[:, a:b], T.mF[:, a:b], 8191, A.bitwise_and), r=["mF" + part], w=["iF" + part])
             else:
                 op("V", tcopy(T.offF[:, a:b], T.fi[:, a:b]), r=["iF" + part], w=["offF" + part])
 
         def gather(qn, x):
-            role, c, e = x[0], int(x[1]), int(x[-1]) + 1
-            o = T.xg[:, 512 * c + (role == "S"):512 * e:2]
-            i = T.X[:].indirect(offs[role][:, 16 * c:16 * e])
+            role, c = x[0], 2 * int(x[1]) + (x[-1] == "b")
+            e = c + 1 if x[-1] in "ab" else 2 * int(x[-1]) + 2
+            o = T.xg[:, 256 * c + (role == "S"):256 * e:2]
+            i = T.X[:].indirect(offs[role][:, 8 * c:8 * e])
             op(qn, tcopy(o, i) if qn == "V" else act(o, i, F.Copy),
-               r=["X", "X0"] + (["L%s0" % role] if t == 0 else ["off" + role + "ab"[k > 1] for k in range(c, e)]),
-               w=["x%s%d" % (role, k) for k in range(c, e)])
+               r=["X", "X0"] + (["L%s0" % role] if t == 0 else ["off" + role + "ab"[k > 3] for k in range(c, e)]),
+               w=["x%s%d%s" % (role, k // 2, "ab"[k % 2]) for k in range(c, e)])
 
         def fix(c, e):
             op("V", tt(T.zrep[:, 512 * c:512 * e:32], T.xg[:, 512 * c:512 * e:32], T.zl[:, 128 * t + 16 * c:128 * t + 16 * e], A.min),
-               r=["xF%d" % k for k in range(c, e)] + ["Lz%d" % t], w=["zf%d" % k for k in range(c, e)])
+               r=["xF%d%s" % (k, x) for k in range(c, e) for x in "ab"] + ["Lz%d" % t], w=["zf%d" % k for k in range(c, e)])
             if e == 8:
                 op("P", [mm(T.ph[32 * j:32 * j + 32, 272:280], T.zrep[:, 32 * j:4096:128], T.gp[:]) for j in range(4)],
                    r=["zf%d" % k for k in range(8)] + ["k1"], w=["s0"], banks=["ph"])
@@ -364,7 +387,7 @@ def rank_program(g, core, T, topo):
             a, b = a + 512 * c, b + 512 * c
             key = "top%d%s" % (c, part)
             op("V", lambda: V.tensor_tensor_scan(T.top[:, PAD + a:PAD + b], T.xg[:, a:b], T.zrep[:, a:b], 0.0, A.max, A.min),
-               r=["xF%d" % c, "xS%d" % c, "zf%d" % c, "zr0", "zr1", "zr2", "zr3"], w=[key])
+               r=["x%s%d%s" % (x, c, y) for x in "FS" for y in part or "ab"] + ["zf%d" % c, "zr0", "zr1", "zr2", "zr3"], w=[key])
             fns = []
             for ib in range(a // 128, b // 128):
                 c0 = PAD + 128 * ib
@@ -373,7 +396,6 @@ def rank_program(g, core, T, topo):
             k = tops.index(key)
             op("P", fns, r=[key, tops[k - 1] if k else "pad", "k1"], w=["gain" + key], banks=["pg"])
 
-        op("P", mm(T.pg[:, 0:256], T.onen[:], T.tm[:], True, False), r=["k3", "ones"], w=["gain" + k for k in tops], banks=["pg"])
         seqS, seqV = SEQ0 if t == 0 else SEQ
         for x in seqV.split():
             if x[0] in "mao":
@@ -382,8 +404,10 @@ def rank_program(g, core, T, topo):
                 for y in seqS.split():
                     gather("S", y)
             elif x == "b":
-                base("S", T.lst[:, 24 * t - 16:24 * t - 8], "lst%d" % (t - 1))
+                base("S", T.pip[:], "pip")
                 turn_base("S")
+            elif x == "M":
+                op("V", tt(T.cF[:], T.pc[:, 128:256], T.lA1[:, 128 * t - 128:128 * t], A.max), r=["BF", "BFp", "LAa%d" % t], w=["cF"], banks=["pc"])
             elif x == "B":
                 base("F", T.pip[:], "pip")
                 turn_base("F")
@@ -397,12 +421,12 @@ def rank_program(g, core, T, topo):
             send([(q + RO, T.hi0[:], T.lH0[:], "H0")], ["hi0", "top0"])
         scan(7, "a")
         scan(7, "b")
-        if t and "B" not in seqV:
-            base("F", T.pip[:], "pip")
-            turn_base("F")
         op("V", tt(T.u0[:, 0:128:16], T.ph[:, 272:280], T.trep[:], A.is_lt), r=["s0", "trep"], w=["u0"], banks=["ph"])
         op("P", mm(T.pb[:, 0:128], T.ibf[:], T.u0[:], False, True), r=["u0"], w=["kF"], banks=["pb"])
         op("P", mm(T.ph[:, 256:264], E, T.wgr[:]), r=tops + ["k3"], w=["v2"], banks=["ph"])
+
+        if last:
+            op("V", tt(T.junk[:, 128:256], T.lH2[:, 128:256].indirect(T.ulF[:]), T.lH1[:, 128:256], A.max), r=["LHa1", "LHb1", "LuF", "tot"], w=["jk1"])
 
         op("P", [mm(T.pc[:, 0:128], T.ibf[:], zslot(t), True, False), mm(T.pc[:, 0:128], T.ibf[:], E, False, True)],
            r=tops + ["Lz%d" % t, "k1"], w=["ze"], banks=["pc"])
@@ -425,9 +449,16 @@ def rank_program(g, core, T, topo):
             op("V", ts2(T.u3[:, 128 * h:128 * h + 128], T.pg[:, 128 * h:128 * h + 128], 0.0, cf[:, 11:12], A.is_lt, A.mult),
                r=["gain" + k for k in tops] + ["k1"], w=["u3%d" % h], banks=["pg"])
         fill.pop(0)()
+        op("P", [mm(T.ph[:, 0:128], T.zer[:], T.ibf[:], True, False)]
+           + [mm(T.ph[:, j:128:4], T.imk[:], T.basF[:, 32 * j:32 * j + 32], False, False) for j in range(4)],
+           r=["basF", "k1", "ab0z"], w=["ht0"], banks=["ph"])
+        if last:
+            op("V", tt(T.fin[:, 0:128], T.junk[:, 128:256], T.hacc[:], A.max), r=["jk1", "hacc"], w=["fin0"])
         for h in (0, 1):
             op("V", lambda: V.transpose(T.u2[:, 128 * h:128 * h + 128], T.u3[:, 128 * h:128 * h + 128]), r=["u3%d" % h], w=["u2%d" % h])
         fill.pop(0)()
+        if last:
+            op("V", ts1(T.fin2[:, 0:128], T.fin[:, 0:128], 8191, A.bitwise_and), r=["fin0"], w=["msk0"])
         for h in (0, 1):
             op("V", [tt(T.kF[:, 64 * h:64 * h + 64], T.u2[:, 128 * h:128 * h + 128:2], T.pb[:, 64 * h:64 * h + 64], A.add),
                      tt(T.pu[:, 128 + 64 * h:192 + 64 * h], T.u2[:, 128 * h + 1:128 * h + 128:2], T.pt[:, 128 + 64 * h:192 + 64 * h], A.add)],
@@ -439,18 +470,20 @@ def rank_program(g, core, T, topo):
             lambda: op("V", lambda: V.tensor_tensor_scan(T.alt[:], T.sgn[:], T.u2[:], 0.0, A.mult, A.add), r=uk + ["k4"], w=["alt"]),
             lambda: op("V", tt(T.ab0[:, 0:128:16], T.alt[:, 31:256:32], T.u0[:, 0:128:16], A.subtract), r=["alt", "u0"], w=["ab0"]),
             lambda: op("V", lambda: V.tensor_tensor_scan(T.ab[:], T.hold[:], T.ab0[:], 0.0, A.mult, A.add), r=["ab0", "k4"], w=["ab"]),
-            lambda: op("V", [ts2(T.s1[:], T.ab[:], 0.0, 0.5, A.is_lt, A.subtract), ts2(T.s2[:], T.ab[:], 0.0, 0.5, A.is_gt, A.subtract)],
+            lambda: op("V", [ts2(T.s1[:], T.ab[:], 0.0, 0.5, A.is_lt, A.subtract), ts2(T.s2[:, 128 * t:128 * t + 128], T.ab[:], 0.0, 0.5, A.is_gt, A.subtract)],
                        r=["ab"], w=["s1", "s2"]),
         ]
         won.pop(0)()
         if not last:
             op("P", [mm(T.pd[:, 0:256], T.ones[:], T.u2[:], True, False), mm(T.pd[:, 0:128], T.ones[:], T.u0[:], False, True)],
                r=uk + ["ones"], w=["pd"], banks=["pd"])
-            op("S", act(T.junk[:], T.pd[:, 0:256], F.Identity, accum_out=T.tot[:, 0:1]), r=["pd"], w=["tot"], banks=["pd"])
+            op("S", act(T.junk[:], T.pd[:, 0:256], F.Identity, accum_out=T.tot[:, t:t + 1]), r=["pd"], w=["tot"], banks=["pd"])
             op("P", [mm(T.pc[:, 264:272], T.ww[:, 15 - c:143 - c], T.top[:, PAD + 32 * c + 31:PAD + 4096:512], c == 0, c == 15)
                      for c in range(16)], r=tops + ["k3"], w=["vd"], banks=["pc"])
 
-        l0, o0 = 24 * t, 256 * t
+        l0, o0 = 16 * t, 256 * t
+        sl = slice(128 * t, 128 * t + 128)
+        col, tot = T.col[:, 4 * t:4 * t + 4], T.tot[:, t:t + 1]
         for s in range(10):
             stage(s, 0)
             stage(s, 1)
@@ -462,106 +495,130 @@ def rank_program(g, core, T, topo):
                 skip(s - 1, 2)
             if s < 2:
                 fill.pop(0)()
-            if s in (0, 2, 3):
+            if s < 3:
                 won.pop(0)()
+            if s == 0 and last:
+                op("V", tcopy(T.hacc[:], T.fin2[:, 0:128]), r=["msk0"], w=["hacc"])
+                op("P", mm(T.pw[:, 0:128], T.idf[:], T.hacc[:], True, False), r=["hacc", "k1"], w=["pw0"], banks=["pw"])
             if s == 1:
-                op("P", [mm(T.ph[:, 0:128], T.hpad[:], T.idf[:], True, False)]
-                   + [mm(T.ph[:, j:128:4], T.imk[:], T.basF[:, 32 * j:32 * j + 32], False, j == 3) for j in range(4)],
-                   r=["hpad", "basF", "k1"], w=["ht"], banks=["ph"])
-                op("S", act(T.a3[:], T.ph[:, 0:128], F.Identity, bias=cf[:, 12:13]), r=["ht", "k1"], w=["a3"], banks=["ph"])
-            if s == 3:
-                op("P", mm(T.pw[:, 0:128], T.s2[:], T.pri[:, 256 * t + 128:256 * t + 256]), r=["s2", "k2"], w=["pw"], banks=["pw"])
-                op("S", act(T.dl[:], T.pw[:, 0:128], F.Copy), r=["pw"], w=["dl"], banks=["pw"])
-                for key, ps, bk in TURN:
-                    op("P", mm(ps, T.s1[:], T.pri[:, 256 * t:256 * t + 128], True, False), r=["s1", "k2"], w=[key], banks=[bk])
-                if not last:
+                op("P", mm(T.ph[:, 0:128], T.hpad[:], T.idf[:], False, False), r=["hpad", "k1"], w=["ht1"], banks=["ph"])
+            if s == 2:
+                send([(q + 1 if last else q + d + 2, T.s2[:, sl], T.lT[:, sl], "T%d" % d)], ["s2"])
+                op("P", mm(T.ph[:, 0:128], T.s1[:], T.prin[:], False, True), r=["s1", "k2"], w=["ht"], banks=["ph"])
+                if last:
+                    op("P", mm(T.pw[:, 0:128], T.s1[:], T.prin[:], False, True), r=["s1", "k2"], w=["pw"], banks=["pw"])
+                a3 = T.o1[:, o0:o0 + 128]
+                op("S", act(a3, T.ph[:, 0:128], F.Identity, bias=cf[:, 12:13]), r=["ht0", "ht1", "ht", "k1"], w=["a3"], banks=["ph"])
+                if last:
+                    op("S", act(T.o1[:, o0 + 128:o0 + 256], T.pw[:, 0:128], F.Copy), r=["pw0", "pw"], w=["a3h"], banks=["pw"])
+                    send([(q - d, T.o1[:, o0:o0 + 256], T.lAE[:], "AE")], ["a3", "a3h"])
+                else:
+                    send([(q - d - 1, a3, T.lA2[:, sl], "Ab%d" % d), (q + 1, a3, T.lA1[:, sl], "Aa%d" % d)], ["a3"])
+                    op("P", mm(T.pw[:, 0:128], T.s2[:, sl], T.pri[:, 256 * t + 128:256 * t + 256]), r=["s2", "k2"], w=["pw"], banks=["pw"])
+                    op("S", act(T.dl[:], T.pw[:, 0:128], F.Copy), r=["pw"], w=["dl"], banks=["pw"])
+                    op("P", mm(T.pd[:, 256:384], T.s1[:], T.pri[:, 256 * t:256 * t + 128], True, False), r=["s1", "k2"], w=["1hi"], banks=["pd"])
                     spread_z(d, "S", 1, 21, ["zr0"])
-            if last and s in (5, 7, 8, 9):
-                a, b, o, r, w = {5: (T.lH2[:, 0:128], T.lH1[:, 0:128], T.junk[:, 0:128], ["LHa0", "LHb0", "tot"], "jk0"),
-                                 7: (T.junk[:, 0:128], T.lH0[:], T.hx[:], ["jk0", "LH0"], "hx"),
-                                 8: (T.lH2[:, 128:256].indirect(T.ulF[:]), T.lH1[:, 128:256], T.junk[:, 128:256], ["LHa1", "LHb1", "LuF"], "jk1"),
-                                 9: (T.junk[:, 128:256], T.hx[:], T.hacc[:], ["jk1", "hx"], "jk6")}[s]
-                op("V", tt(o, a, b, A.max), r=r, w=[w])
+            if s == 8 and t:
+                order(*((T.r1, T.r2b, T.lc[:, 6:7], "LcE", "r4") if last else (T.r3, T.r3b, T.lc[:, 2:3], "LcF", "r3")))
+            if last:
+                continue
+            if s == 5:
+                op("V", [ts2(T.tl[:, 0:8], T.jl[:, 0:8], tot, 32768.0, A.subtract, A.add), ts1(T.tl[:, 8:16], T.jl[:, 0:8], tot, A.add)],
+                   r=["tot", "k5"], w=["tla"])
+            if s == 9:
+                op("V", [ts1(T.tl[:, 16:17], T.jl[:, 8:9], tot, A.add), ts1(T.tl[:, 18:20], T.jl[:, 8:10], tot, A.subtract),
+                         ts2(T.tl[:, 17:18], T.jl[:, 8:9], tot, T.tot[:, 0:1], A.add, A.subtract) if t else ts1(T.tl[:, 17:18], T.jl[:, 8:9], tot, A.add)],
+                   r=["tot", "kc"], w=["tlb"])
 
-        p1lo, p1hi, p2lo, p2hi = T.o1[:, o0:o0 + 128], T.o1[:, o0 + 128:o0 + 256], T.o2[:, o0:o0 + 128], T.o2[:, o0 + 128:o0 + 256]
-        sl = slice(128 * t, 128 * t + 128)
-        if not last:
-            op("V", [ts2(T.tl[:, 0:16], T.jl[:], T.tot[:, 0:1], 32768.0, A.subtract, A.add),
-                     ts1(T.tl[:, 16:24], T.jl[:, 0:8], T.tot[:, 0:1], A.add)], r=["tot", "k5"], w=["tl"])
+        dlo, dhi = T.dd[:, o0:o0 + 128], T.dd[:, o0 + 128:o0 + 256]
         last_phase(10, "lo")
         skip(10, 1)
+        if not last:
+            op("V", ts1(T.tl2[:], T.tl[:], 127, A.bitwise_and), r=["tla", "tlb"], w=["tl2"])
         last_phase(11, "lo")
         skip(10, 2)
-        last_phase(12, "lo")
         if last:
+            last_phase(12, "lo")
             last_phase(12, "hi")
             last_phase(13, "lo")
             last_phase(13, "hi")
             last_phase(14, "lo")
-            turn_back("lo")
             last_phase(14, "hi")
-            turn_back("hi")
-        else:
-            op("V", tcopy(T.pa_[:], T.pc[:, 264:272]), r=["vd"], w=["pa_"], banks=["pc"])
-            op("V", ts1(T.tl2[:], T.tl[:], 127, A.bitwise_and), r=["tl"], w=["tl2"])
-            last_phase(13, "lo")
-            op("V", ts1(T.pb_[:], T.pa_[:], 63, A.bitwise_and), r=["pa_"], w=["pb_"])
-            op("V", tcopy(T.lst[:, l0:l0 + 24], T.tl2[:]), r=["tl2"], w=["lst%d" % t])
-            last_phase(14, "lo")
-            turn_back("lo")
-            op("V", tt(T.pc_[:], T.pb_[:], T.plb[:], A.add), r=["pb_", "k2"], w=["pc_"])
-            last_phase(12, "hi")
-            op("V", tcopy(T.pl[:], T.pc_[:]), r=["pc_"], w=["pl"])
-            spread_z(d, "V", 21, 24, ["zr1"])
-
-        def upper():
-            op("V", [tcopy(p1hi, T.pd[:, 256:384]), tt(p2hi, T.pd[:, 256:384], T.dl[:], A.add)], r=["1hi", "dl"], w=["phi"], banks=["pd"])
-
-        op("V", tt(p1lo, T.pt[:, 0:128], T.a3[:], A.max), r=["1lo", "a3"], w=["p1lo"], banks=["pt"])
-        if not last:
-            send([(q - d - 1, p1lo, T.lS[:, sl], "S%d" % d)], ["p1lo"])
-        op("V", tt(p2lo, T.pt[:, 0:128], T.dl[:], A.add), r=["1lo", "dl"], w=["p2lo"], banks=["pt"])
-        if last:
-            op("V", tt(p2hi, T.pd[:, 256:384], T.dl[:], A.add), r=["1hi", "dl"], w=["p2hi"], banks=["pd"])
-            send([(q + 1, T.o2[:, o0:o0 + 256], T.lE2[:], "Eb")], ["p2lo", "p2hi"])
-            op("V", tt(p1hi, T.pd[:, 256:384], T.hacc[:], A.max), r=["1hi", "jk6"], w=["p1hi"], banks=["pd"])
-            send([(q - d, T.o1[:, o0:o0 + 256], T.lE1[:], "Ea")], ["p1lo", "p1hi"])
+            send([(q + 1, T.dd[:, o0:o0 + 256], T.lE2[:], "Eb")], ["lo15", "hi15"])
+            send([(q - d, T.dd[:, o0:o0 + 256], T.lE1[:], "Ea")], ["lo15", "hi15"])
             break
-        send([(q + 1, p1lo, T.lF1[:, sl], "Fa%d" % d), (q + d + 2, p2lo, T.lF2[:, sl], "Fb%d" % d)], ["p1lo", "p2lo"])
-
+        op("V", [tcopy(T.lst[:, l0:l0 + 16], T.tl2[:, 0:16]), tcopy(col, T.tl2[:, 16:20])], r=["tl2"], w=["lst%d" % t])
+        last_phase(12, "lo")
+        op("V", tcopy(T.pa_[:], T.pc[:, 264:272]), r=["vd"], w=["pa_"], banks=["pc"])
+        last_phase(12, "hi")
+        last_phase(13, "lo")
+        op("V", ts1(T.pb_[:], T.pa_[:], 63, A.bitwise_and), r=["pa_"], w=["pb_"])
+        order(T.r2, T.r2b, T.col[:, 4 * t + 1:4 * t + 2], "lst%d" % t, "r2")
+        last_phase(14, "lo")
         if t:
-            op("S", act(T.hx[:], p2lo.indirect(T.lst[:, 16:24]), F.Copy), r=["p2lo", "lst0"], w=["hx"])
-        last_phase(13, "hi")
-        op("V", tcopy(T.X[:].indirect(T.pl[:]), E), r=["pl"] + tops, w=["X"])
-        last_phase(14, "hi")
-        turn_back("hi")
-        spread_z(d, "V", 24, 28, ["zr2"])
-        spread_z(d, "S", 28, 32, ["zr3"])
-        un = T.lst[:, l0 + 16:l0 + 24]
-        if t == 0:
-            send([(q + 4, un, T.ulF[:], "uF")], ["lst0"])
-        else:
-            send([(q + 1, un, T.ulH2[:], "uH2")], ["lst1"])
+            order(T.r1, None, T.col[:, 4 * t:4 * t + 1], "lst%d" % t, "r1")
 
-        op("V", tt(T.mS[:], T.hx[:] if t else p2lo, T.lS[:, sl], A.max), r=["hx", "p2lo", "LS%d" % d], w=["mS"])
-        upper()
+        send([(q - d - 1, dlo, T.lS[:, sl], "S%d" % d)], ["lo15"])
+        send([(q + d + 2, dlo, T.lF2[:, sl], "Fb%d" % d)], ["lo15"])
+        send([(q + 1, dlo, T.lF1[:, sl], "Fa%d" % d)], ["lo15"])
+        if t == 0:
+            send([(q + 4, T.lst[:, 8:16], T.ulF[:], "uF"), (q + 4, col, T.lc[:, 0:4], "cF")], ["lst0"])
+        else:
+            send([(q + 1, col, T.lc[:, 4:8], "cE")], ["lst1"])
+
+        minus_threshold()
+        op("S", act(T.hx[:], T.lA2[:, sl].indirect(T.lst[:, l0:l0 + 8]), F.Copy), r=["LAb%d" % d, "lst%d" % t], w=["hx"])
+        fallback(T.pt[:, 0:128], "pt", T.s2[:, sl], "s2", T.r2, T.r2b, "r2", T.hx[:], "hx", T.sgS[:], dlo, "lo15", "BS")
+        op("V", tt(T.pc_[:], T.pb_[:], T.plb[:], A.add), r=["pb_", "k2"], w=["pc_"])
+        last_phase(13, "hi")
+        spread_z(d, "V", 21, 24, ["zr1"])
+        op("V", tcopy(T.pl[:], T.pc_[:]), r=["pc_"], w=["pl"])
+        if t:
+            op("V", tt(T.junk[:, 0:128], T.lH2[:, 0:128], T.lH1[:, 0:128], A.max), r=["LHa0", "LHb0", "tot"], w=["jk0"])
+        last_phase(14, "hi")
+        op("P", mm(T.pd[:, 256:384], dhi, T.p0[:], False, True), r=["hi15", "k2"], w=["1hi"], banks=["pd"])
+        spread_z(d, "V", 24, 27, ["zr2"])
+        op("V", tcopy(T.X[:].indirect(T.pl[:]), E), r=["pl"] + tops, w=["X"])
+        op("V", tt(T.cS[:], T.pt[:, 0:128], T.hx[:], A.max), r=["BS", "BSp", "hx"], w=["cS"], banks=["pt"])
+        if t:
+            op("V", tt(T.hacc[:], T.junk[:, 0:128], T.lH0[:], A.max), r=["jk0", "LH0"], w=["hacc"])
+        p1hi, p2hi = T.o1[:, o0 + 128:o0 + 256], T.o2[:, sl]
+        op("V", [tcopy(p1hi, T.pd[:, 256:384]), tt(p2hi, T.pd[:, 256:384], T.dl[:], A.add)], r=["1hi", "dl"], w=["phi"], banks=["pd"])
         send([(q - d + RO, p1hi, T.lH1[:, sl], "Ha%d" % t), (q + 1 + RO, p2hi, T.lH2[:, sl], "Hb%d" % t)], ["phi"])
-        op("V", ts1(T.si[:], T.mS[:], 8191, A.bitwise_and), r=["mS"], w=["iSa", "iSb"])
-        op("V", tcopy(T.offS[:, 0:32], T.si[:].indirect(T.lst[:, l0:l0 + 2])), r=["iSa", "lst%d" % t], w=["offSa"])
-        op("V", tcopy(T.offS[:, 32:128], T.si[:].indirect(T.lst[:, l0 + 2:l0 + 8])), r=["iSa", "lst%d" % t], w=["offSb"])
+
+        r1, k1 = (T.r1, "r1") if t else (T.r2, "r2")
+        for x, ps, bk in ((PARTS[0], T.pu[:, 0:32], "pu"), (PARTS[1], T.pw[:, 128:224], "pw")):
+            op("P", mm(ps, T.lS[:, sl], r1[:, x[1]:x[2]]), r=["LS%d" % d, k1], w=["AS" + x[0]], banks=[bk])
+        rF, rFb, kF = (T.r3, T.r3b, "r3") if t else (T.p0, T.pb22, "k2")
+        fallback(T.pc[:, 128:256], "pc", T.lT[:, sl], "LT%d" % d, rF, rFb, kF, T.lA1[:, sl], "LAa%d" % d, T.sgF[:], T.lF2[:, sl], "LFb%d" % d, "BF")
+        for x, ps, bk in ((PARTS[0], T.ph[:, 128:160], "ph"), (PARTS[1], T.pb[:, 128:224], "pb")):
+            op("P", mm(ps, T.lF1[:, sl], T.p0[:, x[1]:x[2]]), r=["LFa%d" % d, "k2"], w=["AF" + x[0]], banks=[bk])
+        spread_z(d, "S", 27, 32, ["zr3"])
+        for (x, a, b), ps, bk in ((PARTS[0], T.pu[:, 0:32], "pu"), (PARTS[1], T.pw[:, 128:224], "pw")):
+            op("V", tt(T.mS[:, a:b], ps, T.cS[:, a:b], A.max), r=["AS" + x, "cS"], w=["mS" + x], banks=[bk])
+        for x, a, b in PARTS:
+            op("V", ts1(T.si[:, a:b], T.mS[:, a:b], 8191, A.bitwise_and), r=["mS" + x], w=["iS" + x])
+        for x, a, b in PARTS:
+            op("V", tcopy(T.offS[:, a:b], T.si[:, a:b]), r=["iS" + x], w=["offS" + x])
 
     wait("Y", [lastw["Lzf"]])
     op("Y", lambda: Y.dma_start(T.yz[:], T.zfin[:]), w=["yz"], inc=16)
     halves = [(k, slice(128 * k, 128 * k + 128)) for k in (0, 1)]
+    psB, psA = ((T.pt[:, 0:128], "pt"), (T.pc[:, 128:256], "pc")), ((T.pu[:, 0:128], "pu"), (T.pw[:, 128:256], "pw"))
     for k, c in halves:
-        op("V", tcopy(T.junk[:, c], T.lE2[:, c].indirect(T.ulH2[:])), r=["LEb", "LuH2"], w=["jk%d" % k])
+        fallback(psB[k][0], psB[k][1], T.lT[:, 256:384], "LT3", T.r1, T.r2b, "r4", T.lAE[:, c], "LAE", (T.sgS, T.sgF)[k][:], T.lE2[:, c], "LEb", "B%d" % k)
     for k, c in halves:
-        op("V", tt(T.fin[:, c], T.junk[:, c], T.lE1[:, c], A.max), r=["LEa", "jk%d" % k], w=["fin%d" % k])
+        op("V", tt(T.fb[:, k], psB[k][0], T.lAE[:, c], A.max), r=["B%d" % k, "B%dp" % k, "LAE"], w=["jk%d" % k], banks=[psB[k][1]])
+    for k, c in halves:
+        op("P", [mm(T[psA[k][1]][:, 128 + 64 * x:192 + 64 * x], T.lE1[:, 128 * x:128 * x + 128], T.p0[:, 64 * k:64 * k + 64]) for x in (0, 1)],
+           r=["LEa", "k2"], w=["A%d" % k], banks=[psA[k][1]])
+    for k, c in halves:
+        op("V", tt(T.fin[:, c], T[psA[k][1]][:, 128:256], T.fb[:, :, 64 * k:64 * k + 64], A.max), r=["A%d" % k, "jk0", "jk1"], w=["fin%d" % k], banks=[psA[k][1]])
     for k, c in halves:
         op("V", ts1(T.fin2[:, c], T.fin[:, c], 8191, A.bitwise_and), r=["fin%d" % k], w=["msk%d" % k])
     for k, c in halves:
-        op("V", tcopy(T.yo[:, k:256:2], T.fin2[:, c]), r=["msk%d" % k], w=["yo%d" % k])
-    op("Y", lambda: Y.dma_start(T.ya[:], T.yo[:]), r=["yo0", "yo1"], w=["ya"], inc=16)
+        op("V", [tcopy(T.yo[:, 128 * k + x:128 * k + 128:2], T.fin2[:, 128 * k + 64 * x:128 * k + 64 * x + 64]) for x in (0, 1)], r=["msk%d" % k], w=["yo%d" % k])
+        op("SY"[k], lambda: (S, Y)[k].dma_start(T.ya[:, c], T.yo[:, c]), r=["yo%d" % k], w=["ya%d" % k], inc=16)
     for s in cnt:
         if s[0] != "Y" and waited.get(s, 0) < cnt[s]:
             g.wait_ge(T.sem[s], cnt[s])

@@ -4,6 +4,8 @@ from concourse.mybir import AluOpType, ActivationFunctionType
 A = AluOpType
 F = ActivationFunctionType
 N, RO, PAD, XA = 8, 3, 2, 4096
+TAG = float(1 << 19)
+UP = float(1 << 21)
 f32, bf, i32, u16 = "float32", "bfloat16", "int32", "uint16"
 
 
@@ -14,50 +16,53 @@ def sb(shape, d):
 SCRATCH = {
     "X": sb([8192], bf), "xg": sb([4096], bf), "zrep": sb([4096], bf), "top": sb([4096 + 16], bf),
     "rai": sb([256], i32), "zown": sb([128], bf), "wi": sb([256], i32), "wf": sb([256], f32), "lo0": sb([128], u16),
-    "jf": sb([144], f32), "jt": sb([256], f32), "ci": sb([8], i32), "cf": sb([16], f32),
-    "ibf": sb([128], bf), "isc": sb([128], f32), "p0": sb([128], f32), "pbp": sb([128], bf),
+    "jf": sb([144], f32), "jb": sb([128], bf), "jp": sb([128], bf), "jt": sb([256], f32), "ci": sb([8], i32), "cf": sb([32], f32),
+    "ibf": sb([128], bf), "p0": sb([128], f32), "pbp": sb([128], bf), "tri": sb([128], bf), "kc0": sb([256], bf),
+    "gp16": sb([128], bf), "mh": sb([128], bf), "c0": sb([128], bf), "sgj": sb([64], bf),
     "gp": sb([8], bf), "gn": sb([8], bf), "wgr": sb([8], bf), "ones": sb([128], bf),
-    "onen": sb([128], f32), "ww": sb([144], bf), "tm": sb([256], f32), "trep": sb([8], f32),
-    "jl": sb([16], f32), "ja": sb([8], i32), "pip": sb([8], u16), "plb": sb([8], i32),
+    "onen": sb([128], f32), "ww": sb([144], bf), "tm": sb([256], f32),
+    "jl": sb([8], f32), "jq": sb([20], f32), "ja": sb([8], i32), "pip": sb([8], u16), "plb": sb([8], i32),
     "zl": sb([384], bf), "zfin": sb([128], f32), "nzb": sb([256], bf), "nzf": sb([128], f32),
     "offF": sb([128], u16), "offS": sb([128], u16), "off0F": sb([128], u16), "off0S": sb([128], u16),
     "mF": sb([128], i32), "mS": sb([128], i32), "fi": sb([128], i32), "si": sb([128], i32),
-    "basF": sb([128], f32), "basS": sb([128], f32),
-    "u3": sb([256], bf), "u2": sb([256], bf), "u0": sb([128], bf), "imk": sb([128], f32),
-    "kF": sb([128], f32), "e0": sb([4, 8, 32], f32), "e1": sb([4, 8, 32], f32),
-    "j16": sb([8, 1, 2, 2, 8], f32), "j8": sb([8, 2, 2, 2, 4], f32), "j4": sb([8, 4, 2, 2, 2], f32), "j2": sb([8, 8, 2, 2], f32),
+    "basF": sb([128], f32), "basS": sb([128], f32), "u3": sb([256], bf), "imk": sb([128], f32),
+    "ki": sb([8, 2, 8, 2], i32), "km": sb([8, 2, 8, 2], i32), "n1": sb([8, 2, 4, 2, 2], f32), "n3": sb([8, 2, 2, 2, 6], f32),
+    "n4": sb([8, 2, 2, 2, 4], f32), "n6": sb([8, 2, 6, 4], f32), "n7": sb([8, 16], i32), "nb": sb([8, 2, 2, 4], i32),
+    "n8": sb([8, 2, 2, 4], f32), "n9": sb([8, 2, 2, 4], f32), "na": sb([8, 4, 2, 2], f32),
     "dd": sb([768], f32),
     "ha": sb([8], i32), "hb": sb([8], i32), "hc": sb([8], i32), "hpad": sb([128], f32),
-    "sgn": sb([256], bf), "alt": sb([256], bf), "hold": sb([128], bf), "ab0": sb([128], bf), "ab": sb([128], bf),
-    "s1": sb([128], bf), "s2": sb([384], bf), "pri": sb([512], bf), "idf": sb([128], f32),
-    "prin": sb([128], bf), "pb22": sb([128], bf), "ic3": sb([128], bf), "sgS": sb([128], bf), "sgF": sb([128], bf),
-    "r1": sb([128], f32), "r2": sb([128], f32), "r3": sb([128], f32), "r2b": sb([128], bf), "r3b": sb([128], bf),
-    "zer": sb([128], bf), "fb": sb([2, 128], f32), "cS": sb([128], f32), "cF": sb([128], f32), "col": sb([12], f32), "lc": sb([8], f32),
-    "lA1": sb([256], f32), "lA2": sb([256], f32), "lAE": sb([256], f32), "lT": sb([384], bf),
-    "junk": sb([256], f32), "tot": sb([4], f32), "tl": sb([20], i32), "tl2": sb([20], i32), "lst": sb([32], u16),
+    "s1": sb([384], bf), "s2": sb([384], bf), "pri": sb([4, 128], bf), "idf": sb([128], f32),
+    "prin": sb([128], bf), "pb21": sb([128], bf), "ic3": sb([128], bf), "sgS": sb([128], bf), "sgF": sb([128], bf),
+    "r1": sb([128], f32), "r2": sb([128], f32), "r3": sb([128], f32), "rh": sb([128], f32),
+    "r1b": sb([128], bf), "r2b": sb([128], bf), "r3b": sb([128], bf), "rhb": sb([128], bf),
+    "fb": sb([128], f32), "cS": sb([128], f32), "cF": sb([128], f32), "col": sb([12], f32), "lc": sb([8], f32),
+    "lA1": sb([256], f32), "lA2": sb([256], f32), "lAE": sb([128], f32), "lT": sb([512], bf),
+    "junk": sb([256], f32), "jk": sb([128], f32), "tot": sb([8], f32), "tlf": sb([20], f32), "tl": sb([20], i32), "tl2": sb([20], i32), "lst": sb([32], u16),
     "pa_": sb([8], i32), "pb_": sb([8], i32), "pc_": sb([8], i32), "pl": sb([8], u16),
-    "o1": sb([768], f32), "o2": sb([256], f32),
+    "o1": sb([384], f32), "oh": sb([512], f32),
     "lS": sb([256], f32), "lF1": sb([256], f32), "lF2": sb([256], f32),
     "lH1": sb([256], f32), "lH2": sb([256], f32), "lE1": sb([256], f32), "lE2": sb([256], f32),
-    "ulF": sb([8], u16), "ulH2": sb([8], u16), "hi0": sb([128], f32), "lH0": sb([128], f32), "hacc": sb([128], f32),
-    "dl": sb([128], bf),
-    "hx": sb([128], f32), "fin": sb([256], i32), "fin2": sb([256], i32), "yo": sb([256], f32),
+    "hi0": sb([128], f32), "hacc": sb([128], f32),
+    "hx": sb([128], f32), "yo": sb([256], f32),
     "pg": ("psum", [128, 512], f32), "pb": ("psum", [128, 512], f32),
     "pt": ("psum", [128, 512], f32), "ph": ("psum", [128, 512], f32),
     "pc": ("psum", [128, 512], f32), "pd": ("psum", [128, 512], f32),
     "pu": ("psum", [128, 512], f32), "pw": ("psum", [128, 512], f32),
 }
-POOL = {"V": 38, "S": 28, "P": 38, "G": 4, "Y": 10}
+POOL = {"V": 38, "S": 28, "P": 36, "G": 6, "Y": 10}
 ARR = ["z0", "z1", "z2", "zf", "F0", "S0", "S1", "S2", "Fa1", "Fa2", "Fb1", "Fb2", "Ha0", "Ha1", "Hb0", "Hb1",
-       "Ea", "Eb", "uF", "H0", "cF", "cE", "Aa1", "Aa2", "Ab1", "Ab2", "AE", "T1", "T2", "T3"]
+       "Ea", "Eb", "Ua", "Ub", "cF", "cE", "Aa1", "Aa2", "Ab1", "Ab2", "AE", "T1", "T2", "T3", "TL"]
 SEMAPHORES = [q + str(k) for q in POOL for k in range(POOL[q])] + ["r" + a for a in ARR] + ["sent"]
-STAGES = [(p, sh) for p in (16, 8, 4, 2, 1) for sh in [0] + [x for x in (8, 4, 2, 1) if x >= p]]
-SLOT = {2: 0, 4: 1, 5: 0, 7: 1, 8: 0, 9: 2, 11: 3, 12: 1, 13: 0, 14: 2}
 SEQ0 = ["F1 S0 S1 S23 F6 S45 S6 S7", "A F0 F2 f01 F3 s0 s1 f23 F45 s2 s3 f46 F7 s4 s5 f7 s6"]
-SEQ = ["S0 S13 F1 F2 F46 S4 S6 S7a S7b", "M b S5a ma mb aa ab oa S5b ob A F0 B f01 F3 s0 s1 f23 F7 s2 f4 f57 s3 s4 s5 s6"]
+SEQ = ["S0 S13 F1 F2 F46 S4 S6 S7a S7b", "M b S5a ma mb aa ab oa S5b ob A H F0 B f01 F3 s0 s1 f23 F7 s2 f4 f57 s3 s4 s5 s6"]
+NET = "ha hb k0 k1 00 hh 01 10 11 20 21 30 hc 31 40 hp 41 far 50 51 tl 60 61 tm 70 71 tn 80 pa 81 r2 90 91 r1 pb a0 a1 pc b0 b1 pl c0 c1"
+LAST = "ha k0 hb k1 00 hh 01 10 11 20 hc 21 30 hp 31 40 41 rh 50 51 far 60 61 up 70 71 80 81 j0 90 91 a0 a1 j1 b0 b1 c0 c1 j2"
+HOP = "up X zS24 rh zV46 cS j0 zV68 j1 ma mb aa ab oa ob"
+END = "u1 u2 80 81 90 91 a0 a1 fb b0 b1 c0 c1 l0 l1 l2"
+ZS, ZG = 2, 0
 
 
-RELAYED = ["H0", "T1", "Aa1", "T2", "Aa2", "T3"]
+RELAYED = ["T1", "Aa1", "Ha0", "Hb0", "T2", "Aa2", "Ha1", "Hb1", "T3", "TL"]
 
 
 def helper(core, T, topo):
@@ -70,8 +75,9 @@ def spare(core, T, topo):
 
 
 def helper_program(g, core, q, T, topo):
-    land = {"H0": (q + RO, T.lH0[:]), "T1": (q + 3, T.lT[:, 0:128]), "Aa1": (q + 1, T.lA1[:, 0:128]), "T2": (q + 4, T.lT[:, 128:256]),
-            "Aa2": (q + 1, T.lA1[:, 128:256]), "T3": (q + 1, T.lT[:, 256:384])}
+    land = {"T1": (q + 3, T.lT[:, 0:128]), "Aa1": (q + 1, T.lA1[:, 0:128]), "T2": (q + 4, T.lT[:, 128:256]),
+            "Aa2": (q + 1, T.lA1[:, 128:256]), "T3": (q + 1, T.lT[:, 256:384]), "TL": (q - RO, T.lT[:, 384:512]),
+            "Ha0": (q - 1, T.lH1[:, 0:128]), "Hb0": (q + 1, T.lH2[:, 0:128]), "Ha1": (q - 2, T.lH1[:, 128:256]), "Hb1": (q + 1, T.lH2[:, 128:256])}
     n = 0
     for name in RELAYED:
         dst, ap = land[name]
@@ -164,7 +170,7 @@ def rank_program(g, core, T, topo):
             g.remote_dma_fused([RemoteDMATransfer(dst_ids=[DstId(rid=a, pnc=b)], dma_engine_mask=m, remote_sem=T.sem["r" + nm],
                                                   src=s, dst=l) for a, b, m, s, l, nm in ts], local_sem=T.sem.sent)
 
-    def expect(name, src, share):
+    def expect(name, src, share=1):
         n = len(topo.engines(T.cores[src % N], core)) // share
         cnt["r" + name] = n
         lastw["L" + name] = ("r" + name, n, {})
@@ -190,28 +196,29 @@ def rank_program(g, core, T, topo):
     def act(o, i, fn, **kw):
         return lambda: S.activation(o, i, fn, **kw)
 
-    expect("z0", q - 1, 1)
+    def copy(qn, o, i):
+        if qn == "G":
+            return lambda: g.affine_select(o, i, [[0, 128]], A.is_ge, 0.0, 0, 0)
+        return tcopy(o, i) if qn == "V" else act(o, i, F.Copy)
+
+    expect("z0", q - 1)
     expect("F0", q - 1, 2)
     expect("S0", q + 1, 2)
     for t in (1, 2):
-        expect("z%d" % t, q - 1, 1)
-        expect("S%d" % t, q + t + 1, 1)
-        expect("Fa%d" % t, q - 1, 1)
-        expect("Fb%d" % t, q - t - 2, 1)
-        expect("Aa%d" % t, q - 1, 1)
-        expect("Ab%d" % t, q + t + 1, 1)
-        expect("T%d" % t, q - t - 2, 1)
-        expect("Ha%d" % (t - 1), q + t - RO, 2)
-        expect("Hb%d" % (t - 1), q - 1 - RO, 2)
-    expect("zf", q + 3, 1)
-    expect("Ea", q + 3, 1)
-    expect("Eb", q - 1, 1)
-    expect("uF", q - 4, 2)
-    expect("cF", q - 4, 2)
-    expect("H0", q - RO, 1)
-    expect("cE", q - 1, 1)
-    expect("T3", q - 1, 1)
-    expect("AE", q + 3, 1)
+        expect("z%d" % t, q - 1)
+        expect("S%d" % t, q + t + 1)
+        expect("Fa%d" % t, q - 1)
+        expect("Fb%d" % t, q - t - 2)
+        expect("Aa%d" % t, q - 1)
+        expect("Ab%d" % t, q + t + 1)
+        expect("T%d" % t, q - t - 2)
+        expect("Ha%d" % (t - 1), q + t)
+        expect("Hb%d" % (t - 1), q - 1)
+    for name in ("zf", "Ea", "Ua", "AE", "TL"):
+        expect(name, q + RO)
+    for name in ("Eb", "Ub", "cE", "T3"):
+        expect(name, q - 1)
+    expect("cF", q - 4)
 
     op("Y", lambda: Y.dma_start(T.zown[:], T.zu[:]), w=["zown"], inc=16)
     op("S", lambda: S.dma_start(T.rai[:], T.ra[:]), w=["rai"], inc=16)
@@ -225,153 +232,165 @@ def rank_program(g, core, T, topo):
     op("G", lambda: g.iota(jf[:], [[1, 144]], 0, 0, allow_small_or_imprecise_dtypes=True), w=["jf"])
     send([(q + 1, T.zown[:], T.zl[:, 0:128], "z0")], ["zown"])
 
-    op("V", [fillc(T.top[:, 0:PAD], 0.0), fillc(T.ones[:], 1.0), fillc(T.onen[:], -1.0), fillc(T.sgn[:], -1.0), fillc(T.hold[:], 1.0)],
-       w=["pad", "ones"])
+    op("V", [fillc(T.top[:, 0:PAD], 0.0), fillc(T.mh[:], -0.5), fillc(T.ones[:], 1.0), fillc(T.onen[:], -1.0)], w=["pad", "ones"])
     op("V", [ts1(ci[:, 1:2], ci[:, 0:1], 15, A.bitwise_and), ts1(ci[:, 2:3], ci[:, 0:1], 4, A.arith_shift_right),
-             ts1(ci[:, 3:4], ci[:, 0:1], 31, A.bitwise_and), ts1(ci[:, 4:5], ci[:, 0:1], 5, A.arith_shift_right)], r=["ci0"], w=["ci"])
-    op("V", [fillc(T.hpad[:], 0.0), fillc(T.u0[:], 0.0), fillc(T.ab0[:], 0.0), fillc(T.zer[:], 0.0)], w=["hpad", "u0", "ab0", "ab0z"])
-    op("V", [tcopy(cf[:, 0:5], ci[:, 0:5]), ts1(cf[:, 5:6], ci[:, 1:2], 16384.0, A.mult),
-             ts2(cf[:, 6:7], ci[:, 1:2], 16384.0, 8192.0, A.mult, A.add), ts2(cf[:, 7:8], ci[:, 2:3], 16.0, 15.0, A.mult, A.add),
-             ts1(cf[:, 13:14], ci[:, 1:2], 4.0, A.mult), ts1(cf[:, 14:15], ci[:, 1:2], 15.0, A.not_equal)], r=["ci", "ci0"], w=["cf"])
+             ts1(ci[:, 3:4], ci[:, 0:1], 31, A.bitwise_and), ts1(ci[:, 4:5], ci[:, 0:1], 5, A.arith_shift_right),
+             ts1(ci[:, 5:6], ci[:, 0:1], 1, A.bitwise_and), ts1(ci[:, 7:8], ci[:, 0:1], 3, A.bitwise_and)], r=["ci0"], w=["ci"])
+    op("V", [fillc(T.hpad[:], 0.0), fillc(cf[:, 27:28], 129.5 + 2.0 ** -14)], w=["hpad"])
+    op("V", [tcopy(cf[:, 0:5], ci[:, 0:5]), ts2(cf[:, 7:8], ci[:, 2:3], 16.0, 15.0, A.mult, A.add),
+             ts1(cf[:, 13:14], ci[:, 1:2], 4.0, A.mult), ts1(cf[:, 14:15], ci[:, 1:2], 15.0, A.not_equal),
+             ts2(cf[:, 15:16], ci[:, 5:6], 2 * TAG, -TAG / 2, A.mult, A.add), ts2(cf[:, 20:21], ci[:, 1:2], 0.0, 2.25 * TAG, A.is_equal, A.mult),
+             ts1(cf[:, 21:22], ci[:, 3:4], 0.0, A.not_equal), ts2(cf[:, 16:17], ci[:, 7:8], -TAG, 3.5 * TAG, A.mult, A.add),
+             ts2(cf[:, 17:18], ci[:, 4:5], 32.0, 32.0, A.mult, A.add), ts2(cf[:, 18:19], ci[:, 5:6], 2.0, -1.0, A.mult, A.add),
+             ts1(cf[:, 23:24], ci[:, 7:8], 1.0, A.is_equal), ts2(cf[:, 24:25], ci[:, 7:8], 2.0, -1.0, A.is_equal, A.mult),
+             ts1(cf[:, 25:26], ci[:, 1:2], 8192.0, A.mult)], r=["ci", "ci0"], w=["cf"])
     op("V", tcopy(T.lo0[:], T.rai[:, 0:256:2]), r=["rai"], w=["lo0"])
     send([(q + 1, T.lo0[:], T.off0F[:], "F0"), (q - 1, T.lo0[:], T.off0S[:], "S0")], ["lo0"])
     op("G", lambda: g.iota(jt[:], [[1, 8], [0, 32]], 0, 0, allow_small_or_imprecise_dtypes=True), w=["jt"])
+    op("G", lambda: g.iota(T.jp[:], [[1, 4], [4, 32]], 0, 0, allow_small_or_imprecise_dtypes=True), w=["jp"])
     op("V", tcopy(T.wf[0:1, :], T.wi[0:1, :]), r=["wi", "ti"], w=["wf"])
     op("P", [mm(T.pd[:, 8 + k:9 + k], T.wf[0:1, 128 * k:128 * k + 128], T.onen[0:1, 0:1]) for k in (0, 1)], r=["wf", "ones"], w=["wt"], banks=["pd"])
     op("V", [ts2(cf[:, 10:11], ci[:, 3:4], 4.0, cf[:, 4:5], A.mult, A.add),
+             ts2(cf[:, 22:23], ci[:, 1:2], 16384.0, cf[:, 15:16], A.mult, A.add),
+             ts2(cf[:, 26:27], cf[:, 0:1], cf[:, 23:24], cf[:, 24:25], A.add, A.add),
              ts1(T.pip[:], T.ja[:], cf[:, 13:14], A.add),
-             ts2(T.jl[:, 0:8], jf[:, 0:8], 16.0, cf[:, 1:2], A.mult, A.add),
-             ts1(T.ibf[:], jf[:, 0:128], cf[:, 0:1], A.is_equal),
+             ts2(T.jl[:], jf[:, 0:8], 16.0, cf[:, 1:2], A.mult, A.add),
+             ts1(T.ibf[:], jf[:, 0:128], cf[:, 0:1], A.is_equal), tcopy(T.jb[:], jf[:, 0:128]),
              ts1(T.gp[:], jf[:, 0:8], cf[:, 2:3], A.is_equal),
-             ts1(cf[:, 11:12], cf[:, 3:4], 0.0, A.not_equal), ts2(cf[:, 12:13], cf[:, 5:6], cf[:, 14:15], -1.0, A.mult, A.mult),
-             ts2(T.gn[:], jf[:, 0:8], cf[:, 2:3], -1.0, A.is_equal, A.mult)], r=["cf", "ci", "jf", "ja"], w=["kb", "k5", "pip"])
-    op("V", [fillc(T.e0[:, :, :, 24:26], 4.0), fillc(T.e1[:, :, :, 6:8], -1.0)], w=["pads"])
+             ts2(T.gn[:], jf[:, 0:8], cf[:, 2:3], -1.0, A.is_equal, A.mult),
+             ts2(T.dd[:, 0:128], jf[:, 0:128], cf[:, 0:1], -TAG, A.is_gt, A.mult), ts2(T.dd[:, 128:256], jf[:, 0:128], cf[:, 17:18], TAG, A.is_ge, A.mult),
+             ts2(T.dd[:, 256:384], jf[:, 0:128], cf[:, 0:1], cf[:, 16:17], A.is_equal, A.mult)], r=["cf", "ci", "jf", "ja"], w=["kb", "pip"])
     op("V", [ts1(cf[:, 8:9], T.pd[:, 8:9], -1.0, A.mult), ts1(cf[:, 9:10], T.pd[:, 9:10], -1.0 / 16, A.mult)], r=["wt"], w=["k0"], banks=["pd"])
-    op("V", [ts1(T.plb[:], T.jl[:, 0:8], 64.0, A.mult), ts1(T.pbp[:], jf[:, 0:128], cf[:, 10:11], A.is_equal),
-             ts2(T.jl[:, 8:10], T.onen[:, 0:2], -32768.0, cf[:, 10:11], A.mult, A.add),
-             fillc(T.sgn[:, 0:256:32], 0.0), fillc(T.hold[:, 0:128:16], 0.0)], r=["kb", "ones"], w=["kc", "k4"])
+    op("V", [ts1(T.plb[:], T.jl[:], 64.0, A.mult), ts1(T.pbp[:], jf[:, 0:128], cf[:, 10:11], A.is_equal),
+             ts1(T.jq[:, 0:8], T.jl[:], 32768.0, A.add), tcopy(T.jq[:, 8:16], T.jl[:]),
+             ts2(T.jq[:, 16:20], T.onen[:, 0:4], -32768.0, cf[:, 10:11], A.mult, A.add),
+             ts1(cf[:, 6:7], cf[:, 22:23], 8192.0 + TAG, A.add), ts1(cf[:, 5:6], cf[:, 22:23], cf[:, 20:21], A.add),
+             ts2(cf[:, 19:20], cf[:, 22:23], cf[:, 20:21], cf[:, 14:15], A.add, A.mult),
+             tt(T.dd[:, 0:128], T.dd[:, 0:128], T.dd[:, 128:256], A.add), ts1(T.hi0[:], T.rai[:, 1:256:2], cf[:, 25:26], A.add),
+             ts1(T.jk[:, 0:128], jf[:, 0:128], cf[:, 26:27], A.is_equal)], r=["kb", "ones", "rai"], w=["kc", "jk"])
     op("Y", lambda: Y.dma_start(T.X[:, XA:8192], T.xd[:, XA:8192]), r=["jt"], w=["X"], inc=16)
-    op("S", [act(T.isc[:], T.ibf[:], F.Identity, scale=2.0 ** -18), act(T.idf[:], T.ibf[:], F.Copy),
-             act(T.imk[:], T.ibf[:], F.Identity, scale=cf[:, 14:15])], r=["kb"], w=["k1"])
+    op("S", [act(T.idf[:], T.ibf[:], F.Copy), act(T.imk[:], T.ibf[:], F.Identity, scale=cf[:, 14:15])]
+       + [act(T.pri[:, k], T.ibf[:], F.Identity, scale=x * UP) for k, x in ((0, 2), (1, 4), (3, 1))], r=["kb"], w=["k1"])
     op("V", [ts2(T.tm[:], jt[:], cf[:, 2:3], cf[:, 9:10], A.is_equal, A.mult),
              ts2(T.wgr[:], jf[:, 0:8], cf[:, 2:3], cf[:, 8:9], A.is_equal, A.mult),
-             ts2(T.ww[:], jf[:], cf[:, 7:8], cf[:, 8:9], A.is_equal, A.mult)], r=["k0", "kb", "jt"], w=["k3"])
-    op("S", [act(T.p0[:], T.pbp[:], F.Identity, scale=2.0 ** 18), act(T.prin[:], T.pbp[:], F.Identity, scale=-2.0 ** 22),
-             act(T.pb22[:], T.pbp[:], F.Identity, scale=2.0 ** 22), act(T.ic3[:], T.ibf[:], F.Identity, scale=3 * 2.0 ** 20)]
-       + [act(T.pri[:, 256 * t + 128 * k:256 * t + 128 * k + 128], T.pbp[:], F.Identity, scale=float((3 * t + 3 + k * (3 * t + 2)) << 20))
-          for t in range(RO - 1) for k in (0, 1)], r=["kc"], w=["k2"])
-    op("P", mm(T.pd[:, 0:8], T.onen[:], T.tm[:, 0:256:32]), r=["k3", "ones"], w=["pd"], banks=["pd"])
-    op("V", tcopy(T.hi0[:], T.rai[:, 1:256:2]), r=["rai"], w=["hi0"])
+             ts2(T.ww[:], jf[:], cf[:, 7:8], cf[:, 8:9], A.is_equal, A.mult),
+             ts2(T.sgj[:], jt[:, 0:128:2], cf[:, 4:5], cf[:, 18:19], A.is_equal, A.mult),
+             tt(T.tri[:], T.dd[:, 0:128], T.dd[:, 256:384], A.add), ts1(cf[:, 12:13], cf[:, 19:20], -1.0, A.mult),
+             ts2(T.gp16[:], jt[:, 0:256:2], cf[:, 0:1], 0.5, A.is_equal, A.mult),
+             ts2(T.kc0[:], jt[:], cf[:, 0:1], TAG / 2, A.is_equal, A.mult)], r=["k0", "kb", "kc", "jt"], w=["k3"])
+    op("V", ts2(T.kc0[:, 0:256:32], jf[:, 0:8], cf[:, 0:1], -1.75 * TAG, A.is_equal, A.mult), r=["k3"], w=["k4"])
+    op("S", [act(T.p0[:], T.pbp[:], F.Copy), act(T.prin[:], T.pbp[:], F.Identity, scale=-2.0 ** 21),
+             act(T.pb21[:], T.pbp[:], F.Identity, scale=2.0 ** 21), act(T.ic3[:], T.ibf[:], F.Identity, scale=3 * 2.0 ** 20),
+             act(T.pri[:, 2], T.pbp[:], F.Identity, scale=-8192.0)], r=["kc"], w=["k2"])
+    op("P", [mm(T.pc[32 * j:32 * j + 32, 0:128], T.hi0[:, j:128:4], T.jk[:, 0:128]) for j in range(4)], r=["kc", "jk"], w=["h0"], banks=["pc"])
+    op("S", act(T.hacc[:], T.pc[:, 0:128], F.Copy), r=["h0"], w=["hacc"], banks=["pc"])
 
     def zslot(t):
         return T.zl[:, 128 * t:128 * t + 128]
 
-    def spread_z(t, qn, a, b, keys):
-        op(qn, [tcopy(T.zrep[:, k:4096:32], zslot(t)) if qn == "V" else act(T.zrep[:, k:4096:32], zslot(t), F.Copy) for k in range(a, b)],
-           r=["Lz%d" % t], w=keys)
+    ZR = ["zr%d" % k for k in range(8)]
 
-    def base(role, lst, key):
+    def spread_z(t, qn, a, b):
+        for k in range(a, b):
+            op(qn, [copy(qn, T.zrep[:, x:4096:32], zslot(t)) for x in range(1 + 4 * k, min(5 + 4 * k, 32))], r=["Lz%d" % t], w=[ZR[k]])
+
+    KEYS = ("pu", "pw")
+
+    def base(role):
         src, dst, col = (T.fi, T.basF, 5) if role == "F" else (T.si, T.basS, 6)
-        op("V", ts1(dst[:], src[:].indirect(lst), cf[:, col:col + 1], A.add), r=["i" + role + "a", "i" + role + "b", key, "cf"], w=["bas" + role])
+        op("V", ts1(dst[:], src[:].indirect(T.pip[:]), cf[:, col:col + 1], A.add), r=["i" + role + "a", "i" + role + "b", "pip", "kb", "kc"], w=["bas" + role])
+        for h, bk in enumerate(KEYS):
+            op("P", mm(T[bk][:, 256 + (role == "S"):384:2], dst[:], T.idf[:, 64 * h:64 * h + 64], role == "S", False),
+               r=["bas" + role, "k1"], w=["key%d" % h], banks=[bk])
 
-    def turn_base(role):
-        o, src, bk = (T.pb[:, 0:128], T.basF, "pb") if role == "F" else (T.pt[:, 128:256], T.basS, "pt")
-        op("P", mm(o, src[:], T.isc[:], True, role == "S"), r=["bas" + role, "k1"], w=["k" + role], banks=[bk])
-
-    spread_z(0, "V", 1, 22, ["zr1", "zr2"])
-    spread_z(0, "S", 22, 32, ["zr0", "zr3"])
-    op("S", act(T.trep[:], T.pd[:, 0:8], F.Identity, scale=-1.0), r=["pd"], w=["trep"], banks=["pd"])
+    spread_z(0, "V", 0, 1)
     op("V", [tcopy(T.fi[:], T.off0F[:]), tcopy(T.si[:], T.off0S[:])], r=["LF0", "LS0"], w=["iFa", "iFb", "iSa", "iSb"])
-    base("S", T.pip[:], "pip")
-    turn_base("S")
-    base("F", T.pip[:], "pip")
-    turn_base("F")
+    spread_z(0, "V", 1, 6)
+    spread_z(0, "S", 6, 8)
+    base("S")
+    base("F")
 
     E = T.top[:, PAD + 31:PAD + 4096:32]
     tops = ["top%d" % c for c in range(7)] + ["top7a", "top7b"]
-    ALL = slice(0, 8)
-
-    def wires(kind, s, gs, a, b):
-        p, sh = STAGES[s]
-        if s == 0:
-            return (T.kF, T.pu)[kind][:, 128 * kind + 16 * gs.start:128 * kind + 16 * gs.stop]
-        if sh:
-            return (T.e0, T.e1)[kind][:, SLOT[s], gs, a + 8:b + 8]
-        if p == 8:
-            return T.j16[:, gs, 0, a // 8:b // 8, kind]
-        if b - a < 2 * p:
-            return T["j%d" % (2 * p)][:, gs, a // (2 * p), a // p % 2, kind]
-        return T["j%d" % (2 * p)][:, gs, a // (2 * p):b // (2 * p), :, kind]
-
-    def exchange(s, gs, x, a, b, to):
-        p, sh = STAGES[s]
-        if to == 15:
-            out = T.dd[:, 256 * t + 16 * a + x:256 * t + 16 * a + 128:2]
-        else:
-            out = wires(x, to, gs, a, b) if STAGES[to][0] == p else T["j%d" % p][:, gs, a // p:b // p, x]
-        if x == 0:
-            return tt(out, wires(1, s, gs, a - sh, b - sh), wires(0, s, gs, a, b), A.max if sh else A.min)
-        return tt(out, wires(1, s, gs, a, b), wires(0, s, gs, a + sh, b + sh), A.min if sh else A.max)
-
-    def stage(s, h):
-        sh = 8 if STAGES[s + 1][1] == 8 else STAGES[s][1] if STAGES[s][1] > 2 else 0
-        op("V", [exchange(s, slice(4 * h, 4 * h + 4), 0, sh, 16, s + 1), exchange(s, slice(4 * h, 4 * h + 4), 1, 0, 16 - sh, s + 1)],
-           r=["w%d_%d" % (s, h), "v%d" % s, "v%dx" % s, "pads"], w=["w%d_%d" % (s + 1, h)], banks=["pu"] * (s == 0))
-
-    def skip(s, n):
-        if STAGES[s][0] == 8:
-            parts = [((0, 0, 8), (1, 8, 16))[n - 1] + (s + 2,)]
-        else:
-            parts = [(0, 4, 8, s + 2), (1, 8, 12, s + 2)] if n == 1 else [(0, 0, 4, s + 3), (1, 12, 16, s + 3)]
-        key = "v%d" % parts[0][3] + "x" * (STAGES[s][0] == 8 and n == 1)
-        op("V", [exchange(s, ALL, *x) for x in parts], r=["w%d_0" % s, "w%d_1" % s], w=[key])
-
-    def last_phase(s, half):
-        lo0, cut, hi1 = {10: (8, 16, 8), 11: (8, 16, 8), 12: (4, 10, 12), 13: (0, 9, 16), 14: (0, 8, 16)}[s]
-        parts = [(1, 0, 8), (0, lo0, cut)] if half == "lo" else [(1, 8, hi1), (0, cut, 16)]
-        r = ["w10_0", "w10_1"] if s == 10 else ["lo%d" % s, "v%d" % s] + ["hi%d" % s] * (half == "hi")
-        op("V", [exchange(s, ALL, x, a, b, s + 1) for x, a, b in parts], r=r + ["pads"], w=[half + str(s + 1)])
-
     PARTS = (("a", 0, 32), ("b", 32, 128))
+
+    def minmax(lo, hi, a, b):
+        return [tt(lo, a, b, A.min), tt(hi, a, b, A.max)]
+
+    def step(s, x, o):
+        n1, n3, n4, n6, n7, nb, n8, n9, na = T.n1, T.n3, T.n4, T.n6, T.n7, T.nb, T.n8, T.n9, T.na
+        gs, H, a, b = slice(4 * x, 4 * x + 4), x, o + 64 * x, o + 64 * x + 64
+        fns = [
+            lambda: [ts1(T.km[:, gs], T.ki[:, gs], (1 << 21) - 1, A.bitwise_and)],
+            lambda: minmax(n1[:, gs, :, :, :, 0], n1[:, gs, :, :, :, 1], T.km[:, gs, :, :, 0], T.km[:, gs, :, :, 1]),
+            lambda: minmax(n3[:, gs, :, :, :, 1:6:4], n3[:, gs, :, :, :, 0:5:4], n1[:, gs, :, :, 0], n1[:, gs, :, :, 1]),
+            lambda: minmax(n3[:, gs, :, :, :, 3], n3[:, gs, :, :, :, 2], n3[:, gs, :, :, :, 5], n3[:, gs, :, :, :, 0]),
+            lambda: minmax(n4[:, gs, :, :, 0], n4[:, gs, :, :, 1], n3[:, gs, :, :, 0, 1:5], n3[:, gs, :, :, 1, 1:5]),
+            lambda: minmax(n6[:, :, H, 4:6] if H else n6[:, :, H, 1:6:4], n6[:, :, H, 0:2] if H else n6[:, :, H, 0:5:4], n4[:, :, H, 0], n4[:, :, H, 1]),
+            lambda: minmax(n6[:, :, H, 2 + H], n6[:, :, H, 3 - H], n6[:, :, H, 5], n6[:, :, H, 0]),
+            lambda: [tt(n7[:, gs], n6[:, gs, 0, 1:5], n6[:, gs, 1, 1:5], A.min)],
+            lambda: [ts1(nb[:, gs], n7[:, gs], (1 << 19) - 1, A.bitwise_and)],
+            lambda: minmax(n8[:, gs, 0], n8[:, gs, 1], nb[:, gs, 0], nb[:, gs, 1]),
+            lambda: minmax(n9[:, gs, :, 0], n9[:, gs, :, 1], n8[:, gs, :, 0], n8[:, gs, :, 1]),
+            lambda: minmax(na[:, gs, :, :, 0], na[:, gs, :, :, 1], n9[:, gs, :, :, 0:4:2], n9[:, gs, :, :, 1:4:2]),
+            lambda: minmax(T.dd[:, a:b:2], T.dd[:, a + 1:b:2], na[:, gs, :, 0], na[:, gs, :, 1]),
+        ][s]()
+        r = ["o4_0", "o4_1"] if s == 5 else ["o5_0", "o5_1", "o6_0", "o6_1"] if s == 7 else ["o%d_%d" % (s - 1, x)]
+        op("V", fns, r=r, w=["o%d_%d" % (s, x)])
 
     def minus_threshold():
         op("P", mm(T.pg[:, 0:256], T.onen[:], T.tm[:], True, False), r=["k3", "ones"], w=["gain" + k for k in tops], banks=["pg"])
+        op("P", mm(T.ph[0:8, 384:512], T.tm[:, 0:256:32], T.onen[:], True, False), r=["k3"], w=["s0"], banks=["ph"])
 
     minus_threshold()
 
-    def order(r, rb, c, key, name):
-        op("V", ts2(r[:], jf[:, 0:128], c, 2.0 ** 18, A.is_equal, A.mult), r=[key, "jf"], w=[name + "f"])
-        if rb is None:
-            lastw[name] = lastw[name + "f"]
-        else:
-            op("S", act(rb[:], r[:], F.Identity, scale=16.0), r=[name + "f"], w=[name])
+    def order(r, rb, c, key, name, row=T.jb, scale=2.0 ** 21):
+        op("V", ts2(rb[:], row[:], c, scale, A.is_equal, A.mult), r=[key, "kb", "jp"], w=[name + "b"])
+        op("S", act(r[:], rb[:], F.Sign), r=[name + "b"], w=[name])
 
     def fallback(ps, bk, s2, ks, r, rb, kr, old, ko, sg, src, kd, name):
         op("S", act(sg, old, F.Sign), r=[ko], w=["sg" + name])
         op("P", [mm(ps, s2, rb[:], True, False), mm(ps, T.ic3[:], sg, False, False)], r=[ks, kr, "sg" + name, "k2"], w=[name + "p"], banks=[bk])
-        op("P", mm(ps, src, r[:], False, True), r=[kd, kr], w=[name], banks=[bk])
+        op("P", mm(ps, src, r[:], False, True), r=kd + [kr], w=[name], banks=[bk])
+
+    def upper_out(t):
+        o0, sl = 256 * t, slice(128 * t, 128 * t + 128)
+        rot, rotb, dhi = (T.rh[:], T.rhb[:], T.dd[:, 384:512]) if t else (T.idf[:], T.pri[:, 3], T.dd[:, 128:256])
+        op("P", [mm(T.pd[:, 0:128], T.pri[:, t], T.s1[:, sl], True, False), mm(T.pd[:, 0:128], T.idf[:], dhi, False, True),
+                 mm(T.pd[:, 128:256], rotb, T.s2[:, sl], True, False), mm(T.pd[:, 128:256], rot, dhi, False, True)],
+           r=["up", "k1", "rh", "rhb"], w=["phi"], banks=["pd"])
+        op("S", act(T.oh[:, o0:o0 + 256], T.pd[:, 0:256], F.Copy), r=["phi"], w=["oh"], banks=["pd"])
+        send([(q - t - 1, T.oh[:, o0:o0 + 128], T.lH1[:, sl], "Ha%d" % t)], ["oh"])
+        send([(q + 1, T.oh[:, o0 + 128:o0 + 256], T.lH2[:, sl], "Hb%d" % t)], ["oh"])
+
+    def keep(t, k):
+        if k == 0:
+            op("V", tt(T.jk[:], T.lH1[:, 128 * t:128 * t + 128], T.lH2[:, 128 * t:128 * t + 128], A.max), r=["LHa%d" % t, "LHb%d" % t], w=["jk"])
+        else:
+            op("V", tt(T.hacc[:], T.jk[:], T.hacc[:], A.max), r=["jk"], w=["hacc"])
 
     for t in range(RO):
         d = t + 1
         last = t == RO - 1
         offs = {"F": T.off0F if t == 0 else T.offF, "S": T.off0S if t == 0 else T.offS}
+        psS = {"a": (T.pu[:, 0:32], "pu"), "b": (T.pw[:, 128:224], "pw")}
+        psF = {"a": (T.pt[:, 256:288], "pt"), "b": (T.pb[:, 128:224], "pb")}
 
-        def merge(step, part):
+        def merge(role, x):
+            kind, part = x
             a, b = (0, 32) if part == "a" else (32, 128)
-            if step == "m":
-                ps, bk = (T.ph[:, 128:160], "ph") if part == "a" else (T.pb[:, 128:224], "pb")
-                op("V", tt(T.mF[:, a:b], ps, T.cF[:, a:b], A.max), r=["AF" + part, "cF"], w=["mF" + part], banks=[bk])
-            elif step == "a":
-                op("V", ts1(T.fi[:, a:b], T.mF[:, a:b], 8191, A.bitwise_and), r=["mF" + part], w=["iF" + part])
+            (ps, bk), m, c, i, o = (psF[part], T.mF, T.cF, T.fi, T.offF) if role == "F" else (psS[part], T.mS, T.cS, T.si, T.offS)
+            if kind == "m":
+                op("V", tt(m[:, a:b], ps, c[:, a:b], A.max), r=["A" + role + part, "c" + role], w=["m" + role + part], banks=[bk])
+            elif kind == "a":
+                op("V", ts1(i[:, a:b], m[:, a:b], 8191, A.bitwise_and), r=["m" + role + part], w=["i" + role + part])
             else:
-                op("V", tcopy(T.offF[:, a:b], T.fi[:, a:b]), r=["iF" + part], w=["offF" + part])
+                op("V", tcopy(o[:, a:b], i[:, a:b]), r=["i" + role + part], w=["off" + role + part])
 
         def gather(qn, x):
             role, c = x[0], 2 * int(x[1]) + (x[-1] == "b")
             e = c + 1 if x[-1] in "ab" else 2 * int(x[-1]) + 2
-            o = T.xg[:, 256 * c + (role == "S"):256 * e:2]
-            i = T.X[:].indirect(offs[role][:, 8 * c:8 * e])
-            op(qn, tcopy(o, i) if qn == "V" else act(o, i, F.Copy),
+            op(qn, copy(qn, T.xg[:, 256 * c + (role == "S"):256 * e:2], T.X[:].indirect(offs[role][:, 8 * c:8 * e])),
                r=["X", "X0"] + (["L%s0" % role] if t == 0 else ["off" + role + "ab"[k > 3] for k in range(c, e)]),
                w=["x%s%d%s" % (role, k // 2, "ab"[k % 2]) for k in range(c, e)])
 
@@ -379,57 +398,51 @@ def rank_program(g, core, T, topo):
             op("V", tt(T.zrep[:, 512 * c:512 * e:32], T.xg[:, 512 * c:512 * e:32], T.zl[:, 128 * t + 16 * c:128 * t + 16 * e], A.min),
                r=["xF%d%s" % (k, x) for k in range(c, e) for x in "ab"] + ["Lz%d" % t], w=["zf%d" % k for k in range(c, e)])
             if e == 8:
-                op("P", [mm(T.ph[32 * j:32 * j + 32, 272:280], T.zrep[:, 32 * j:4096:128], T.gp[:]) for j in range(4)],
-                   r=["zf%d" % k for k in range(8)] + ["k1"], w=["s0"], banks=["ph"])
+                op("P", [mm(T.ph[0:8, 384 + 32 * j:416 + 32 * j], T.gp[:], T.zrep[:, 32 * j:4096:128], False, j == 3) for j in range(4)],
+                   r=["zf%d" % k for k in range(8)] + ["k3"], w=["s0"], banks=["ph"])
+                op("S", act(T.c0[0:8, :], T.ph[0:8, 384:512], F.Sign, bias=0.5), r=["s0"], w=["c0"], banks=["ph"])
 
         def scan(c, part=""):
-            a, b = {"": (0, 512), "a": (0, 256), "b": (256, 512)}[part]
-            a, b = a + 512 * c, b + 512 * c
+            a, b = {"": (0, 16), "a": (0, 8), "b": (8, 16)}[part]
+            a, b = a + 16 * c, b + 16 * c
             key = "top%d%s" % (c, part)
-            op("V", lambda: V.tensor_tensor_scan(T.top[:, PAD + a:PAD + b], T.xg[:, a:b], T.zrep[:, a:b], 0.0, A.max, A.min),
-               r=["x%s%d%s" % (x, c, y) for x in "FS" for y in part or "ab"] + ["zf%d" % c, "zr0", "zr1", "zr2", "zr3"], w=[key])
+            op("V", lambda: V.tensor_tensor_scan(T.top[:, PAD + 32 * a:PAD + 32 * b], T.xg[:, 32 * a:32 * b], T.zrep[:, 32 * a:32 * b], 0.0, A.max, A.min),
+               r=["x%s%d%s" % (x, c, y) for x in "FS" for y in part or "ab"] + ZR + ["zf%d" % c], w=[key])
             fns = []
-            for ib in range(a // 128, b // 128):
+            for ib in range(a // 4, b // 4):
                 c0 = PAD + 128 * ib
                 fns += [mm(T.pg[:, ib:256:32], T.top[:, c0:c0 + 128], T.gp[:], False, False),
                         mm(T.pg[:, ib:256:32], T.top[:, c0 - 1:c0 + 127], T.gn[:], False, ib == 31)]
             k = tops.index(key)
-            op("P", fns, r=[key, tops[k - 1] if k else "pad", "k1"], w=["gain" + key], banks=["pg"])
+            op("P", fns, r=[key, tops[k - 1] if k else "pad", "kb"], w=["gain" + key], banks=["pg"])
 
         seqS, seqV = SEQ0 if t == 0 else SEQ
         for x in seqV.split():
             if x[0] in "mao":
-                merge(x[0], x[1])
+                merge("F", x)
             elif x == "A":
                 for y in seqS.split():
                     gather("S", y)
-            elif x == "b":
-                base("S", T.pip[:], "pip")
-                turn_base("S")
+            elif x in "bB":
+                base("SF"[x == "B"])
             elif x == "M":
                 op("V", tt(T.cF[:], T.pc[:, 128:256], T.lA1[:, 128 * t - 128:128 * t], A.max), r=["BF", "BFp", "LAa%d" % t], w=["cF"], banks=["pc"])
-            elif x == "B":
-                base("F", T.pip[:], "pip")
-                turn_base("F")
+            elif x == "H":
+                upper_out(t - 1)
             elif x[0] == "f":
                 fix(int(x[1]), int(x[-1]) + 1)
             elif x[0] == "s":
                 scan(int(x[1]))
             else:
                 gather("V", x)
-        if t == 0:
-            send([(q + RO, T.hi0[:], T.lH0[:], "H0")], ["hi0", "top0"])
         scan(7, "a")
         scan(7, "b")
-        op("V", tt(T.u0[:, 0:128:16], T.ph[:, 272:280], T.trep[:], A.is_lt), r=["s0", "trep"], w=["u0"], banks=["ph"])
-        op("P", mm(T.pb[:, 0:128], T.ibf[:], T.u0[:], False, True), r=["u0"], w=["kF"], banks=["pb"])
         op("P", mm(T.ph[:, 256:264], E, T.wgr[:]), r=tops + ["k3"], w=["v2"], banks=["ph"])
-
-        if last:
-            op("V", tt(T.junk[:, 128:256], T.lH2[:, 128:256].indirect(T.ulF[:]), T.lH1[:, 128:256], A.max), r=["LHa1", "LHb1", "LuF", "tot"], w=["jk1"])
+        for h, bk in enumerate(KEYS):
+            op("P", mm(T[bk][:, 256:384], T.c0[0:8, :], T.kc0[0:8, 128 * h:128 * h + 128], False, False), r=["c0", "k4"], w=["key%d" % h], banks=[bk])
 
         op("P", [mm(T.pc[:, 0:128], T.ibf[:], zslot(t), True, False), mm(T.pc[:, 0:128], T.ibf[:], E, False, True)],
-           r=tops + ["Lz%d" % t, "k1"], w=["ze"], banks=["pc"])
+           r=tops + ["Lz%d" % t, "kb"], w=["ze"], banks=["pc"])
         nz = T.nzf[:] if last else T.nzb[:, 128 * t:128 * t + 128]
         op("S", act(nz, T.pc[:, 0:128], F.Abs, bias=255.0, scale=-1.0), r=["ze"], w=["nz%d" % t], banks=["pc"])
         if last:
@@ -437,188 +450,154 @@ def rank_program(g, core, T, topo):
         else:
             send([(q + 1, nz, zslot(t + 1), "z%d" % (t + 1))], ["nz%d" % t])
 
-        fill = [
-            lambda: op("V", tcopy(T.ha[:], T.ph[:, 256:264]), r=["v2"], w=["ha"], banks=["ph"]),
-            lambda: op("V", ts1(T.hb[:], T.ha[:], 4095, A.bitwise_and), r=["ha"], w=["hb"]),
-            lambda: op("V", tt(T.ha[:], T.hb[:], T.hb[:], A.mult), r=["hb"], w=["ha"]),
-            lambda: op("V", ts2(T.hc[:], T.ha[:], 4, 8191, A.arith_shift_right, A.bitwise_and), r=["ha"], w=["hc"]),
-            lambda: op("V", tt(T.hpad[:, 15:128:16], T.hc[:], T.hb[:], A.add), r=["hc", "hb"], w=["hpad"]),
-        ]
-
-        for h in (0, 1):
-            op("V", ts2(T.u3[:, 128 * h:128 * h + 128], T.pg[:, 128 * h:128 * h + 128], 0.0, cf[:, 11:12], A.is_lt, A.mult),
-               r=["gain" + k for k in tops] + ["k1"], w=["u3%d" % h], banks=["pg"])
-        fill.pop(0)()
-        op("P", [mm(T.ph[:, 0:128], T.zer[:], T.ibf[:], True, False)]
-           + [mm(T.ph[:, j:128:4], T.imk[:], T.basF[:, 32 * j:32 * j + 32], False, False) for j in range(4)],
-           r=["basF", "k1", "ab0z"], w=["ht0"], banks=["ph"])
-        if last:
-            op("V", tt(T.fin[:, 0:128], T.junk[:, 128:256], T.hacc[:], A.max), r=["jk1", "hacc"], w=["fin0"])
-        for h in (0, 1):
-            op("V", lambda: V.transpose(T.u2[:, 128 * h:128 * h + 128], T.u3[:, 128 * h:128 * h + 128]), r=["u3%d" % h], w=["u2%d" % h])
-        fill.pop(0)()
-        if last:
-            op("V", ts1(T.fin2[:, 0:128], T.fin[:, 0:128], 8191, A.bitwise_and), r=["fin0"], w=["msk0"])
-        for h in (0, 1):
-            op("V", [tt(T.kF[:, 64 * h:64 * h + 64], T.u2[:, 128 * h:128 * h + 128:2], T.pb[:, 64 * h:64 * h + 64], A.add),
-                     tt(T.pu[:, 128 + 64 * h:192 + 64 * h], T.u2[:, 128 * h + 1:128 * h + 128:2], T.pt[:, 128 + 64 * h:192 + 64 * h], A.add)],
-               r=["u2%d" % h, "kF", "kS"], w=["w0_%d" % h], banks=["pb", "pt", "pu"])
-        fill.pop(0)()
-
-        uk = ["u20", "u21", "u0"]
-        won = [
-            lambda: op("V", lambda: V.tensor_tensor_scan(T.alt[:], T.sgn[:], T.u2[:], 0.0, A.mult, A.add), r=uk + ["k4"], w=["alt"]),
-            lambda: op("V", tt(T.ab0[:, 0:128:16], T.alt[:, 31:256:32], T.u0[:, 0:128:16], A.subtract), r=["alt", "u0"], w=["ab0"]),
-            lambda: op("V", lambda: V.tensor_tensor_scan(T.ab[:], T.hold[:], T.ab0[:], 0.0, A.mult, A.add), r=["ab0", "k4"], w=["ab"]),
-            lambda: op("V", [ts2(T.s1[:], T.ab[:], 0.0, 0.5, A.is_lt, A.subtract), ts2(T.s2[:, 128 * t:128 * t + 128], T.ab[:], 0.0, 0.5, A.is_gt, A.subtract)],
-                       r=["ab"], w=["s1", "s2"]),
-        ]
-        won.pop(0)()
-        if not last:
-            op("P", [mm(T.pd[:, 0:256], T.ones[:], T.u2[:], True, False), mm(T.pd[:, 0:128], T.ones[:], T.u0[:], False, True)],
-               r=uk + ["ones"], w=["pd"], banks=["pd"])
-            op("S", act(T.junk[:], T.pd[:, 0:256], F.Identity, accum_out=T.tot[:, t:t + 1]), r=["pd"], w=["tot"], banks=["pd"])
-            op("P", [mm(T.pc[:, 264:272], T.ww[:, 15 - c:143 - c], T.top[:, PAD + 32 * c + 31:PAD + 4096:512], c == 0, c == 15)
-                     for c in range(16)], r=tops + ["k3"], w=["vd"], banks=["pc"])
-
         l0, o0 = 16 * t, 256 * t
         sl = slice(128 * t, 128 * t + 128)
         col, tot = T.col[:, 4 * t:4 * t + 4], T.tot[:, t:t + 1]
-        for s in range(10):
-            stage(s, 0)
-            stage(s, 1)
-            if STAGES[s + 1][1] == 8:
-                skip(s, 1)
-                if s == 1:
-                    skip(s, 2)
-            elif STAGES[s][1] == 8 and s > 2:
-                skip(s - 1, 2)
-            if s < 2:
-                fill.pop(0)()
-            if s < 3:
-                won.pop(0)()
-            if s == 0 and last:
-                op("V", tcopy(T.hacc[:], T.fin2[:, 0:128]), r=["msk0"], w=["hacc"])
-                op("P", mm(T.pw[:, 0:128], T.idf[:], T.hacc[:], True, False), r=["hacc", "k1"], w=["pw0"], banks=["pw"])
-            if s == 1:
-                op("P", mm(T.ph[:, 0:128], T.hpad[:], T.idf[:], False, False), r=["hpad", "k1"], w=["ht1"], banks=["ph"])
-            if s == 2:
-                send([(q + 1 if last else q + d + 2, T.s2[:, sl], T.lT[:, sl], "T%d" % d)], ["s2"])
-                op("P", mm(T.ph[:, 0:128], T.s1[:], T.prin[:], False, True), r=["s1", "k2"], w=["ht"], banks=["ph"])
-                if last:
-                    op("P", mm(T.pw[:, 0:128], T.s1[:], T.prin[:], False, True), r=["s1", "k2"], w=["pw"], banks=["pw"])
-                a3 = T.o1[:, o0:o0 + 128]
-                op("S", act(a3, T.ph[:, 0:128], F.Identity, bias=cf[:, 12:13]), r=["ht0", "ht1", "ht", "k1"], w=["a3"], banks=["ph"])
-                if last:
-                    op("S", act(T.o1[:, o0 + 128:o0 + 256], T.pw[:, 0:128], F.Copy), r=["pw0", "pw"], w=["a3h"], banks=["pw"])
-                    send([(q - d, T.o1[:, o0:o0 + 256], T.lAE[:], "AE")], ["a3", "a3h"])
-                else:
-                    send([(q - d - 1, a3, T.lA2[:, sl], "Ab%d" % d), (q + 1, a3, T.lA1[:, sl], "Aa%d" % d)], ["a3"])
-                    op("P", mm(T.pw[:, 0:128], T.s2[:, sl], T.pri[:, 256 * t + 128:256 * t + 256]), r=["s2", "k2"], w=["pw"], banks=["pw"])
-                    op("S", act(T.dl[:], T.pw[:, 0:128], F.Copy), r=["pw"], w=["dl"], banks=["pw"])
-                    op("P", mm(T.pd[:, 256:384], T.s1[:], T.pri[:, 256 * t:256 * t + 128], True, False), r=["s1", "k2"], w=["1hi"], banks=["pd"])
-                    spread_z(d, "S", 1, 21, ["zr0"])
-            if s == 8 and t:
-                order(*((T.r1, T.r2b, T.lc[:, 6:7], "LcE", "r4") if last else (T.r3, T.r3b, T.lc[:, 2:3], "LcF", "r3")))
-            if last:
-                continue
-            if s == 5:
-                op("V", [ts2(T.tl[:, 0:8], T.jl[:, 0:8], tot, 32768.0, A.subtract, A.add), ts1(T.tl[:, 8:16], T.jl[:, 0:8], tot, A.add)],
-                   r=["tot", "k5"], w=["tla"])
-            if s == 9:
-                op("V", [ts1(T.tl[:, 16:17], T.jl[:, 8:9], tot, A.add), ts1(T.tl[:, 18:20], T.jl[:, 8:10], tot, A.subtract),
-                         ts2(T.tl[:, 17:18], T.jl[:, 8:9], tot, T.tot[:, 0:1], A.add, A.subtract) if t else ts1(T.tl[:, 17:18], T.jl[:, 8:9], tot, A.add)],
-                   r=["tot", "kc"], w=["tlb"])
+        a3, dlo, dhi = T.o1[:, sl], T.dd[:, o0:o0 + 128], T.dd[:, o0 + 128:o0 + 256]
 
-        dlo, dhi = T.dd[:, o0:o0 + 128], T.dd[:, o0 + 128:o0 + 256]
-        last_phase(10, "lo")
-        skip(10, 1)
-        if not last:
-            op("V", ts1(T.tl2[:], T.tl[:], 127, A.bitwise_and), r=["tla", "tlb"], w=["tl2"])
-        last_phase(11, "lo")
-        skip(10, 2)
+        for h, bk in enumerate(KEYS):
+            hs = slice(128 * h, 128 * h + 128)
+            op("V", ts2(T.u3[:, hs], T.pg[:, hs], 0.0, cf[:, 21:22], A.is_lt, A.mult), r=["gain" + k for k in tops], w=["u3%d" % h], banks=["pg"])
+            op("P", [mm(T[bk][32 * j:32 * j + 32, 256 + 32 * x:288 + 32 * x], T.u3[:, 128 * h + 32 * x:128 * h + 32 * x + 32], T.tri[:, 32 * j:32 * j + 32], False, x == 3)
+                     for x in range(4) for j in range(4)], r=["u3%d" % h, "k3"], w=["key%d" % h], banks=[bk])
+        op("P", [mm(T.pd[:, 384:512], T.c0[0:8, :], T.gp16[0:8, :], True, False)]
+           + [mm(T.pd[32 * j:32 * j + 32, 384 + 16 * x:400 + 16 * x], T.u3[:, 32 * x:32 * x + 32], T.sgj[:, 16 * j:16 * j + 16], False, x == 7)
+              for x in range(8) for j in range(4)]
+           + [mm(T.pd[:, 0:256], T.ones[:], T.u3[:], True, False), mm(T.pd[:, 0:128], T.mh[0:8, :], T.c0[0:8, :], False, True)] * (not last),
+           r=["u30", "u31", "c0", "k3", "ones"], w=["ab"], banks=["pd"])
+        op("S", [act(T.s1[:, sl], T.pd[:, 384:512], F.Sign, scale=-1.0), act(T.s2[:, sl], T.pd[:, 384:512], F.Sign, bias=-1.0)],
+           r=["ab"], w=["s1", "s2"], banks=["pd"])
+        send([(q + 1 if last else q + d + 2, T.s2[:, sl], T.lT[:, sl], "T%d" % d)], ["s2"])
         if last:
-            last_phase(12, "lo")
-            last_phase(12, "hi")
-            last_phase(13, "lo")
-            last_phase(13, "hi")
-            last_phase(14, "lo")
-            last_phase(14, "hi")
-            send([(q + 1, T.dd[:, o0:o0 + 256], T.lE2[:], "Eb")], ["lo15", "hi15"])
-            send([(q - d, T.dd[:, o0:o0 + 256], T.lE1[:], "Ea")], ["lo15", "hi15"])
-            break
-        op("V", [tcopy(T.lst[:, l0:l0 + 16], T.tl2[:, 0:16]), tcopy(col, T.tl2[:, 16:20])], r=["tl2"], w=["lst%d" % t])
-        last_phase(12, "lo")
-        op("V", tcopy(T.pa_[:], T.pc[:, 264:272]), r=["vd"], w=["pa_"], banks=["pc"])
-        last_phase(12, "hi")
-        last_phase(13, "lo")
-        op("V", ts1(T.pb_[:], T.pa_[:], 63, A.bitwise_and), r=["pa_"], w=["pb_"])
-        order(T.r2, T.r2b, T.col[:, 4 * t + 1:4 * t + 2], "lst%d" % t, "r2")
-        last_phase(14, "lo")
-        if t:
-            order(T.r1, None, T.col[:, 4 * t:4 * t + 1], "lst%d" % t, "r1")
-
-        send([(q - d - 1, dlo, T.lS[:, sl], "S%d" % d)], ["lo15"])
-        send([(q + d + 2, dlo, T.lF2[:, sl], "Fb%d" % d)], ["lo15"])
-        send([(q + 1, dlo, T.lF1[:, sl], "Fa%d" % d)], ["lo15"])
-        if t == 0:
-            send([(q + 4, T.lst[:, 8:16], T.ulF[:], "uF"), (q + 4, col, T.lc[:, 0:4], "cF")], ["lst0"])
+            send([(q - d, T.s1[:, sl], T.lT[:, 384:512], "TL")], ["s1"])
         else:
-            send([(q + 1, col, T.lc[:, 4:8], "cE")], ["lst1"])
+            op("S", act(T.junk[:], T.pd[:, 0:256], F.Identity, accum_out=tot), r=["ab"], w=["tot"], banks=["pd"])
+            op("S", [act(T.tot[:, 4 + t:5 + t], tot, F.Identity, scale=-1.0)] + [act(T.tot[:, 6:7], tot, F.Identity, bias=T.tot[:, 4:5])] * t,
+               r=["tot"], w=["ntot"])
+            op("S", [act(T.tlf[:, a:b], T.jq[:, a:b], F.Identity, bias=T.tot[:, c:c + 1])
+                     for a, b, c in ((0, 8, 4 + t), (8, 17, t), (17, 18, 6 * t), (18, 20, 4 + t))], r=["ntot", "kc"], w=["tlf"])
+
+        def after_v():
+            op("V", tcopy(T.ha[:], T.ph[:, 256:264]), r=["v2"], w=["ha"], banks=["ph"])
+            op("P", [mm(T.pb[:, j:128:4], T.imk[:], T.basF[:, 32 * j:32 * j + 32], j == 0, False) for j in range(4)], r=["basF", "k1"], w=["ht0"], banks=["pb"])
+            op("P", mm(T.pb[:, 0:128], T.s1[:, sl], T.prin[:], False, False), r=["s1", "k2"], w=["ht0"], banks=["pb"])
+
+        def old_list():
+            op("V", tt(T.hpad[:, 15:128:16], T.hc[:], T.hb[:], A.add), r=["hc", "hb"], w=["hpad"])
+            op("P", mm(T.pb[:, 0:128], T.hpad[:], T.idf[:], False, True), r=["hpad", "k1"], w=["ht"], banks=["pb"])
+            op("S", act(a3, T.pb[:, 0:128], F.Identity, bias=cf[:, 12:13]), r=["ht0", "ht", "k3"], w=["a3"], banks=["pb"])
+            if last:
+                send([(q - d, a3, T.lAE[:], "AE")], ["a3"])
+            else:
+                send([(q - d - 1, a3, T.lA2[:, sl], "Ab%d" % d), (q + 1, a3, T.lA1[:, sl], "Aa%d" % d)], ["a3"])
+                op("P", [mm(T.ph[:, 264:272], T.ww[:, 15 - c:143 - c], T.top[:, PAD + 32 * c + 31:PAD + 4096:512], c == 0, c == 15)
+                         for c in range(16)], r=tops + ["k3"], w=["vd"], banks=["ph"])
+                spread_z(d, "S", 0, ZS)
+                spread_z(d, "G", ZS, ZS + ZG)
+
+        def far_order():
+            if t:
+                order(*((T.r1, T.r1b, T.lc[:, 6:7], "LcE", "r4") if last else (T.r3, T.r3b, T.lc[:, 2:3], "LcF", "r3")))
+
+        def upper():
+            op("V", tt(dhi, T.n6[:, :, 0, 1:5], T.n6[:, :, 1, 1:5], A.max), r=["o5_0", "o5_1", "o6_0", "o6_1"], w=["up"])
+            if last:
+                send([(q + 1, dhi, T.lE2[:, 128:256], "Ub")], ["up"])
+                send([(q - d, dhi, T.lE1[:, 128:256], "Ua")], ["up"])
+
+        def sink():
+            op("S", act(T.cF[:], T.lT[:, 384:512], F.Identity, scale=-3.5 * UP, bias=-2.5 * UP), r=["LTL"], w=["cF"])
+            op("V", tt(T.cS[:], T.cF[:], T.hacc[:], A.add), r=["cF", "hacc"], w=["cS"])
+
+        side = {
+            "ha": after_v,
+            "hb": lambda: op("V", ts1(T.hb[:], T.ha[:], 4095, A.bitwise_and), r=["ha"], w=["hb"]),
+            "hh": lambda: op("V", tt(T.ha[:], T.hb[:], T.hb[:], A.mult), r=["hb"], w=["ha"]),
+            "hc": lambda: op("V", ts2(T.hc[:], T.ha[:], 4, 8191, A.arith_shift_right, A.bitwise_and), r=["ha"], w=["hc"]),
+            "hp": old_list, "far": far_order, "up": upper, "j0": lambda: t and keep(t - 1, 0), "j1": lambda: t and keep(t - 1, 1), "j2": sink,
+            "tl": lambda: op("V", tcopy(T.tl[:], T.tlf[:]), r=["tlf"], w=["tl"]),
+            "tm": lambda: op("V", ts1(T.tl2[:], T.tl[:], 127, A.bitwise_and), r=["tl"], w=["tl2"]),
+            "tn": lambda: op("V", [tcopy(T.lst[:, l0:l0 + 16], T.tl2[:, 0:16]), tcopy(col, T.tl2[:, 16:20])], r=["tl2"], w=["lst%d" % t]),
+            "r2": lambda: order(T.r2, T.r2b, T.col[:, 4 * t + 1:4 * t + 2], "lst%d" % t, "r2"),
+            "r1": lambda: t and order(T.r1, T.r1b, T.col[:, 4 * t:4 * t + 1], "lst%d" % t, "r1"),
+            "rh": lambda: t and order(T.rh, T.rhb, T.lc[:, 6:7] if last else T.col[:, 2:3], "LcE" if last else "lst0", "rh", T.jp, (2 * t + 1) * UP),
+            "pa": lambda: op("V", tcopy(T.pa_[:], T.ph[:, 264:272]), r=["vd"], w=["pa_"], banks=["ph"]),
+            "pb": lambda: op("V", ts1(T.pb_[:], T.pa_[:], 63, A.bitwise_and), r=["pa_"], w=["pb_"]),
+            "pc": lambda: op("V", tt(T.pc_[:], T.pb_[:], T.plb[:], A.add), r=["pb_", "kc"], w=["pc_"]),
+            "pl": lambda: op("V", tcopy(T.pl[:], T.pc_[:]), r=["pc_"], w=["pl"]),
+            "X": lambda: op("V", tcopy(T.X[:].indirect(T.pl[:]), E), r=["pl"] + tops, w=["X"]),
+            "cS": lambda: op("V", tt(T.cS[:], T.pt[:, 0:128], T.hx[:], A.max), r=["BS", "BSp", "hx"], w=["cS"], banks=["pt"]),
+        }
+        for x in (LAST if last else NET).split():
+            if x in side:
+                side[x]()
+            elif x[0] == "k":
+                h = int(x[1])
+                op("V", tcopy(T.ki[:, 4 * h:4 * h + 4], T[KEYS[h]][:, 256:384]), r=["key%d" % h], w=["o-1_%d" % h], banks=[KEYS[h]])
+            else:
+                step(int(x[0], 16), int(x[1]), o0)
+        lo = ["o12_0", "o12_1"]
+        if last:
+            send([(q + 1, dlo, T.lE2[:, 0:128], "Eb")], lo)
+            send([(q - d, dlo, T.lE1[:, 0:128], "Ea")], lo)
+            break
+
+        send([(q - d - 1, dlo, T.lS[:, sl], "S%d" % d)], lo)
+        send([(q + d + 2, dlo, T.lF2[:, sl], "Fb%d" % d)], lo)
+        send([(q + 1, dlo, T.lF1[:, sl], "Fa%d" % d)], lo)
+        send([(q + 1, col, T.lc[:, 4:8], "cE") if t else (q + 4, col, T.lc[:, 0:4], "cF")], ["lst%d" % t])
 
         minus_threshold()
         op("S", act(T.hx[:], T.lA2[:, sl].indirect(T.lst[:, l0:l0 + 8]), F.Copy), r=["LAb%d" % d, "lst%d" % t], w=["hx"])
-        fallback(T.pt[:, 0:128], "pt", T.s2[:, sl], "s2", T.r2, T.r2b, "r2", T.hx[:], "hx", T.sgS[:], dlo, "lo15", "BS")
-        op("V", tt(T.pc_[:], T.pb_[:], T.plb[:], A.add), r=["pb_", "k2"], w=["pc_"])
-        last_phase(13, "hi")
-        spread_z(d, "V", 21, 24, ["zr1"])
-        op("V", tcopy(T.pl[:], T.pc_[:]), r=["pc_"], w=["pl"])
-        if t:
-            op("V", tt(T.junk[:, 0:128], T.lH2[:, 0:128], T.lH1[:, 0:128], A.max), r=["LHa0", "LHb0", "tot"], w=["jk0"])
-        last_phase(14, "hi")
-        op("P", mm(T.pd[:, 256:384], dhi, T.p0[:], False, True), r=["hi15", "k2"], w=["1hi"], banks=["pd"])
-        spread_z(d, "V", 24, 27, ["zr2"])
-        op("V", tcopy(T.X[:].indirect(T.pl[:]), E), r=["pl"] + tops, w=["X"])
-        op("V", tt(T.cS[:], T.pt[:, 0:128], T.hx[:], A.max), r=["BS", "BSp", "hx"], w=["cS"], banks=["pt"])
-        if t:
-            op("V", tt(T.hacc[:], T.junk[:, 0:128], T.lH0[:], A.max), r=["jk0", "LH0"], w=["hacc"])
-        p1hi, p2hi = T.o1[:, o0 + 128:o0 + 256], T.o2[:, sl]
-        op("V", [tcopy(p1hi, T.pd[:, 256:384]), tt(p2hi, T.pd[:, 256:384], T.dl[:], A.add)], r=["1hi", "dl"], w=["phi"], banks=["pd"])
-        send([(q - d + RO, p1hi, T.lH1[:, sl], "Ha%d" % t), (q + 1 + RO, p2hi, T.lH2[:, sl], "Hb%d" % t)], ["phi"])
-
-        r1, k1 = (T.r1, "r1") if t else (T.r2, "r2")
-        for x, ps, bk in ((PARTS[0], T.pu[:, 0:32], "pu"), (PARTS[1], T.pw[:, 128:224], "pw")):
-            op("P", mm(ps, T.lS[:, sl], r1[:, x[1]:x[2]]), r=["LS%d" % d, k1], w=["AS" + x[0]], banks=[bk])
-        rF, rFb, kF = (T.r3, T.r3b, "r3") if t else (T.p0, T.pb22, "k2")
-        fallback(T.pc[:, 128:256], "pc", T.lT[:, sl], "LT%d" % d, rF, rFb, kF, T.lA1[:, sl], "LAa%d" % d, T.sgF[:], T.lF2[:, sl], "LFb%d" % d, "BF")
-        for x, ps, bk in ((PARTS[0], T.ph[:, 128:160], "ph"), (PARTS[1], T.pb[:, 128:224], "pb")):
-            op("P", mm(ps, T.lF1[:, sl], T.p0[:, x[1]:x[2]]), r=["LFa%d" % d, "k2"], w=["AF" + x[0]], banks=[bk])
-        spread_z(d, "S", 27, 32, ["zr3"])
-        for (x, a, b), ps, bk in ((PARTS[0], T.pu[:, 0:32], "pu"), (PARTS[1], T.pw[:, 128:224], "pw")):
-            op("V", tt(T.mS[:, a:b], ps, T.cS[:, a:b], A.max), r=["AS" + x, "cS"], w=["mS" + x], banks=[bk])
-        for x, a, b in PARTS:
-            op("V", ts1(T.si[:, a:b], T.mS[:, a:b], 8191, A.bitwise_and), r=["mS" + x], w=["iS" + x])
-        for x, a, b in PARTS:
-            op("V", tcopy(T.offS[:, a:b], T.si[:, a:b]), r=["iS" + x], w=["offS" + x])
+        fallback(T.pt[:, 0:128], "pt", T.s2[:, sl], "s2", T.r2, T.r2b, "r2", T.hx[:], "hx", T.sgS[:], dlo, lo, "BS")
+        for x in HOP.split():
+            if x in side:
+                side[x]()
+                continue
+            if x[0] == "z":
+                spread_z(d, x[1], int(x[2]), int(x[3]))
+                continue
+            if x == "ma":
+                r1, k1 = (T.r1, "r1") if t else (T.r2, "r2")
+                for y, a, b in PARTS:
+                    op("P", mm(psS[y][0], T.lS[:, sl], r1[:, a:b]), r=["LS%d" % d, k1], w=["AS" + y], banks=[psS[y][1]])
+                rF, rFb, kF = (T.r3, T.r3b, "r3") if t else (T.p0, T.pb21, "k2")
+                fallback(T.pc[:, 128:256], "pc", T.lT[:, sl], "LT%d" % d, rF, rFb, kF, T.lA1[:, sl], "LAa%d" % d, T.sgF[:], T.lF2[:, sl], ["LFb%d" % d], "BF")
+                for y, a, b in PARTS:
+                    op("P", mm(psF[y][0], T.lF1[:, sl], T.p0[:, a:b]), r=["LFa%d" % d, "k2"], w=["AF" + y], banks=[psF[y][1]])
+            merge("S", x)
 
     wait("Y", [lastw["Lzf"]])
     op("Y", lambda: Y.dma_start(T.yz[:], T.zfin[:]), w=["yz"], inc=16)
-    halves = [(k, slice(128 * k, 128 * k + 128)) for k in (0, 1)]
-    psB, psA = ((T.pt[:, 0:128], "pt"), (T.pc[:, 128:256], "pc")), ((T.pu[:, 0:128], "pu"), (T.pw[:, 128:256], "pw"))
-    for k, c in halves:
-        fallback(psB[k][0], psB[k][1], T.lT[:, 256:384], "LT3", T.r1, T.r2b, "r4", T.lAE[:, c], "LAE", (T.sgS, T.sgF)[k][:], T.lE2[:, c], "LEb", "B%d" % k)
-    for k, c in halves:
-        op("V", tt(T.fb[:, k], psB[k][0], T.lAE[:, c], A.max), r=["B%d" % k, "B%dp" % k, "LAE"], w=["jk%d" % k], banks=[psB[k][1]])
-    for k, c in halves:
-        op("P", [mm(T[psA[k][1]][:, 128 + 64 * x:192 + 64 * x], T.lE1[:, 128 * x:128 * x + 128], T.p0[:, 64 * k:64 * k + 64]) for x in (0, 1)],
-           r=["LEa", "k2"], w=["A%d" % k], banks=[psA[k][1]])
-    for k, c in halves:
-        op("V", tt(T.fin[:, c], T[psA[k][1]][:, 128:256], T.fb[:, :, 64 * k:64 * k + 64], A.max), r=["A%d" % k, "jk0", "jk1"], w=["fin%d" % k], banks=[psA[k][1]])
-    for k, c in halves:
-        op("V", ts1(T.fin2[:, c], T.fin[:, c], 8191, A.bitwise_and), r=["fin%d" % k], w=["msk%d" % k])
-    for k, c in halves:
-        op("V", [tcopy(T.yo[:, 128 * k + x:128 * k + 128:2], T.fin2[:, 128 * k + 64 * x:128 * k + 64 * x + 64]) for x in (0, 1)], r=["msk%d" % k], w=["yo%d" % k])
-        op("SY"[k], lambda: (S, Y)[k].dma_start(T.ya[:, c], T.yo[:, c]), r=["yo%d" % k], w=["ya%d" % k], inc=16)
+    op("P", [mm(T.pc[:, 0:128], T.rhb[:], T.lT[:, 256:384], True, False), mm(T.pc[:, 0:128], T.idf[:], T.cF[:], False, False)],
+       r=["rh", "LT3", "cF"], w=["U2"], banks=["pc"])
+    op("P", mm(T.pc[:, 0:128], T.rh[:], T.lE2[:, 128:256], False, True), r=["LUb"], w=["U2"], banks=["pc"])
+    fallback(T.pt[:, 0:128], "pt", T.lT[:, 256:384], "LT3", T.r1, T.r1b, "r4", T.lAE[:], "LAE", T.sgS[:], T.lE2[:, 0:128], ["LEb"], "B")
+    op("P", mm(T.pu[:, 0:128], T.lE1[:, 0:128], T.p0[:]), r=["LEa", "k2"], w=["A"], banks=["pu"])
+    side = {
+        "u1": lambda: op("V", tt(T.hx[:], T.pc[:, 0:128], T.cS[:], A.max), r=["U2", "cS"], w=["hx"], banks=["pc"]),
+        "u2": lambda: op("V", tt(T.n7[:], T.lE1[:, 128:256], T.hx[:], A.max), r=["LUa", "hx"], w=["o7_0", "o7_1"]),
+        "fb": lambda: op("V", tt(T.fb[:], T.pt[:, 0:128], T.lAE[:], A.max), r=["B", "Bp", "LAE"], w=["fb"], banks=["pt"]),
+        "l0": lambda: op("V", tt(T.mF[:], T.pu[:, 0:128], T.fb[:], A.max), r=["A", "fb"], w=["l0"], banks=["pu"]),
+        "l1": lambda: op("V", ts1(T.fi[:], T.mF[:], 8191, A.bitwise_and), r=["l0"], w=["l1"]),
+        "l2": lambda: op("V", tcopy(T.yo[:, 0:256:2], T.fi[:]), r=["l1"], w=["l2"]),
+    }
+    for x in END.split():
+        if x in side:
+            side[x]()
+            continue
+        step(int(x[0], 16), int(x[1]), 128)
+        if x[0] == "c":
+            c = 64 * int(x[1])
+            op("S", act(T.sgF[:, c:c + 64], T.dd[:, 128 + c:192 + c], F.Identity, scale=2.0 ** -13, bias=cf[:, 27:28]), r=["o12_" + x[1]], w=["f" + x[1]])
+    halves = [(k, slice(64 * k, 64 * k + 64), ("pb", "ph")[k]) for k in (0, 1)]
+    for k, c, bk in halves:
+        op("P", mm(T[bk][:, 0:64], T.dd[:, 128:256], T.p0[:, c], True, False), r=lo + ["k2"], w=["H%d" % k], banks=[bk])
+    for k, c, bk in halves:
+        op("P", mm(T[bk][:, 0:64], T.sgF[:], T.pri[:, 2, c], False, True), r=["f0", "f1"], w=["H%d" % k], banks=[bk])
+    for k, c, bk in halves:
+        op("V", ts1(T.yo[:, 128 * k + 1:128 * k + 128:2], T[bk][:, 0:64], 130 * 8192.0, A.add), r=["H%d" % k], w=["yo%d" % k], banks=[bk])
+        op("SY"[k], lambda: (S, Y)[k].dma_start(T.ya[:, 128 * k:128 * k + 128], T.yo[:, 128 * k:128 * k + 128]), r=["yo%d" % k, "l2"], w=["ya%d" % k], inc=16)
     for s in cnt:
         if s[0] != "Y" and waited.get(s, 0) < cnt[s]:
             g.wait_ge(T.sem[s], cnt[s])

@@ -3,7 +3,8 @@ from concourse.mybir import AluOpType, ActivationFunctionType
 
 A = AluOpType
 F = ActivationFunctionType
-N, RO, PAD, XA = 8, 3, 2, 4096
+XP = [0, 4096, 5632, 8192]
+N, RO, PAD, LB = 8, 3, 2, 24
 TAG = float(1 << 19)
 UP = float(1 << 21)
 f32, bf, i32, u16 = "float32", "bfloat16", "int32", "uint16"
@@ -16,18 +17,18 @@ def sb(shape, d):
 SCRATCH = {
     "X": sb([8192], bf), "xg": sb([4096], bf), "zrep": sb([4096], bf), "top": sb([4096 + 16], bf),
     "rai": sb([256], i32), "zown": sb([128], bf), "wi": sb([256], i32), "wf": sb([256], f32), "lo0": sb([128], u16),
-    "jf": sb([144], f32), "jb": sb([128], bf), "jp": sb([128], bf), "jt": sb([256], f32), "ci": sb([8], i32), "cf": sb([32], f32),
-    "ibf": sb([128], bf), "p0": sb([128], f32), "pbp": sb([128], bf), "tri": sb([128], bf), "kc0": sb([256], bf),
-    "gp16": sb([128], bf), "mh": sb([128], bf), "c0": sb([128], bf), "sgj": sb([64], bf),
+    "jf": sb([8], f32), "jb": sb([128], bf), "jp": sb([128], bf), "ci": sb([8], i32), "cf": sb([32], f32),
+    "ibf": sb([128], bf), "p0": sb([128], f32), "pbp": sb([128], bf), "tri": sb([128], bf), "kc0": sb([8, 32], bf),
+    "sgj": sb([64], bf), "gp16": sb([128], bf), "mh": sb([128], bf), "c0": sb([128], bf), "j8": sb([64], bf),
     "gp": sb([8], bf), "gn": sb([8], bf), "wgr": sb([8], bf), "ones": sb([128], bf),
     "onen": sb([128], f32), "ww": sb([144], bf), "tm": sb([256], f32),
-    "jl": sb([8], f32), "jq": sb([20], f32), "ja": sb([8], i32), "pip": sb([8], u16), "plb": sb([8], i32),
+    "jl": sb([8], f32), "jq": sb([12], f32), "ja": sb([8], i32), "pip": sb([8], u16), "plb": sb([8], i32),
     "zl": sb([384], bf), "zfin": sb([128], f32), "nzb": sb([256], bf), "nzf": sb([128], f32),
     "offF": sb([128], u16), "offS": sb([128], u16), "off0F": sb([128], u16), "off0S": sb([128], u16),
     "mF": sb([128], i32), "mS": sb([128], i32), "fi": sb([128], i32), "si": sb([128], i32),
     "basF": sb([128], f32), "basS": sb([128], f32), "u3": sb([256], bf), "imk": sb([128], f32),
-    "ki": sb([8, 2, 8, 2], i32), "km": sb([8, 2, 8, 2], i32), "n1": sb([8, 2, 4, 2, 2], f32), "n3": sb([8, 2, 2, 2, 6], f32),
-    "n4": sb([8, 2, 2, 2, 4], f32), "n6": sb([8, 2, 6, 4], f32), "n7": sb([8, 16], i32), "nb": sb([8, 2, 2, 4], i32),
+    "ki": sb([256], i32), "km": sb([64, 2, 2], i32), "n1": sb([64, 2, 2], f32), "n3": sb([16, 2, 2, 6], f32),
+    "n4": sb([32, 2, 4], f32), "n6": sb([2, 12, 8, 4], f32), "n7": sb([8, 16], i32), "nb": sb([8, 2, 2, 4], i32),
     "n8": sb([8, 2, 2, 4], f32), "n9": sb([8, 2, 2, 4], f32), "na": sb([8, 4, 2, 2], f32),
     "dd": sb([768], f32),
     "ha": sb([8], i32), "hb": sb([8], i32), "hc": sb([8], i32), "hpad": sb([128], f32),
@@ -37,11 +38,12 @@ SCRATCH = {
     "r1b": sb([128], bf), "r2b": sb([128], bf), "r3b": sb([128], bf), "rhb": sb([128], bf),
     "fb": sb([128], f32), "cS": sb([128], f32), "cF": sb([128], f32), "col": sb([12], f32), "lc": sb([8], f32),
     "lA1": sb([256], f32), "lA2": sb([256], f32), "lAE": sb([128], f32), "lT": sb([512], bf),
-    "junk": sb([256], f32), "jk": sb([128], f32), "tot": sb([8], f32), "tlf": sb([20], f32), "tl": sb([20], i32), "tl2": sb([20], i32), "lst": sb([32], u16),
+    "junk": sb([256], f32), "jk": sb([128], f32), "tot": sb([8], f32), "tl": sb([12], i32), "tl2": sb([12], i32), "lst": sb([32], u16),
     "pa_": sb([8], i32), "pb_": sb([8], i32), "pc_": sb([8], i32), "pl": sb([8], u16),
     "o1": sb([384], f32), "oh": sb([512], f32),
     "lS": sb([256], f32), "lF1": sb([256], f32), "lF2": sb([256], f32),
     "lH1": sb([256], f32), "lH2": sb([256], f32), "lE1": sb([256], f32), "lE2": sb([256], f32),
+    "ua": sb([128], f32), "hiA": sb([128], bf), "ce": sb([7 * 128], bf),
     "hi0": sb([128], f32), "hacc": sb([128], f32),
     "hx": sb([128], f32), "yo": sb([256], f32),
     "pg": ("psum", [128, 512], f32), "pb": ("psum", [128, 512], f32),
@@ -49,20 +51,23 @@ SCRATCH = {
     "pc": ("psum", [128, 512], f32), "pd": ("psum", [128, 512], f32),
     "pu": ("psum", [128, 512], f32), "pw": ("psum", [128, 512], f32),
 }
-POOL = {"V": 38, "S": 28, "P": 36, "G": 6, "Y": 10}
+POOL = {"V": 38, "S": 28, "P": 36, "G": 9, "Y": 7}
 ARR = ["z0", "z1", "z2", "zf", "F0", "S0", "S1", "S2", "Fa1", "Fa2", "Fb1", "Fb2", "Ha0", "Ha1", "Hb0", "Hb1",
        "Ea", "Eb", "Ua", "Ub", "cF", "cE", "Aa1", "Aa2", "Ab1", "Ab2", "AE", "T1", "T2", "T3", "TL"]
 SEMAPHORES = [q + str(k) for q in POOL for k in range(POOL[q])] + ["r" + a for a in ARR] + ["sent"]
-SEQ0 = ["F1 S0 S1 S23 F6 S45 S6 S7", "A F0 F2 f01 F3 s0 s1 f23 F45 s2 s3 f46 F7 s4 s5 f7 s6"]
-SEQ = ["S0 S13 F1 F2 F46 S4 S6 S7a S7b", "M b S5a ma mb aa ab oa S5b ob A H F0 B f01 F3 s0 s1 f23 F7 s2 f4 f57 s3 s4 s5 s6"]
-NET = "ha hb k0 k1 00 hh 01 10 11 20 21 30 hc 31 40 hp 41 far 50 51 tl 60 61 tm 70 71 tn 80 pa 81 r2 90 91 r1 pb a0 a1 pc b0 b1 pl c0 c1"
-LAST = "ha k0 hb k1 00 hh 01 10 11 20 hc 21 30 hp 31 40 41 rh 50 51 far 60 61 up 70 71 80 81 j0 90 91 a0 a1 j1 b0 b1 c0 c1 j2"
-HOP = "up X zS24 rh zV46 cS j0 zV68 j1 ma mb aa ab oa ob"
-END = "u1 u2 80 81 90 91 a0 a1 fb b0 b1 c0 c1 l0 l1 l2"
-ZS, ZG = 2, 0
+SEQ0 = ["S03 S47 Fbf S8b Scd Se Sf",
+        "A F03 F45 f01 F67 s0 f23 s1 F8a s2a s2b f47 r s3a s3b s4a s4b s5a s5b s6a s6b s7a s7c s7d B c"]
+SEQ = ["S02 S49 | F23 F67 Fab Fcf Sa Se Sf",
+       "A b S3 Sb ma mb Sc aa ab Sd oa ob Z F01 F45 f01 F89 s0 f23 s1 s2a s2b f45 s3a s3b s4a s4b f67 r s5a s5b s6a s6b s7a s7c s7d B c"]
+NET = "C far rh ha j0 hb k0 hh k1 00 hc 01 10 11 20 21 30 hp tl 31 zS4 40 41 50 51 60 tk 61 70 tm 71 80 tn 81 90 pa r2 91 a0 pb r1 a1 b0 pc b1 c0 pl c1"
+LAST = ("j0 C far rh ha j1 hb k0 hh k1 00 hc 01 10 hd 11 20 he 21 30 hp j2 31 40 41 50 51 60 j4 61 p0 70 p1 71 80 q0 81 q1 90 91 "
+        "a0 a1 b0 b1 c0 c1 j3 u0 u1")
+HOP = "gS gF zG3 p0 p1 zS5 H zG3 X zV8 cS j1 zV4 PS PF ma zV2 mb aa zV2 ab oa M ob"
+FIRST = "S"
+END = "u0 u1 90 91 a0 a1 b0 b1 c0 c1 h0 g0 g1 f0 f1 m0 y0 s0 m1 y1 s1"
 
 
-RELAYED = ["T1", "Aa1", "Ha0", "Hb0", "T2", "Aa2", "Ha1", "Hb1", "T3", "TL"]
+RELAYED = ["T1", "Ha0", "Hb0", "T2", "Ha1", "Hb1", "zf", "T3", "AE"]
 
 
 def helper(core, T, topo):
@@ -76,7 +81,7 @@ def spare(core, T, topo):
 
 def helper_program(g, core, q, T, topo):
     land = {"T1": (q + 3, T.lT[:, 0:128]), "Aa1": (q + 1, T.lA1[:, 0:128]), "T2": (q + 4, T.lT[:, 128:256]),
-            "Aa2": (q + 1, T.lA1[:, 128:256]), "T3": (q + 1, T.lT[:, 256:384]), "TL": (q - RO, T.lT[:, 384:512]),
+            "Aa2": (q + 1, T.lA1[:, 128:256]), "Fa1": (q + 1, T.lF1[:, 0:128]), "Fa2": (q + 1, T.lF1[:, 128:256]), "T3": (q + 1, T.lT[:, 256:384]), "zf": (q - RO, T.zfin[:]), "AE": (q - RO, T.lAE[:]),
             "Ha0": (q - 1, T.lH1[:, 0:128]), "Hb0": (q + 1, T.lH2[:, 0:128]), "Ha1": (q - 2, T.lH1[:, 128:256]), "Hb1": (q + 1, T.lH2[:, 128:256])}
     n = 0
     for name in RELAYED:
@@ -125,9 +130,9 @@ def rank_program(g, core, T, topo):
             d += [e for o, e in bank.get(b, {}).items() if o != qn]
         return d
 
-    def op(qn, fns, r=(), w=(), banks=(), inc=1):
-        wait(qn, deps_of(qn, r, w, banks))
-        s = [x for x in (qn + str(k) for k in range(POOL[qn])) if know[qn].get(x, 0) == cnt.get(x, 0)][0]
+    def op(qn, fns, r=(), w=(), banks=(), inc=1, acc=False):
+        wait(qn, deps_of(qn, r, () if acc else w, banks))
+        s = lastw[w[0]][0] if acc else [x for x in (qn + str(k) for k in range(POOL[qn])) if know[qn].get(x, 0) == cnt.get(x, 0)][0]
         fns = fns if isinstance(fns, list) else [fns]
         for fn in fns:
             fn().then_inc(T.sem[s], inc)
@@ -224,94 +229,113 @@ def rank_program(g, core, T, topo):
     op("S", lambda: S.dma_start(T.rai[:], T.ra[:]), w=["rai"], inc=16)
     op("Y", lambda: Y.dma_start(T.wi[0:1, 0:128], T.wg[:]), w=["wi"], inc=16)
     op("S", lambda: S.dma_start(T.wi[0:1, 128:256], T.th[:]), w=["ti"], inc=16)
-    op("Y", lambda: Y.dma_start(T.X[:, 0:XA], T.xd[:, 0:XA]), w=["X0"], inc=16)
+    op("Y", lambda: Y.dma_start(T.X[:, 0:XP[1]], T.xd[:, 0:XP[1]]), w=["X0"], inc=16)
 
-    cf, ci, jf, jt = T.cf, T.ci, T.jf, T.jt
+    def lin(o, i, scale, bias=0.0):
+        return act(o, i, F.Identity, scale=scale, bias=bias)
+
+    def count(o, pattern, base=0):
+        return lambda: g.iota(o, pattern, base, 0, allow_small_or_imprecise_dtypes=True)
+
+    def where(o, i, pattern, x, fill=0.0, sign=1):
+        return lambda: g.affine_select(o, i, pattern, x, fill, 0, sign)
+
+    def ce(a, n=128):
+        return T.ce[:, a:a + n]
+
+    cf, ci, jf = T.cf, T.ci, T.jf
+    op("V", [fillc(T.ones[:], 1.0), fillc(T.top[:, 0:PAD], 0.0), fillc(T.mh[:], -0.5), fillc(T.onen[:], -1.0)], w=["pad", "ones"])
     op("G", lambda: g.iota(ci[:, 0:1], [[0, 1]], 0, 1), w=["ci0"])
-    op("G", lambda: g.iota(T.ja[:], [[1, 4], [64, 2]], 0, 0), w=["ja"])
-    op("G", lambda: g.iota(jf[:], [[1, 144]], 0, 0, allow_small_or_imprecise_dtypes=True), w=["jf"])
-    send([(q + 1, T.zown[:], T.zl[:, 0:128], "z0")], ["zown"])
+    op("G", [lambda: g.iota(T.ja[:], [[1, 4], [64, 2]], 0, 0), count(jf[:], [[1, 8]])], w=["ja", "jf"])
+    op("G", where(T.ibf[:], T.ones[:], [[-1, 128]], A.is_equal), r=["ones"], w=["ibf"])
 
-    op("V", [fillc(T.top[:, 0:PAD], 0.0), fillc(T.mh[:], -0.5), fillc(T.ones[:], 1.0), fillc(T.onen[:], -1.0)], w=["pad", "ones"])
     op("V", [ts1(ci[:, 1:2], ci[:, 0:1], 15, A.bitwise_and), ts1(ci[:, 2:3], ci[:, 0:1], 4, A.arith_shift_right),
              ts1(ci[:, 3:4], ci[:, 0:1], 31, A.bitwise_and), ts1(ci[:, 4:5], ci[:, 0:1], 5, A.arith_shift_right),
-             ts1(ci[:, 5:6], ci[:, 0:1], 1, A.bitwise_and), ts1(ci[:, 7:8], ci[:, 0:1], 3, A.bitwise_and)], r=["ci0"], w=["ci"])
-    op("V", [fillc(T.hpad[:], 0.0), fillc(cf[:, 27:28], 129.5 + 2.0 ** -14)], w=["hpad"])
-    op("V", [tcopy(cf[:, 0:5], ci[:, 0:5]), ts2(cf[:, 7:8], ci[:, 2:3], 16.0, 15.0, A.mult, A.add),
-             ts1(cf[:, 13:14], ci[:, 1:2], 4.0, A.mult), ts1(cf[:, 14:15], ci[:, 1:2], 15.0, A.not_equal),
-             ts2(cf[:, 15:16], ci[:, 5:6], 2 * TAG, -TAG / 2, A.mult, A.add), ts2(cf[:, 20:21], ci[:, 1:2], 0.0, 2.25 * TAG, A.is_equal, A.mult),
-             ts1(cf[:, 21:22], ci[:, 3:4], 0.0, A.not_equal), ts2(cf[:, 16:17], ci[:, 7:8], -TAG, 3.5 * TAG, A.mult, A.add),
-             ts2(cf[:, 17:18], ci[:, 4:5], 32.0, 32.0, A.mult, A.add), ts2(cf[:, 18:19], ci[:, 5:6], 2.0, -1.0, A.mult, A.add),
-             ts1(cf[:, 23:24], ci[:, 7:8], 1.0, A.is_equal), ts2(cf[:, 24:25], ci[:, 7:8], 2.0, -1.0, A.is_equal, A.mult),
-             ts1(cf[:, 25:26], ci[:, 1:2], 8192.0, A.mult)], r=["ci", "ci0"], w=["cf"])
+             ts1(ci[:, 5:6], ci[:, 0:1], 1, A.bitwise_and)], r=["ci0"], w=["ci"])
+    op("V", [fillc(T.hpad[:], 0.0), fillc(cf[:, 27:28], 129.5 + 2.0 ** -14), fillc(T.ww[:], 0.0),
+             fillc(T.kc0[0:8, :, 0], -1.75 * TAG), fillc(T.kc0[0:8, :, 1:32], TAG / 2)], w=["hpad", "fill"])
     op("V", tcopy(T.lo0[:], T.rai[:, 0:256:2]), r=["rai"], w=["lo0"])
+    op("V", [tcopy(cf[:, 0:5], ci[:, 0:5]), tcopy(cf[:, 7:8], ci[:, 5:6]), ts1(cf[:, 14:15], ci[:, 1:2], 15.0, A.not_equal),
+             ts2(cf[:, 23:24], ci[:, 1:2], 15.0, -1.0, A.not_equal, A.mult), ts2(cf[:, 20:21], ci[:, 1:2], 0.0, 2.25 * TAG, A.is_equal, A.mult),
+             ts1(cf[:, 21:22], ci[:, 3:4], 0.0, A.not_equal)], r=["ci", "ci0"], w=["cf"])
+    send([(q + 1, T.zown[:], T.zl[:, 0:128], "z0")], ["zown"])
     send([(q + 1, T.lo0[:], T.off0F[:], "F0"), (q - 1, T.lo0[:], T.off0S[:], "S0")], ["lo0"])
-    op("G", lambda: g.iota(jt[:], [[1, 8], [0, 32]], 0, 0, allow_small_or_imprecise_dtypes=True), w=["jt"])
-    op("G", lambda: g.iota(T.jp[:], [[1, 4], [4, 32]], 0, 0, allow_small_or_imprecise_dtypes=True), w=["jp"])
+    op("V", [fillc(T.tri[:, k:128:4], (3.5 - k) * TAG) for k in range(4)], w=["tri"])
+    kcl, c130, c65, nT, pT, nT3, rneg = range(0, 7 * 128, 128)
+    op("V", [fillc(T.ce[0:8, k:128:4], (x * TAG + UP) / 4) for k, x in enumerate((0, 2, 1, 3))], w=["kcl"])
+    op("S", [lin(cf[:, 13:14], cf[:, 1:2], 4.0), lin(cf[:, 15:16], cf[:, 7:8], 2 * TAG, -TAG / 2), lin(cf[:, 18:19], cf[:, 7:8], 4.0, -2.0),
+             lin(cf[:, 25:26], cf[:, 1:2], 8192.0), lin(cf[:, 10:11], cf[:, 3:4], 4.0, cf[:, 4:5]), lin(T.jl[:], jf[:, 0:8], 16.0, cf[:, 1:2])],
+       r=["cf", "jf"], w=["ka"])
+    op("S", [lin(cf[:, 22:23], cf[:, 1:2], 16384.0, cf[:, 15:16]), lin(T.jq[:, 0:8], T.jl[:], 1.0, 32768.0),
+             lin(T.jq[:, 8:12], T.onen[:, 0:4], -32768.0, cf[:, 10:11])], r=["ka", "ones"], w=["kd"])
+    op("S", [lin(cf[:, 6:7], cf[:, 22:23], 1.0, 8192.0 + TAG), lin(cf[:, 5:6], cf[:, 22:23], 1.0, cf[:, 20:21])], r=["kd"], w=["kc"])
+    op("G", where(T.kc0[0:8], T.kc0[0:8], [[-1, 8], [0, 32]], A.is_equal), r=["fill"], w=["k4"])
+    op("Y", lambda: Y.dma_start(T.X[:, XP[1]:XP[2]], T.xd[:, XP[1]:XP[2]]), r=["k4"], w=["X1"], inc=16)
+    op("Y", lambda: Y.dma_start(T.X[:, XP[2]:XP[3]], T.xd[:, XP[2]:XP[3]]), r=["X0"], w=["X2"], inc=16)
+    op("G", where(T.pbp[:], T.ones[:], [[-1, 32], [-32, 4]], A.is_equal), w=["pbp"])
+    op("G", where(T.tri[:], T.tri[:], [[-1, 128]], A.is_equal, -TAG), w=["tri"])
+    op("G", where(T.jk[:], T.ones[:], [[-4, 32], [-1, 2], [-2, 2]], A.is_equal), w=["jk"])
+    op("G", where(T.tri[:], T.tri[:], [[1, 128]], A.is_ge, sign=-1), w=["tri"])
     op("V", tcopy(T.wf[0:1, :], T.wi[0:1, :]), r=["wi", "ti"], w=["wf"])
     op("P", [mm(T.pd[:, 8 + k:9 + k], T.wf[0:1, 128 * k:128 * k + 128], T.onen[0:1, 0:1]) for k in (0, 1)], r=["wf", "ones"], w=["wt"], banks=["pd"])
-    op("V", [ts2(cf[:, 10:11], ci[:, 3:4], 4.0, cf[:, 4:5], A.mult, A.add),
-             ts2(cf[:, 22:23], ci[:, 1:2], 16384.0, cf[:, 15:16], A.mult, A.add),
-             ts2(cf[:, 26:27], cf[:, 0:1], cf[:, 23:24], cf[:, 24:25], A.add, A.add),
-             ts1(T.pip[:], T.ja[:], cf[:, 13:14], A.add),
-             ts2(T.jl[:], jf[:, 0:8], 16.0, cf[:, 1:2], A.mult, A.add),
-             ts1(T.ibf[:], jf[:, 0:128], cf[:, 0:1], A.is_equal), tcopy(T.jb[:], jf[:, 0:128]),
-             ts1(T.gp[:], jf[:, 0:8], cf[:, 2:3], A.is_equal),
-             ts2(T.gn[:], jf[:, 0:8], cf[:, 2:3], -1.0, A.is_equal, A.mult),
-             ts2(T.dd[:, 0:128], jf[:, 0:128], cf[:, 0:1], -TAG, A.is_gt, A.mult), ts2(T.dd[:, 128:256], jf[:, 0:128], cf[:, 17:18], TAG, A.is_ge, A.mult),
-             ts2(T.dd[:, 256:384], jf[:, 0:128], cf[:, 0:1], cf[:, 16:17], A.is_equal, A.mult)], r=["cf", "ci", "jf", "ja"], w=["kb", "pip"])
-    op("V", [ts1(cf[:, 8:9], T.pd[:, 8:9], -1.0, A.mult), ts1(cf[:, 9:10], T.pd[:, 9:10], -1.0 / 16, A.mult)], r=["wt"], w=["k0"], banks=["pd"])
-    op("V", [ts1(T.plb[:], T.jl[:], 64.0, A.mult), ts1(T.pbp[:], jf[:, 0:128], cf[:, 10:11], A.is_equal),
-             ts1(T.jq[:, 0:8], T.jl[:], 32768.0, A.add), tcopy(T.jq[:, 8:16], T.jl[:]),
-             ts2(T.jq[:, 16:20], T.onen[:, 0:4], -32768.0, cf[:, 10:11], A.mult, A.add),
-             ts1(cf[:, 6:7], cf[:, 22:23], 8192.0 + TAG, A.add), ts1(cf[:, 5:6], cf[:, 22:23], cf[:, 20:21], A.add),
-             ts2(cf[:, 19:20], cf[:, 22:23], cf[:, 20:21], cf[:, 14:15], A.add, A.mult),
-             tt(T.dd[:, 0:128], T.dd[:, 0:128], T.dd[:, 128:256], A.add), ts1(T.hi0[:], T.rai[:, 1:256:2], cf[:, 25:26], A.add),
-             ts1(T.jk[:, 0:128], jf[:, 0:128], cf[:, 26:27], A.is_equal)], r=["kb", "ones", "rai"], w=["kc", "jk"])
-    op("Y", lambda: Y.dma_start(T.X[:, XA:8192], T.xd[:, XA:8192]), r=["jt"], w=["X"], inc=16)
-    op("S", [act(T.idf[:], T.ibf[:], F.Copy), act(T.imk[:], T.ibf[:], F.Identity, scale=cf[:, 14:15])]
-       + [act(T.pri[:, k], T.ibf[:], F.Identity, scale=x * UP) for k, x in ((0, 2), (1, 4), (3, 1))], r=["kb"], w=["k1"])
-    op("V", [ts2(T.tm[:], jt[:], cf[:, 2:3], cf[:, 9:10], A.is_equal, A.mult),
-             ts2(T.wgr[:], jf[:, 0:8], cf[:, 2:3], cf[:, 8:9], A.is_equal, A.mult),
-             ts2(T.ww[:], jf[:], cf[:, 7:8], cf[:, 8:9], A.is_equal, A.mult),
-             ts2(T.sgj[:], jt[:, 0:128:2], cf[:, 4:5], cf[:, 18:19], A.is_equal, A.mult),
-             tt(T.tri[:], T.dd[:, 0:128], T.dd[:, 256:384], A.add), ts1(cf[:, 12:13], cf[:, 19:20], -1.0, A.mult),
-             ts2(T.gp16[:], jt[:, 0:256:2], cf[:, 0:1], 0.5, A.is_equal, A.mult),
-             ts2(T.kc0[:], jt[:], cf[:, 0:1], TAG / 2, A.is_equal, A.mult)], r=["k0", "kb", "kc", "jt"], w=["k3"])
-    op("V", ts2(T.kc0[:, 0:256:32], jf[:, 0:8], cf[:, 0:1], -1.75 * TAG, A.is_equal, A.mult), r=["k3"], w=["k4"])
-    op("S", [act(T.p0[:], T.pbp[:], F.Copy), act(T.prin[:], T.pbp[:], F.Identity, scale=-2.0 ** 21),
-             act(T.pb21[:], T.pbp[:], F.Identity, scale=2.0 ** 21), act(T.ic3[:], T.ibf[:], F.Identity, scale=3 * 2.0 ** 20),
-             act(T.pri[:, 2], T.pbp[:], F.Identity, scale=-8192.0)], r=["kc"], w=["k2"])
-    op("P", [mm(T.pc[32 * j:32 * j + 32, 0:128], T.hi0[:, j:128:4], T.jk[:, 0:128]) for j in range(4)], r=["kc", "jk"], w=["h0"], banks=["pc"])
-    op("S", act(T.hacc[:], T.pc[:, 0:128], F.Copy), r=["h0"], w=["hacc"], banks=["pc"])
+    op("V", [ts1(T.gp[:], jf[:, 0:8], cf[:, 2:3], A.is_equal), ts2(T.gn[:], jf[:, 0:8], cf[:, 2:3], -1.0, A.is_equal, A.mult),
+             ts1(T.pip[:], T.ja[:], cf[:, 13:14], A.add), ts1(T.plb[:], T.jl[:], 64.0, A.mult),
+             ts1(T.hi0[:], T.rai[:, 1:256:2], cf[:, 25:26], A.add)], r=["cf", "ci", "ka", "jf", "ja", "rai"], w=["kb", "pip"])
+    op("S", [lin(cf[:, 8:9], T.pd[:, 8:9], -1.0), lin(cf[:, 9:10], T.pd[:, 9:10], -1.0 / 16), lin(cf[:, 12:13], cf[:, 5:6], cf[:, 23:24])],
+       r=["wt", "kc"], w=["k0"], banks=["pd"])
+    op("S", [lin(T.tm[:, 0:8], T.gp[:], cf[:, 9:10]), lin(T.wgr[:], T.gp[:], cf[:, 8:9]), lin(T.ww[:, 15:143:16], T.gp[:], cf[:, 8:9])],
+       r=["kb", "k0", "fill"], w=["kw"])
+    op("S", [lin(T.tm[:, 8 + x:256:8], T.onen[:, 0:31], 0.0, T.tm[:, x:x + 1]) for x in range(8)], r=["kw"], w=["tm"])
+    op("V", [tcopy(T.idf[:], T.ibf[:]), ts1(T.imk[:], T.ibf[:], cf[:, 14:15], A.mult), ts1(T.ic3[:], T.ibf[:], 3 * 2.0 ** 20, A.mult)]
+       + [ts1(T.pri[:, k], T.ibf[:], x * UP, A.mult) for k, x in ((0, 2), (1, 4), (3, 1))], r=["ibf"], w=["k1"])
+    op("P", mm(T.pd[0:8, 10:11], T.tm[:, 0:8], T.onen[:, 0:1]), r=["kw", "ones"], w=["t8"], banks=["pd"])
+    op("S", act(cf[0:8, 28:29], T.pd[0:8, 10:11], F.Identity, bias=0.5), r=["t8"], w=["k5"], banks=["pd"])
+    op("S", lin(cf[:, 11:12], cf[:, 12:13], 1.0, -UP), r=["k0"], w=["k6"])
+
 
     def zslot(t):
         return T.zl[:, 128 * t:128 * t + 128]
 
-    ZR = ["zr%d" % k for k in range(8)]
+    ZR = ["zr%d" % k for k in range(31)]
+    zdone = [0] * RO
 
-    def spread_z(t, qn, a, b):
-        for k in range(a, b):
-            op(qn, [copy(qn, T.zrep[:, x:4096:32], zslot(t)) for x in range(1 + 4 * k, min(5 + 4 * k, 32))], r=["Lz%d" % t], w=[ZR[k]])
+    def spread_z(t, qn, n):
+        rows = range(zdone[t], zdone[t] + n)
+        op(qn, [copy(qn, T.zrep[:, 1 + x:4096:32], zslot(t)) for x in rows], r=["Lz%d" % t], w=[ZR[x] for x in rows])
+        zdone[t] += n
 
     KEYS = ("pu", "pw")
 
-    def base(role):
-        src, dst, col = (T.fi, T.basF, 5) if role == "F" else (T.si, T.basS, 6)
+    def base(role, first=None):
+        src, dst, col = (T.fi, T.basF, 5) if role == "F" else (T.si if first is None else first, T.basS, 6)
+        if role == "S":
+            op("V", ts1(dst[:], src[:], cf[:, col:col + 1], A.add), r=["iSa", "iSb", "LS0", "kc"], w=["basS"])
+            for h, bk in enumerate(KEYS):
+                op("P", [mm(T[bk][:, 256:384], T.mh[0:8, :], T.ww[0:8, 16:144], True, False)]
+                   + [mm(T[bk][32 * j:32 * j + 32, 257:384:2], dst[:, j:128:4], T.idf[:, 64 * h:64 * h + 64], False, False) for j in range(4)],
+                   r=["basS", "k1", "kw"], w=["key%d" % h], banks=[bk])
+            return
         op("V", ts1(dst[:], src[:].indirect(T.pip[:]), cf[:, col:col + 1], A.add), r=["i" + role + "a", "i" + role + "b", "pip", "kb", "kc"], w=["bas" + role])
-        for h, bk in enumerate(KEYS):
-            op("P", mm(T[bk][:, 256 + (role == "S"):384:2], dst[:], T.idf[:, 64 * h:64 * h + 64], role == "S", False),
-               r=["bas" + role, "k1"], w=["key%d" % h], banks=[bk])
 
-    spread_z(0, "V", 0, 1)
-    op("V", [tcopy(T.fi[:], T.off0F[:]), tcopy(T.si[:], T.off0S[:])], r=["LF0", "LS0"], w=["iFa", "iFb", "iSa", "iSb"])
-    spread_z(0, "V", 1, 6)
-    spread_z(0, "S", 6, 8)
-    base("S")
-    base("F")
+    def turn():
+        for h, bk in enumerate(KEYS):
+            op("P", mm(T[bk][:, 256:384:2], T.basF[:], T.idf[:, 64 * h:64 * h + 64], False, False), r=["basF", "k1"], w=["key%d" % h], banks=[bk], acc=True)
+
+    spread_z(0, "G", 6)
+    op("G", [where(T.gp16[0:8, :], T.ones[0:8, :], [[-1, 8], [0, 16]], A.is_equal), count(T.j8[:], [[1, 4], [0, 16]])], w=["g16"])
+    op("G", where(T.tri[:], T.tri[:], [[-32, 4], [0, 32]], A.is_ge), w=["tri"])
+    op("G", [count(T.jb[:], [[1, 128]]), count(T.jp[:], [[1, 4], [4, 32]])], w=["jp"])
+    op("V", [tcopy(T.p0[:], T.pbp[:])] + [ts1(o, T.pbp[:], x, A.mult) for o, x in (
+        (T.prin[:], -UP), (T.pb21[:], UP), (T.pri[:, 2], -8192.0), (ce(c130), 130 * 8192.0), (ce(c65), -65 * 8192.0))], r=["pbp"], w=["k2"])
+    spread_z(0, "V", 8)
+    base(FIRST, T.off0S)
+    op("V", tcopy(T.fi[:], T.off0F[:]), r=["LF0"], w=["iFa", "iFb"])
+    spread_z(0, "V", 17)
 
     E = T.top[:, PAD + 31:PAD + 4096:32]
-    tops = ["top%d" % c for c in range(7)] + ["top7a", "top7b"]
+    tops = ["top" + x[1:] for x in sorted(SEQ[1].split()) if x[0] == "s"]
+    gains = ["gain" + k for k in tops]
+    early = len([k for k in tops if int(k[3]) < LB // 4])
     PARTS = (("a", 0, 32), ("b", 32, 128))
 
     def minmax(lo, hi, a, b):
@@ -319,46 +343,47 @@ def rank_program(g, core, T, topo):
 
     def step(s, x, o):
         n1, n3, n4, n6, n7, nb, n8, n9, na = T.n1, T.n3, T.n4, T.n6, T.n7, T.nb, T.n8, T.n9, T.na
-        gs, H, a, b = slice(4 * x, 4 * x + 4), x, o + 64 * x, o + 64 * x + 64
+        gs, a, b = slice(4 * x, 4 * x + 4), o + 64 * x, o + 64 * x + 64
+        bs, hs, km, ps = slice(32 * x, 32 * x + 32), slice(8 * x, 8 * x + 8), T.km, T[KEYS[x]]
         fns = [
-            lambda: [ts1(T.km[:, gs], T.ki[:, gs], (1 << 21) - 1, A.bitwise_and)],
-            lambda: minmax(n1[:, gs, :, :, :, 0], n1[:, gs, :, :, :, 1], T.km[:, gs, :, :, 0], T.km[:, gs, :, :, 1]),
-            lambda: minmax(n3[:, gs, :, :, :, 1:6:4], n3[:, gs, :, :, :, 0:5:4], n1[:, gs, :, :, 0], n1[:, gs, :, :, 1]),
-            lambda: minmax(n3[:, gs, :, :, :, 3], n3[:, gs, :, :, :, 2], n3[:, gs, :, :, :, 5], n3[:, gs, :, :, :, 0]),
-            lambda: minmax(n4[:, gs, :, :, 0], n4[:, gs, :, :, 1], n3[:, gs, :, :, 0, 1:5], n3[:, gs, :, :, 1, 1:5]),
-            lambda: minmax(n6[:, :, H, 4:6] if H else n6[:, :, H, 1:6:4], n6[:, :, H, 0:2] if H else n6[:, :, H, 0:5:4], n4[:, :, H, 0], n4[:, :, H, 1]),
-            lambda: minmax(n6[:, :, H, 2 + H], n6[:, :, H, 3 - H], n6[:, :, H, 5], n6[:, :, H, 0]),
-            lambda: [tt(n7[:, gs], n6[:, gs, 0, 1:5], n6[:, gs, 1, 1:5], A.min)],
+            lambda: [ts1(km[:, bs], T.ki[:, 128 * x:128 * x + 128], (1 << 21) - 1, A.bitwise_and)],
+            lambda: minmax(n1[:, bs, :, 0], n1[:, bs, :, 1], km[:, bs, :, 0], km[:, bs, :, 1]),
+            lambda: minmax(n3[:, hs, :, :, 1:6:4], n3[:, hs, :, :, 0:5:4], n1[:, bs, 0], n1[:, bs, 1]),
+            lambda: minmax(n3[:, hs, :, :, 3], n3[:, hs, :, :, 2], n3[:, hs, :, :, 5], n3[:, hs, :, :, 0]),
+            lambda: minmax(n4[:, 16 * x:16 * x + 8], n4[:, 16 * x + 8:16 * x + 16], n3[:, hs, :, 0, 1:5], n3[:, hs, :, 1, 1:5]),
+            lambda: minmax(n6[:, x, 4:12, 0:8:7], n6[:, x, 0:8, 3:5], n4[:, 16 * x:16 * x + 16, 0], n4[:, 16 * x:16 * x + 16, 1]),
+            lambda: minmax(n6[:, x, 4:8, 1:7:5], n6[:, x, 4:8, 2:6:3], n6[:, x, 8:12, 0:8:7], n6[:, x, 0:4, 3:5]),
+            lambda: [tt(n7[:, gs], n6[:, x, 4:8, 0:4], n6[:, x, 4:8, 4:8], A.min)],
             lambda: [ts1(nb[:, gs], n7[:, gs], (1 << 19) - 1, A.bitwise_and)],
             lambda: minmax(n8[:, gs, 0], n8[:, gs, 1], nb[:, gs, 0], nb[:, gs, 1]),
             lambda: minmax(n9[:, gs, :, 0], n9[:, gs, :, 1], n8[:, gs, :, 0], n8[:, gs, :, 1]),
             lambda: minmax(na[:, gs, :, :, 0], na[:, gs, :, :, 1], n9[:, gs, :, :, 0:4:2], n9[:, gs, :, :, 1:4:2]),
             lambda: minmax(T.dd[:, a:b:2], T.dd[:, a + 1:b:2], na[:, gs, :, 0], na[:, gs, :, 1]),
         ][s]()
-        r = ["o4_0", "o4_1"] if s == 5 else ["o5_0", "o5_1", "o6_0", "o6_1"] if s == 7 else ["o%d_%d" % (s - 1, x)]
-        op("V", fns, r=r, w=["o%d_%d" % (s, x)])
+        op("V", fns, r=["o%d_%d" % (s - 1, x)], w=["o%d_%d" % (s, x)])
 
     def minus_threshold():
-        op("P", mm(T.pg[:, 0:256], T.onen[:], T.tm[:], True, False), r=["k3", "ones"], w=["gain" + k for k in tops], banks=["pg"])
-        op("P", mm(T.ph[0:8, 384:512], T.tm[:, 0:256:32], T.onen[:], True, False), r=["k3"], w=["s0"], banks=["ph"])
+        op("P", mm(T.pg[:, 0:8 * LB], T.onen[:], T.tm[:, 0:8 * LB], True, False), r=["tm", "ones"], w=gains[:early], banks=["pg"])
+        op("P", mm(T.ph[:, 8 * LB:256], T.onen[:], T.tm[:, 8 * LB:256], True, False), r=["tm", "ones"], w=gains[early:], banks=["ph"])
 
     minus_threshold()
+    op("P", [mm(T.pd[32 * j:32 * j + 32, 0:128], T.hi0[:, j:128:4], T.jk[:, 0:128]) for j in range(4)], r=["kb", "jk"], w=["h0"], banks=["pd"])
 
     def order(r, rb, c, key, name, row=T.jb, scale=2.0 ** 21):
-        op("V", ts2(rb[:], row[:], c, scale, A.is_equal, A.mult), r=[key, "kb", "jp"], w=[name + "b"])
+        op("V", ts2(rb[:], row[:], c, scale, A.is_equal, A.mult), r=[key, "jp"], w=[name + "b"])
         op("S", act(r[:], rb[:], F.Sign), r=[name + "b"], w=[name])
 
     def fallback(ps, bk, s2, ks, r, rb, kr, old, ko, sg, src, kd, name):
         op("S", act(sg, old, F.Sign), r=[ko], w=["sg" + name])
-        op("P", [mm(ps, s2, rb[:], True, False), mm(ps, T.ic3[:], sg, False, False)], r=[ks, kr, "sg" + name, "k2"], w=[name + "p"], banks=[bk])
-        op("P", mm(ps, src, r[:], False, True), r=kd + [kr], w=[name], banks=[bk])
+        return [lambda: op("P", [mm(ps, s2, rb[:], True, False), mm(ps, T.ic3[:], sg, False, False)], r=[ks, kr, "sg" + name, "k2"], w=[name], banks=[bk]),
+                lambda: op("P", mm(ps, src, r[:], False, True), r=kd + [kr], w=[name], banks=[bk], acc=True)]
 
     def upper_out(t):
         o0, sl = 256 * t, slice(128 * t, 128 * t + 128)
         rot, rotb, dhi = (T.rh[:], T.rhb[:], T.dd[:, 384:512]) if t else (T.idf[:], T.pri[:, 3], T.dd[:, 128:256])
         op("P", [mm(T.pd[:, 0:128], T.pri[:, t], T.s1[:, sl], True, False), mm(T.pd[:, 0:128], T.idf[:], dhi, False, True),
                  mm(T.pd[:, 128:256], rotb, T.s2[:, sl], True, False), mm(T.pd[:, 128:256], rot, dhi, False, True)],
-           r=["up", "k1", "rh", "rhb"], w=["phi"], banks=["pd"])
+           r=["up0", "up1", "k1", "rh", "rhb"], w=["phi"], banks=["pd"])
         op("S", act(T.oh[:, o0:o0 + 256], T.pd[:, 0:256], F.Copy), r=["phi"], w=["oh"], banks=["pd"])
         send([(q - t - 1, T.oh[:, o0:o0 + 128], T.lH1[:, sl], "Ha%d" % t)], ["oh"])
         send([(q + 1, T.oh[:, o0 + 128:o0 + 256], T.lH2[:, sl], "Hb%d" % t)], ["oh"])
@@ -367,14 +392,16 @@ def rank_program(g, core, T, topo):
         if k == 0:
             op("V", tt(T.jk[:], T.lH1[:, 128 * t:128 * t + 128], T.lH2[:, 128 * t:128 * t + 128], A.max), r=["LHa%d" % t, "LHb%d" % t], w=["jk"])
         else:
-            op("V", tt(T.hacc[:], T.jk[:], T.hacc[:], A.max), r=["jk"], w=["hacc"])
+            op("V", tt(T.mF[:] if t else T.hacc[:], T.jk[:], T.hacc[:], A.max), r=["jk", "iFa", "iFb"], w=["hacc"])
 
     for t in range(RO):
         d = t + 1
         last = t == RO - 1
         offs = {"F": T.off0F if t == 0 else T.offF, "S": T.off0S if t == 0 else T.offS}
-        psS = {"a": (T.pu[:, 0:32], "pu"), "b": (T.pw[:, 128:224], "pw")}
-        psF = {"a": (T.pt[:, 256:288], "pt"), "b": (T.pb[:, 128:224], "pb")}
+        psF = {"a": (T.pu[:, 0:32], "pu"), "b": (T.pw[:, 128:224], "pw")}
+        psS = {"a": (T.pt[:, 256:288], "pt"), "b": (T.pb[:, 128:224], "pb")}
+        if FIRST == "S":
+            psF, psS = psS, psF
 
         def merge(role, x):
             kind, part = x
@@ -388,152 +415,196 @@ def rank_program(g, core, T, topo):
                 op("V", tcopy(o[:, a:b], i[:, a:b]), r=["i" + role + part], w=["off" + role + part])
 
         def gather(qn, x):
-            role, c = x[0], 2 * int(x[1]) + (x[-1] == "b")
-            e = c + 1 if x[-1] in "ab" else 2 * int(x[-1]) + 2
+            role, c, e = x[0], int(x[1], 16), int(x[-1], 16) + 1
             op(qn, copy(qn, T.xg[:, 256 * c + (role == "S"):256 * e:2], T.X[:].indirect(offs[role][:, 8 * c:8 * e])),
-               r=["X", "X0"] + (["L%s0" % role] if t == 0 else ["off" + role + "ab"[k > 3] for k in range(c, e)]),
+               r=["X"] + ["X%d" % k for k in range(len(XP) - 1)] + (["L%s0" % role] if t == 0 else ["off" + role + "ab"[k > 3] for k in range(c, e)]),
                w=["x%s%d%s" % (role, k // 2, "ab"[k % 2]) for k in range(c, e)])
+
+        def scan(c, part=""):
+            a, b, src = {"": (0, 16, "ab"), "a": (0, 8, "a"), "b": (8, 16, "b"), "c": (8, 12, "b"), "d": (12, 16, "b")}[part]
+            a, b = a + 16 * c, b + 16 * c
+            key = "top%d%s" % (c, part)
+            op("V", lambda: V.tensor_tensor_scan(T.top[:, PAD + 32 * a:PAD + 32 * b], T.xg[:, 32 * a:32 * b], T.zrep[:, 32 * a:32 * b], 0.0, A.max, A.min),
+               r=["x%s%d%s" % (x, c, y) for x in "FS" for y in src] + ZR + ["zf%d" % c], w=[key])
+            fns, bk = [], "pg" if a < 4 * LB else "ph"
+            for ib in range(a // 4, b // 4):
+                c0, gs = PAD + 128 * ib, slice(8 * ib, 8 * ib + 8)
+                fns += [mm(T[bk][:, gs], T.top[:, c0:c0 + 128], T.gp[:], False, False),
+                        mm(T[bk][:, gs], T.top[:, c0 - 1:c0 + 127], T.gn[:], False, ib in (LB - 1, 31))]
+            k = tops.index(key)
+            op("P", fns, r=[key, tops[k - 1] if k else "pad", "kb"], w=["gain" + key], banks=[bk])
 
         def fix(c, e):
             op("V", tt(T.zrep[:, 512 * c:512 * e:32], T.xg[:, 512 * c:512 * e:32], T.zl[:, 128 * t + 16 * c:128 * t + 16 * e], A.min),
                r=["xF%d%s" % (k, x) for k in range(c, e) for x in "ab"] + ["Lz%d" % t], w=["zf%d" % k for k in range(c, e)])
-            if e == 8:
-                op("P", [mm(T.ph[0:8, 384 + 32 * j:416 + 32 * j], T.gp[:], T.zrep[:, 32 * j:4096:128], False, j == 3) for j in range(4)],
-                   r=["zf%d" % k for k in range(8)] + ["k3"], w=["s0"], banks=["ph"])
-                op("S", act(T.c0[0:8, :], T.ph[0:8, 384:512], F.Sign, bias=0.5), r=["s0"], w=["c0"], banks=["ph"])
 
-        def scan(c, part=""):
-            a, b = {"": (0, 16), "a": (0, 8), "b": (8, 16)}[part]
-            a, b = a + 16 * c, b + 16 * c
-            key = "top%d%s" % (c, part)
-            op("V", lambda: V.tensor_tensor_scan(T.top[:, PAD + 32 * a:PAD + 32 * b], T.xg[:, 32 * a:32 * b], T.zrep[:, 32 * a:32 * b], 0.0, A.max, A.min),
-               r=["x%s%d%s" % (x, c, y) for x in "FS" for y in part or "ab"] + ZR + ["zf%d" % c], w=[key])
-            fns = []
-            for ib in range(a // 4, b // 4):
-                c0 = PAD + 128 * ib
-                fns += [mm(T.pg[:, ib:256:32], T.top[:, c0:c0 + 128], T.gp[:], False, False),
-                        mm(T.pg[:, ib:256:32], T.top[:, c0 - 1:c0 + 127], T.gn[:], False, ib == 31)]
-            k = tops.index(key)
-            op("P", fns, r=[key, tops[k - 1] if k else "pad", "kb"], w=["gain" + key], banks=["pg"])
+        def row0():
+            op("P", [mm(T.pb[0:8, 384 + 32 * j:416 + 32 * j], T.gp[:], T.zrep[:, 32 * j:4096:128]) for j in range(4)],
+               r=["zf%d" % k for k in range(8)] + ["kb"], w=["s0"], banks=["pb"])
+            op("S", act(T.c0[0:8, :], T.pb[0:8, 384:512], F.Sign, bias=cf[0:8, 28:29]), r=["s0", "k5"], w=["c0"], banks=["pb"])
 
         seqS, seqV = SEQ0 if t == 0 else SEQ
         for x in seqV.split():
             if x[0] in "mao":
-                merge("F", x)
-            elif x == "A":
-                for y in seqS.split():
+                merge("F" if FIRST == "S" else "S", x)
+            elif x == "M":
+                op("V", tt(T.cF[:], T.pc[:, 128:256], T.lA1[:, 128 * t - 128:128 * t], A.max), r=["BF", "LAa%d" % t], w=["cF"], banks=["pc"])
+            elif x in "AZ":
+                for y in seqS.split("|")[x == "Z"].split():
                     gather("S", y)
             elif x in "bB":
                 base("SF"[x == "B"])
-            elif x == "M":
-                op("V", tt(T.cF[:], T.pc[:, 128:256], T.lA1[:, 128 * t - 128:128 * t], A.max), r=["BF", "BFp", "LAa%d" % t], w=["cF"], banks=["pc"])
-            elif x == "H":
-                upper_out(t - 1)
+            elif x[0] == "s":
+                scan(int(x[1]), x[2:])
             elif x[0] == "f":
                 fix(int(x[1]), int(x[-1]) + 1)
-            elif x[0] == "s":
-                scan(int(x[1]))
+            elif x == "r":
+                row0()
+            elif x == "c":
+                op("V", ts2(T.u3[:, 0:8 * LB], T.pg[:, 0:8 * LB], 0.0, cf[:, 21:22], A.is_lt, A.mult), r=gains[:early], w=["u3a"], banks=["pg"])
+            elif x[0] == "z":
+                spread_z(t, x[1], int(x[2:]))
             else:
                 gather("V", x)
-        scan(7, "a")
-        scan(7, "b")
-        op("P", mm(T.ph[:, 256:264], E, T.wgr[:]), r=tops + ["k3"], w=["v2"], banks=["ph"])
-        for h, bk in enumerate(KEYS):
-            op("P", mm(T[bk][:, 256:384], T.c0[0:8, :], T.kc0[0:8, 128 * h:128 * h + 128], False, False), r=["c0", "k4"], w=["key%d" % h], banks=[bk])
+        turn()
+        op("P", mm(T.pt[:, 384:392], E, T.wgr[:]), r=tops + ["kw"], w=["v2"], banks=["pt"])
 
-        op("P", [mm(T.pc[:, 0:128], T.ibf[:], zslot(t), True, False), mm(T.pc[:, 0:128], T.ibf[:], E, False, True)],
-           r=tops + ["Lz%d" % t, "kb"], w=["ze"], banks=["pc"])
-        nz = T.nzf[:] if last else T.nzb[:, 128 * t:128 * t + 128]
-        op("S", act(nz, T.pc[:, 0:128], F.Abs, bias=255.0, scale=-1.0), r=["ze"], w=["nz%d" % t], banks=["pc"])
-        if last:
-            send([(q - d, nz, T.zfin[:], "zf")], ["nz%d" % t])
-        else:
-            send([(q + 1, nz, zslot(t + 1), "z%d" % (t + 1))], ["nz%d" % t])
+        if t == 0:
+            op("S", act(T.hacc[:], T.pd[:, 0:128], F.Copy), r=["h0"], w=["hacc"], banks=["pd"])
+
+        def users():
+            op("P", [mm(T.pc[:, 0:128], T.ibf[:], zslot(t), True, False), mm(T.pc[:, 0:128], T.ibf[:], E, False, True)],
+               r=tops + ["Lz%d" % t, "ibf"], w=["ze"], banks=["pc"])
+            nz = T.nzf[:] if last else T.nzb[:, 128 * t:128 * t + 128]
+            op("S", act(nz, T.pc[:, 0:128], F.Abs, bias=255.0, scale=-1.0), r=["ze"], w=["nz%d" % t], banks=["pc"])
+            if last:
+                send([(q - d, nz, T.zfin[:], "zf")], ["nz%d" % t])
+            else:
+                send([(q + 1, nz, zslot(t + 1), "z%d" % (t + 1))], ["nz%d" % t])
 
         l0, o0 = 16 * t, 256 * t
         sl = slice(128 * t, 128 * t + 128)
         col, tot = T.col[:, 4 * t:4 * t + 4], T.tot[:, t:t + 1]
         a3, dlo, dhi = T.o1[:, sl], T.dd[:, o0:o0 + 128], T.dd[:, o0 + 128:o0 + 256]
 
-        for h, bk in enumerate(KEYS):
-            hs = slice(128 * h, 128 * h + 128)
-            op("V", ts2(T.u3[:, hs], T.pg[:, hs], 0.0, cf[:, 21:22], A.is_lt, A.mult), r=["gain" + k for k in tops], w=["u3%d" % h], banks=["pg"])
-            op("P", [mm(T[bk][32 * j:32 * j + 32, 256 + 32 * x:288 + 32 * x], T.u3[:, 128 * h + 32 * x:128 * h + 32 * x + 32], T.tri[:, 32 * j:32 * j + 32], False, x == 3)
-                     for x in range(4) for j in range(4)], r=["u3%d" % h, "k3"], w=["key%d" % h], banks=[bk])
-        op("P", [mm(T.pd[:, 384:512], T.c0[0:8, :], T.gp16[0:8, :], True, False)]
-           + [mm(T.pd[32 * j:32 * j + 32, 384 + 16 * x:400 + 16 * x], T.u3[:, 32 * x:32 * x + 32], T.sgj[:, 16 * j:16 * j + 16], False, x == 7)
-              for x in range(8) for j in range(4)]
-           + [mm(T.pd[:, 0:256], T.ones[:], T.u3[:], True, False), mm(T.pd[:, 0:128], T.mh[0:8, :], T.c0[0:8, :], False, True)] * (not last),
-           r=["u30", "u31", "c0", "k3", "ones"], w=["ab"], banks=["pd"])
-        op("S", [act(T.s1[:, sl], T.pd[:, 384:512], F.Sign, scale=-1.0), act(T.s2[:, sl], T.pd[:, 384:512], F.Sign, bias=-1.0)],
-           r=["ab"], w=["s1", "s2"], banks=["pd"])
-        send([(q + 1 if last else q + d + 2, T.s2[:, sl], T.lT[:, sl], "T%d" % d)], ["s2"])
-        if last:
-            send([(q - d, T.s1[:, sl], T.lT[:, 384:512], "TL")], ["s1"])
-        else:
-            op("S", act(T.junk[:], T.pd[:, 0:256], F.Identity, accum_out=tot), r=["ab"], w=["tot"], banks=["pd"])
-            op("S", [act(T.tot[:, 4 + t:5 + t], tot, F.Identity, scale=-1.0)] + [act(T.tot[:, 6:7], tot, F.Identity, bias=T.tot[:, 4:5])] * t,
-               r=["tot"], w=["ntot"])
-            op("S", [act(T.tlf[:, a:b], T.jq[:, a:b], F.Identity, bias=T.tot[:, c:c + 1])
-                     for a, b, c in ((0, 8, 4 + t), (8, 17, t), (17, 18, 6 * t), (18, 20, 4 + t))], r=["ntot", "kc"], w=["tlf"])
-
-        def after_v():
-            op("V", tcopy(T.ha[:], T.ph[:, 256:264]), r=["v2"], w=["ha"], banks=["ph"])
-            op("P", [mm(T.pb[:, j:128:4], T.imk[:], T.basF[:, 32 * j:32 * j + 32], j == 0, False) for j in range(4)], r=["basF", "k1"], w=["ht0"], banks=["pb"])
-            op("P", mm(T.pb[:, 0:128], T.s1[:, sl], T.prin[:], False, False), r=["s1", "k2"], w=["ht0"], banks=["pb"])
+        def clicks():
+            op("V", ts2(T.u3[:, 8 * LB:256], T.ph[:, 8 * LB:256], 0.0, cf[:, 21:22], A.is_lt, A.mult), r=gains[early:], w=["u3b"], banks=["ph"])
+            if t == 0:
+                op("V", ts2(T.sgj[:], T.j8[:], cf[:, 4:5], cf[:, 18:19], A.is_equal, A.mult), r=["g16", "ka"], w=["k3"])
+            for h, bk in enumerate(KEYS):
+                op("P", mm(T[bk][:, 256:384], T.c0[0:8, :], T.kc0[0:8, 4 * h:4 * h + 4], False, False), r=["c0", "k4"], w=["key%d" % h], banks=[bk], acc=True)
+            for h, bk in enumerate(KEYS):
+                op("P", [mm(T[bk][32 * j:32 * j + 32, 256 + 32 * x:288 + 32 * x], T.u3[:, 4 * h + x:256:8], T.tri[:, 32 * j:32 * j + 32], False, x == 3)
+                         for x in range(4) for j in range(4)], r=["u3a", "u3b", "tri"], w=["key%d" % h], banks=[bk], acc=True)
+            users()
+            if not last:
+                op("P", [mm(T.pg[:, 256:512], T.ones[:], T.u3[:], True, False), mm(T.pg[:, 256:384], T.mh[0:8, :], T.c0[0:8, :], False, True)],
+                   r=["u3a", "u3b", "c0", "ones"], w=["sum"], banks=["pg"])
+                op("S", act(T.junk[:], T.pg[:, 256:512], F.Identity, accum_out=tot), r=["sum"], w=["tot"], banks=["pg"])
+            op("P", [mm(T.pd[:, 384:512], T.c0[0:8, :], T.gp16[0:8, :], True, False)]
+               + [mm(T.pd[32 * j:32 * j + 32, 384 + 16 * x:400 + 16 * x], T.u3[:, x:256:8], T.sgj[:, 16 * j:16 * j + 16], False, x == 7)
+                  for x in range(8) for j in range(4)], r=["u3a", "u3b", "c0", "k3", "g16"], w=["ab"], banks=["pd"])
+            op("S", [act(T.s1[:, sl], T.pd[:, 384:512], F.Sign, scale=-1.0), act(T.s2[:, sl], T.pd[:, 384:512], F.Sign, bias=-2.0)],
+               r=["ab"], w=["s1", "s2"], banks=["pd"])
+            send([(q + 1 if last else q + d + 2, T.s2[:, sl], T.lT[:, sl], "T%d" % d)], ["s2"])
+            if last:
+                send([(q - d, T.s1[:, sl], T.lT[:, 384:512], "TL")], ["s1"])
+            op("P", [mm(T.pb[:, j:128:4], T.imk[:], T.basF[:, 32 * j:32 * j + 32], j == 0, False) for j in range(4)], r=["basF", "k1"], w=["ht"], banks=["pb"])
+            op("P", mm(T.pb[:, 0:128], T.s1[:, sl], T.prin[:], False, False), r=["s1", "k2"], w=["ht"], banks=["pb"], acc=True)
+            if last:
+                op("P", [mm(T.pg[:, 0:128], T.mh[0:8, :], T.ce[0:8, 0:128], True, False), mm(T.pg[:, 0:128], T.pri[:, 3], T.s1[:, sl], False, True)],
+                   r=["s1", "k1", "kcl"], w=["sk"], banks=["pg"])
 
         def old_list():
-            op("V", tt(T.hpad[:, 15:128:16], T.hc[:], T.hb[:], A.add), r=["hc", "hb"], w=["hpad"])
-            op("P", mm(T.pb[:, 0:128], T.hpad[:], T.idf[:], False, True), r=["hpad", "k1"], w=["ht"], banks=["pb"])
-            op("S", act(a3, T.pb[:, 0:128], F.Identity, bias=cf[:, 12:13]), r=["ht0", "ht", "k3"], w=["a3"], banks=["pb"])
+            if last:
+                op("V", tcopy(T.hpad[:, 15:128:16], T.hc[:]), r=["hc"], w=["hpad"])
+            else:
+                op("V", tt(T.hpad[:, 15:128:16], T.hc[:], T.hb[:], A.add), r=["hc", "hb"], w=["hpad"])
+            op("P", mm(T.pb[:, 0:128], T.hpad[:], T.idf[:], False, True), r=["hpad", "k1"], w=["ht"], banks=["pb"], acc=True)
+            op("S", act(a3, T.pb[:, 0:128], F.Identity, bias=cf[:, 11:12] if last else cf[:, 12:13]), r=["ht", "k0", "k6"], w=["a3"], banks=["pb"])
             if last:
                 send([(q - d, a3, T.lAE[:], "AE")], ["a3"])
             else:
-                send([(q - d - 1, a3, T.lA2[:, sl], "Ab%d" % d), (q + 1, a3, T.lA1[:, sl], "Aa%d" % d)], ["a3"])
-                op("P", [mm(T.ph[:, 264:272], T.ww[:, 15 - c:143 - c], T.top[:, PAD + 32 * c + 31:PAD + 4096:512], c == 0, c == 15)
-                         for c in range(16)], r=tops + ["k3"], w=["vd"], banks=["ph"])
-                spread_z(d, "S", 0, ZS)
-                spread_z(d, "G", ZS, ZS + ZG)
+                send([(q - d - 1, a3, T.lA2[:, sl], "Ab%d" % d)], ["a3"])
+                send([(q + 1, a3, T.lA1[:, sl], "Aa%d" % d)], ["a3"])
+                op("P", [mm(T.pt[:, 392:400], T.ww[:, 15 - c:143 - c], T.top[:, PAD + 32 * c + 31:PAD + 4096:512], c == 0, c == 15)
+                         for c in range(16)], r=tops + ["kw"], w=["vd"], banks=["pt"])
+
 
         def far_order():
             if t:
-                order(*((T.r1, T.r1b, T.lc[:, 6:7], "LcE", "r4") if last else (T.r3, T.r3b, T.lc[:, 2:3], "LcF", "r3")))
+                order(*((T.r1, T.r1b, T.lc[:, 4:5], "LcE", "r4", T.jb, 65 * 8192.0) if last else (T.r3, T.r3b, T.lc[:, 0:1], "LcF", "r3")))
 
-        def upper():
-            op("V", tt(dhi, T.n6[:, :, 0, 1:5], T.n6[:, :, 1, 1:5], A.max), r=["o5_0", "o5_1", "o6_0", "o6_1"], w=["up"])
-            if last:
-                send([(q + 1, dhi, T.lE2[:, 128:256], "Ub")], ["up"])
-                send([(q - d, dhi, T.lE1[:, 128:256], "Ua")], ["up"])
+        def upper(x):
+            op("V", tt(T.dd[:, o0 + 128 + 64 * x:o0 + 192 + 64 * x], T.n6[:, x, 4:8, 0:4], T.n6[:, x, 4:8, 4:8], A.max), r=["o5_%d" % x, "o6_%d" % x], w=["up%d" % x])
+            if last and x:
+                send([(q + 1, dhi, T.lE2[:, 128:256], "Ub")], ["up0", "up1"])
+
+        def lost(x):
+            c = slice(64 * x, 64 * x + 64)
+            op("V", tt(T.ua[:, c], T.pg[:, c], T.dd[:, o0 + 128 + 64 * x:o0 + 192 + 64 * x], A.add), r=["sk", "up%d" % x], w=["ua%d" % x], banks=["pg"])
+            if x:
+                send([(q - d, T.ua[:], T.lE1[:, 128:256], "Ua")], ["ua0", "ua1"])
 
         def sink():
-            op("S", act(T.cF[:], T.lT[:, 384:512], F.Identity, scale=-3.5 * UP, bias=-2.5 * UP), r=["LTL"], w=["cF"])
-            op("V", tt(T.cS[:], T.cF[:], T.hacc[:], A.add), r=["cF", "hacc"], w=["cS"])
+            T3, TL = T.lT[:, 256:384], T.lT[:, 384:512]
+            op("S", [lin(ce(nT), TL, -1.0, -1.0), lin(ce(pT), TL, 1.0, 2.0), lin(ce(rneg), T.r1[:], -8192.0)], r=["LTL", "r4"], w=["nT"])
+            op("S", lin(ce(nT3), T3, -1.0, -1.0), r=["LT3"], w=["nT3"])
+            op("P", [mm(T.ph[:, 0:128], T.pri[:, 3], ce(pT), True, False), mm(T.ph[:, 0:128], T.rhb[:], T3, False, True)], r=["rh", "LT3", "nT"], w=["sc"], banks=["ph"])
+            for x, bk in enumerate(("pc", "pd")):
+                c = slice(64 * x, 64 * x + 64)
+                op("P", [mm(T[bk][:, 0:64], T.rhb[:], T.lT[:, 256 + 64 * x:320 + 64 * x], True, False), mm(T[bk][:, 0:64], T.pri[:, 3], ce(nT + 64 * x, 64), False, False),
+                         mm(T[bk][:, 0:64], T.mh[0:8, :], T.ce[0:8, c], False, False)], r=["rh", "LT3", "nT"], w=["U%d" % x], banks=[bk])
+            op("P", [mm(T.pt[:, 0:128], T3, T.r1b[:], True, False), mm(T.pt[:, 0:128], TL, ce(c65), False, False)], r=["r4", "k2"], w=["B"], banks=["pt"])
+            for x, bk in enumerate(KEYS):
+                op("P", mm(T[bk][:, 128:192], TL, ce(c130 + 64 * x, 64), True, False), r=["LTL", "k2"], w=["A%d" % x], banks=[bk])
+            for x, bk in enumerate(("pc", "pd")):
+                op("P", mm(T[bk][:, 0:64], T.rh[:], T.lE2[:, 128 + 64 * x:192 + 64 * x], False, True), r=["LUb"], w=["U%d" % x], banks=[bk], acc=True)
+
+        def beaten(x):
+            c, bk = slice(64 * x, 64 * x + 64), ("pc", "pd")[x]
+            op("V", tt(T.hx[:, c], T[bk][:, 0:64], T.cS[:, c], A.max), r=["U%d" % x, "cS"], w=["hx%d" % x], banks=[bk])
 
         side = {
-            "ha": after_v,
+            "ha": lambda: op("V", tcopy(T.ha[:], T.pt[:, 384:392]), r=["v2"], w=["ha"], banks=["pt"]),
             "hb": lambda: op("V", ts1(T.hb[:], T.ha[:], 4095, A.bitwise_and), r=["ha"], w=["hb"]),
             "hh": lambda: op("V", tt(T.ha[:], T.hb[:], T.hb[:], A.mult), r=["hb"], w=["ha"]),
             "hc": lambda: op("V", ts2(T.hc[:], T.ha[:], 4, 8191, A.arith_shift_right, A.bitwise_and), r=["ha"], w=["hc"]),
-            "hp": old_list, "far": far_order, "up": upper, "j0": lambda: t and keep(t - 1, 0), "j1": lambda: t and keep(t - 1, 1), "j2": sink,
-            "tl": lambda: op("V", tcopy(T.tl[:], T.tlf[:]), r=["tlf"], w=["tl"]),
-            "tm": lambda: op("V", ts1(T.tl2[:], T.tl[:], 127, A.bitwise_and), r=["tl"], w=["tl2"]),
-            "tn": lambda: op("V", [tcopy(T.lst[:, l0:l0 + 16], T.tl2[:, 0:16]), tcopy(col, T.tl2[:, 16:20])], r=["tl2"], w=["lst%d" % t]),
-            "r2": lambda: order(T.r2, T.r2b, T.col[:, 4 * t + 1:4 * t + 2], "lst%d" % t, "r2"),
-            "r1": lambda: t and order(T.r1, T.r1b, T.col[:, 4 * t:4 * t + 1], "lst%d" % t, "r1"),
-            "rh": lambda: t and order(T.rh, T.rhb, T.lc[:, 6:7] if last else T.col[:, 2:3], "LcE" if last else "lst0", "rh", T.jp, (2 * t + 1) * UP),
-            "pa": lambda: op("V", tcopy(T.pa_[:], T.ph[:, 264:272]), r=["vd"], w=["pa_"], banks=["ph"]),
+            "hp": old_list, "far": far_order, "p0": lambda: upper(0), "p1": lambda: upper(1), "j0": lambda: t and keep(t - 1, 0), "j1": lambda: t and keep(t - 1, 1), "j2": sink,
+            "j3": lambda: op("V", tt(T.cS[:], T.mS[:], T.ph[:, 0:128], A.subtract), r=["sc", "kept"], w=["cS"], banks=["ph"]),
+            "j4": lambda: op("V", ts1(T.mS[:], T.mF[:], (1 << 19) - 1, A.bitwise_and), r=["hacc"], w=["kept"]),
+            "q0": lambda: lost(0), "q1": lambda: lost(1),
+            "hd": lambda: op("V", tt(T.ha[:], T.hc[:], T.hb[:], A.add), r=["hc", "hb"], w=["ha"]),
+            "he": lambda: op("V", ts1(T.hc[:], T.ha[:], 8191, A.bitwise_and), r=["ha"], w=["hc"]),
+            "tl": lambda: op("V", ts1(T.tl[:, 0:10], T.jq[:, 0:10], tot, A.subtract), r=["tot", "kd"], w=["tl"]),
+            "tk": lambda: op("V", [ts1(T.tl[:, 10:12 - t], T.jq[:, 10:12 - t], tot, A.add)]
+                             + [ts2(T.tl[:, 11:12], T.jq[:, 11:12], tot, T.tot[:, 0:1], A.add, A.subtract)] * t, r=["tot", "kd"], w=["tk"]),
+            "tm": lambda: op("V", ts1(T.tl2[:], T.tl[:], 127, A.bitwise_and), r=["tl", "tk"], w=["tl2"]),
+            "tn": lambda: op("V", [tcopy(col, T.tl2[:, 8:12]), tcopy(T.lst[:, l0:l0 + 8], T.tl2[:, 0:8])], r=["tl2"], w=["lst%d" % t]),
+            "r2": lambda: order(T.r2, T.r2b, T.col[:, 4 * t + 3:4 * t + 4], "lst%d" % t, "r2"),
+            "r1": lambda: t and order(T.r1, T.r1b, T.col[:, 4 * t + 2:4 * t + 3], "lst%d" % t, "r1"),
+            "rh": lambda: t and order(T.rh, T.rhb, T.lc[:, 4:5] if last else T.col[:, 0:1], "LcE" if last else "lst0", "rh", T.jp, UP if last else 3 * UP),
+            "pa": lambda: op("V", tcopy(T.pa_[:], T.pt[:, 392:400]), r=["vd"], w=["pa_"], banks=["pt"]),
             "pb": lambda: op("V", ts1(T.pb_[:], T.pa_[:], 63, A.bitwise_and), r=["pa_"], w=["pb_"]),
-            "pc": lambda: op("V", tt(T.pc_[:], T.pb_[:], T.plb[:], A.add), r=["pb_", "kc"], w=["pc_"]),
+            "pc": lambda: op("V", tt(T.pc_[:], T.pb_[:], T.plb[:], A.add), r=["pb_", "kb"], w=["pc_"]),
             "pl": lambda: op("V", tcopy(T.pl[:], T.pc_[:]), r=["pc_"], w=["pl"]),
             "X": lambda: op("V", tcopy(T.X[:].indirect(T.pl[:]), E), r=["pl"] + tops, w=["X"]),
-            "cS": lambda: op("V", tt(T.cS[:], T.pt[:, 0:128], T.hx[:], A.max), r=["BS", "BSp", "hx"], w=["cS"], banks=["pt"]),
+            "H": lambda: upper_out(t),
+            "u0": lambda: beaten(0), "u1": lambda: beaten(1),
+            "cS": lambda: op("V", tt(T.cS[:], T.pt[:, 0:128], T.hx[:], A.max), r=["BS", "hx"], w=["cS"], banks=["pt"]),
         }
         for x in (LAST if last else NET).split():
             if x in side:
                 side[x]()
+            elif x[0] == "z":
+                spread_z(d, x[1], int(x[2:]))
+            elif x == "B":
+                base("F")
+            elif x == "C":
+                clicks()
             elif x[0] == "k":
                 h = int(x[1])
-                op("V", tcopy(T.ki[:, 4 * h:4 * h + 4], T[KEYS[h]][:, 256:384]), r=["key%d" % h], w=["o-1_%d" % h], banks=[KEYS[h]])
+                op("V", tcopy(T.ki[:, 128 * h:128 * h + 128], T[KEYS[h]][:, 256:384]), r=["key%d" % h], w=["o-1_%d" % h], banks=[KEYS[h]])
             else:
                 step(int(x[0], 16), int(x[1]), o0)
         lo = ["o12_0", "o12_1"]
@@ -542,62 +613,81 @@ def rank_program(g, core, T, topo):
             send([(q - d, dlo, T.lE1[:, 0:128], "Ea")], lo)
             break
 
-        send([(q - d - 1, dlo, T.lS[:, sl], "S%d" % d)], lo)
-        send([(q + d + 2, dlo, T.lF2[:, sl], "Fb%d" % d)], lo)
-        send([(q + 1, dlo, T.lF1[:, sl], "Fa%d" % d)], lo)
+        lists = [(q - d - 1, dlo, T.lS[:, sl], "S%d" % d), (q + d + 2, dlo, T.lF2[:, sl], "Fb%d" % d), (q + 1, dlo, T.lF1[:, sl], "Fa%d" % d)]
+        if "Fa1" in RELAYED:
+            send([lists[0], lists[2]], lo)
+            send([lists[1]], lo)
+        else:
+            for x in lists:
+                send([x], lo)
         send([(q + 1, col, T.lc[:, 4:8], "cE") if t else (q + 4, col, T.lc[:, 0:4], "cF")], ["lst%d" % t])
 
         minus_threshold()
-        op("S", act(T.hx[:], T.lA2[:, sl].indirect(T.lst[:, l0:l0 + 8]), F.Copy), r=["LAb%d" % d, "lst%d" % t], w=["hx"])
-        fallback(T.pt[:, 0:128], "pt", T.s2[:, sl], "s2", T.r2, T.r2b, "r2", T.hx[:], "hx", T.sgS[:], dlo, lo, "BS")
+        rF, rFb, kF = (T.r3, T.r3b, "r3") if t else (T.p0, T.pb21, "k2")
+        r1, k1 = (T.r1, "r1") if t else (T.r2, "r2")
+        addF = []
         for x in HOP.split():
             if x in side:
                 side[x]()
-                continue
-            if x[0] == "z":
-                spread_z(d, x[1], int(x[2]), int(x[3]))
-                continue
-            if x == "ma":
-                r1, k1 = (T.r1, "r1") if t else (T.r2, "r2")
+            elif x[0] == "z":
+                spread_z(d, x[1], int(x[2:]))
+            elif x == "gS":
+                op("S", act(T.hx[:], T.lA2[:, sl].indirect(T.lst[:, l0:l0 + 8]), F.Copy), r=["LAb%d" % d, "lst%d" % t], w=["hx"])
+                for fn in fallback(T.pt[:, 0:128], "pt", T.s2[:, sl], "s2", T.r2, T.r2b, "r2", T.hx[:], "hx", T.sgS[:], dlo, lo, "BS"):
+                    fn()
+            elif x == "gF":
+                addF += fallback(T.pc[:, 128:256], "pc", T.lT[:, sl], "LT%d" % d, rF, rFb, kF, T.lA1[:, sl], "LAa%d" % d, T.sgF[:], T.lF2[:, sl],
+                                 ["LFb%d" % d], "BF")
+            elif x == "M":
+                op("V", tt(T.cF[:], T.pc[:, 128:256], T.lA1[:, sl], A.max), r=["BF", "LAa%d" % d], w=["cF"], banks=["pc"])
+            elif x == "PS":
                 for y, a, b in PARTS:
                     op("P", mm(psS[y][0], T.lS[:, sl], r1[:, a:b]), r=["LS%d" % d, k1], w=["AS" + y], banks=[psS[y][1]])
-                rF, rFb, kF = (T.r3, T.r3b, "r3") if t else (T.p0, T.pb21, "k2")
-                fallback(T.pc[:, 128:256], "pc", T.lT[:, sl], "LT%d" % d, rF, rFb, kF, T.lA1[:, sl], "LAa%d" % d, T.sgF[:], T.lF2[:, sl], ["LFb%d" % d], "BF")
+            elif x == "PF":
+                for fn in addF:
+                    fn()
                 for y, a, b in PARTS:
                     op("P", mm(psF[y][0], T.lF1[:, sl], T.p0[:, a:b]), r=["LFa%d" % d, "k2"], w=["AF" + y], banks=[psF[y][1]])
-            merge("S", x)
+            else:
+                merge(FIRST, x)
 
-    wait("Y", [lastw["Lzf"]])
+    wait("Y", [lastw["Lzf"], lastw["LEa"]])
     op("Y", lambda: Y.dma_start(T.yz[:], T.zfin[:]), w=["yz"], inc=16)
-    op("P", [mm(T.pc[:, 0:128], T.rhb[:], T.lT[:, 256:384], True, False), mm(T.pc[:, 0:128], T.idf[:], T.cF[:], False, False)],
-       r=["rh", "LT3", "cF"], w=["U2"], banks=["pc"])
-    op("P", mm(T.pc[:, 0:128], T.rh[:], T.lE2[:, 128:256], False, True), r=["LUb"], w=["U2"], banks=["pc"])
-    fallback(T.pt[:, 0:128], "pt", T.lT[:, 256:384], "LT3", T.r1, T.r1b, "r4", T.lAE[:], "LAE", T.sgS[:], T.lE2[:, 0:128], ["LEb"], "B")
-    op("P", mm(T.pu[:, 0:128], T.lE1[:, 0:128], T.p0[:]), r=["LEa", "k2"], w=["A"], banks=["pu"])
-    side = {
-        "u1": lambda: op("V", tt(T.hx[:], T.pc[:, 0:128], T.cS[:], A.max), r=["U2", "cS"], w=["hx"], banks=["pc"]),
-        "u2": lambda: op("V", tt(T.n7[:], T.lE1[:, 128:256], T.hx[:], A.max), r=["LUa", "hx"], w=["o7_0", "o7_1"]),
-        "fb": lambda: op("V", tt(T.fb[:], T.pt[:, 0:128], T.lAE[:], A.max), r=["B", "Bp", "LAE"], w=["fb"], banks=["pt"]),
-        "l0": lambda: op("V", tt(T.mF[:], T.pu[:, 0:128], T.fb[:], A.max), r=["A", "fb"], w=["l0"], banks=["pu"]),
-        "l1": lambda: op("V", ts1(T.fi[:], T.mF[:], 8191, A.bitwise_and), r=["l0"], w=["l1"]),
-        "l2": lambda: op("V", tcopy(T.yo[:, 0:256:2], T.fi[:]), r=["l1"], w=["l2"]),
-    }
-    for x in END.split():
-        if x in side:
-            side[x]()
-            continue
-        step(int(x[0], 16), int(x[1]), 128)
-        if x[0] == "c":
-            c = 64 * int(x[1])
-            op("S", act(T.sgF[:, c:c + 64], T.dd[:, 128 + c:192 + c], F.Identity, scale=2.0 ** -13, bias=cf[:, 27:28]), r=["o12_" + x[1]], w=["f" + x[1]])
+    op("P", [mm(T.pb[:, 0:128], T.idf[:], T.lAE[:], True, False), mm(T.pb[:, 0:128], ce(nT3), T.r1b[:], False, True)], r=["LAE", "nT3", "r4"], w=["C"], banks=["pb"])
+    op("S", act(T.cF[:], T.pb[:, 0:128], F.Copy), r=["C"], w=["cF"], banks=["pb"])
+    op("S", lin(T.sgS[:], T.lE2[:, 0:128], 2.0 ** -13, cf[:, 27:28]), r=["LEb"], w=["hiB"])
+    op("P", mm(T.pt[:, 0:128], T.lE2[:, 0:128], T.r1[:], False, False), r=["LEb"], w=["B"], banks=["pt"], acc=True)
+    op("P", mm(T.pt[:, 0:128], T.sgS[:], ce(rneg), False, True), r=["hiB", "nT"], w=["B"], banks=["pt"], acc=True)
     halves = [(k, slice(64 * k, 64 * k + 64), ("pb", "ph")[k]) for k in (0, 1)]
-    for k, c, bk in halves:
-        op("P", mm(T[bk][:, 0:64], T.dd[:, 128:256], T.p0[:, c], True, False), r=lo + ["k2"], w=["H%d" % k], banks=[bk])
-    for k, c, bk in halves:
-        op("P", mm(T[bk][:, 0:64], T.sgF[:], T.pri[:, 2, c], False, True), r=["f0", "f1"], w=["H%d" % k], banks=[bk])
-    for k, c, bk in halves:
-        op("V", ts1(T.yo[:, 128 * k + 1:128 * k + 128:2], T[bk][:, 0:64], 130 * 8192.0, A.add), r=["H%d" % k], w=["yo%d" % k], banks=[bk])
-        op("SY"[k], lambda: (S, Y)[k].dma_start(T.ya[:, 128 * k:128 * k + 128], T.yo[:, 128 * k:128 * k + 128]), r=["yo%d" % k, "l2"], w=["ya%d" % k], inc=16)
+    for x in END.split():
+        k, c, bk = halves[int(x[1])]
+        if x[0] == "u":
+            op("V", tt(T.nb[:, 4 * k:4 * k + 4], T.lE1[:, 128 + 64 * k:192 + 64 * k], T.hx[:, c], A.max), r=["LUa", "hx%d" % k], w=["o8_%d" % k])
+        elif x[0] == "f":
+            op("V", tt(T.fb[:, c], T.pt[:, c], T.cF[:, c], A.max), r=["B", "cF"], w=["fb%d" % k], banks=["pt"])
+        elif x[0] == "h":
+            op("V", ts2(T.hiA[:], T.lE1[:, 0:128], 2.0 ** -13, 129.5 + 2.0 ** -14, A.mult, A.add), r=["LEa"], w=["hiA"])
+            for k, c, bk in halves:
+                op("P", mm(T[KEYS[k]][:, 128:192], T.lE1[:, 0:128], T.p0[:, c], False, False), r=["LEa"], w=["A%d" % k], banks=[KEYS[k]], acc=True)
+            for k, c, bk in halves:
+                op("P", mm(T[bk][:, 0:64], T.dd[:, 128:256], T.p0[:, c], True, False), r=lo + ["k2"], w=["H%d" % k], banks=[bk])
+            for k, c, bk in halves:
+                op("P", mm(T[KEYS[k]][:, 128:192], T.hiA[:], T.pri[:, 2, c], False, True), r=["hiA"], w=["A%d" % k], banks=[KEYS[k]], acc=True)
+        elif x[0] == "g":
+            op("V", ts2(T.sgF[:, c], T.dd[:, 128 + 64 * k:192 + 64 * k], 2.0 ** -13, 129.5 + 2.0 ** -14, A.mult, A.add), r=["o12_" + x[1]], w=["f" + x[1]])
+            if k:
+                for k, c, bk in halves:
+                    op("P", mm(T[bk][:, 0:64], T.sgF[:], T.pri[:, 2, c], False, True), r=["f0", "f1"], w=["H%d" % k], banks=[bk], acc=True)
+        elif x[0] == "y":
+            op("V", ts1(T.yo[:, 128 * k + 1:128 * k + 128:2], T[bk][:, 0:64], 130 * 8192.0, A.add), r=["H%d" % k], w=["yo%d" % k], banks=[bk])
+        elif x[0] == "m":
+            op("V", tt(T.yo[:, 128 * k:128 * k + 128:2], T[KEYS[k]][:, 128:192], T.fb[:, c], A.max), r=["A%d" % k, "fb%d" % k], w=["l2%d" % k], banks=[KEYS[k]])
+        elif x[0] == "s":
+            op("SY"[k], lambda: (S, Y)[k].dma_start(T.ya[:, 128 * k:128 * k + 128], T.yo[:, 128 * k:128 * k + 128]),
+               r=["yo%d" % k, "l2%d" % k], w=["ya%d" % k], inc=16)
+        else:
+            step(int(x[0], 16), k, 128)
+
     for s in cnt:
         if s[0] != "Y" and waited.get(s, 0) < cnt[s]:
             g.wait_ge(T.sem[s], cnt[s])

from concourse.bass import DstId, RemoteDMATransfer
from concourse.mybir import AluOpType, ActivationFunctionType

A = AluOpType
F = ActivationFunctionType
XP = [0, 4096, 5632, 8192]
N, RO, PAD, LB = 8, 3, 2, 24
TAG = float(1 << 19)
UP = float(1 << 21)
f32, bf, i32, u16 = "float32", "bfloat16", "int32", "uint16"


def sb(shape, d):
    return ("sbuf", [128] + list(shape), d)


SCRATCH = {
    "X": sb([8192], bf), "xg": sb([4096], bf), "zrep": sb([4096], bf), "top": sb([4096 + 16], bf),
    "rai": sb([256], i32), "zown": sb([128], bf), "wi": sb([256], i32), "wf": sb([256], f32), "lo0": sb([128], u16),
    "jf": sb([8], f32), "jb": sb([128], bf), "jp": sb([128], bf), "ci": sb([8], i32), "cf": sb([32], f32),
    "ibf": sb([128], bf), "p0": sb([128], f32), "pbp": sb([128], bf), "tri": sb([128], bf), "kc0": sb([8, 32], bf),
    "sgj": sb([64], bf), "gp16": sb([128], bf), "mh": sb([128], bf), "c0": sb([128], bf), "j8": sb([64], bf),
    "gp": sb([8], bf), "gn": sb([8], bf), "wgr": sb([8], bf), "ones": sb([128], bf),
    "onen": sb([128], f32), "ww": sb([144], bf), "tm": sb([256], f32),
    "jl": sb([8], f32), "jq": sb([12], f32), "ja": sb([8], i32), "pip": sb([8], u16), "plb": sb([8], i32),
    "zl": sb([384], bf), "zfin": sb([128], f32), "nzb": sb([256], bf), "nzf": sb([128], f32),
    "offF": sb([128], u16), "offS": sb([128], u16), "off0F": sb([128], u16), "off0S": sb([128], u16),
    "mF": sb([128], i32), "mS": sb([128], i32), "fi": sb([128], i32), "si": sb([128], i32),
    "basF": sb([128], f32), "basS": sb([128], f32), "u3": sb([256], bf), "imk": sb([128], f32),
    "ki": sb([256], i32), "km": sb([64, 2, 2], i32), "n1": sb([64, 2, 2], f32), "n3": sb([16, 2, 2, 6], f32),
    "n4": sb([32, 2, 4], f32), "n6": sb([2, 12, 8, 4], f32), "n7": sb([8, 16], i32), "nb": sb([8, 2, 2, 4], i32),
    "n8": sb([8, 2, 2, 4], f32), "n9": sb([8, 2, 2, 4], f32), "na": sb([8, 4, 2, 2], f32),
    "dd": sb([768], f32),
    "ha": sb([8], i32), "hb": sb([8], i32), "hc": sb([8], i32), "hpad": sb([128], f32),
    "s1": sb([384], bf), "s2": sb([384], bf), "pri": sb([4, 128], bf), "idf": sb([128], f32),
    "prin": sb([128], bf), "pb21": sb([128], bf), "ic3": sb([128], bf), "sgS": sb([128], bf), "sgF": sb([128], bf),
    "r1": sb([128], f32), "r2": sb([128], f32), "r3": sb([128], f32), "rh": sb([128], f32),
    "r1b": sb([128], bf), "r2b": sb([128], bf), "r3b": sb([128], bf), "rhb": sb([128], bf),
    "fb": sb([128], f32), "cS": sb([128], f32), "cF": sb([128], f32), "col": sb([12], f32), "lc": sb([8], f32),
    "lA1": sb([256], f32), "lA2": sb([256], f32), "lAE": sb([128], f32), "lT": sb([512], bf),
    "junk": sb([256], f32), "jk": sb([128], f32), "tot": sb([8], f32), "tl": sb([12], i32), "tl2": sb([12], i32), "lst": sb([32], u16),
    "pa_": sb([8], i32), "pb_": sb([8], i32), "pc_": sb([8], i32), "pl": sb([8], u16),
    "o1": sb([384], f32), "oh": sb([512], f32),
    "lS": sb([256], f32), "lF1": sb([256], f32), "lF2": sb([256], f32),
    "lH1": sb([256], f32), "lH2": sb([256], f32), "lE1": sb([256], f32), "lE2": sb([256], f32),
    "ua": sb([128], f32), "hiA": sb([128], bf), "ce": sb([7 * 128], bf),
    "hi0": sb([128], f32), "hacc": sb([128], f32),
    "hx": sb([128], f32), "yo": sb([256], f32),
    "pg": ("psum", [128, 512], f32), "pb": ("psum", [128, 512], f32),
    "pt": ("psum", [128, 512], f32), "ph": ("psum", [128, 512], f32),
    "pc": ("psum", [128, 512], f32), "pd": ("psum", [128, 512], f32),
    "pu": ("psum", [128, 512], f32), "pw": ("psum", [128, 512], f32),
}
POOL = {"V": 38, "S": 28, "P": 36, "G": 9, "Y": 7}
ARR = ["z0", "z1", "z2", "zf", "F0", "S0", "S1", "S2", "Fa1", "Fa2", "Fb1", "Fb2", "Ha0", "Ha1", "Hb0", "Hb1",
       "Ea", "Eb", "Ua", "Ub", "cF", "cE", "Aa1", "Aa2", "Ab1", "Ab2", "AE", "T1", "T2", "T3", "TL"]
SEMAPHORES = [q + str(k) for q in POOL for k in range(POOL[q])] + ["r" + a for a in ARR] + ["sent"]
SEQ0 = ["S03 S47 Fbf S8b Scd Se Sf",
        "A F03 F45 f01 F67 s0 f23 s1 F8a s2a s2b f47 r s3a s3b s4a s4b s5a s5b s6a s6b s7a s7c s7d B c"]
SEQ = ["S02 S49 | F23 F67 Fab Fcf Sa Se Sf",
       "A b S3 Sb ma mb Sc aa ab Sd oa ob Z F01 F45 f01 F89 s0 f23 s1 s2a s2b f45 s3a s3b s4a s4b f67 r s5a s5b s6a s6b s7a s7c s7d B c"]
NET = "C far rh ha j0 hb k0 hh k1 00 hc 01 10 11 20 21 30 hp tl 31 zS4 40 41 50 51 60 tk 61 70 tm 71 80 tn 81 90 pa r2 91 a0 pb r1 a1 b0 pc b1 c0 pl c1"
LAST = ("j0 C far rh ha j1 hb k0 hh k1 00 hc 01 10 hd 11 20 he 21 30 hp j2 31 40 41 50 51 60 j4 61 p0 70 p1 71 80 q0 81 q1 90 91 "
        "a0 a1 b0 b1 c0 c1 j3 u0 u1")
HOP = "gS gF zG3 p0 p1 zS5 H zG3 X zV8 cS j1 zV4 PS PF ma zV2 mb aa zV2 ab oa M ob"
FIRST = "S"
END = "u0 u1 90 91 a0 a1 b0 b1 c0 c1 h0 g0 g1 f0 f1 m0 y0 s0 m1 y1 s1"


RELAYED = ["T1", "Ha0", "Hb0", "T2", "Ha1", "Hb1", "zf", "T3", "AE"]


def helper(core, T, topo):
    return [c for c in topo.cores_of(core) if topo.die(c) != topo.die(core) and all(topo.may_write(c, x) for x in T.cores if x != core)][0]


def spare(core, T, topo):
    far = topo.engines(core, [x for x in T.cores if x != core][0])
    return [e for e in topo.engines(core, helper(core, T, topo)) if e not in far]


def helper_program(g, core, q, T, topo):
    land = {"T1": (q + 3, T.lT[:, 0:128]), "Aa1": (q + 1, T.lA1[:, 0:128]), "T2": (q + 4, T.lT[:, 128:256]),
            "Aa2": (q + 1, T.lA1[:, 128:256]), "Fa1": (q + 1, T.lF1[:, 0:128]), "Fa2": (q + 1, T.lF1[:, 128:256]), "T3": (q + 1, T.lT[:, 256:384]), "zf": (q - RO, T.zfin[:]), "AE": (q - RO, T.lAE[:]),
            "Ha0": (q - 1, T.lH1[:, 0:128]), "Hb0": (q + 1, T.lH2[:, 0:128]), "Ha1": (q - 2, T.lH1[:, 128:256]), "Hb1": (q + 1, T.lH2[:, 128:256])}
    n = 0
    for name in RELAYED:
        dst, ap = land[name]
        dc = T.cores[dst % N]
        rid, pid = topo.addr(dc)[:2]
        g.wait_ge(T.sem["r" + name], len(spare(T.cores[q], T, topo)))
        g.remote_dma(ap, ap, T.sem["r" + name], T.sem.sent, pid, rid, topo.mask(core, dc))
        n += len(topo.engines(core, dc))
    g.wait_ge(T.sem.sent, n)


def rank_program(g, core, T, topo):
    q = T.rank_of(core)
    if q is None:
        for r in range(N):
            if helper(T.cores[r], T, topo) == core:
                helper_program(g, core, r, T, topo)
        return
    V, S, P, Y = g.vector, g.scalar, g.tensor, g.sync
    Q = {"V": V, "S": S, "P": P, "G": g, "Y": Y}
    know = {k: {} for k in Q}
    cnt, waited, lastw, readers, bank = {}, {}, {}, {}, {}

    def wait(qn, deps):
        need = {}
        for e in deps:
            if know[qn].get(e[0], 0) < e[1] and (e[0] not in need or need[e[0]][1] < e[1]):
                need[e[0]] = e
        for s in sorted(need, key=lambda x: -len(need[x][2])):
            e = need[s]
            if know[qn].get(s, 0) >= e[1]:
                continue
            Q[qn].wait_ge(T.sem[s], e[1])
            waited[s] = max(waited.get(s, 0), e[1])
            know[qn][s] = e[1]
            for k, v in e[2].items():
                if know[qn].get(k, 0) < v:
                    know[qn][k] = v

    def deps_of(qn, r, w, banks):
        d = [lastw[k] for k in list(r) + list(w) if k in lastw]
        for k in w:
            d += readers.get(k, [])
        for b in banks:
            d += [e for o, e in bank.get(b, {}).items() if o != qn]
        return d

    def op(qn, fns, r=(), w=(), banks=(), inc=1, acc=False):
        wait(qn, deps_of(qn, r, () if acc else w, banks))
        s = lastw[w[0]][0] if acc else [x for x in (qn + str(k) for k in range(POOL[qn])) if know[qn].get(x, 0) == cnt.get(x, 0)][0]
        fns = fns if isinstance(fns, list) else [fns]
        for fn in fns:
            fn().then_inc(T.sem[s], inc)
        cnt[s] = cnt.get(s, 0) + inc * len(fns)
        e = (s, cnt[s], dict(know[qn]))
        for k in r:
            readers.setdefault(k, []).append(e)
        for k in w:
            lastw[k] = e
            readers[k] = []
        for b in banks:
            bank.setdefault(b, {})[qn] = e
        return e

    def send(parts, r):
        wait("G", deps_of("G", r, (), ()))
        ts = []
        direct = [x for x in parts if x[3] not in RELAYED]
        for dst, src, land, name in parts:
            dc = T.cores[dst % N]
            eng = topo.engines(core, dc)
            if name in RELAYED:
                dc = helper(core, T, topo)
                eng = spare(core, T, topo)
                m = len(eng)
            else:
                m = len(eng) // len(direct)
                k = [x[3] for x in direct].index(name)
                eng = eng[k * m:(k + 1) * m]
            mask = 0
            for e in eng:
                mask |= 1 << e
            rid, pid = topo.addr(dc)[:2]
            ts.append((rid, pid, mask, src, land, name))
            cnt["sent"] = cnt.get("sent", 0) + m
        if len(ts) == 1:
            rid, pid, mask, src, land, name = ts[0]
            g.remote_dma(land, src, T.sem["r" + name], T.sem.sent, pid, rid, mask)
        else:
            g.remote_dma_fused([RemoteDMATransfer(dst_ids=[DstId(rid=a, pnc=b)], dma_engine_mask=m, remote_sem=T.sem["r" + nm],
                                                  src=s, dst=l) for a, b, m, s, l, nm in ts], local_sem=T.sem.sent)

    def expect(name, src, share=1):
        n = len(topo.engines(T.cores[src % N], core)) // share
        cnt["r" + name] = n
        lastw["L" + name] = ("r" + name, n, {})

    def tcopy(o, i):
        return lambda: V.tensor_copy(o, i)

    def tt(o, a, b, x):
        return lambda: V.tensor_tensor(o, a, b, x)

    def ts1(o, a, s, x):
        return lambda: V.tensor_scalar(o, a, s, None, x)

    def ts2(o, a, s1, s2, x1, x2):
        return lambda: V.tensor_scalar(o, a, s1, s2, x1, x2)

    def fillc(o, c):
        return lambda: V.memset(o, c)

    def mm(o, l, r, st=True, sp=True):
        return lambda: P.matmul(o, l, r, st, sp)

    def act(o, i, fn, **kw):
        return lambda: S.activation(o, i, fn, **kw)

    def copy(qn, o, i):
        if qn == "G":
            return lambda: g.affine_select(o, i, [[0, 128]], A.is_ge, 0.0, 0, 0)
        return tcopy(o, i) if qn == "V" else act(o, i, F.Copy)

    expect("z0", q - 1)
    expect("F0", q - 1, 2)
    expect("S0", q + 1, 2)
    for t in (1, 2):
        expect("z%d" % t, q - 1)
        expect("S%d" % t, q + t + 1)
        expect("Fa%d" % t, q - 1)
        expect("Fb%d" % t, q - t - 2)
        expect("Aa%d" % t, q - 1)
        expect("Ab%d" % t, q + t + 1)
        expect("T%d" % t, q - t - 2)
        expect("Ha%d" % (t - 1), q + t)
        expect("Hb%d" % (t - 1), q - 1)
    for name in ("zf", "Ea", "Ua", "AE", "TL"):
        expect(name, q + RO)
    for name in ("Eb", "Ub", "cE", "T3"):
        expect(name, q - 1)
    expect("cF", q - 4)

    op("Y", lambda: Y.dma_start(T.zown[:], T.zu[:]), w=["zown"], inc=16)
    op("S", lambda: S.dma_start(T.rai[:], T.ra[:]), w=["rai"], inc=16)
    op("Y", lambda: Y.dma_start(T.wi[0:1, 0:128], T.wg[:]), w=["wi"], inc=16)
    op("S", lambda: S.dma_start(T.wi[0:1, 128:256], T.th[:]), w=["ti"], inc=16)
    op("Y", lambda: Y.dma_start(T.X[:, 0:XP[1]], T.xd[:, 0:XP[1]]), w=["X0"], inc=16)

    def lin(o, i, scale, bias=0.0):
        return act(o, i, F.Identity, scale=scale, bias=bias)

    def count(o, pattern, base=0):
        return lambda: g.iota(o, pattern, base, 0, allow_small_or_imprecise_dtypes=True)

    def where(o, i, pattern, x, fill=0.0, sign=1):
        return lambda: g.affine_select(o, i, pattern, x, fill, 0, sign)

    def ce(a, n=128):
        return T.ce[:, a:a + n]

    cf, ci, jf = T.cf, T.ci, T.jf
    op("V", [fillc(T.ones[:], 1.0), fillc(T.top[:, 0:PAD], 0.0), fillc(T.mh[:], -0.5), fillc(T.onen[:], -1.0)], w=["pad", "ones"])
    op("G", lambda: g.iota(ci[:, 0:1], [[0, 1]], 0, 1), w=["ci0"])
    op("G", [lambda: g.iota(T.ja[:], [[1, 4], [64, 2]], 0, 0), count(jf[:], [[1, 8]])], w=["ja", "jf"])
    op("G", where(T.ibf[:], T.ones[:], [[-1, 128]], A.is_equal), r=["ones"], w=["ibf"])

    op("V", [ts1(ci[:, 1:2], ci[:, 0:1], 15, A.bitwise_and), ts1(ci[:, 2:3], ci[:, 0:1], 4, A.arith_shift_right),
             ts1(ci[:, 3:4], ci[:, 0:1], 31, A.bitwise_and), ts1(ci[:, 4:5], ci[:, 0:1], 5, A.arith_shift_right),
             ts1(ci[:, 5:6], ci[:, 0:1], 1, A.bitwise_and)], r=["ci0"], w=["ci"])
    op("V", [fillc(T.hpad[:], 0.0), fillc(cf[:, 27:28], 129.5 + 2.0 ** -14), fillc(T.ww[:], 0.0),
             fillc(T.kc0[0:8, :, 0], -1.75 * TAG), fillc(T.kc0[0:8, :, 1:32], TAG / 2)], w=["hpad", "fill"])
    op("V", tcopy(T.lo0[:], T.rai[:, 0:256:2]), r=["rai"], w=["lo0"])
    op("V", [tcopy(cf[:, 0:5], ci[:, 0:5]), tcopy(cf[:, 7:8], ci[:, 5:6]), ts1(cf[:, 14:15], ci[:, 1:2], 15.0, A.not_equal),
             ts2(cf[:, 23:24], ci[:, 1:2], 15.0, -1.0, A.not_equal, A.mult), ts2(cf[:, 20:21], ci[:, 1:2], 0.0, 2.25 * TAG, A.is_equal, A.mult),
             ts1(cf[:, 21:22], ci[:, 3:4], 0.0, A.not_equal)], r=["ci", "ci0"], w=["cf"])
    send([(q + 1, T.zown[:], T.zl[:, 0:128], "z0")], ["zown"])
    send([(q + 1, T.lo0[:], T.off0F[:], "F0"), (q - 1, T.lo0[:], T.off0S[:], "S0")], ["lo0"])
    op("V", [fillc(T.tri[:, k:128:4], (3.5 - k) * TAG) for k in range(4)], w=["tri"])
    kcl, c130, c65, nT, pT, nT3, rneg = range(0, 7 * 128, 128)
    op("V", [fillc(T.ce[0:8, k:128:4], (x * TAG + UP) / 4) for k, x in enumerate((0, 2, 1, 3))], w=["kcl"])
    op("S", [lin(cf[:, 13:14], cf[:, 1:2], 4.0), lin(cf[:, 15:16], cf[:, 7:8], 2 * TAG, -TAG / 2), lin(cf[:, 18:19], cf[:, 7:8], 4.0, -2.0),
             lin(cf[:, 25:26], cf[:, 1:2], 8192.0), lin(cf[:, 10:11], cf[:, 3:4], 4.0, cf[:, 4:5]), lin(T.jl[:], jf[:, 0:8], 16.0, cf[:, 1:2])],
       r=["cf", "jf"], w=["ka"])
    op("S", [lin(cf[:, 22:23], cf[:, 1:2], 16384.0, cf[:, 15:16]), lin(T.jq[:, 0:8], T.jl[:], 1.0, 32768.0),
             lin(T.jq[:, 8:12], T.onen[:, 0:4], -32768.0, cf[:, 10:11])], r=["ka", "ones"], w=["kd"])
    op("S", [lin(cf[:, 6:7], cf[:, 22:23], 1.0, 8192.0 + TAG), lin(cf[:, 5:6], cf[:, 22:23], 1.0, cf[:, 20:21])], r=["kd"], w=["kc"])
    op("G", where(T.kc0[0:8], T.kc0[0:8], [[-1, 8], [0, 32]], A.is_equal), r=["fill"], w=["k4"])
    op("Y", lambda: Y.dma_start(T.X[:, XP[1]:XP[2]], T.xd[:, XP[1]:XP[2]]), r=["k4"], w=["X1"], inc=16)
    op("Y", lambda: Y.dma_start(T.X[:, XP[2]:XP[3]], T.xd[:, XP[2]:XP[3]]), r=["X0"], w=["X2"], inc=16)
    op("G", where(T.pbp[:], T.ones[:], [[-1, 32], [-32, 4]], A.is_equal), w=["pbp"])
    op("G", where(T.tri[:], T.tri[:], [[-1, 128]], A.is_equal, -TAG), w=["tri"])
    op("G", where(T.jk[:], T.ones[:], [[-4, 32], [-1, 2], [-2, 2]], A.is_equal), w=["jk"])
    op("G", where(T.tri[:], T.tri[:], [[1, 128]], A.is_ge, sign=-1), w=["tri"])
    op("V", tcopy(T.wf[0:1, :], T.wi[0:1, :]), r=["wi", "ti"], w=["wf"])
    op("P", [mm(T.pd[:, 8 + k:9 + k], T.wf[0:1, 128 * k:128 * k + 128], T.onen[0:1, 0:1]) for k in (0, 1)], r=["wf", "ones"], w=["wt"], banks=["pd"])
    op("V", [ts1(T.gp[:], jf[:, 0:8], cf[:, 2:3], A.is_equal), ts2(T.gn[:], jf[:, 0:8], cf[:, 2:3], -1.0, A.is_equal, A.mult),
             ts1(T.pip[:], T.ja[:], cf[:, 13:14], A.add), ts1(T.plb[:], T.jl[:], 64.0, A.mult),
             ts1(T.hi0[:], T.rai[:, 1:256:2], cf[:, 25:26], A.add)], r=["cf", "ci", "ka", "jf", "ja", "rai"], w=["kb", "pip"])
    op("S", [lin(cf[:, 8:9], T.pd[:, 8:9], -1.0), lin(cf[:, 9:10], T.pd[:, 9:10], -1.0 / 16), lin(cf[:, 12:13], cf[:, 5:6], cf[:, 23:24])],
       r=["wt", "kc"], w=["k0"], banks=["pd"])
    op("S", [lin(T.tm[:, 0:8], T.gp[:], cf[:, 9:10]), lin(T.wgr[:], T.gp[:], cf[:, 8:9]), lin(T.ww[:, 15:143:16], T.gp[:], cf[:, 8:9])],
       r=["kb", "k0", "fill"], w=["kw"])
    op("S", [lin(T.tm[:, 8 + x:256:8], T.onen[:, 0:31], 0.0, T.tm[:, x:x + 1]) for x in range(8)], r=["kw"], w=["tm"])
    op("V", [tcopy(T.idf[:], T.ibf[:]), ts1(T.imk[:], T.ibf[:], cf[:, 14:15], A.mult), ts1(T.ic3[:], T.ibf[:], 3 * 2.0 ** 20, A.mult)]
       + [ts1(T.pri[:, k], T.ibf[:], x * UP, A.mult) for k, x in ((0, 2), (1, 4), (3, 1))], r=["ibf"], w=["k1"])
    op("P", mm(T.pd[0:8, 10:11], T.tm[:, 0:8], T.onen[:, 0:1]), r=["kw", "ones"], w=["t8"], banks=["pd"])
    op("S", act(cf[0:8, 28:29], T.pd[0:8, 10:11], F.Identity, bias=0.5), r=["t8"], w=["k5"], banks=["pd"])
    op("S", lin(cf[:, 11:12], cf[:, 12:13], 1.0, -UP), r=["k0"], w=["k6"])


    def zslot(t):
        return T.zl[:, 128 * t:128 * t + 128]

    ZR = ["zr%d" % k for k in range(31)]
    zdone = [0] * RO

    def spread_z(t, qn, n):
        rows = range(zdone[t], zdone[t] + n)
        op(qn, [copy(qn, T.zrep[:, 1 + x:4096:32], zslot(t)) for x in rows], r=["Lz%d" % t], w=[ZR[x] for x in rows])
        zdone[t] += n

    KEYS = ("pu", "pw")

    def base(role, first=None):
        src, dst, col = (T.fi, T.basF, 5) if role == "F" else (T.si if first is None else first, T.basS, 6)
        if role == "S":
            op("V", ts1(dst[:], src[:], cf[:, col:col + 1], A.add), r=["iSa", "iSb", "LS0", "kc"], w=["basS"])
            for h, bk in enumerate(KEYS):
                op("P", [mm(T[bk][:, 256:384], T.mh[0:8, :], T.ww[0:8, 16:144], True, False)]
                   + [mm(T[bk][32 * j:32 * j + 32, 257:384:2], dst[:, j:128:4], T.idf[:, 64 * h:64 * h + 64], False, False) for j in range(4)],
                   r=["basS", "k1", "kw"], w=["key%d" % h], banks=[bk])
            return
        op("V", ts1(dst[:], src[:].indirect(T.pip[:]), cf[:, col:col + 1], A.add), r=["i" + role + "a", "i" + role + "b", "pip", "kb", "kc"], w=["bas" + role])

    def turn():
        for h, bk in enumerate(KEYS):
            op("P", mm(T[bk][:, 256:384:2], T.basF[:], T.idf[:, 64 * h:64 * h + 64], False, False), r=["basF", "k1"], w=["key%d" % h], banks=[bk], acc=True)

    spread_z(0, "G", 6)
    op("G", [where(T.gp16[0:8, :], T.ones[0:8, :], [[-1, 8], [0, 16]], A.is_equal), count(T.j8[:], [[1, 4], [0, 16]])], w=["g16"])
    op("G", where(T.tri[:], T.tri[:], [[-32, 4], [0, 32]], A.is_ge), w=["tri"])
    op("G", [count(T.jb[:], [[1, 128]]), count(T.jp[:], [[1, 4], [4, 32]])], w=["jp"])
    op("V", [tcopy(T.p0[:], T.pbp[:])] + [ts1(o, T.pbp[:], x, A.mult) for o, x in (
        (T.prin[:], -UP), (T.pb21[:], UP), (T.pri[:, 2], -8192.0), (ce(c130), 130 * 8192.0), (ce(c65), -65 * 8192.0))], r=["pbp"], w=["k2"])
    spread_z(0, "V", 8)
    base(FIRST, T.off0S)
    op("V", tcopy(T.fi[:], T.off0F[:]), r=["LF0"], w=["iFa", "iFb"])
    spread_z(0, "V", 17)

    E = T.top[:, PAD + 31:PAD + 4096:32]
    tops = ["top" + x[1:] for x in sorted(SEQ[1].split()) if x[0] == "s"]
    gains = ["gain" + k for k in tops]
    early = len([k for k in tops if int(k[3]) < LB // 4])
    PARTS = (("a", 0, 32), ("b", 32, 128))

    def minmax(lo, hi, a, b):
        return [tt(lo, a, b, A.min), tt(hi, a, b, A.max)]

    def step(s, x, o):
        n1, n3, n4, n6, n7, nb, n8, n9, na = T.n1, T.n3, T.n4, T.n6, T.n7, T.nb, T.n8, T.n9, T.na
        gs, a, b = slice(4 * x, 4 * x + 4), o + 64 * x, o + 64 * x + 64
        bs, hs, km, ps = slice(32 * x, 32 * x + 32), slice(8 * x, 8 * x + 8), T.km, T[KEYS[x]]
        fns = [
            lambda: [ts1(km[:, bs], T.ki[:, 128 * x:128 * x + 128], (1 << 21) - 1, A.bitwise_and)],
            lambda: minmax(n1[:, bs, :, 0], n1[:, bs, :, 1], km[:, bs, :, 0], km[:, bs, :, 1]),
            lambda: minmax(n3[:, hs, :, :, 1:6:4], n3[:, hs, :, :, 0:5:4], n1[:, bs, 0], n1[:, bs, 1]),
            lambda: minmax(n3[:, hs, :, :, 3], n3[:, hs, :, :, 2], n3[:, hs, :, :, 5], n3[:, hs, :, :, 0]),
            lambda: minmax(n4[:, 16 * x:16 * x + 8], n4[:, 16 * x + 8:16 * x + 16], n3[:, hs, :, 0, 1:5], n3[:, hs, :, 1, 1:5]),
            lambda: minmax(n6[:, x, 4:12, 0:8:7], n6[:, x, 0:8, 3:5], n4[:, 16 * x:16 * x + 16, 0], n4[:, 16 * x:16 * x + 16, 1]),
            lambda: minmax(n6[:, x, 4:8, 1:7:5], n6[:, x, 4:8, 2:6:3], n6[:, x, 8:12, 0:8:7], n6[:, x, 0:4, 3:5]),
            lambda: [tt(n7[:, gs], n6[:, x, 4:8, 0:4], n6[:, x, 4:8, 4:8], A.min)],
            lambda: [ts1(nb[:, gs], n7[:, gs], (1 << 19) - 1, A.bitwise_and)],
            lambda: minmax(n8[:, gs, 0], n8[:, gs, 1], nb[:, gs, 0], nb[:, gs, 1]),
            lambda: minmax(n9[:, gs, :, 0], n9[:, gs, :, 1], n8[:, gs, :, 0], n8[:, gs, :, 1]),
            lambda: minmax(na[:, gs, :, :, 0], na[:, gs, :, :, 1], n9[:, gs, :, :, 0:4:2], n9[:, gs, :, :, 1:4:2]),
            lambda: minmax(T.dd[:, a:b:2], T.dd[:, a + 1:b:2], na[:, gs, :, 0], na[:, gs, :, 1]),
        ][s]()
        op("V", fns, r=["o%d_%d" % (s - 1, x)], w=["o%d_%d" % (s, x)])

    def minus_threshold():
        op("P", mm(T.pg[:, 0:8 * LB], T.onen[:], T.tm[:, 0:8 * LB], True, False), r=["tm", "ones"], w=gains[:early], banks=["pg"])
        op("P", mm(T.ph[:, 8 * LB:256], T.onen[:], T.tm[:, 8 * LB:256], True, False), r=["tm", "ones"], w=gains[early:], banks=["ph"])

    minus_threshold()
    op("P", [mm(T.pd[32 * j:32 * j + 32, 0:128], T.hi0[:, j:128:4], T.jk[:, 0:128]) for j in range(4)], r=["kb", "jk"], w=["h0"], banks=["pd"])

    def order(r, rb, c, key, name, row=T.jb, scale=2.0 ** 21):
        op("V", ts2(rb[:], row[:], c, scale, A.is_equal, A.mult), r=[key, "jp"], w=[name + "b"])
        op("S", act(r[:], rb[:], F.Sign), r=[name + "b"], w=[name])

    def fallback(ps, bk, s2, ks, r, rb, kr, old, ko, sg, src, kd, name):
        op("S", act(sg, old, F.Sign), r=[ko], w=["sg" + name])
        return [lambda: op("P", [mm(ps, s2, rb[:], True, False), mm(ps, T.ic3[:], sg, False, False)], r=[ks, kr, "sg" + name, "k2"], w=[name], banks=[bk]),
                lambda: op("P", mm(ps, src, r[:], False, True), r=kd + [kr], w=[name], banks=[bk], acc=True)]

    def upper_out(t):
        o0, sl = 256 * t, slice(128 * t, 128 * t + 128)
        rot, rotb, dhi = (T.rh[:], T.rhb[:], T.dd[:, 384:512]) if t else (T.idf[:], T.pri[:, 3], T.dd[:, 128:256])
        op("P", [mm(T.pd[:, 0:128], T.pri[:, t], T.s1[:, sl], True, False), mm(T.pd[:, 0:128], T.idf[:], dhi, False, True),
                 mm(T.pd[:, 128:256], rotb, T.s2[:, sl], True, False), mm(T.pd[:, 128:256], rot, dhi, False, True)],
           r=["up0", "up1", "k1", "rh", "rhb"], w=["phi"], banks=["pd"])
        op("S", act(T.oh[:, o0:o0 + 256], T.pd[:, 0:256], F.Copy), r=["phi"], w=["oh"], banks=["pd"])
        send([(q - t - 1, T.oh[:, o0:o0 + 128], T.lH1[:, sl], "Ha%d" % t)], ["oh"])
        send([(q + 1, T.oh[:, o0 + 128:o0 + 256], T.lH2[:, sl], "Hb%d" % t)], ["oh"])

    def keep(t, k):
        if k == 0:
            op("V", tt(T.jk[:], T.lH1[:, 128 * t:128 * t + 128], T.lH2[:, 128 * t:128 * t + 128], A.max), r=["LHa%d" % t, "LHb%d" % t], w=["jk"])
        else:
            op("V", tt(T.mF[:] if t else T.hacc[:], T.jk[:], T.hacc[:], A.max), r=["jk", "iFa", "iFb"], w=["hacc"])

    for t in range(RO):
        d = t + 1
        last = t == RO - 1
        offs = {"F": T.off0F if t == 0 else T.offF, "S": T.off0S if t == 0 else T.offS}
        psF = {"a": (T.pu[:, 0:32], "pu"), "b": (T.pw[:, 128:224], "pw")}
        psS = {"a": (T.pt[:, 256:288], "pt"), "b": (T.pb[:, 128:224], "pb")}
        if FIRST == "S":
            psF, psS = psS, psF

        def merge(role, x):
            kind, part = x
            a, b = (0, 32) if part == "a" else (32, 128)
            (ps, bk), m, c, i, o = (psF[part], T.mF, T.cF, T.fi, T.offF) if role == "F" else (psS[part], T.mS, T.cS, T.si, T.offS)
            if kind == "m":
                op("V", tt(m[:, a:b], ps, c[:, a:b], A.max), r=["A" + role + part, "c" + role], w=["m" + role + part], banks=[bk])
            elif kind == "a":
                op("V", ts1(i[:, a:b], m[:, a:b], 8191, A.bitwise_and), r=["m" + role + part], w=["i" + role + part])
            else:
                op("V", tcopy(o[:, a:b], i[:, a:b]), r=["i" + role + part], w=["off" + role + part])

        def gather(qn, x):
            role, c, e = x[0], int(x[1], 16), int(x[-1], 16) + 1
            op(qn, copy(qn, T.xg[:, 256 * c + (role == "S"):256 * e:2], T.X[:].indirect(offs[role][:, 8 * c:8 * e])),
               r=["X"] + ["X%d" % k for k in range(len(XP) - 1)] + (["L%s0" % role] if t == 0 else ["off" + role + "ab"[k > 3] for k in range(c, e)]),
               w=["x%s%d%s" % (role, k // 2, "ab"[k % 2]) for k in range(c, e)])

        def scan(c, part=""):
            a, b, src = {"": (0, 16, "ab"), "a": (0, 8, "a"), "b": (8, 16, "b"), "c": (8, 12, "b"), "d": (12, 16, "b")}[part]
            a, b = a + 16 * c, b + 16 * c
            key = "top%d%s" % (c, part)
            op("V", lambda: V.tensor_tensor_scan(T.top[:, PAD + 32 * a:PAD + 32 * b], T.xg[:, 32 * a:32 * b], T.zrep[:, 32 * a:32 * b], 0.0, A.max, A.min),
               r=["x%s%d%s" % (x, c, y) for x in "FS" for y in src] + ZR + ["zf%d" % c], w=[key])
            fns, bk = [], "pg" if a < 4 * LB else "ph"
            for ib in range(a // 4, b // 4):
                c0, gs = PAD + 128 * ib, slice(8 * ib, 8 * ib + 8)
                fns += [mm(T[bk][:, gs], T.top[:, c0:c0 + 128], T.gp[:], False, False),
                        mm(T[bk][:, gs], T.top[:, c0 - 1:c0 + 127], T.gn[:], False, ib in (LB - 1, 31))]
            k = tops.index(key)
            op("P", fns, r=[key, tops[k - 1] if k else "pad", "kb"], w=["gain" + key], banks=[bk])

        def fix(c, e):
            op("V", tt(T.zrep[:, 512 * c:512 * e:32], T.xg[:, 512 * c:512 * e:32], T.zl[:, 128 * t + 16 * c:128 * t + 16 * e], A.min),
               r=["xF%d%s" % (k, x) for k in range(c, e) for x in "ab"] + ["Lz%d" % t], w=["zf%d" % k for k in range(c, e)])

        def row0():
            op("P", [mm(T.pb[0:8, 384 + 32 * j:416 + 32 * j], T.gp[:], T.zrep[:, 32 * j:4096:128]) for j in range(4)],
               r=["zf%d" % k for k in range(8)] + ["kb"], w=["s0"], banks=["pb"])
            op("S", act(T.c0[0:8, :], T.pb[0:8, 384:512], F.Sign, bias=cf[0:8, 28:29]), r=["s0", "k5"], w=["c0"], banks=["pb"])

        seqS, seqV = SEQ0 if t == 0 else SEQ
        for x in seqV.split():
            if x[0] in "mao":
                merge("F" if FIRST == "S" else "S", x)
            elif x == "M":
                op("V", tt(T.cF[:], T.pc[:, 128:256], T.lA1[:, 128 * t - 128:128 * t], A.max), r=["BF", "LAa%d" % t], w=["cF"], banks=["pc"])
            elif x in "AZ":
                for y in seqS.split("|")[x == "Z"].split():
                    gather("S", y)
            elif x in "bB":
                base("SF"[x == "B"])
            elif x[0] == "s":
                scan(int(x[1]), x[2:])
            elif x[0] == "f":
                fix(int(x[1]), int(x[-1]) + 1)
            elif x == "r":
                row0()
            elif x == "c":
                op("V", ts2(T.u3[:, 0:8 * LB], T.pg[:, 0:8 * LB], 0.0, cf[:, 21:22], A.is_lt, A.mult), r=gains[:early], w=["u3a"], banks=["pg"])
            elif x[0] == "z":
                spread_z(t, x[1], int(x[2:]))
            else:
                gather("V", x)
        turn()
        op("P", mm(T.pt[:, 384:392], E, T.wgr[:]), r=tops + ["kw"], w=["v2"], banks=["pt"])

        if t == 0:
            op("S", act(T.hacc[:], T.pd[:, 0:128], F.Copy), r=["h0"], w=["hacc"], banks=["pd"])

        def users():
            op("P", [mm(T.pc[:, 0:128], T.ibf[:], zslot(t), True, False), mm(T.pc[:, 0:128], T.ibf[:], E, False, True)],
               r=tops + ["Lz%d" % t, "ibf"], w=["ze"], banks=["pc"])
            nz = T.nzf[:] if last else T.nzb[:, 128 * t:128 * t + 128]
            op("S", act(nz, T.pc[:, 0:128], F.Abs, bias=255.0, scale=-1.0), r=["ze"], w=["nz%d" % t], banks=["pc"])
            if last:
                send([(q - d, nz, T.zfin[:], "zf")], ["nz%d" % t])
            else:
                send([(q + 1, nz, zslot(t + 1), "z%d" % (t + 1))], ["nz%d" % t])

        l0, o0 = 16 * t, 256 * t
        sl = slice(128 * t, 128 * t + 128)
        col, tot = T.col[:, 4 * t:4 * t + 4], T.tot[:, t:t + 1]
        a3, dlo, dhi = T.o1[:, sl], T.dd[:, o0:o0 + 128], T.dd[:, o0 + 128:o0 + 256]

        def clicks():
            op("V", ts2(T.u3[:, 8 * LB:256], T.ph[:, 8 * LB:256], 0.0, cf[:, 21:22], A.is_lt, A.mult), r=gains[early:], w=["u3b"], banks=["ph"])
            if t == 0:
                op("V", ts2(T.sgj[:], T.j8[:], cf[:, 4:5], cf[:, 18:19], A.is_equal, A.mult), r=["g16", "ka"], w=["k3"])
            for h, bk in enumerate(KEYS):
                op("P", mm(T[bk][:, 256:384], T.c0[0:8, :], T.kc0[0:8, 4 * h:4 * h + 4], False, False), r=["c0", "k4"], w=["key%d" % h], banks=[bk], acc=True)
            for h, bk in enumerate(KEYS):
                op("P", [mm(T[bk][32 * j:32 * j + 32, 256 + 32 * x:288 + 32 * x], T.u3[:, 4 * h + x:256:8], T.tri[:, 32 * j:32 * j + 32], False, x == 3)
                         for x in range(4) for j in range(4)], r=["u3a", "u3b", "tri"], w=["key%d" % h], banks=[bk], acc=True)
            users()
            if not last:
                op("P", [mm(T.pg[:, 256:512], T.ones[:], T.u3[:], True, False), mm(T.pg[:, 256:384], T.mh[0:8, :], T.c0[0:8, :], False, True)],
                   r=["u3a", "u3b", "c0", "ones"], w=["sum"], banks=["pg"])
                op("S", act(T.junk[:], T.pg[:, 256:512], F.Identity, accum_out=tot), r=["sum"], w=["tot"], banks=["pg"])
            op("P", [mm(T.pd[:, 384:512], T.c0[0:8, :], T.gp16[0:8, :], True, False)]
               + [mm(T.pd[32 * j:32 * j + 32, 384 + 16 * x:400 + 16 * x], T.u3[:, x:256:8], T.sgj[:, 16 * j:16 * j + 16], False, x == 7)
                  for x in range(8) for j in range(4)], r=["u3a", "u3b", "c0", "k3", "g16"], w=["ab"], banks=["pd"])
            op("S", [act(T.s1[:, sl], T.pd[:, 384:512], F.Sign, scale=-1.0), act(T.s2[:, sl], T.pd[:, 384:512], F.Sign, bias=-2.0)],
               r=["ab"], w=["s1", "s2"], banks=["pd"])
            send([(q + 1 if last else q + d + 2, T.s2[:, sl], T.lT[:, sl], "T%d" % d)], ["s2"])
            if last:
                send([(q - d, T.s1[:, sl], T.lT[:, 384:512], "TL")], ["s1"])
            op("P", [mm(T.pb[:, j:128:4], T.imk[:], T.basF[:, 32 * j:32 * j + 32], j == 0, False) for j in range(4)], r=["basF", "k1"], w=["ht"], banks=["pb"])
            op("P", mm(T.pb[:, 0:128], T.s1[:, sl], T.prin[:], False, False), r=["s1", "k2"], w=["ht"], banks=["pb"], acc=True)
            if last:
                op("P", [mm(T.pg[:, 0:128], T.mh[0:8, :], T.ce[0:8, 0:128], True, False), mm(T.pg[:, 0:128], T.pri[:, 3], T.s1[:, sl], False, True)],
                   r=["s1", "k1", "kcl"], w=["sk"], banks=["pg"])

        def old_list():
            if last:
                op("V", tcopy(T.hpad[:, 15:128:16], T.hc[:]), r=["hc"], w=["hpad"])
            else:
                op("V", tt(T.hpad[:, 15:128:16], T.hc[:], T.hb[:], A.add), r=["hc", "hb"], w=["hpad"])
            op("P", mm(T.pb[:, 0:128], T.hpad[:], T.idf[:], False, True), r=["hpad", "k1"], w=["ht"], banks=["pb"], acc=True)
            op("S", act(a3, T.pb[:, 0:128], F.Identity, bias=cf[:, 11:12] if last else cf[:, 12:13]), r=["ht", "k0", "k6"], w=["a3"], banks=["pb"])
            if last:
                send([(q - d, a3, T.lAE[:], "AE")], ["a3"])
            else:
                send([(q - d - 1, a3, T.lA2[:, sl], "Ab%d" % d)], ["a3"])
                send([(q + 1, a3, T.lA1[:, sl], "Aa%d" % d)], ["a3"])
                op("P", [mm(T.pt[:, 392:400], T.ww[:, 15 - c:143 - c], T.top[:, PAD + 32 * c + 31:PAD + 4096:512], c == 0, c == 15)
                         for c in range(16)], r=tops + ["kw"], w=["vd"], banks=["pt"])


        def far_order():
            if t:
                order(*((T.r1, T.r1b, T.lc[:, 4:5], "LcE", "r4", T.jb, 65 * 8192.0) if last else (T.r3, T.r3b, T.lc[:, 0:1], "LcF", "r3")))

        def upper(x):
            op("V", tt(T.dd[:, o0 + 128 + 64 * x:o0 + 192 + 64 * x], T.n6[:, x, 4:8, 0:4], T.n6[:, x, 4:8, 4:8], A.max), r=["o5_%d" % x, "o6_%d" % x], w=["up%d" % x])
            if last and x:
                send([(q + 1, dhi, T.lE2[:, 128:256], "Ub")], ["up0", "up1"])

        def lost(x):
            c = slice(64 * x, 64 * x + 64)
            op("V", tt(T.ua[:, c], T.pg[:, c], T.dd[:, o0 + 128 + 64 * x:o0 + 192 + 64 * x], A.add), r=["sk", "up%d" % x], w=["ua%d" % x], banks=["pg"])
            if x:
                send([(q - d, T.ua[:], T.lE1[:, 128:256], "Ua")], ["ua0", "ua1"])

        def sink():
            T3, TL = T.lT[:, 256:384], T.lT[:, 384:512]
            op("S", [lin(ce(nT), TL, -1.0, -1.0), lin(ce(pT), TL, 1.0, 2.0), lin(ce(rneg), T.r1[:], -8192.0)], r=["LTL", "r4"], w=["nT"])
            op("S", lin(ce(nT3), T3, -1.0, -1.0), r=["LT3"], w=["nT3"])
            op("P", [mm(T.ph[:, 0:128], T.pri[:, 3], ce(pT), True, False), mm(T.ph[:, 0:128], T.rhb[:], T3, False, True)], r=["rh", "LT3", "nT"], w=["sc"], banks=["ph"])
            for x, bk in enumerate(("pc", "pd")):
                c = slice(64 * x, 64 * x + 64)
                op("P", [mm(T[bk][:, 0:64], T.rhb[:], T.lT[:, 256 + 64 * x:320 + 64 * x], True, False), mm(T[bk][:, 0:64], T.pri[:, 3], ce(nT + 64 * x, 64), False, False),
                         mm(T[bk][:, 0:64], T.mh[0:8, :], T.ce[0:8, c], False, False)], r=["rh", "LT3", "nT"], w=["U%d" % x], banks=[bk])
            op("P", [mm(T.pt[:, 0:128], T3, T.r1b[:], True, False), mm(T.pt[:, 0:128], TL, ce(c65), False, False)], r=["r4", "k2"], w=["B"], banks=["pt"])
            for x, bk in enumerate(KEYS):
                op("P", mm(T[bk][:, 128:192], TL, ce(c130 + 64 * x, 64), True, False), r=["LTL", "k2"], w=["A%d" % x], banks=[bk])
            for x, bk in enumerate(("pc", "pd")):
                op("P", mm(T[bk][:, 0:64], T.rh[:], T.lE2[:, 128 + 64 * x:192 + 64 * x], False, True), r=["LUb"], w=["U%d" % x], banks=[bk], acc=True)

        def beaten(x):
            c, bk = slice(64 * x, 64 * x + 64), ("pc", "pd")[x]
            op("V", tt(T.hx[:, c], T[bk][:, 0:64], T.cS[:, c], A.max), r=["U%d" % x, "cS"], w=["hx%d" % x], banks=[bk])

        side = {
            "ha": lambda: op("V", tcopy(T.ha[:], T.pt[:, 384:392]), r=["v2"], w=["ha"], banks=["pt"]),
            "hb": lambda: op("V", ts1(T.hb[:], T.ha[:], 4095, A.bitwise_and), r=["ha"], w=["hb"]),
            "hh": lambda: op("V", tt(T.ha[:], T.hb[:], T.hb[:], A.mult), r=["hb"], w=["ha"]),
            "hc": lambda: op("V", ts2(T.hc[:], T.ha[:], 4, 8191, A.arith_shift_right, A.bitwise_and), r=["ha"], w=["hc"]),
            "hp": old_list, "far": far_order, "p0": lambda: upper(0), "p1": lambda: upper(1), "j0": lambda: t and keep(t - 1, 0), "j1": lambda: t and keep(t - 1, 1), "j2": sink,
            "j3": lambda: op("V", tt(T.cS[:], T.mS[:], T.ph[:, 0:128], A.subtract), r=["sc", "kept"], w=["cS"], banks=["ph"]),
            "j4": lambda: op("V", ts1(T.mS[:], T.mF[:], (1 << 19) - 1, A.bitwise_and), r=["hacc"], w=["kept"]),
            "q0": lambda: lost(0), "q1": lambda: lost(1),
            "hd": lambda: op("V", tt(T.ha[:], T.hc[:], T.hb[:], A.add), r=["hc", "hb"], w=["ha"]),
            "he": lambda: op("V", ts1(T.hc[:], T.ha[:], 8191, A.bitwise_and), r=["ha"], w=["hc"]),
            "tl": lambda: op("V", ts1(T.tl[:, 0:10], T.jq[:, 0:10], tot, A.subtract), r=["tot", "kd"], w=["tl"]),
            "tk": lambda: op("V", [ts1(T.tl[:, 10:12 - t], T.jq[:, 10:12 - t], tot, A.add)]
                             + [ts2(T.tl[:, 11:12], T.jq[:, 11:12], tot, T.tot[:, 0:1], A.add, A.subtract)] * t, r=["tot", "kd"], w=["tk"]),
            "tm": lambda: op("V", ts1(T.tl2[:], T.tl[:], 127, A.bitwise_and), r=["tl", "tk"], w=["tl2"]),
            "tn": lambda: op("V", [tcopy(col, T.tl2[:, 8:12]), tcopy(T.lst[:, l0:l0 + 8], T.tl2[:, 0:8])], r=["tl2"], w=["lst%d" % t]),
            "r2": lambda: order(T.r2, T.r2b, T.col[:, 4 * t + 3:4 * t + 4], "lst%d" % t, "r2"),
            "r1": lambda: t and order(T.r1, T.r1b, T.col[:, 4 * t + 2:4 * t + 3], "lst%d" % t, "r1"),
            "rh": lambda: t and order(T.rh, T.rhb, T.lc[:, 4:5] if last else T.col[:, 0:1], "LcE" if last else "lst0", "rh", T.jp, UP if last else 3 * UP),
            "pa": lambda: op("V", tcopy(T.pa_[:], T.pt[:, 392:400]), r=["vd"], w=["pa_"], banks=["pt"]),
            "pb": lambda: op("V", ts1(T.pb_[:], T.pa_[:], 63, A.bitwise_and), r=["pa_"], w=["pb_"]),
            "pc": lambda: op("V", tt(T.pc_[:], T.pb_[:], T.plb[:], A.add), r=["pb_", "kb"], w=["pc_"]),
            "pl": lambda: op("V", tcopy(T.pl[:], T.pc_[:]), r=["pc_"], w=["pl"]),
            "X": lambda: op("V", tcopy(T.X[:].indirect(T.pl[:]), E), r=["pl"] + tops, w=["X"]),
            "H": lambda: upper_out(t),
            "u0": lambda: beaten(0), "u1": lambda: beaten(1),
            "cS": lambda: op("V", tt(T.cS[:], T.pt[:, 0:128], T.hx[:], A.max), r=["BS", "hx"], w=["cS"], banks=["pt"]),
        }
        for x in (LAST if last else NET).split():
            if x in side:
                side[x]()
            elif x[0] == "z":
                spread_z(d, x[1], int(x[2:]))
            elif x == "B":
                base("F")
            elif x == "C":
                clicks()
            elif x[0] == "k":
                h = int(x[1])
                op("V", tcopy(T.ki[:, 128 * h:128 * h + 128], T[KEYS[h]][:, 256:384]), r=["key%d" % h], w=["o-1_%d" % h], banks=[KEYS[h]])
            else:
                step(int(x[0], 16), int(x[1]), o0)
        lo = ["o12_0", "o12_1"]
        if last:
            send([(q + 1, dlo, T.lE2[:, 0:128], "Eb")], lo)
            send([(q - d, dlo, T.lE1[:, 0:128], "Ea")], lo)
            break

        lists = [(q - d - 1, dlo, T.lS[:, sl], "S%d" % d), (q + d + 2, dlo, T.lF2[:, sl], "Fb%d" % d), (q + 1, dlo, T.lF1[:, sl], "Fa%d" % d)]
        if "Fa1" in RELAYED:
            send([lists[0], lists[2]], lo)
            send([lists[1]], lo)
        else:
            for x in lists:
                send([x], lo)
        send([(q + 1, col, T.lc[:, 4:8], "cE") if t else (q + 4, col, T.lc[:, 0:4], "cF")], ["lst%d" % t])

        minus_threshold()
        rF, rFb, kF = (T.r3, T.r3b, "r3") if t else (T.p0, T.pb21, "k2")
        r1, k1 = (T.r1, "r1") if t else (T.r2, "r2")
        addF = []
        for x in HOP.split():
            if x in side:
                side[x]()
            elif x[0] == "z":
                spread_z(d, x[1], int(x[2:]))
            elif x == "gS":
                op("S", act(T.hx[:], T.lA2[:, sl].indirect(T.lst[:, l0:l0 + 8]), F.Copy), r=["LAb%d" % d, "lst%d" % t], w=["hx"])
                for fn in fallback(T.pt[:, 0:128], "pt", T.s2[:, sl], "s2", T.r2, T.r2b, "r2", T.hx[:], "hx", T.sgS[:], dlo, lo, "BS"):
                    fn()
            elif x == "gF":
                addF += fallback(T.pc[:, 128:256], "pc", T.lT[:, sl], "LT%d" % d, rF, rFb, kF, T.lA1[:, sl], "LAa%d" % d, T.sgF[:], T.lF2[:, sl],
                                 ["LFb%d" % d], "BF")
            elif x == "M":
                op("V", tt(T.cF[:], T.pc[:, 128:256], T.lA1[:, sl], A.max), r=["BF", "LAa%d" % d], w=["cF"], banks=["pc"])
            elif x == "PS":
                for y, a, b in PARTS:
                    op("P", mm(psS[y][0], T.lS[:, sl], r1[:, a:b]), r=["LS%d" % d, k1], w=["AS" + y], banks=[psS[y][1]])
            elif x == "PF":
                for fn in addF:
                    fn()
                for y, a, b in PARTS:
                    op("P", mm(psF[y][0], T.lF1[:, sl], T.p0[:, a:b]), r=["LFa%d" % d, "k2"], w=["AF" + y], banks=[psF[y][1]])
            else:
                merge(FIRST, x)

    wait("Y", [lastw["Lzf"], lastw["LEa"]])
    op("Y", lambda: Y.dma_start(T.yz[:], T.zfin[:]), w=["yz"], inc=16)
    op("P", [mm(T.pb[:, 0:128], T.idf[:], T.lAE[:], True, False), mm(T.pb[:, 0:128], ce(nT3), T.r1b[:], False, True)], r=["LAE", "nT3", "r4"], w=["C"], banks=["pb"])
    op("S", act(T.cF[:], T.pb[:, 0:128], F.Copy), r=["C"], w=["cF"], banks=["pb"])
    op("S", lin(T.sgS[:], T.lE2[:, 0:128], 2.0 ** -13, cf[:, 27:28]), r=["LEb"], w=["hiB"])
    op("P", mm(T.pt[:, 0:128], T.lE2[:, 0:128], T.r1[:], False, False), r=["LEb"], w=["B"], banks=["pt"], acc=True)
    op("P", mm(T.pt[:, 0:128], T.sgS[:], ce(rneg), False, True), r=["hiB", "nT"], w=["B"], banks=["pt"], acc=True)
    halves = [(k, slice(64 * k, 64 * k + 64), ("pb", "ph")[k]) for k in (0, 1)]
    for x in END.split():
        k, c, bk = halves[int(x[1])]
        if x[0] == "u":
            op("V", tt(T.nb[:, 4 * k:4 * k + 4], T.lE1[:, 128 + 64 * k:192 + 64 * k], T.hx[:, c], A.max), r=["LUa", "hx%d" % k], w=["o8_%d" % k])
        elif x[0] == "f":
            op("V", tt(T.fb[:, c], T.pt[:, c], T.cF[:, c], A.max), r=["B", "cF"], w=["fb%d" % k], banks=["pt"])
        elif x[0] == "h":
            op("V", ts2(T.hiA[:], T.lE1[:, 0:128], 2.0 ** -13, 129.5 + 2.0 ** -14, A.mult, A.add), r=["LEa"], w=["hiA"])
            for k, c, bk in halves:
                op("P", mm(T[KEYS[k]][:, 128:192], T.lE1[:, 0:128], T.p0[:, c], False, False), r=["LEa"], w=["A%d" % k], banks=[KEYS[k]], acc=True)
            for k, c, bk in halves:
                op("P", mm(T[bk][:, 0:64], T.dd[:, 128:256], T.p0[:, c], True, False), r=lo + ["k2"], w=["H%d" % k], banks=[bk])
            for k, c, bk in halves:
                op("P", mm(T[KEYS[k]][:, 128:192], T.hiA[:], T.pri[:, 2, c], False, True), r=["hiA"], w=["A%d" % k], banks=[KEYS[k]], acc=True)
        elif x[0] == "g":
            op("V", ts2(T.sgF[:, c], T.dd[:, 128 + 64 * k:192 + 64 * k], 2.0 ** -13, 129.5 + 2.0 ** -14, A.mult, A.add), r=["o12_" + x[1]], w=["f" + x[1]])
            if k:
                for k, c, bk in halves:
                    op("P", mm(T[bk][:, 0:64], T.sgF[:], T.pri[:, 2, c], False, True), r=["f0", "f1"], w=["H%d" % k], banks=[bk], acc=True)
        elif x[0] == "y":
            op("V", ts1(T.yo[:, 128 * k + 1:128 * k + 128:2], T[bk][:, 0:64], 130 * 8192.0, A.add), r=["H%d" % k], w=["yo%d" % k], banks=[bk])
        elif x[0] == "m":
            op("V", tt(T.yo[:, 128 * k:128 * k + 128:2], T[KEYS[k]][:, 128:192], T.fb[:, c], A.max), r=["A%d" % k, "fb%d" % k], w=["l2%d" % k], banks=[KEYS[k]])
        elif x[0] == "s":
            op("SY"[k], lambda: (S, Y)[k].dma_start(T.ya[:, 128 * k:128 * k + 128], T.yo[:, 128 * k:128 * k + 128]),
               r=["yo%d" % k, "l2%d" % k], w=["ya%d" % k], inc=16)
        else:
            step(int(x[0], 16), k, 128)

    for s in cnt:
        if s[0] != "Y" and waited.get(s, 0) < cnt[s]:
            g.wait_ge(T.sem[s], cnt[s])
    for s in cnt:
        if s[0] == "Y" and waited.get(s, 0) < cnt[s]:
            Y.wait_ge(T.sem[s], cnt[s])
